import numpy as np, ml_dtypes
CORES = [9,25,41,57]
N = 4
BF = ml_dtypes.bfloat16
S, J, RO = 512, 1, 3
SH, HALF, QLO, QHI = 12, 2048, 1024, 3072
B0, B1, B2, W = 4, 4, 4, 4096
def pack(pos, pf, rf, th, lv):
    turn = lambda a: np.ascontiguousarray(a.transpose(0, 1, 3, 2)).astype(np.float32).astype(BF)
    return {"pos": turn(pos).reshape(N, 24, S), "pf": turn(pf).reshape(N, 128, S), "rf": turn(rf).reshape(N, 128, W),
            "th": np.ascontiguousarray(th.reshape(N, 128, 1)).astype(np.int32), "lv": np.ascontiguousarray(lv.reshape(N, 8, S)).astype(np.int32)}
def parts(rng):
    pos = rng.integers(-31, 32, (N, 8, S, 3)); pf = rng.integers(0, 16, (N, 8, S, 16)); rf = rng.integers(-15, 16, (N, 8, W, 16)); th = rng.integers(0, 301, (N, 8, 16))
    share = rng.choice(np.array([0.8, 0.9, 1.0]), (N, 8, 1))
    return pos, pf, rf, th, (rng.random((N, 8, S)) < share).astype(np.int64)
def setup_inputs(rng):
    pos, pf, rf, th, lv = parts(rng); g = int(rng.integers(0, 8))
    lv[:, g] = rng.random((N, S)) < 0.07
    return pack(pos, pf, rf, th, lv)
def setup_inputs_spread(rng):
    pos, pf, rf, th, lv = parts(rng)
    pos = np.rint(rng.choice(np.array([2, 6, 13, 22, 31, 31, 31, 31]), (N, 8, S, 1)) * (2 * rng.random(pos.shape) - 1)).astype(np.int64)
    pf = np.minimum(np.floor(16 * rng.random(pf.shape) ** rng.choice(np.array([0.25, 1.0, 4.0]), (N, 8, S, 1))), 15).astype(np.int64)
    c = rng.choice(np.array([0, 1, 4, 15]), (N, 8, W, 1)); rf = np.clip(rf, -c, c)
    th = np.clip(np.where(rng.random(th.shape) < 0.5, -1, 1) * np.exp2(12 * rng.random(th.shape)).astype(np.int64), -3600, 3600)
    return pack(pos, pf, rf, th, lv)
def setup_inputs_ends(rng):
    pos = 31 * (2 * rng.integers(0, 2, (N, 8, S, 3)) - 1)
    loose = rng.random((N, 8, S, 1)) < 0.25; loose[:, 7] = False
    pos = np.where(loose, rng.integers(-31, 32, pos.shape), pos)
    u = rng.random((N, 8, S, 1)); pf = np.where(u < 0.45, 15, np.where(u < 0.6, 0, 15 * rng.integers(0, 2, (N, 8, S, 16))))
    u = rng.random((N, 8, W, 1)); c = rng.choice(np.array([0.15, 0.25, 0.35]), (N, 8, 1, 1))
    rf = np.where(u < c, 15, np.where(u > 0.75, -15, 30 * rng.integers(0, 2, (N, 8, W, 16)) - 15))
    lv = (rng.random((N, 8, S)) < 0.85).astype(np.int64); lv[:, 7] = 1; lv[:, :, S - 1] = 1
    th = np.full((N, 8, 16), 3600, np.int64); e = int(rng.integers(0, 7))
    th[:, e] = np.where(rng.random((N, 16)) < 0.5, -3600, 3600); th[:, 7, 15] = -3600; th[:, 7, int(rng.integers(0, 7)) * 2] = -3600
    for a in range(N):
        for g in range(8):
            on = np.flatnonzero(lv[a, g])[45:48]; pos[a, g, on] = 31 * np.array([[1, 1, -1], [1, -1, 1], [-1, 1, 1]])
    pos[:, :, S - 1] = 1; pf[:, :, S - 1] = 15; rf[:, :, W - 1] = 15
    return pack(pos, pf, rf, th, lv)
def setup_inputs_corners(rng):
    pos, pf, rf, th, lv = parts(rng)
    n_ = np.array([0, 1, 2, 3, 4, 5, 46, 47, 48, 49, S - 1, S])[rng.permutation(12)]
    for a in range(N):
        for g in range(8):
            n = int(n_[(8 * a + g) % 12]); w = int(rng.integers(0, 3))
            on = np.arange(n) if w == 0 else (np.arange(S - n, S) if w == 1 else rng.permutation(S)[:n])
            lv[a, g] = 0; lv[a, g, on] = 1
    u = rng.random((N, 8, S, 1)); pf = np.where(u < 0.2, 0, np.where(u > 0.9, 15, pf))
    th = rng.choice(np.array([0, 0, 1, 1, 100, 200, 300, 3600]), (N, 8, 16)); e = rng.permutation(8)[:2]
    th[:, e] = rng.choice(np.array([-3600, -1, 0, 300, 3600]), (N, 2, 16))
    return pack(pos, pf, rf, th, lv)
def setup_inputs_crowd(rng):
    pos, pf, rf, th, lv = parts(rng); lv[:] = 1; gp = rng.permutation(8); m = np.arange(16)
    rf[:, :, 0, :8] = 15; rf[:, :, 0, 8:] = -15
    one = int(rng.integers(0, N)); ms = int(rng.integers(1, 16))
    for i in range(8):
        g = int(gp[i]); m0 = int(rng.integers(1, 16) if i == 0 else rng.integers(0, 16 if i < 4 else 17))
        if i == 4: m0 = (ms + 1 + int(rng.integers(0, 15))) % 16
        for a in range(N):
            if i == 0: n = 0
            elif i == 1: n = a % 4
            elif i < 4: n = 2 + (a >> 1) % 2 if a % 2 == i - 2 else S // 2
            elif i == 4: n = 1 if a == one else 0
            else: n = int(rng.choice(np.array([1, 3, 47, 48, 49, S // 2])))
            o = np.concatenate([np.arange(48), 48 + rng.permutation(S - 48)]); herd, left = o[:S - n], o[S - n:]
            pos[a, g, herd] = rng.integers(-5, 6, (1, 3)) * rng.integers(-6, 7, (S - n, 1))
            b = np.zeros((S - n, 16), np.int64); b[:, :8] = rng.integers(3, 16, (S - n, 8))
            w = int(rng.integers(2 if i == 4 else 1, 16)); b[-1] = 0; b[-1, 0] = w
            pf[a, g, herd] = b
            x = rng.integers(0, 11, (n, 8)); pf[a, g, left] = np.concatenate([x, x + rng.integers(0, 6, (n, 8))], axis=1)
            v = int(rng.integers(1, w)) if i == 4 else 0
            first = 0 if i == 0 and a != one else m0
            th[a, g] = np.where(m < first, 15 * w + 1, rng.integers(15 * v + 1, 15 * w + 1, 16))
            if m0 < 16: th[a, g, m0] = 15 * w
            if i == 4:
                th[a, g, ms] = 15 * v; pf[a, g, left] = 0; pf[a, g, left, 0] = v
                pos[a, g, 48:, 0] = 5 * (2 * rng.integers(0, 2, S - 48) - 1); pos[a, g, 3 * ms:3 * ms + 3] = 16 * np.eye(3, dtype=np.int64)
    return pack(pos, pf, rf, th, lv)
def setup_inputs_ties(rng):
    pos, pf, rf, th, lv = parts(rng); gp = rng.permutation(8)
    base = rng.integers(0, 16, (N, 8, 1, 15)); o = np.argsort(rng.random((N, 8, S, 15)), axis=-1)
    pf[..., :15] = np.take_along_axis(np.broadcast_to(base, (N, 8, S, 15)), o, 3); pf[..., 15] = 1
    b = rng.choice(np.array([15, 14, 13, -15]), (N, 8, 1, 1)); rf[..., :15] = b; rf[..., 15] = rng.integers(-1, 2, (N, 8, W))
    th = (b * np.sum(base, axis=-1, keepdims=True)).reshape(N, 8, 1) + rng.integers(0, 2, (N, 8, 16))
    four = gp[3:6]; pos[:, four] = 4 * rng.integers(-7, 8, (N, 3, S, 3))
    up = ((HALF + 4096 >> SH) & 15) << (B1 + B2); dn = ((HALF - 4096 >> SH) & 15) << (B1 + B2)
    for i in range(3):
        g = int(gp[i])
        for a in range(N):
            kind = rng.integers(0, 2, 16); kind[0] = i % 2; kind[15] = 1 - i % 2
            pos[a, g] = 0; pf[a, g] = 0; lv[a, g] = 1; th[a, g] = rng.integers(1, 361, 16)
            pos[a, g, :48] = (16 * np.eye(3, dtype=np.int64)[None] * kind[:, None, None]).reshape(48, 3)
            x = 48 + rng.permutation(S - 48); h = (S - 48) // 2; one, two = x[:h], x[h:]
            pos[a, g, one, 0] = 16; pos[a, g, two, 0] = -16
            pf[a, g, one, :8] = rng.integers(3, 16, (h, 8)); pf[a, g, two, 8:] = rng.integers(3, 16, (S - 48 - h, 8))
            if i == 2 and a % 2 == 1: pf[a, g, one[0]] = 0
            rf[a, g, 0, :8] = 15; rf[a, g, 0, 8:] = 0; rf[a, g, up] = 0; rf[a, g, dn, :8] = 0; rf[a, g, dn, 8:] = 15
    g = int(gp[6]); s1 = 1 - 2 * ((np.arange(N) + int(rng.integers(0, 2))) % 2); lv[:, g] = 1
    pf[:, g] = 15; pf[:, g, :, 15] = rng.choice(np.array([1, 14, 15]), (N, S)); pf[:, g, S - 1, 15] = 14
    rf[:, g] = 15 * s1[:, None, None]
    rf[:, g, 1:, 15] = np.where(rng.random((N, W - 1)) < 0.4, 15 * s1[:, None], rng.choice(np.array([-14, -1, 0, 1, 14]), (N, W - 1)))
    th[:, g] = np.where(s1[:, None] > 0, rng.choice(np.array([3375, 3376, 3390, 3391, 3585, 3586, 3600]), (N, 16)), rng.choice(np.array([-3599, -3586, -3585, -3584, -3390, -3389, -3375]), (N, 16)))
    th[:, g, 15] = np.where(s1 > 0, 3586, -3585); th[:, g, 14] = np.where(s1 > 0, 3585, -3584)
    flat = rng.random((N, 16)) < 0.4; flat[:, 14:] = True
    pos[:, g, :48] = np.where(np.repeat(flat, 3, axis=1)[..., None], 0, pos[:, g, :48])
    g = int(gp[7]); lv[:, g] = 1; k = int(rng.integers(16, 31)); mm = int(rng.integers(0, 15))
    tri = np.array([[0, 0, 0], [k + 1, 31, -31], [k, 31, 31]]); e = np.arange(-31, 32)
    grid = np.stack(np.meshgrid(e, e, e, indexing="ij"), axis=-1).reshape(-1, 3)
    y = np.matmul(grid, np.cross(tri[1], tri[2])) + HALF
    c1 = y & (2 * HALF - 1); c2 = (y - grid[:, 0]) & (2 * HALF - 1)
    edge = grid[(c1 >= QLO) & (c1 < QHI) & ((c2 < QLO) | (c2 >= QHI))]
    pos[:, g, 45:48] = tri; pos[:, g, 3 * mm:3 * mm + 3] = tri[[0, 2, 1]]
    for a in range(N):
        x = np.append(48 + rng.permutation(S - 49)[:S // 4], S - 1); pos[a, g, x] = edge[rng.integers(0, len(edge), len(x))]
    th[:, g, mm] = -3600; th[:, g, 15] = -3600
    return pack(pos, pf, rf, th, lv)
def check_inputs(d):
    bad = []
    for k, lo, hi in (("pos", -31, 31), ("pf", 0, 15), ("rf", -15, 15), ("th", -3600, 3600), ("lv", 0, 1)):
        v = np.asarray(d[k]).astype(np.float32)
        if not (np.min(v) >= lo and np.max(v) <= hi): bad.append("range of " + k)
        if not np.all(np.floor(v) == v): bad.append("whole numbers in " + k)
    return bad
def judge(ax, P, I, R, T):
    y = np.matmul(ax, P[:, None]) + HALF
    c = y & (2 * HALF - 1); inside = np.all((c >= QLO) & (c < QHI), axis=2); n = y >> SH
    place = ((n[:, :, 0] & (2 ** B0 - 1)) << (B1 + B2)) + ((n[:, :, 1] & (2 ** B1 - 1)) << B2) + (n[:, :, 2] & (2 ** B2 - 1))
    score = np.add.reduce(R[np.arange(8)[:, None, None], place] * I[:, None], axis=-1)
    return inside & (score >= T)
def reference(pos, pf, rf, th, lv):
    P = pos.astype(np.float32).astype(np.int64).reshape(N, 8, 3, S)
    I = np.ascontiguousarray(pf.astype(np.float32).astype(np.int32).reshape(N, 8, 16, S).transpose(0, 1, 3, 2))
    R = np.ascontiguousarray(rf.astype(np.float32).astype(np.int32).reshape(N, 8, 16, W).transpose(0, 1, 3, 2))
    T = th.astype(np.int64).reshape(N, 8, 16, 1); live = lv.reshape(N, 8, S) != 0
    age = live.astype(np.int64); counts = []
    for t in range(RO):
        order = np.argsort(np.where(live, 0, 1), axis=-1, kind="stable")[..., :48]
        there = np.arange(48) < np.add.reduce(live, axis=-1, dtype=np.int64)[..., None]
        seed = (np.take_along_axis(P, order[:, :, None, :], 3) * there[:, :, None, :]).transpose(0, 1, 3, 2)
        p, q, s = seed[:, :, 0::3], seed[:, :, 1::3], seed[:, :, 2::3]
        ax = np.stack([np.cross(q, s), np.cross(s, p), np.cross(p, q)], axis=3)
        cnt = np.zeros((N, 8, 16), np.int64); hits = []
        for a in range(N):
            for i in range(J + 1):
                b = a if i == 0 else (a + t * J + i) % N
                h = judge(ax[a], P[b], I[b], R[b], T[b]); hits.append((a, b, h))
                cnt[a] = cnt[a] + np.add.reduce(h & live[b][:, None, :], axis=-1, dtype=np.int64)
        win = np.argmax(cnt, axis=2)
        die = np.zeros((N, 8, S), bool)
        for a, b, h in hits: die[b] = die[b] | h[np.arange(8), win[a]]
        live = live & ~die; age = age + live; counts.append(cnt)
    return {"yc": np.stack(counts, axis=-1).reshape(N, 128, RO).astype(np.float32), "ya": age.astype(np.float32)}

@@ -1,0 +1,529 @@
+from concourse.bass import DstId, RemoteDMATransfer
+from concourse.mybir import dt, AluOpType, AxisListType, ActivationFunctionType
+
+A = AluOpType
+F = ActivationFunctionType
+RO = 3
+KCH = 32
+NCH = 256 // KCH
+LOOK, NOISE, SEED, BACK, STAG = 0.05, 2.0, 439, 2.0, 5.0
+PEN = 16384.0
+MAGIC = 12582912.0
+CY, PC, HOP, NET = 1.04e-3, 0.53e-3, 0.12, 2.6
+GATH = 1.56
+AS, BS = 1, 1
+
+PLAN = "360J4H1438100V12181:164<0P1<0L2N0N342:002@4J2P5J3I2R3W1P411>3M1R3G1T452B3K503:3Q283D432>3U3B1V3@3S2V3>07204N0T3O4R020R5L1C303<544P5S5Q584V5O1J0<5T320>5V0@4U1N0D600B532208620:2E5<46684>56241F4F4@7V05885E0F5;480H1A8H808S4L5A5?902U6:841E4B2<6=6J4D6M1L6P646>666B6N86722F6D924:6A6F7T6H265G6R5H8;748>957D2H996T7F8M6V2L9770777H8<7:9:7J1I7<2J797>9<7@9>8A7B827L9@7N5B7P9F;=8B7R;?8F;C;R<:8D;O:0<6;K;:9H;M;@<2;G;V<49B9J<>9D9P:@9R9L:B;I;P:R<1;T9T:D<@;E9N8N<88U<<:39V8Q:4:8:7:::T:<8V:J:G;0:L:H:N<G:>:P<I:V;2<E?H;4<C?J;6<J;8<L<N8J<P?T?O<R?E<V?G<T@1=0@@=2@2=4?W=6@5@>=:@7=<=A?L@<=C@D=??P=D@8@F@;@H?S=F@B=H@J=J@O=P@Q=R@M>:@S=TA0>2=L=W>4=N>0>6>J>8>=>L>A?4>?=8>B>N>D@T>R>F@V?7>T>HA2?:?9A4>Q>VA8?0A6A:?2?<CSCN?>CTA=?@?BA>CWA@CQD>D9ADD;AFDHAID<DNAKDLAMD6D@ANAPDJARD1DFATDPB2B4DCD2BDDEB6DRD5B<AVDTB0B8B>BGBTB@BVDWB:C>E5BBE3BHE1BLBKBNBPC@C1E:CDC6C2C8C5C:E6BRC<E8H2CFH6E<CCE>H1CHEBH9CJE@H5EDCLEGH@EHEJHGHPENHEEPHHESI0EUHBHTEWHLF0F2F4HRH=F6I4HVF<H?F>HOFNHKH:I6F@I2FDFFF8FBFHF:FJFQG6FLFTABG8I;FRFVI=G0I?G2I9GHELG;IDG4G@I@G<GBIBGJGDL:IFIHG?ILGFIJGPGLINGNGRIPLELBIRL=GTITL?GVLAJ0LKJ2LLJ5M4J7LRM2J9LNJ:J<M:J>LQM6J@M8JFLGK0LWLTJHJJM>JPJLJRJBJNJTJDK3JVK@K8LIIVKBM1K4KRK7K:KTK<KEKVM<K>KJKFKLKIKNKPNBL2L0L4NINENFL6NAL8O1M@NPNUO8MGNLO@O5MIMENRO<O:ODMCNVMNNJO3O>NNMJO7OBMLOFMPOIOMMVOKMROOMTN0OPOTORN:OVP0N3P4N4P2P@P6P9N6N<P:N8N>P<PBP>PD"
+
+SCRATCH = {}
+
+
+def _buf(name, cols, dtype, where="sbuf"):
+    SCRATCH[name] = (where, [128, cols], dtype)
+
+
+for _h in range(2):
+    _buf("tab%d" % _h, 4112, "bfloat16")
+    _buf("gat%d" % _h, 8192, "bfloat16")
+    _buf("pfl%d" % _h, 512, "bfloat16")
+    _buf("pfb%d" % _h, 2048, "bfloat16")
+    _buf("posl%d" % _h, 512, "bfloat16")
+    _buf("xw%d" % _h, 528, "bfloat16")
+    _buf("yw%d" % _h, 528, "bfloat16")
+    _buf("py%d" % _h, 256, "float16")
+    _buf("lvl%d" % _h, 128, "int32")
+    _buf("live%d" % _h, 512, "bfloat16")
+    _buf("age%d" % _h, 128, "float32")
+    _buf("cum%d" % _h, 256, "bfloat16")
+    _buf("junk%d" % _h, 768, "bfloat16")
+    _buf("ac3%d" % _h, 4, "float32")
+    _buf("sl%d" % _h, 4, "uint16")
+    _buf("xb%d" % _h, 80, "float32")
+    _buf("prod%d" % _h, 64 * RO, "float32")
+    _buf("prin%d" % _h, 64 * RO, "float32")
+    _buf("lh%d" % _h, 768, "float16")
+    _buf("rr%d" % _h, 1536, "bfloat16")
+    _buf("aa%d" % _h, 1536, "bfloat16")
+    _buf("bb%d" % _h, 1536, "bfloat16")
+    _buf("off%d" % _h, 512, "uint16")
+    _buf("hit%d" % _h, 512, "bfloat16")
+    _buf("acc%d" % _h, 4 * RO, "float32")
+    _buf("ina%d" % _h, 32 + 4 * RO, "float32")
+    _buf("inc%d" % _h, 4 * RO, "float32")
+    _buf("mx%d" % _h, 4, "float32")
+    _buf("wt%d" % _h, 32, "bfloat16")
+    _buf("wq%d" % _h, 64, "bfloat16")
+    _buf("ycm%d" % _h, 48, "float32")
+    _buf("yco%d" % _h, 48, "float32")
+    _buf("sc%d" % _h, 512, "float32", "psum")
+    _buf("cb%d" % _h, 512, "float32", "psum")
+for _j in range(4):
+    _buf("yb%d" % _j, 512, "float32", "psum")
+for _n, _c, _d in [("ip", 4, "int32"), ("ci", 8, "int32"), ("cf", 8, "float32"), ("i128", 128, "float32"), ("iom", 128, "float32"),
+                   ("ioe", 64, "float32"), ("iol", 128, "float32"), ("iob", 24, "float32"), ("idn", 768, "bfloat16"),
+                   ("selm", 128, "float32"), ("sel", 64, "float32"), ("pair", 128, "float32"), ("mg", 8, "float32"), ("mge", 8, "float32"),
+                   ("ee", 256, "bfloat16"), ("lc", 256, "bfloat16"), ("lt", 256, "bfloat16"), ("ld", 256, "bfloat16"),
+                   ("cs", 16, "float32"), ("el", 24, "uint16"), ("bq", 24, "bfloat16"), ("prm", 384, "bfloat16"),
+                   ("kc", 32, "bfloat16"), ("zer", 256, "bfloat16"), ("thl", 4, "int32"), ("thf", 4, "float32"),
+                   ("thm", 8, "float32"), ("thb", 8, "float32"), ("one", 8, "bfloat16")]:
+    _buf(_n, _c, _d)
+
+SEMAPHORES = ["eV", "eS", "eP", "eG", "sent"] + ["d%d" % i for i in range(24)] + ["r%d" % i for i in range(12)]
+
+
+def plan(T, rank, topo):
+    ops = []
+    half = [0]
+    n = len(T.cores)
+    core = T.cores[rank]
+
+    def op(alts, r=(), w=(), ps=(), kind="c", lat=0.0):
+        ps = [b.replace("sm", "sc") for b in ps]
+        ops.append({"alts": alts, "r": list(r), "w": list(w), "ps": list(ps), "kind": kind, "lat": lat, "h": half[0]})
+
+    def vc(k, half=False):
+        return 0.06 + max(64, k / 2 if half else k) * CY
+
+    def V(fn, k, r, w, ps=(), half=False):
+        op({"V": (lambda g: fn(g.vector), vc(k, half))}, r, w, ps)
+
+    def S(fn, k, r, w, ps=()):
+        op({"S": (lambda g: fn(g.scalar), vc(k))}, r, w, ps)
+
+    def G(fn, k, r, w):
+        op({"G": (fn, 0.17 + 2 * k * CY)}, r, w)
+
+    def lin(out, in_, mul, add, k, r, w, ps=(), half=False, bias=None):
+        def fs(g):
+            if add == 0.0:
+                return g.scalar.activation(out, in_, F.Copy, scale=mul)
+            return g.scalar.activation(out, in_, F.Identity, bias=bias, scale=mul)
+        alts = {"V": (lambda g: g.vector.tensor_scalar(out, in_, mul, add, A.mult, A.add), vc(k, half))}
+        if add == 0.0 or bias is not None:
+            alts["S"] = (fs, vc(k))
+        op(alts, list(r) + (["cs"] if bias is not None else []), w, ps)
+
+    def P(mms, r, w, ps):
+        def fn(g):
+            last = None
+            for o, l, rh, st, sp, _c in mms:
+                last = g.tensor.matmul(o, l, rh, st, sp)
+            return last
+        op({"P": (fn, 0.05 + sum(m[5] for m in mms) * PC)}, r, w, ps)
+
+    def D(q, out, in_, us, r, w):
+        def fn(g):
+            return (g.sync if q == "Y" else g.scalar).dma_start(out, in_)
+        op({q: (fn, 0.1)}, r, w, kind="d", lat=us)
+
+    for h in range(2):
+        D("Y", T["lvl%d" % h][0:16, :], T.lv[4 * h:4 * h + 4, :], 2.0, [], ["lvl%d" % h])
+        D("Y", T["posl%d" % h][0:12, :], T.pos[12 * h:12 * h + 12, :], 2.0, [], ["posl%d" % h])
+        for u in range(2):
+            D("S" if h == 0 else "Y", T["tab%d" % h][64 * u:64 * u + 64, 16:4112], T.rf[64 * h:64 * h + 64, :], 5.0 + 4 * h, [], ["tab%d%d" % (h, u)])
+        for u in range(2):
+            D("Y", T["pfl%d" % h][64 * u:64 * u + 64, :], T.pf[64 * h:64 * h + 64, :], 2.5, [], ["pfl%d%d" % (h, u)])
+        if h == 0:
+            D("Y", T.thl[:, 0:1], T.th[:], 2.5, [], ["thl"])
+
+    def iota(name, rows, pat, base=0):
+        k = 1
+        for _s, c in pat:
+            k *= c
+        G(lambda g: g.iota(T[name][0:rows, :], pat, base, 0, allow_small_or_imprecise_dtypes=True), k, [], [name])
+    G(lambda g: g.iota(T.ip[:, 0:1], [[0, 1]], 0, 1), 1, [], ["ip"])
+    iota("iol", 16, [[2, 2], [4, 4], [0, 16]])
+    iota("iob", 12, [[1, 3], [0, 2], [3, 4]])
+    iota("i128", 128, [[1, 128]])
+    iota("iom", 128, [[0, 4], [1, 16], [0, 2]])
+    iota("ioe", 64, [[-63, 4], [64, 4], [1024, 4]])
+    pc = T.ip[:, 0:1]
+    bits = [(A.bitwise_and, 15, None, None), (A.arith_shift_right, 4, None, None), (A.bitwise_and, 63, None, None),
+            (A.bitwise_and, 1, None, None), (A.bitwise_and, 31, None, None), (A.bitwise_and, 127, None, None),
+            (A.arith_shift_right, 1, A.bitwise_and, 15)]
+    for i, (o0, s0, o1, s1) in enumerate(bits):
+        if o1 is None:
+            V(lambda v, i=i, o0=o0, s0=s0: v.tensor_scalar(T.ci[:, i:i + 1], pc, s0, None, o0), 1, ["ip"], ["ci%d" % i])
+        else:
+            V(lambda v, i=i, o0=o0, s0=s0, o1=o1, s1=s1: v.tensor_scalar(T.ci[:, i:i + 1], pc, s0, s1, o0, o1), 1, ["ip"], ["ci%d" % i])
+    V(lambda v: v.tensor_copy(T.cf[:, 0:7], T.ci[:, 0:7]), 7, ["ci%d" % i for i in range(7)], ["cf"])
+    cm, cg, c63, csx, c31, cp, cm2 = [T.cf[:, i:i + 1] for i in range(7)]
+    coef = [1.0, 16.0, 256.0, PEN, PEN + 256.0, -2.0]
+    for i, c in enumerate(coef):
+        k = 16 if i == 5 else 128
+        if i:
+            lin(T.idn[0:k, 128 * i:128 * i + k], T.idn[0:k, 0:k], c, 0.0, k, ["idn0"], ["idn%d" % i], half=True)
+            continue
+        V(lambda v, i=i, c=c, k=k: v.tensor_scalar(T.idn[0:k, 128 * i:128 * i + k], T.i128[0:k, 0:k], T.cf[0:k, 5:6], c, A.is_equal, A.mult),
+          k, ["i128", "cf"], ["idn%d" % i])
+
+    def ident(i, k=128):
+        return T.idn[0:k, 128 * i:128 * i + k]
+    V(lambda v: v.tensor_scalar(T.selm[:], T.iom[:], cm, None, A.is_equal), 128, ["iom", "cf"], ["selm"])
+    V(lambda v: v.tensor_scalar(T.cs[:, 0:1], csx, -8.0, 8.0, A.mult, A.add), 1, ["cf"], ["cs0"])
+    V(lambda v: v.tensor_scalar(T.cs[:, 1:2], csx, 8.0, None, A.mult), 1, ["cf"], ["cs1"])
+    V(lambda v: v.tensor_scalar(T.cs[:, 2:3], cm, 3.0, 0.5, A.mult, A.add), 1, ["cf"], ["cs2"])
+    V(lambda v: v.tensor_scalar(T.cs[:, 4:7], T.i128[:, 0:3], T.cs[:, 2:3], None, A.add), 3, ["cs2", "i128"], ["cs4"])
+    V(lambda v: v.tensor_scalar(T.cs[:, 8:11], T.i128[:, 16:64:16], cm, None, A.add), 3, ["cf", "i128"], ["cs8"])
+    BR, BA, BB, BY = -(96.0 + 0.5 / 4096), 63.75, -2040.25, MAGIC + 512.0
+    for i, c in enumerate([BR, BA, BB, BY]):
+        V(lambda v, i=i, c=c: v.memset(T.cs[:, 12 + i:13 + i], c), 1, [], ["cs"])
+    for s in range(2):
+        V(lambda v, s=s: v.tensor_scalar(T.sel[:, 32 * s:32 * s + 32], T.iom[:, 0:32], cm2, T.cs[:, s:s + 1], A.is_equal, A.mult),
+          32, ["iom", "cf", "cs%d" % s], ["sel%d" % s])
+        V(lambda v, s=s: v.tensor_scalar(T.pair[:, 64 * s:64 * s + 64], T.i128[:, 0:64], c63, None, A.is_equal), 64, ["i128", "cf"], ["pair%d" % s])
+        V(lambda v, s=s: v.tensor_scalar(T.lc[0:16, 128 * s:128 * s + 128], T.iol[0:16, :], float(s), T.cf[0:16, 5:6], A.add, A.is_equal),
+          128, ["iol", "cf"], ["lc%d" % s])
+    V(lambda v: v.tensor_scalar(T.mg[:], T.i128[:, 0:8], cg, None, A.is_equal), 8, ["i128", "cf"], ["mg"])
+    lin(T.mge[:], T.mg[:], 2.0 ** -10, 0.0, 8, ["mg"], ["mge"])
+    for q in range(4):
+        V(lambda v, q=q: v.tensor_scalar(T.ee[0:36, 64 * q:64 * q + 64], T.ioe[0:36, :], -1024.0 * q, T.cf[0:36, 4:5], A.add, A.is_equal),
+          64, ["ioe", "cf"], ["ee%d" % q])
+    V(lambda v: v.memset(T.lt[0:16, 0:64], 0.0), 32, [], ["lt0a"])
+    V(lambda v: v.tensor_tensor(T.lt[0:16, 64:128], T.lc[0:16, 0:64], T.lc[0:16, 128:192], A.add), 128, ["lc0", "lc1"], ["lt0b"])
+    V(lambda v: v.tensor_tensor(T.lt[0:16, 128:256], T.lt[0:16, 0:128], T.lc[0:16, 0:128], A.add), 256, ["lc0", "lt0a", "lt0b"], ["lt1"])
+    lin(T.ld[0:16, :], T.lc[0:16, :], PEN / 2, 0.0, 256, ["lc0", "lc1"], ["ld"], half=True)
+    for j in range(3):
+        V(lambda v, j=j: v.tensor_scalar(T.el[:, 8 * j:8 * j + 8], T.mg[:], T.cs[:, 8 + j:9 + j], None, A.mult), 8, ["mg", "cs8"], ["el%d" % j])
+    V(lambda v: v.tensor_scalar(T.bq[0:12, :], T.iob[0:12, :], T.cf[0:12, 5:6], None, A.is_equal), 24, ["iob", "cf"], ["bq"])
+    V(lambda v: v.memset(T.prm[0:12, :], 0.0), 192, [], ["permz"])
+    V(lambda v: v.memset(T.one[0:12, :], 1.0), 8, [], ["one"])
+    rows = [(1, 2, 0, 2, 0, 1), (2, 0, 1, 1, 2, 0), (0, 1, 2, 0, 1, 2)]
+    for k in range(3):
+        for r in range(6):
+            c = rows[k][r]
+            out = T.prm[0:12, 128 * k + r:128 * k + 128:16]
+            if k == 0:
+                G(lambda g, out=out, c=c: g.affine_select(out, T.one[0:12, :], [[0, 2], [-3, 4]], A.is_equal, 0.0, -c, 1), 8,
+                  ["one", "permz"], ["perm%d%d" % (k, r)])
+            else:
+                lin(out, T.bq[0:12, 8 * c:8 * c + 8], -1.0 if (k == 2 and r >= 3) else 1.0, 0.0, 8, ["bq", "permz"], ["perm%d%d" % (k, r)])
+    V(lambda v: v.tensor_scalar(T.kc[0:64, :], T.iom[0:64, 0:32], -1.0, 7.5, A.mult, A.add), 32, ["iom"], ["kc"])
+    V(lambda v: v.memset(T.kc[0:32, 1:32:2], -65536.0), 16, [], ["kc"])
+    V(lambda v: v.memset(T.kc[32:64, 0:32:2], -65536.0), 16, [], ["kc"])
+    V(lambda v: v.memset(T.zer[0:16, :], 0.0), 128, [], ["zer"])
+    V(lambda v: v.tensor_copy(T.thf[:, 0:1], T.thl[:, 0:1]), 1, ["thl"], ["thf"])
+    V(lambda v: v.tensor_scalar(T.thm[:], T.mg[:], T.thf[:, 0:1], None, A.mult), 8, ["mg", "thf"], ["thm"])
+    P([(T.sc1[:, 0:8], T.selm[:], T.thm[:], True, True, 256)], ["selm", "thm"], ["sc1a"], ["sc1"])
+    V(lambda v: v.tensor_scalar(T.thb[:], T.sc1[:, 0:8], -1.0, 0.5, A.mult, A.add), 8, ["sc1a"], ["thb"], ["sc1"])
+
+    def setup(h):
+        B = lambda s: T[s + str(h)]
+        K = lambda s: s + str(h)
+        V(lambda v: v.memset(B("tab")[:, 0:16], -1073741824.0), 8, [], [K("tabz")])
+        V(lambda v: v.memset(B("live")[0:16, 128:512], 0.0), 192, [], [K("livez")])
+        V(lambda v: v.tensor_copy(B("live")[0:16, 0:128], B("lvl")[0:16, :]), 128, [K("lvl")], [K("live0")])
+        V(lambda v: v.memset(B("ina")[:, 0:32], 0.0), 32, [], [K("inaz")])
+        V(lambda v: v.memset(B("xb")[:, 0:16], 0.0), 16, [], [K("xbz")])
+        for k, nm in enumerate(["xw", "yw", "py"]):
+            yb = T["yb%d" % k]
+            P([(yb[:], T.prm[0:12, 128 * k:128 * k + 128], B("posl")[0:12, :], True, True, 512)],
+              [K("posl")] + ["perm%d%d" % (k, r) for r in range(6)], ["ys%d" % k], ["yb%d" % k])
+            if k < 2:
+                V(lambda v, nm=nm: v.memset(B(nm)[:, 512:528], 0.0), 8, [], [K(nm + "z")])
+                lin(B(nm)[:, 0:512], yb[:], 1.0, 0.0, 512, ["ys%d" % k], [K(nm)], ["yb%d" % k])
+            else:
+                for u in range(2):
+                    V(lambda v, u=u, yb=yb: v.tensor_copy(B("py")[64 * u:64 * u + 64, :], yb[64 * u:64 * u + 64, u:512:2]), 256,
+                      ["ys2"], [K("py%d" % u)], ["yb2"])
+        for q in range(8):
+            o, i_, mc, ec = B("pfb")[:, q:2048:8], B("pfl")[:, q // 4:512:2], T.mg[:, q:q + 1], T.mge[:, q:q + 1]
+            op({"V": (lambda g, o=o, i_=i_, mc=mc: g.vector.tensor_scalar(o, i_, 2.0 ** -10, mc, A.max, A.mult), vc(256, True)),
+                "S": (lambda g, o=o, i_=i_, mc=mc, ec=ec: g.scalar.activation(o, i_, F.Identity, bias=ec, scale=mc), vc(256))},
+               [K("pfl") + "0", K("pfl") + "1", "mg", "mge"], [K("pfb%d" % q)])
+
+    nrem = [0]
+
+    def send(src, dsts, key, land):
+        sem = T.sem["r%d" % nrem[0]]
+        nrem[0] += 1
+        mask = topo.mask(core, dsts[0][0])
+        for d, _ap in dsts:
+            mask &= topo.mask(core, d)
+        ne = bin(mask).count("1")
+
+        def fn(g):
+            ids = [DstId(rid=topo.addr(d)[0], pnc=topo.addr(d)[1]) for d, _ap in dsts]
+            tr = RemoteDMATransfer(dst_ids=ids, dma_engine_mask=mask, remote_sem=sem, src=src, dsts=[ap for _d, ap in dsts])
+            g.remote_dma_fused([tr], local_sem=T.sem.sent)
+            return ne
+        op({"G": (fn, 0.3)}, key, [land + "s"], kind="s")
+        op({"N": ((sem, ne * len(dsts)), 0.0)}, [land + "s"], [land], kind="a", lat=NET)
+
+    def front(h, t):
+        B = lambda s: T[s + str(h)]
+        K = lambda s: s + str(h)
+        live = B("live")[0:16, 128 * t:128 * t + 256]
+        lk = K("live%d" % t)
+        sc, sm, cum = B("sc"), B("sc"), B("cum")
+        V(lambda v: v.tensor_tensor_scan(cum[0:16, :], live, T.zer[0:16, :], 0.0, A.add, A.add), 256, [lk, "zer", K("livez"), K("live%d" % (t + 1))], [K("cum")], half=True)
+        mm = []
+        for b in range(2):
+            o = sc[:, 128 + 128 * b:256 + 128 * b]
+            mm.append((o, T.lc[0:16, 128 * b:128 * b + 128], cum[0:16, 0:128], True, False, 128))
+            mm.append((o, T.lt[0:16, 128 * b:128 * b + 128], cum[0:16, 128:256], False, True, 128))
+        P(mm, [K("cum"), "lc0", "lc1", "lt0a", "lt0b", "lt1"], [K("cn")], [K("sc")])
+        for i in range(3):
+            S(lambda a, i=i: a.activation(B("junk")[:, 256 * i:256 * i + 256], sc[:, 128:384], F.Sign, bias=T.cs[:, 4 + i:5 + i], scale=-1.0,
+                                          accum_out=B("ac3")[:, i:i + 1]),
+              276, [K("cn"), "cs4"], [K("ac3%d" % i)], [K("sc")])
+        P([(sm[:, 256:259], T.pair[:], B("ac3")[:, 0:3], True, True, 256), (sm[:, 259:260], T.pair[:], B("ac3")[:, 0:1], True, True, 256)],
+          [K("ac3%d" % i) for i in range(3)] + ["pair0", "pair1"], [K("pr")], [K("sm")])
+        V(lambda v: v.tensor_scalar(B("sl")[:], sm[:, 256:260], 0.5, 256.0, A.mult, A.add), 4, [K("pr")], [K("sl")], [K("sm")])
+        V(lambda v: v.tensor_copy(B("xb")[:, 16:80], B("xw")[:].indirect(B("sl")[:])), 100, [K("sl"), K("xw"), K("xwz")], [K("xb")])
+        prod = B("prod")[:, 64 * t:64 * t + 64]
+        prin = B("prin")[:, 64 * t:64 * t + 64]
+        V(lambda v: v.tensor_tensor(prod, B("yw")[:].indirect(B("sl")[:]), B("xb")[:, 0:64], A.mult), 100,
+          [K("sl"), K("yw"), K("ywz"), K("xb"), K("xbz")], [K("prod%d" % t)])
+        send(prod, [(T.cores[(rank + t + 1) % n], prin)], [K("prod%d" % t)], K("prin%d" % t))
+        cj = [0, 2, 1]
+        c0 = 16.0 + 273 * 1984.0 - 3 * PEN * 64 - PEN / 2
+        for s in range(2):
+            src = prin if s else prod
+            V(lambda v, s=s, src=src: v.tensor_copy(B("lh")[:, 384 * s:384 * s + 384], src.indirect(T.el[:])), 384 * GATH,
+              [K(("prin%d" if s else "prod%d") % t), "el0", "el1", "el2"], [K("lh%d" % s)])
+            cb, cw = "cb%d" % s, "cw%d" % s
+            cbs = T[cb][:, 0:256]
+            for part, (js, bank, c1) in enumerate([((0, 1), "yb%d" % (2 * s), 0), ((2,), "yb%d" % (2 * s + 1), 0)]):
+                k = 256 * len(js)
+                yk = "y%d%d" % (part, s)
+                P([(T[bank][:, c1 + 256 * i:c1 + 256 * i + 256], B("lh")[:, 384 * s + 128 * j:384 * s + 128 * j + 128], B("py")[:], True, True, 256)
+                   for i, j in enumerate(js)], [K("lh%d" % s), K("py0"), K("py1")], [yk], [bank])
+                cols = slice(768 * s + 512 * part, 768 * s + 512 * part + k)
+                tag = "%d%d" % (part, s)
+                lin(B("rr")[:, cols], T[bank][:, c1:c1 + k], -1.0 / 4096, BR, k, [yk], [K("rr" + tag)], [bank], bias=T.cs[:, 12:13])
+                lin(B("aa")[:, cols], B("rr")[:, cols], -1.0, BA, k, [K("rr" + tag)], [K("aa" + tag)], half=True, bias=T.cs[:, 13:14] if AS else None)
+                lin(B("bb")[:, cols], B("rr")[:, cols], 1.0, BB, k, [K("rr" + tag)], [K("bb" + tag)], half=True, bias=T.cs[:, 14:15] if BS else None)
+                col = lambda nm, j, s=s: B(nm)[:, 768 * s + 256 * j:768 * s + 256 * j + 256]
+                P([(cbs, ident(3), col("rr", j), j == 0, False, 256) for j in js], [K("rr" + tag), "idn3"], [cw], [cb])
+                if part == 0:
+                    mm = []
+                    for q in range(4):
+                        for u in range(2):
+                            mm.append((T[cb][64 * u:64 * u + 64, 64 * q:64 * q + 64],
+                                       T.ld[0:16, 128 * (q % 2) + 64 * (q // 2):128 * (q % 2) + 64 * (q // 2) + 64],
+                                       B("live")[0:16, 128 * t + u:128 * t + 128:2], False, False, 64))
+                    P(mm, [lk, "ld"], [cw], [cb])
+                mm = []
+                for j in js:
+                    mm += [(cbs, ident(i), col("aa", j), False, False, 256) for i in ([4] if cj[j] == 2 else [3, cj[j]])]
+                P(mm, [K("aa" + tag), "idn3", "idn4", "idn0", "idn1"], [cw], [cb])
+                P([(cbs, ident(cj[j]), col("bb", j), False, j == 2, 256) for j in js], [K("bb" + tag), "idn0", "idn1", "idn2"], [cw], [cb])
+            V(lambda v, s=s, cbs=cbs: v.tensor_scalar(B("off")[:, 256 * s:256 * s + 256], cbs, c0, 0.0, A.add, A.max), 256,
+              [cw], [K("off%d" % s)], [cb])
+
+    def back(h, t):
+        B = lambda s: T[s + str(h)]
+        K = lambda s: s + str(h)
+        sc, sm, gat = B("sc"), B("sc"), B("gat")
+        for s in range(2):
+            for c in range(NCH):
+                o = gat[:, 32 * KCH * c + s:32 * KCH * (c + 1):2]
+                w = B("tab")[:].indirect(B("off")[:, 256 * s + KCH * c:256 * s + KCH * (c + 1)])
+                us = 0.06 + 16 * KCH * GATH * CY
+                op({"V": (lambda g, o=o, w=w: g.vector.tensor_copy(o, w), us), "S": (lambda g, o=o, w=w: g.scalar.activation(o, w, F.Copy), us)},
+                   [K("off%d" % s), K("tab") + "0", K("tab") + "1", K("tabz")], [K("gat%d%d_" % (s, c))])
+                ops[-1]["fill"] = (2 * (NCH - 1 - c) + 1 - s) * us / 2
+        for c in range(NCH):
+            mm = []
+            for x in range(c * KCH, (c + 1) * KCH):
+                q, xh = x // 64, x % 64
+                mm.append((sc[32 * q:32 * q + 32, 8 * xh:8 * xh + 8], gat[:, 32 * x:32 * x + 32], B("pfb")[:, 8 * x:8 * x + 8], True, True, 32))
+            P(mm, [K("gat0%d_" % c), K("gat1%d_" % c)] + [K("pfb%d" % q) for q in range(8)], [K("s%d_" % c)], [K("sc")])
+        acc = B("acc")[:, 4 * t:4 * t + 4]
+        for k in range(4):
+            S(lambda a, k=k: a.activation(B("hit")[:, 128 * k:128 * k + 128], sc[:, k:512:4], F.Sign, bias=T.thb[:, 4 * h + k:4 * h + k + 1],
+                                          accum_out=B("acc")[:, 4 * t + k:4 * t + k + 1]),
+              148, [K("s%d_" % c) for c in range(NCH)] + ["thb"], [K("hit%d" % k), K("acc%d%d" % (t, k))], [K("sc")])
+        ca, cc = T.cores[(rank - t - 1) % n], T.cores[(rank + t + 1) % n]
+        ina, inc = B("ina")[:, 32 + 4 * t:36 + 4 * t], B("inc")[:, 4 * t:4 * t + 4]
+        if ca == cc:
+            inc = ina
+            dsts = [(cc, ina)]
+        else:
+            dsts = [(cc, ina), (ca, inc)]
+        ak = [K("acc%d%d" % (t, k)) for k in range(4)]
+        send(acc, dsts, ak, K("in%d" % t))
+        s0, s1 = T.sel[:, 0:32], T.sel[:, 32:64]
+        P([(sm[0:36, 0:32], ident(0, 36), T.kc[0:36, :], True, False, 36), (sm[0:4, 0:32], acc, s0, False, False, 128),
+           (sm[32:36, 0:32], acc, s1, False, False, 128)], ak + ["kc", "idn0", "sel0", "sel1"], [K("key")], [K("sm")])
+        P([(sm[0:4, 0:32], inc, s1, False, False, 128), (sm[0:36, 0:32], B("ina")[:, 4 * t:4 * t + 36], s0, False, True, 144)],
+          [K("in%d" % t), K("inaz")], [K("key")], [K("sm")])
+        V(lambda v: v.tensor_reduce(B("mx")[0:36, 0:1], sm[0:36, 0:32], AxisListType.X, A.max), 32, [K("key")], [K("mx")], [K("sm")])
+        V(lambda v: v.tensor_scalar(B("wt")[0:36, :], sm[0:36, 0:32], B("mx")[0:36, 0:1], None, A.is_equal), 32, [K("key"), K("mx")], [K("wt")], [K("sm")])
+        V(lambda v: v.tensor_scalar(B("ycm")[0:4, t:48:3], sm[0:4, 0:32:2], 1.0 / 16, BY, A.mult, A.add), 16, [K("key")], [K("ycm%d" % t)], [K("sm")])
+        P([(sc[32 * q:32 * q + 32, 0:64], B("wt")[0:36, :], T.ee[0:36, 64 * q:64 * q + 64], True, True, 64) for q in range(4)],
+          [K("wt")] + ["ee%d" % q for q in range(4)], [K("w")], [K("sc")])
+        lin(B("wq")[:], sc[:, 0:64], 1.0, 0.0, 64, [K("w")], [K("wq")], [K("sc")])
+        live = B("live")[0:16, 128 * t:128 * t + 128]
+        nxt = B("live")[0:16, 128 * t + 128:128 * t + 256]
+        dd = sm[0:16, 64:192]
+        mm = [(dd, ident(5, 16), live, True, False, 128)]
+        for k in range(4):
+            mm.append((dd, B("wq")[:, 16 * k:16 * k + 16], B("hit")[:, 128 * k:128 * k + 128], False, k == 3, 128))
+        P(mm, [K("wq"), K("live%d" % t), "idn5"] + [K("hit%d" % k) for k in range(4)], [K("dd")], [K("sm")])
+        V(lambda v: v.tensor_scalar(nxt, dd, -3.0, None, A.is_lt), 128, [K("dd"), K("livez")], [K("live%d" % (t + 1))], [K("sm")])
+        age = B("age")[0:16, :]
+        V(lambda v: v.tensor_tensor(age, age if t else live, nxt, A.add), 256, [K("live%d" % t), K("live%d" % (t + 1))] + ([K("age")] if t else []), [K("age")])
+        if t == RO - 1:
+            V(lambda v: v.tensor_scalar(B("yco")[0:4, :], B("ycm")[0:4, :], -MAGIC, None, A.add), 48, [K("ycm%d" % i) for i in range(RO)], [K("yco")])
+            D("Y", T.yc[64 * h:64 * h + 64, :], B("yco")[0:4, :], 2.0, [K("yco")], [K("oc")])
+            D("Y", T.ya[4 * h:4 * h + 4, :], age, 2.0, [K("age")], [K("oa")])
+
+    setup(0)
+    front(0, 0)
+    half[0] = 1
+    setup(1)
+    front(1, 0)
+    for t in range(RO):
+        for h in range(2):
+            half[0] = h
+            back(h, t)
+            if t + 1 < RO:
+                front(h, t + 1)
+    return ops
+
+
+def depend(ops):
+    lastw, readers, epoch = {}, {}, {}
+    deps = []
+    for i, o in enumerate(ops):
+        d = {}
+        for k in o["r"]:
+            if k in lastw:
+                d[lastw[k]] = True
+        for k in o["w"]:
+            if k in lastw:
+                d.setdefault(lastw[k], False)
+            for j in readers.get(k, []):
+                d.setdefault(j, False)
+        eng = list(o["alts"])[0] if len(o["alts"]) == 1 else None
+        for b in o["ps"]:
+            e, cur, prev = epoch.get(b, (None, [], []))
+            if eng is not None and e == eng:
+                cur.append(i)
+            else:
+                prev, cur = cur, [i]
+                epoch[b] = (eng, cur, prev)
+            for j in prev:
+                d.setdefault(j, False)
+        for k in o["r"]:
+            readers.setdefault(k, []).append(i)
+        for k in o["w"]:
+            lastw[k] = i
+            readers[k] = []
+        d.pop(i, None)
+        deps.append(d)
+    return deps
+
+
+def order(ops, deps, look=LOOK, noise=NOISE, seed=SEED, back=BACK, stag=STAG, vb=0.0):
+    n = len(ops)
+    succ = [[] for _ in range(n)]
+    for i in range(n):
+        for j in deps[i]:
+            succ[j].append(i)
+    prio = [0.0] * n
+    for i in range(n - 1, -1, -1):
+        c = min(a[1] for a in ops[i]["alts"].values()) + ops[i]["lat"] + HOP + ops[i].get("fill", 0.0)
+        prio[i] = c + max([prio[k] for k in succ[i]] + [0.0])
+    x = seed
+    for i in range(n):
+        x = (x * 1103515245 + 12345) % 2147483648
+        prio[i] += noise * x / 2147483648 - (back if "fill" in ops[i] else 0.0) - stag * ops[i]["h"]
+    left = [len(deps[i]) for i in range(n)]
+    ready = [i for i in range(n) if left[i] == 0]
+    free = {e: 0.0 for e in "VSPGYN"}
+    end, eng, seq = [0.0] * n, [None] * n, []
+    while ready:
+        cand = []
+        for i in ready:
+            for e, a in ops[i]["alts"].items():
+                t0 = free[e] if e != "N" else 0.0
+                for j, raw in deps[i].items():
+                    if eng[j] != e or ops[j]["kind"] != "c":
+                        t0 = max(t0, end[j] + HOP)
+                    elif e != "P":
+                        t0 = max(t0, end[j] + 0.05)
+                cand.append((t0 + (vb if e == "V" and len(ops[i]["alts"]) > 1 else 0.0), i, e, a[1], t0))
+        first = min(c[0] for c in cand)
+        _t, i, e, c, t0 = max((x for x in cand if x[0] <= first + look), key=lambda x: (prio[x[1]], -x[0] - x[3]))
+        free[e] = t0 + c
+        end[i] = t0 + c + ops[i]["lat"]
+        eng[i] = e
+        seq.append(i)
+        ready.remove(i)
+        for k in succ[i]:
+            left[k] -= 1
+            if left[k] == 0:
+                ready.append(k)
+    return seq, eng, end
+
+
+def rank_program(g, core, T, topo):
+    rank = T.rank_of(core)
+    if rank is None:
+        return
+    ops = plan(T, rank, topo)
+    deps = depend(ops)
+    if len(PLAN) == 2 * len(ops):
+        code = [(ord(PLAN[k]) - 48) * 40 + ord(PLAN[k + 1]) - 48 for k in range(0, len(PLAN), 2)]
+        seq, end = [x // 2 for x in code], [0] * len(ops)
+        eng = [list(o["alts"])[0] for o in ops]
+        for k, x in enumerate(code):
+            end[x // 2] = k
+            if len(ops[x // 2]["alts"]) > 1:
+                eng[x // 2] = "S" if x % 2 else "V"
+    else:
+        seq, eng, end = order(ops, deps)
+    chan, idx, cnt = {}, {}, {}
+    for i in seq:
+        ch = eng[i] if ops[i]["kind"] == "c" else ("x", i)
+        cnt[ch] = cnt.get(ch, 0) + 1
+        chan[i], idx[i] = ch, cnt[ch]
+    clock = {e: {} for e in "VSPGYN"}
+    done, waits, marked = {}, {}, set()
+    for i in seq:
+        e = eng[i]
+        if e == "N":
+            done[i] = {chan[i]: 1}
+            continue
+        w = []
+        for j in sorted(deps[i], key=lambda j: -end[j]):
+            if chan[j] == e and e == "P":
+                continue
+            if clock[e].get(chan[j], 0) >= idx[j]:
+                continue
+            w.append(j)
+            marked.add(j)
+            for ch, v in done[j].items():
+                if clock[e].get(ch, 0) < v:
+                    clock[e][ch] = v
+        waits[i] = w
+        done[i] = dict(clock[e])
+        done[i][chan[i]] = idx[i]
+    queue = {"V": g.vector, "S": g.scalar, "P": g.tensor, "G": g, "Y": g.sync}
+    token, ninc, nd, sent, outs = {}, {e: 0 for e in "VSPG"}, 0, 0, []
+    for i in seq:
+        e, o = eng[i], ops[i]
+        if e == "N":
+            token[i] = o["alts"]["N"][0]
+            continue
+        for j in waits[i]:
+            queue[e].wait_ge(token[j][0], token[j][1])
+        ins = o["alts"][e][0](g)
+        if o["kind"] == "s":
+            sent += ins
+        elif o["kind"] == "d":
+            token[i] = (T.sem["d%d" % nd], 16)
+            nd += 1
+            ins.then_inc(token[i][0], 16)
+            if i not in marked:
+                outs.append(i)
+        elif i in marked:
+            ninc[e] += 1
+            token[i] = (T.sem["e" + e], ninc[e])
+            ins.then_inc(token[i][0], 1)
+    for i in outs:
+        g.sync.wait_ge(token[i][0], 16)
+    g.wait_ge(T.sem.sent, sent)

@@ -4,81 +4,50 @@ from concourse.mybir import dt, AluOpType, AxisListType, ActivationFunctionType
 A = AluOpType
 F = ActivationFunctionType
 RO = 3
+NG = 4
+NS = NU = 8 // NG
+W, XH = 64 * NG, 16 * NG
 KCH = 32
-NCH = 256 // KCH
-LOOK, NOISE, SEED, BACK, STAG = 0.05, 2.0, 439, 2.0, 5.0
-PEN = 16384.0
-MAGIC = 12582912.0
-CY, PC, HOP, NET = 1.04e-3, 0.53e-3, 0.12, 2.6
-GATH = 1.56
-AS, BS = 1, 1
+NCH = W // KCH
+LOOK, BACK, STAG, GATE = 0.1, 5.0, 9.0, 0
+C0 = 12582912.0
+COST = {"cy": 0.9e-3, "pc": 0.45e-3, "hop": 0.12, "net": 2.6, "gath": 1.56, "scat": 3.8}
 
-PLAN = "360J4H1438100V12181:164<0P1<0L2N0N342:002@4J2P5J3I2R3W1P411>3M1R3G1T452B3K503:3Q283D432>3U3B1V3@3S2V3>07204N0T3O4R020R5L1C303<544P5S5Q584V5O1J0<5T320>5V0@4U1N0D600B532208620:2E5<46684>56241F4F4@7V05885E0F5;480H1A8H808S4L5A5?902U6:841E4B2<6=6J4D6M1L6P646>666B6N86722F6D924:6A6F7T6H265G6R5H8;748>957D2H996T7F8M6V2L9770777H8<7:9:7J1I7<2J797>9<7@9>8A7B827L9@7N5B7P9F;=8B7R;?8F;C;R<:8D;O:0<6;K;:9H;M;@<2;G;V<49B9J<>9D9P:@9R9L:B;I;P:R<1;T9T:D<@;E9N8N<88U<<:39V8Q:4:8:7:::T:<8V:J:G;0:L:H:N<G:>:P<I:V;2<E?H;4<C?J;6<J;8<L<N8J<P?T?O<R?E<V?G<T@1=0@@=2@2=4?W=6@5@>=:@7=<=A?L@<=C@D=??P=D@8@F@;@H?S=F@B=H@J=J@O=P@Q=R@M>:@S=TA0>2=L=W>4=N>0>6>J>8>=>L>A?4>?=8>B>N>D@T>R>F@V?7>T>HA2?:?9A4>Q>VA8?0A6A:?2?<CSCN?>CTA=?@?BA>CWA@CQD>D9ADD;AFDHAID<DNAKDLAMD6D@ANAPDJARD1DFATDPB2B4DCD2BDDEB6DRD5B<AVDTB0B8B>BGBTB@BVDWB:C>E5BBE3BHE1BLBKBNBPC@C1E:CDC6C2C8C5C:E6BRC<E8H2CFH6E<CCE>H1CHEBH9CJE@H5EDCLEGH@EHEJHGHPENHEEPHHESI0EUHBHTEWHLF0F2F4HRH=F6I4HVF<H?F>HOFNHKH:I6F@I2FDFFF8FBFHF:FJFQG6FLFTABG8I;FRFVI=G0I?G2I9GHELG;IDG4G@I@G<GBIBGJGDL:IFIHG?ILGFIJGPGLINGNGRIPLELBIRL=GTITL?GVLAJ0LKJ2LLJ5M4J7LRM2J9LNJ:J<M:J>LQM6J@M8JFLGK0LWLTJHJJM>JPJLJRJBJNJTJDK3JVK@K8LIIVKBM1K4KRK7K:KTK<KEKVM<K>KJKFKLKIKNKPNBL2L0L4NINENFL6NAL8O1M@NPNUO8MGNLO@O5MIMENRO<O:ODMCNVMNNJO3O>NNMJO7OBMLOFMPOIOMMVOKMROOMTN0OPOTORN:OVP0N3P4N4P2P@P6P9N6N<P:N8N>P<PBP>PD"
-
-SCRATCH = {}
-
-
-def _buf(name, cols, dtype, where="sbuf"):
-    SCRATCH[name] = (where, [128, cols], dtype)
-
-
-for _h in range(2):
-    _buf("tab%d" % _h, 4112, "bfloat16")
-    _buf("gat%d" % _h, 8192, "bfloat16")
-    _buf("pfl%d" % _h, 512, "bfloat16")
-    _buf("pfb%d" % _h, 2048, "bfloat16")
-    _buf("posl%d" % _h, 512, "bfloat16")
-    _buf("xw%d" % _h, 528, "bfloat16")
-    _buf("yw%d" % _h, 528, "bfloat16")
-    _buf("py%d" % _h, 256, "float16")
-    _buf("lvl%d" % _h, 128, "int32")
-    _buf("live%d" % _h, 512, "bfloat16")
-    _buf("age%d" % _h, 128, "float32")
-    _buf("cum%d" % _h, 256, "bfloat16")
-    _buf("junk%d" % _h, 768, "bfloat16")
-    _buf("ac3%d" % _h, 4, "float32")
-    _buf("sl%d" % _h, 4, "uint16")
-    _buf("xb%d" % _h, 80, "float32")
-    _buf("prod%d" % _h, 64 * RO, "float32")
-    _buf("prin%d" % _h, 64 * RO, "float32")
-    _buf("lh%d" % _h, 768, "float16")
-    _buf("rr%d" % _h, 1536, "bfloat16")
-    _buf("aa%d" % _h, 1536, "bfloat16")
-    _buf("bb%d" % _h, 1536, "bfloat16")
-    _buf("off%d" % _h, 512, "uint16")
-    _buf("hit%d" % _h, 512, "bfloat16")
-    _buf("acc%d" % _h, 4 * RO, "float32")
-    _buf("ina%d" % _h, 32 + 4 * RO, "float32")
-    _buf("inc%d" % _h, 4 * RO, "float32")
-    _buf("mx%d" % _h, 4, "float32")
-    _buf("wt%d" % _h, 32, "bfloat16")
-    _buf("wq%d" % _h, 64, "bfloat16")
-    _buf("ycm%d" % _h, 48, "float32")
-    _buf("yco%d" % _h, 48, "float32")
-    _buf("sc%d" % _h, 512, "float32", "psum")
-    _buf("cb%d" % _h, 512, "float32", "psum")
-for _j in range(4):
-    _buf("yb%d" % _j, 512, "float32", "psum")
+PART = {"tab": (4112, "bfloat16"), "gat": (32 * W, "bfloat16"), "pfl": (W, "bfloat16"), "pfb": (8 * W, "bfloat16"),
+        "posl": (512, "bfloat16"), "posh": (512, "bfloat16"), "xw": (528, "bfloat16"), "yw": (528, "bfloat16"),
+        "py": (8 * W, "bfloat16"), "lvl": (XH, "int32"), "live": (4 * XH, "bfloat16"), "age": (XH, "float32"),
+        "cum": (2 * XH, "bfloat16"), "junk": (3 * W, "bfloat16"), "ac3": (4, "float32"), "sl": (8, "uint16"),
+        "xb": (80, "bfloat16"), "prod": (64 * RO, "bfloat16"), "prin": (48 * RO, "bfloat16"),
+        "lh": (768, "bfloat16"), "off": (2 * W, "uint16"), "hit": (128 * NG, "bfloat16"),
+        "acc": (4 * RO, "float32"), "ina": (4 * RO, "float32"), "inc": (4 * RO, "float32"),
+        "mx": (4, "float32"), "wt": (32, "bfloat16"), "wq": (256, "bfloat16"), "yco": (48, "float32")}
+SCRATCH = {_n: ("sbuf", [128, NS * _c], _d) for _n, (_c, _d) in PART.items()}
+for _j in range(8):
+    SCRATCH["ps%d" % _j] = ("psum", [128, 512], "float32")
 for _n, _c, _d in [("ip", 4, "int32"), ("ci", 8, "int32"), ("cf", 8, "float32"), ("i128", 128, "float32"), ("iom", 128, "float32"),
-                   ("ioe", 64, "float32"), ("iol", 128, "float32"), ("iob", 24, "float32"), ("idn", 768, "bfloat16"),
-                   ("selm", 128, "float32"), ("sel", 64, "float32"), ("pair", 128, "float32"), ("mg", 8, "float32"), ("mge", 8, "float32"),
-                   ("ee", 256, "bfloat16"), ("lc", 256, "bfloat16"), ("lt", 256, "bfloat16"), ("ld", 256, "bfloat16"),
-                   ("cs", 16, "float32"), ("el", 24, "uint16"), ("bq", 24, "bfloat16"), ("prm", 384, "bfloat16"),
-                   ("kc", 32, "bfloat16"), ("zer", 256, "bfloat16"), ("thl", 4, "int32"), ("thf", 4, "float32"),
-                   ("thm", 8, "float32"), ("thb", 8, "float32"), ("one", 8, "bfloat16")]:
-    _buf(_n, _c, _d)
+                   ("iot", 128, "bfloat16"), ("iou", 128, "bfloat16"), ("iob", 24, "float32"), ("idn", 112, "bfloat16"),
+                   ("selm", 128, "float32"), ("sel", 32, "float32"), ("pair", 128, "float32"), ("mg", 8, "float32"), ("mge", 8, "float32"),
+                   ("ee", 32, "bfloat16"), ("lc", 512, "bfloat16"), ("lt", 512, "bfloat16"), ("cs", 24, "float32"),
+                   ("el", 4, "uint16"), ("prm", 448, "bfloat16"), ("kc", 32, "bfloat16"), ("cc", 512, "bfloat16"),
+                   ("thl", 4, "int32"), ("thf", 4, "float32"), ("thm", 8, "float32"), ("thb", 8, "float32"), ("one", 48, "bfloat16")]:
+    SCRATCH[_n] = ("sbuf", [128, _c], _d)
 
-SEMAPHORES = ["eV", "eS", "eP", "eG", "sent"] + ["d%d" % i for i in range(24)] + ["r%d" % i for i in range(12)]
+SEMAPHORES = ["eV", "eS", "eP", "eG", "sent"] + ["d%d" % i for i in range(56)] + ["r%d" % i for i in range(6 * NS)]
+
+COPIES = [(1.0, "n"), (-1.0, "q"), (2.0 ** -4, "b"), (-2.0 ** -4, "n"), (2.0 ** -8, "b"), (-2.0 ** -8, "n"), (2.0 ** -12, "b"), (-2.0 ** -12, "n")]
+UNITS = [4096.0, 256.0, 16.0, 1.0]
+LEVELS = [[(0, 0), (1, 0), (2, 0), (0, 1), (1, 1), (2, 1), (0, 2)], [(0, 3), (1, 4)], [(1, 5), (2, 6)], [(2, 7)]]
+NPART = 3
 
 
-def plan(T, rank, topo):
+def plan(T, rank, topo, cost=COST):
     ops = []
     half = [0]
     n = len(T.cores)
     core = T.cores[rank]
+    CY, PC = cost["cy"], cost["pc"]
 
     def op(alts, r=(), w=(), ps=(), kind="c", lat=0.0):
-        ps = [b.replace("sm", "sc") for b in ps]
         ops.append({"alts": alts, "r": list(r), "w": list(w), "ps": list(ps), "kind": kind, "lat": lat, "h": half[0]})
 
     def vc(k, half=False):
@@ -93,15 +62,19 @@ def plan(T, rank, topo):
     def G(fn, k, r, w):
         op({"G": (fn, 0.17 + 2 * k * CY)}, r, w)
 
-    def lin(out, in_, mul, add, k, r, w, ps=(), half=False, bias=None):
+    def fill(out, c, k, w, half=True):
+        op({"V": (lambda g: g.vector.memset(out, c), vc(k, half)),
+            "G": (lambda g: g.iota(out, [[0, k]], int(c), 0, allow_small_or_imprecise_dtypes=True), 0.13 + 2 * k * CY)}, [], w)
+
+    def lin(out, in_, mul, add, k, r, w, ps=(), half=False):
         def fs(g):
-            if add == 0.0:
-                return g.scalar.activation(out, in_, F.Copy, scale=mul)
-            return g.scalar.activation(out, in_, F.Identity, bias=bias, scale=mul)
+            if isinstance(add, float) and add == 0.0:
+                return g.scalar.activation(out, in_, F.Copy if isinstance(mul, float) else F.Identity, scale=mul)
+            return g.scalar.activation(out, in_, F.Identity, bias=add, scale=mul)
         alts = {"V": (lambda g: g.vector.tensor_scalar(out, in_, mul, add, A.mult, A.add), vc(k, half))}
-        if add == 0.0 or bias is not None:
+        if not isinstance(add, float) or add == 0.0:
             alts["S"] = (fs, vc(k))
-        op(alts, list(r) + (["cs"] if bias is not None else []), w, ps)
+        op(alts, r, w, ps)
 
     def P(mms, r, w, ps):
         def fn(g):
@@ -116,121 +89,146 @@ def plan(T, rank, topo):
             return (g.sync if q == "Y" else g.scalar).dma_start(out, in_)
         op({q: (fn, 0.1)}, r, w, kind="d", lat=us)
 
-    for h in range(2):
-        D("Y", T["lvl%d" % h][0:16, :], T.lv[4 * h:4 * h + 4, :], 2.0, [], ["lvl%d" % h])
-        D("Y", T["posl%d" % h][0:12, :], T.pos[12 * h:12 * h + 12, :], 2.0, [], ["posl%d" % h])
-        for u in range(2):
-            D("S" if h == 0 else "Y", T["tab%d" % h][64 * u:64 * u + 64, 16:4112], T.rf[64 * h:64 * h + 64, :], 5.0 + 4 * h, [], ["tab%d%d" % (h, u)])
-        for u in range(2):
-            D("Y", T["pfl%d" % h][64 * u:64 * u + 64, :], T.pf[64 * h:64 * h + 64, :], 2.5, [], ["pfl%d%d" % (h, u)])
-        if h == 0:
-            D("Y", T.thl[:, 0:1], T.th[:], 2.5, [], ["thl"])
+    def part(h):
+        def B(name, a=0, b=None, st=1, p0=0, p1=128):
+            c = PART[name][0]
+            return T[name][p0:p1, c * h + a:c * h + (c if b is None else b):st]
+        return B, (lambda s: s + str(h))
 
-    def iota(name, rows, pat, base=0):
+    def banks(h):
+        k = 8 // NS * h
+        if NS == 2:
+            return "ps%d" % k, "ps%d" % (k + 1), lambda s, c: ("ps%d" % (k + 2 + c), 0), 256
+        return "ps%d" % k, "ps%d" % (k + 1), lambda s, c: ("ps%d" % (k + 1), 256 + 128 * s), 128
+
+    R3, RG = 3 * NG, 16 * NG
+
+    def loads(h, gate):
+        B, K = part(h)
+        D("Y", B("lvl", p1=32), T.lv[NG * h:NG * h + NG, :], 2.0, [], [K("lvl")])
+        D("Y", B("posl", p1=R3), T.pos[R3 * h:R3 * h + R3, :], 2.0, [], [K("posl")])
+        for u in range(NU):
+            D("S" if h == 0 else "Y", B("tab", 0, 4096, 1, RG * u, RG * u + RG), T.rf[RG * h:RG * h + RG, :], 5.0 + (0 if gate else 4 * h), gate, [K("tab%d_" % u)])
+        for u in range(NU):
+            D("Y", B("pfl", p0=RG * u, p1=RG * u + RG), T.pf[RG * h:RG * h + RG, W * u:W * u + W], 2.5, [], [K("pfl%d_" % u)])
+
+    loads(0, [])
+    D("Y", T.thl[:, 0:1], T.th[:], 2.5, [], ["thl"])
+
+    def iota(name, rows, pat, base=0, cm=0, p0=0):
         k = 1
         for _s, c in pat:
             k *= c
-        G(lambda g: g.iota(T[name][0:rows, :], pat, base, 0, allow_small_or_imprecise_dtypes=True), k, [], [name])
-    G(lambda g: g.iota(T.ip[:, 0:1], [[0, 1]], 0, 1), 1, [], ["ip"])
-    iota("iol", 16, [[2, 2], [4, 4], [0, 16]])
-    iota("iob", 12, [[1, 3], [0, 2], [3, 4]])
+        G(lambda g: g.iota(T[name][p0:p0 + rows, 0:k], pat, base, cm, allow_small_or_imprecise_dtypes=True), k, [], [name + (str(p0) if p0 else "")])
+    G(lambda g: g.iota(T.ip[:], [[128, 4]], 0, 1), 4, [], ["ip"])
+    iota("iou", 32, [[4, NU], [4 * NU, NG], [0, 16]], 0, -1)
+    G(lambda g: g.affine_select(T.iot[0:32, :], T.iou[0:32, :], [[0, NU], [-4 * NU, NG], [0, 16]], A.is_ge, -100.0, 0, 1), 128, ["iou"], ["iot"])
     iota("i128", 128, [[1, 128]])
+    iota("iob", R3, [[1, 3], [3, NG], [0, 2]])
     iota("iom", 128, [[0, 4], [1, 16], [0, 2]])
-    iota("ioe", 64, [[-63, 4], [64, 4], [1024, 4]])
+    iota("kc", 64, [[-1, 16], [-30000, 2]])
+    lin(T.kc[32:64, 1:32:2], T.kc[32:64, 0:32:2], 1.0, 0.0, 16, ["kc"], ["kc32"])
+    V(lambda v: v.memset(T.kc[32:64, 0:32:2], -30000.0), 8, ["kc32"], ["kc32"])
     pc = T.ip[:, 0:1]
-    bits = [(A.bitwise_and, 15, None, None), (A.arith_shift_right, 4, None, None), (A.bitwise_and, 63, None, None),
-            (A.bitwise_and, 1, None, None), (A.bitwise_and, 31, None, None), (A.bitwise_and, 127, None, None),
-            (A.arith_shift_right, 1, A.bitwise_and, 15)]
+    bits = [(A.bitwise_and, 15, None, None), (A.arith_shift_right, 4, None, None), (A.bitwise_and, RG - 1, None, None),
+            (A.bitwise_and, 1, None, None), (A.bitwise_and, 31, None, None), (A.arith_shift_right, 1, A.bitwise_and, 15)]
+    cm, cg, crg, csx, c31, cm2, cp = [T.cf[:, i:i + 1] for i in range(7)]
     for i, (o0, s0, o1, s1) in enumerate(bits):
         if o1 is None:
             V(lambda v, i=i, o0=o0, s0=s0: v.tensor_scalar(T.ci[:, i:i + 1], pc, s0, None, o0), 1, ["ip"], ["ci%d" % i])
         else:
             V(lambda v, i=i, o0=o0, s0=s0, o1=o1, s1=s1: v.tensor_scalar(T.ci[:, i:i + 1], pc, s0, s1, o0, o1), 1, ["ip"], ["ci%d" % i])
-    V(lambda v: v.tensor_copy(T.cf[:, 0:7], T.ci[:, 0:7]), 7, ["ci%d" % i for i in range(7)], ["cf"])
-    cm, cg, c63, csx, c31, cp, cm2 = [T.cf[:, i:i + 1] for i in range(7)]
-    coef = [1.0, 16.0, 256.0, PEN, PEN + 256.0, -2.0]
-    for i, c in enumerate(coef):
-        k = 16 if i == 5 else 128
-        if i:
-            lin(T.idn[0:k, 128 * i:128 * i + k], T.idn[0:k, 0:k], c, 0.0, k, ["idn0"], ["idn%d" % i], half=True)
-            continue
-        V(lambda v, i=i, c=c, k=k: v.tensor_scalar(T.idn[0:k, 128 * i:128 * i + k], T.i128[0:k, 0:k], T.cf[0:k, 5:6], c, A.is_equal, A.mult),
-          k, ["i128", "cf"], ["idn%d" % i])
-
-    def ident(i, k=128):
-        return T.idn[0:k, 128 * i:128 * i + k]
+    V(lambda v: v.tensor_copy(T.cf[:, 0:6], T.ci[:, 0:6]), 6, ["ci%d" % i for i in range(6)], ["cf"])
+    V(lambda v: v.tensor_copy(cp, pc), 1, ["ip"], ["cp"])
+    V(lambda v: v.tensor_copy(T.el[:], T.ip[:]), 4, ["ip"], ["el"])
+    for q in range(4):
+        V(lambda v, q=q: v.tensor_scalar(T.lc[0:32, 128 * q:128 * q + 128], T.iot[0:32, :], float(-q), -UNITS[0], A.is_equal, A.mult), 128, ["iot"], ["lc%d" % q], half=True)
+        V(lambda v, q=q: v.tensor_scalar(T.lt[0:32, 128 * q:128 * q + 128], T.iot[0:32, :], float(-q), -UNITS[0], A.is_gt, A.mult), 128, ["iot"], ["lt%d" % q], half=True)
+    V(lambda v: v.memset(T.lc[32:33, :], C0 * UNITS[0]), 256, [], ["lcz"])
+    for i in range(3):
+        V(lambda v, i=i: v.memset(T.cc[0:1, 128 * i:128 * i + 128], C0 * (UNITS[i + 1] - UNITS[i])), 64, [], ["cc%d" % i])
+    V(lambda v: v.memset(T.cc[0:1, 384:512], 1.0), 64, [], ["cc3"])
+    V(lambda v: v.memset(T.live[32:33, :], 1.0), 256, [], ["livey"])
+    V(lambda v: v.tensor_scalar(T.idn[0:36, 0:36], T.i128[0:36, 0:36], T.cf[0:36, 6:7], None, A.is_equal), 36, ["i128", "cp"], ["idn0"])
+    lin(T.idn[0:32, 48:80], T.idn[0:32, 0:32], 0.375, 0.0, 32, ["idn0"], ["idn1"])
+    lin(T.idn[0:32, 80:112], T.idn[0:32, 0:32], 1.0, 0.0, 32, ["idn0"], ["idn2"])
+    V(lambda v: v.memset(T.idn[32:33, 80:112], C0), 16, [], ["idn3"])
     V(lambda v: v.tensor_scalar(T.selm[:], T.iom[:], cm, None, A.is_equal), 128, ["iom", "cf"], ["selm"])
-    V(lambda v: v.tensor_scalar(T.cs[:, 0:1], csx, -8.0, 8.0, A.mult, A.add), 1, ["cf"], ["cs0"])
-    V(lambda v: v.tensor_scalar(T.cs[:, 1:2], csx, 8.0, None, A.mult), 1, ["cf"], ["cs1"])
-    V(lambda v: v.tensor_scalar(T.cs[:, 2:3], cm, 3.0, 0.5, A.mult, A.add), 1, ["cf"], ["cs2"])
-    V(lambda v: v.tensor_scalar(T.cs[:, 4:7], T.i128[:, 0:3], T.cs[:, 2:3], None, A.add), 3, ["cs2", "i128"], ["cs4"])
-    V(lambda v: v.tensor_scalar(T.cs[:, 8:11], T.i128[:, 16:64:16], cm, None, A.add), 3, ["cf", "i128"], ["cs8"])
-    BR, BA, BB, BY = -(96.0 + 0.5 / 4096), 63.75, -2040.25, MAGIC + 512.0
-    for i, c in enumerate([BR, BA, BB, BY]):
-        V(lambda v, i=i, c=c: v.memset(T.cs[:, 12 + i:13 + i], c), 1, [], ["cs"])
+    col = lambda i: T.cs[:, i:i + 1]
+    V(lambda v: v.tensor_scalar(col(0), csx, -16.0, 16.0, A.mult, A.add), 1, ["cf"], ["cs0"])
+    lin(col(1), csx, 16.0, 0.0, 1, ["cf"], ["cs1"])
+    V(lambda v: v.tensor_scalar(col(2), cm, 3.0, 0.5, A.mult, A.add), 1, ["cf"], ["cs2"])
+    lin(T.cs[:, 4:7], T.i128[:, 0:3], 1.0, col(2), 3, ["cs2", "i128"], ["cs4"])
+    V(lambda v: v.tensor_scalar(col(8), cm, 6.0, None, A.not_equal), 1, ["cf"], ["csq"])
+    V(lambda v: v.tensor_scalar(col(9), col(8), -30.0, 31.0, A.mult, A.add), 1, ["csq"], ["csb"])
+    V(lambda v: v.tensor_scalar(col(10), cm, 7.0, 2047.0, A.not_equal, A.add), 1, ["cf"], ["cs10"])
+    lin(col(11), col(8), -2048.0, col(10), 1, ["csq", "cs10"], ["cs11"])
+    V(lambda v: v.tensor_scalar(col(12), col(11), 0.0, None, A.not_equal), 1, ["cs11"], ["cs12"])
+    V(lambda v: v.tensor_scalar(col(13), c31, float(NG), -0.1875, A.is_lt, A.mult), 1, ["cf"], ["cs13"])
+    lin(col(14), col(11), 0.5, 0.0, 1, ["cs11"], ["csc0"])
+    lin(col(15), col(8), -2.0, 1.0, 1, ["csq"], ["csc1"])
+    for i, (f, kind) in enumerate(COPIES):
+        if kind == "b":
+            lin(col(14 + i), col(9), f, 0.0, 1, ["csb"], ["csc%d" % i])
     for s in range(2):
-        V(lambda v, s=s: v.tensor_scalar(T.sel[:, 32 * s:32 * s + 32], T.iom[:, 0:32], cm2, T.cs[:, s:s + 1], A.is_equal, A.mult),
-          32, ["iom", "cf", "cs%d" % s], ["sel%d" % s])
-        V(lambda v, s=s: v.tensor_scalar(T.pair[:, 64 * s:64 * s + 64], T.i128[:, 0:64], c63, None, A.is_equal), 64, ["i128", "cf"], ["pair%d" % s])
-        V(lambda v, s=s: v.tensor_scalar(T.lc[0:16, 128 * s:128 * s + 128], T.iol[0:16, :], float(s), T.cf[0:16, 5:6], A.add, A.is_equal),
-          128, ["iol", "cf"], ["lc%d" % s])
+        V(lambda v, s=s: v.tensor_scalar(T.sel[:, 16 * s:16 * s + 16], T.i128[:, 0:16], cm2, col(s), A.is_equal, A.mult),
+          16, ["i128", "cf", "cs%d" % s], ["sel%d" % s])
+    for u in range(NU):
+        V(lambda v, u=u: v.tensor_scalar(T.pair[:, RG * u:RG * u + RG], T.i128[:, 0:RG], crg, None, A.is_equal), RG, ["i128", "cf"], ["pair%d" % u])
     V(lambda v: v.tensor_scalar(T.mg[:], T.i128[:, 0:8], cg, None, A.is_equal), 8, ["i128", "cf"], ["mg"])
     lin(T.mge[:], T.mg[:], 2.0 ** -10, 0.0, 8, ["mg"], ["mge"])
-    for q in range(4):
-        V(lambda v, q=q: v.tensor_scalar(T.ee[0:36, 64 * q:64 * q + 64], T.ioe[0:36, :], -1024.0 * q, T.cf[0:36, 4:5], A.add, A.is_equal),
-          64, ["ioe", "cf"], ["ee%d" % q])
-    V(lambda v: v.memset(T.lt[0:16, 0:64], 0.0), 32, [], ["lt0a"])
-    V(lambda v: v.tensor_tensor(T.lt[0:16, 64:128], T.lc[0:16, 0:64], T.lc[0:16, 128:192], A.add), 128, ["lc0", "lc1"], ["lt0b"])
-    V(lambda v: v.tensor_tensor(T.lt[0:16, 128:256], T.lt[0:16, 0:128], T.lc[0:16, 0:128], A.add), 256, ["lc0", "lt0a", "lt0b"], ["lt1"])
-    lin(T.ld[0:16, :], T.lc[0:16, :], PEN / 2, 0.0, 256, ["lc0", "lc1"], ["ld"], half=True)
-    for j in range(3):
-        V(lambda v, j=j: v.tensor_scalar(T.el[:, 8 * j:8 * j + 8], T.mg[:], T.cs[:, 8 + j:9 + j], None, A.mult), 8, ["mg", "cs8"], ["el%d" % j])
-    V(lambda v: v.tensor_scalar(T.bq[0:12, :], T.iob[0:12, :], T.cf[0:12, 5:6], None, A.is_equal), 24, ["iob", "cf"], ["bq"])
-    V(lambda v: v.memset(T.prm[0:12, :], 0.0), 192, [], ["permz"])
-    V(lambda v: v.memset(T.one[0:12, :], 1.0), 8, [], ["one"])
+    fill(T.ee[0:36, :], 0.0, 32, ["eez"])
+    V(lambda v: v.tensor_scalar(T.ee[0:36, R3:R3 + NG], T.i128[0:36, 0:NG], T.cf[0:36, 4:5], T.cs[0:36, 13:14], A.is_equal, A.mult), 4, ["i128", "cf", "cs13", "eez"], ["ee"])
+    V(lambda v: v.memset(T.prm[0:R3, :], 0.0), 224, [], ["permz"])
+    V(lambda v: v.memset(T.one[0:R3, 0:32], 1.0), 16, [], ["one"])
+    V(lambda v: v.memset(T.one[0:R3, 17:32:2], -1.0), 8, ["one"], ["one"])
     rows = [(1, 2, 0, 2, 0, 1), (2, 0, 1, 1, 2, 0), (0, 1, 2, 0, 1, 2)]
-    for k in range(3):
+    for k in range(2):
         for r in range(6):
-            c = rows[k][r]
-            out = T.prm[0:12, 128 * k + r:128 * k + 128:16]
-            if k == 0:
-                G(lambda g, out=out, c=c: g.affine_select(out, T.one[0:12, :], [[0, 2], [-3, 4]], A.is_equal, 0.0, -c, 1), 8,
-                  ["one", "permz"], ["perm%d%d" % (k, r)])
-            else:
-                lin(out, T.bq[0:12, 8 * c:8 * c + 8], -1.0 if (k == 2 and r >= 3) else 1.0, 0.0, 8, ["bq", "permz"], ["perm%d%d" % (k, r)])
-    V(lambda v: v.tensor_scalar(T.kc[0:64, :], T.iom[0:64, 0:32], -1.0, 7.5, A.mult, A.add), 32, ["iom"], ["kc"])
-    V(lambda v: v.memset(T.kc[0:32, 1:32:2], -65536.0), 16, [], ["kc"])
-    V(lambda v: v.memset(T.kc[32:64, 0:32:2], -65536.0), 16, [], ["kc"])
-    V(lambda v: v.memset(T.zer[0:16, :], 0.0), 128, [], ["zer"])
+            out = T.prm[0:R3, 256 * k + r:256 * k + 128:8]
+            G(lambda g, out=out, c=rows[k][r], k=k: g.affine_select(out, T.one[0:R3, 16 - 16 * k:32 - 16 * k], [[0, NU], [-3, NG], [0, 2]], A.is_equal, 0.0, -c, 1),
+              16, ["one", "permz"], ["perm%d%d" % (k, r)])
+    V(lambda v: v.tensor_scalar(T.prm[0:R3, 128:256], T.prm[0:R3, 0:128], -1.0, 0.0, A.mult, A.max), 128, ["perm0%d" % r for r in range(6)] + ["permz"], ["permlo"], half=True)
+    for r in range(6):
+        c = rows[2][r]
+        V(lambda v, r=r, c=c: v.tensor_scalar(T.prm[0:R3, 384 + r:384 + RG:8], T.iob[0:R3, 2 * NG * c:2 * NG * (c + 1)], T.cf[0:R3, 6:7], -1.0 if r >= 3 else 1.0,
+                                              A.is_equal, A.mult), 8, ["iob", "cp", "permz"], ["perm2%d" % r])
     V(lambda v: v.tensor_copy(T.thf[:, 0:1], T.thl[:, 0:1]), 1, ["thl"], ["thf"])
-    V(lambda v: v.tensor_scalar(T.thm[:], T.mg[:], T.thf[:, 0:1], None, A.mult), 8, ["mg", "thf"], ["thm"])
-    P([(T.sc1[:, 0:8], T.selm[:], T.thm[:], True, True, 256)], ["selm", "thm"], ["sc1a"], ["sc1"])
-    V(lambda v: v.tensor_scalar(T.thb[:], T.sc1[:, 0:8], -1.0, 0.5, A.mult, A.add), 8, ["sc1a"], ["thb"], ["sc1"])
+    lin(T.thm[:], T.mg[:], T.thf[:, 0:1], 0.0, 8, ["mg", "thf"], ["thm"])
+    P([(T.ps7[:, 0:8], T.selm[:], T.thm[:], True, True, 256)], ["selm", "thm"], ["ps7"], ["ps7"])
+    V(lambda v: v.tensor_scalar(T.thb[:], T.ps7[:, 0:8], -1.0, 0.5, A.mult, A.add), 8, ["ps7"], ["thb"], ["ps7"])
 
     def setup(h):
-        B = lambda s: T[s + str(h)]
-        K = lambda s: s + str(h)
-        V(lambda v: v.memset(B("tab")[:, 0:16], -1073741824.0), 8, [], [K("tabz")])
-        V(lambda v: v.memset(B("live")[0:16, 128:512], 0.0), 192, [], [K("livez")])
-        V(lambda v: v.tensor_copy(B("live")[0:16, 0:128], B("lvl")[0:16, :]), 128, [K("lvl")], [K("live0")])
-        V(lambda v: v.memset(B("ina")[:, 0:32], 0.0), 32, [], [K("inaz")])
-        V(lambda v: v.memset(B("xb")[:, 0:16], 0.0), 16, [], [K("xbz")])
-        for k, nm in enumerate(["xw", "yw", "py"]):
-            yb = T["yb%d" % k]
-            P([(yb[:], T.prm[0:12, 128 * k:128 * k + 128], B("posl")[0:12, :], True, True, 512)],
-              [K("posl")] + ["perm%d%d" % (k, r) for r in range(6)], ["ys%d" % k], ["yb%d" % k])
-            if k < 2:
-                V(lambda v, nm=nm: v.memset(B(nm)[:, 512:528], 0.0), 8, [], [K(nm + "z")])
-                lin(B(nm)[:, 0:512], yb[:], 1.0, 0.0, 512, ["ys%d" % k], [K(nm)], ["yb%d" % k])
-            else:
-                for u in range(2):
-                    V(lambda v, u=u, yb=yb: v.tensor_copy(B("py")[64 * u:64 * u + 64, :], yb[64 * u:64 * u + 64, u:512:2]), 256,
-                      ["ys2"], [K("py%d" % u)], ["yb2"])
+        B, K = part(h)
+        sc, sm, blk, _cn = banks(h)
+        fill(B("tab", 4096, 4112), -8388608.0, 16, [K("tabz")])
+        fill(B("live", XH, p1=32), 0.0, 3 * XH, [K("livez")])
+        V(lambda v: v.tensor_copy(B("live", 0, XH, p1=32), B("lvl", p1=32)), XH, [K("lvl")], [K("live0")])
+        fill(B("xb", 0, 16), 0.0, 16, [K("xbz")])
+        fill(B("wq"), 0.0, 256, [K("wq")])
+        for s in range(2):
+            fill(B("lh", 384 * s, 384 * s + 384), 0.0, 384, [K("lh%d" % s)])
+        pos, posh = B("posl", p1=R3), B("posh", p1=R3)
+        V(lambda v: v.tensor_scalar(posh, pos, 8 * C0, 8 * C0, A.add, A.subtract), 512, [K("posl")], [K("posh")], half=True)
+        pa, pb = (blk(0, 0)[0], blk(0, 1)[0]) if NS == 2 else (sc, sm)
+        P([(T[pa][:], T.prm[0:R3, 128:256], pos, True, False, 512), (T[pa][:], T.prm[0:R3, 0:128], posh, False, True, 512)],
+          [K("posl"), K("posh"), "permlo"], [pa], [pa])
+        P([(T[pb][:], T.prm[0:R3, 256:384], pos, True, True, 512)], [K("posl")] + ["perm1%d" % r for r in range(6)], [pb], [pb])
+        for nm, bank in (("xw", pa), ("yw", pb)):
+            lin(B(nm, 0, 512), T[bank][:], 1.0, col(12), 512, [bank, "cs12"], [K(nm)], [bank])
+            lin(B(nm, 512, 528), T.i128[:, 0:16], 0.0, col(12), 16, ["i128", "cs12"], [K(nm + "z")])
+        P([(T[sc][RG * u:RG * u + RG, 0:W], T.prm[0:R3, 384:384 + RG], B("posl", W * u, W * u + W, p1=R3), True, True, W) for u in range(NU)],
+          [K("posl")] + ["perm2%d" % r for r in range(6)], [sc], [sc])
+        lin(B("py", 0, W), T[sc][:, 0:W], -1.0, col(14), W, [sc, "csc0"], [K("py0")], [sc])
+        for i, (f, kind) in enumerate(COPIES):
+            if i:
+                lin(B("py", W * i, W * i + W), B("py", 0, W), f if kind == "n" else col(14 + i), 0.0, W,
+                    [K("py0")] + ([] if kind == "n" else ["csc%d" % i]), [K("py%d" % i)], half=True)
         for q in range(8):
-            o, i_, mc, ec = B("pfb")[:, q:2048:8], B("pfl")[:, q // 4:512:2], T.mg[:, q:q + 1], T.mge[:, q:q + 1]
-            op({"V": (lambda g, o=o, i_=i_, mc=mc: g.vector.tensor_scalar(o, i_, 2.0 ** -10, mc, A.max, A.mult), vc(256, True)),
-                "S": (lambda g, o=o, i_=i_, mc=mc, ec=ec: g.scalar.activation(o, i_, F.Identity, bias=ec, scale=mc), vc(256))},
-               [K("pfl") + "0", K("pfl") + "1", "mg", "mge"], [K("pfb%d" % q)])
+            o, i_, mc, ec = B("pfb", q, 8 * W, 8), B("pfl"), T.mg[:, q:q + 1], T.mge[:, q:q + 1]
+            op({"V": (lambda g, o=o, i_=i_, mc=mc: g.vector.tensor_scalar(o, i_, 2.0 ** -10, mc, A.max, A.mult), vc(W, True)),
+                "S": (lambda g, o=o, i_=i_, mc=mc, ec=ec: g.scalar.activation(o, i_, F.Identity, bias=ec, scale=mc), vc(W))},
+               [K("pfl%d_" % u) for u in range(NU)] + ["mg", "mge"], [K("pfb%d" % q)])
 
     nrem = [0]
 
@@ -248,135 +246,137 @@ def plan(T, rank, topo):
             g.remote_dma_fused([tr], local_sem=T.sem.sent)
             return ne
         op({"G": (fn, 0.3)}, key, [land + "s"], kind="s")
-        op({"N": ((sem, ne * len(dsts)), 0.0)}, [land + "s"], [land], kind="a", lat=NET)
+        op({"N": ((sem, ne * len(dsts)), 0.0)}, [land + "s"], [land], kind="a", lat=cost["net"])
 
     def front(h, t):
-        B = lambda s: T[s + str(h)]
-        K = lambda s: s + str(h)
-        live = B("live")[0:16, 128 * t:128 * t + 256]
-        lk = K("live%d" % t)
-        sc, sm, cum = B("sc"), B("sc"), B("cum")
-        V(lambda v: v.tensor_tensor_scan(cum[0:16, :], live, T.zer[0:16, :], 0.0, A.add, A.add), 256, [lk, "zer", K("livez"), K("live%d" % (t + 1))], [K("cum")], half=True)
+        B, K = part(h)
+        _sc, smn, blk, cn0 = banks(h)
+        sm = T[smn]
+        live = B("live", XH * t, XH * t + 2 * XH, p1=32)
+        V(lambda v: v.tensor_tensor_scan(B("cum", p1=32), live, live, 0.0, A.add, A.max), 2 * XH,
+          [K("live%d" % t), K("livez"), K("live%d" % (t + 1))], [K("cum")], half=True)
         mm = []
-        for b in range(2):
-            o = sc[:, 128 + 128 * b:256 + 128 * b]
-            mm.append((o, T.lc[0:16, 128 * b:128 * b + 128], cum[0:16, 0:128], True, False, 128))
-            mm.append((o, T.lt[0:16, 128 * b:128 * b + 128], cum[0:16, 128:256], False, True, 128))
-        P(mm, [K("cum"), "lc0", "lc1", "lt0a", "lt0b", "lt1"], [K("cn")], [K("sc")])
-        for i in range(3):
-            S(lambda a, i=i: a.activation(B("junk")[:, 256 * i:256 * i + 256], sc[:, 128:384], F.Sign, bias=T.cs[:, 4 + i:5 + i], scale=-1.0,
-                                          accum_out=B("ac3")[:, i:i + 1]),
-              276, [K("cn"), "cs4"], [K("ac3%d" % i)], [K("sc")])
-        P([(sm[:, 256:259], T.pair[:], B("ac3")[:, 0:3], True, True, 256), (sm[:, 259:260], T.pair[:], B("ac3")[:, 0:1], True, True, 256)],
-          [K("ac3%d" % i) for i in range(3)] + ["pair0", "pair1"], [K("pr")], [K("sm")])
-        V(lambda v: v.tensor_scalar(B("sl")[:], sm[:, 256:260], 0.5, 256.0, A.mult, A.add), 4, [K("pr")], [K("sl")], [K("sm")])
-        V(lambda v: v.tensor_copy(B("xb")[:, 16:80], B("xw")[:].indirect(B("sl")[:])), 100, [K("sl"), K("xw"), K("xwz")], [K("xb")])
-        prod = B("prod")[:, 64 * t:64 * t + 64]
-        prin = B("prin")[:, 64 * t:64 * t + 64]
-        V(lambda v: v.tensor_tensor(prod, B("yw")[:].indirect(B("sl")[:]), B("xb")[:, 0:64], A.mult), 100,
+        for q in range(4):
+            o = sm[:, cn0 + XH * q:cn0 + XH * q + XH]
+            mm.append((o, T.lc[0:32, 128 * q:128 * q + 128], B("cum", 0, XH, p1=32), True, False, 64))
+            mm.append((o, T.lt[0:32, 128 * q:128 * q + 128], B("cum", XH, p1=32), False, True, 64))
+        P(mm, [K("cum")] + ["lc%d" % q for q in range(4)] + ["lt%d" % q for q in range(4)], [K("cn")], [smn])
+        for i, k in enumerate((1, 2, 0)):
+            S(lambda a, i=i, k=k: a.activation(B("junk", W * i, W * i + W), sm[:, cn0:cn0 + W], F.Sign, bias=col(4 + k), scale=1.0 / UNITS[0],
+                                               accum_out=B("ac3", i, i + 1)),
+              W + 20, [K("cn"), "cs4"], [K("ac3%d" % i)], [smn])
+        P([(sm[:, 48:51], T.pair[:], B("ac3", 0, 3), True, True, 256), (sm[:, 51:52], T.pair[:], B("ac3", 0, 1), True, True, 256)],
+          [K("ac3%d" % i) for i in range(3)] + ["pair%d" % u for u in range(NU)], [K("pr")], [smn])
+        sl = B("sl", 0, 4)
+        V(lambda v: v.tensor_scalar(sl, sm[:, 48:52], 0.5, 256.0, A.mult, A.add), 4, [K("pr")], [K("sl")], [smn])
+        V(lambda v: v.tensor_copy(B("xb", 16, 80), B("xw").indirect(sl)), 64 * cost["gath"], [K("sl"), K("xw"), K("xwz")], [K("xb")])
+        prod, prin = B("prod", 64 * t + 16, 64 * t + 64), B("prin", 48 * t, 48 * t + 48)
+        V(lambda v: v.tensor_tensor(B("prod", 64 * t, 64 * t + 64), B("yw").indirect(sl), B("xb", 0, 64), A.mult), 64 * cost["gath"],
           [K("sl"), K("yw"), K("ywz"), K("xb"), K("xbz")], [K("prod%d" % t)])
         send(prod, [(T.cores[(rank + t + 1) % n], prin)], [K("prod%d" % t)], K("prin%d" % t))
-        cj = [0, 2, 1]
-        c0 = 16.0 + 273 * 1984.0 - 3 * PEN * 64 - PEN / 2
         for s in range(2):
-            src = prin if s else prod
-            V(lambda v, s=s, src=src: v.tensor_copy(B("lh")[:, 384 * s:384 * s + 384], src.indirect(T.el[:])), 384 * GATH,
-              [K(("prin%d" if s else "prod%d") % t), "el0", "el1", "el2"], [K("lh%d" % s)])
-            cb, cw = "cb%d" % s, "cw%d" % s
-            cbs = T[cb][:, 0:256]
-            for part, (js, bank, c1) in enumerate([((0, 1), "yb%d" % (2 * s), 0), ((2,), "yb%d" % (2 * s + 1), 0)]):
-                k = 256 * len(js)
-                yk = "y%d%d" % (part, s)
-                P([(T[bank][:, c1 + 256 * i:c1 + 256 * i + 256], B("lh")[:, 384 * s + 128 * j:384 * s + 128 * j + 128], B("py")[:], True, True, 256)
-                   for i, j in enumerate(js)], [K("lh%d" % s), K("py0"), K("py1")], [yk], [bank])
-                cols = slice(768 * s + 512 * part, 768 * s + 512 * part + k)
-                tag = "%d%d" % (part, s)
-                lin(B("rr")[:, cols], T[bank][:, c1:c1 + k], -1.0 / 4096, BR, k, [yk], [K("rr" + tag)], [bank], bias=T.cs[:, 12:13])
-                lin(B("aa")[:, cols], B("rr")[:, cols], -1.0, BA, k, [K("rr" + tag)], [K("aa" + tag)], half=True, bias=T.cs[:, 13:14] if AS else None)
-                lin(B("bb")[:, cols], B("rr")[:, cols], 1.0, BB, k, [K("rr" + tag)], [K("bb" + tag)], half=True, bias=T.cs[:, 14:15] if BS else None)
-                col = lambda nm, j, s=s: B(nm)[:, 768 * s + 256 * j:768 * s + 256 * j + 256]
-                P([(cbs, ident(3), col("rr", j), j == 0, False, 256) for j in js], [K("rr" + tag), "idn3"], [cw], [cb])
-                if part == 0:
-                    mm = []
-                    for q in range(4):
-                        for u in range(2):
-                            mm.append((T[cb][64 * u:64 * u + 64, 64 * q:64 * q + 64],
-                                       T.ld[0:16, 128 * (q % 2) + 64 * (q // 2):128 * (q % 2) + 64 * (q // 2) + 64],
-                                       B("live")[0:16, 128 * t + u:128 * t + 128:2], False, False, 64))
-                    P(mm, [lk, "ld"], [cw], [cb])
+            lh = K("lh%d" % s)
+            V(lambda v, s=s: v.tensor_copy(B("lh", 384 * s, 384 * s + 384).indirect(T.el[:, 0:3]), prin if s else prod), 48 * cost["scat"],
+              [K(("prin%d" if s else "prod%d") % t), "el"], [lh])
+            for c in range(W // 128):
+                bank, c0 = blk(s, c)
+                o, pk, nq = T[bank][:, c0:c0 + 128], K("pl%d" % c0) + bank, 128 // XH
                 mm = []
-                for j in js:
-                    mm += [(cbs, ident(i), col("aa", j), False, False, 256) for i in ([4] if cj[j] == 2 else [3, cj[j]])]
-                P(mm, [K("aa" + tag), "idn3", "idn4", "idn0", "idn1"], [cw], [cb])
-                P([(cbs, ident(cj[j]), col("bb", j), False, j == 2, 256) for j in js], [K("bb" + tag), "idn0", "idn1", "idn2"], [cw], [cb])
-            V(lambda v, s=s, cbs=cbs: v.tensor_scalar(B("off")[:, 256 * s:256 * s + 256], cbs, c0, 0.0, A.add, A.max), 256,
-              [cw], [K("off%d" % s)], [cb])
+                for i, level in enumerate(LEVELS):
+                    if i:
+                        mm.append(((o, T.cc[0:1, 128 * i - 128:128 * i], T.cc[0:1, 384:512], False, False, 128), ["cc%d" % (i - 1), "cc3"]))
+                    for j, k in level:
+                        mm.append(((o, B("lh", 384 * s + 128 * j, 384 * s + 128 * j + 128), B("py", W * k + 128 * c, W * k + 128 * c + 128), not mm, i == 3, 128),
+                                   [lh, K("py%d" % k)]))
+                        if len(mm) == 1:
+                            mm += [((T[bank][:, c0 + XH * q:c0 + XH * q + XH], T.lc[0:33, 128 * (nq * c + q):128 * (nq * c + q + 1)],
+                                     B("live", XH * t, XH * t + XH, p1=33), False, False, 64), [K("live%d" % t), "livey", "lcz", "lc%d" % (nq * c + q)])
+                                   for q in range(nq)]
+                for i in range(NPART):
+                    mp = mm[len(mm) * i // NPART:len(mm) * (i + 1) // NPART]
+                    P([m[0] for m in mp], [k for m in mp for k in m[1]], [pk], [bank])
+                V(lambda v, s=s, c=c, o=o: v.tensor_scalar(B("off", W * s + 128 * c, W * s + 128 * c + 128), o, UNITS[0] - C0, 4096.0, A.add, A.min), 128,
+                  [pk], [K("off%d%d" % (s, c))], [bank])
 
     def back(h, t):
-        B = lambda s: T[s + str(h)]
-        K = lambda s: s + str(h)
-        sc, sm, gat = B("sc"), B("sc"), B("gat")
+        B, K = part(h)
+        scn, smn, _blk, _cn = banks(h)
+        sc, sm = T[scn], T[smn]
         for s in range(2):
             for c in range(NCH):
-                o = gat[:, 32 * KCH * c + s:32 * KCH * (c + 1):2]
-                w = B("tab")[:].indirect(B("off")[:, 256 * s + KCH * c:256 * s + KCH * (c + 1)])
-                us = 0.06 + 16 * KCH * GATH * CY
+                o = B("gat", 32 * KCH * c + s, 32 * KCH * (c + 1), 2)
+                w = B("tab").indirect(B("off", W * s + KCH * c, W * s + KCH * (c + 1)))
+                us = 0.06 + 16 * KCH * cost["gath"] * CY
                 op({"V": (lambda g, o=o, w=w: g.vector.tensor_copy(o, w), us), "S": (lambda g, o=o, w=w: g.scalar.activation(o, w, F.Copy), us)},
-                   [K("off%d" % s), K("tab") + "0", K("tab") + "1", K("tabz")], [K("gat%d%d_" % (s, c))])
+                   [K("off%d%d" % (s, KCH * c // 128)), K("tabz")] + [K("tab%d_" % u) for u in range(NU)], [K("gat%d%d_" % (s, c))])
                 ops[-1]["fill"] = (2 * (NCH - 1 - c) + 1 - s) * us / 2
         for c in range(NCH):
             mm = []
             for x in range(c * KCH, (c + 1) * KCH):
-                q, xh = x // 64, x % 64
-                mm.append((sc[32 * q:32 * q + 32, 8 * xh:8 * xh + 8], gat[:, 32 * x:32 * x + 32], B("pfb")[:, 8 * x:8 * x + 8], True, True, 32))
-            P(mm, [K("gat0%d_" % c), K("gat1%d_" % c)] + [K("pfb%d" % q) for q in range(8)], [K("s%d_" % c)], [K("sc")])
-        acc = B("acc")[:, 4 * t:4 * t + 4]
-        for k in range(4):
-            S(lambda a, k=k: a.activation(B("hit")[:, 128 * k:128 * k + 128], sc[:, k:512:4], F.Sign, bias=T.thb[:, 4 * h + k:4 * h + k + 1],
-                                          accum_out=B("acc")[:, 4 * t + k:4 * t + k + 1]),
-              148, [K("s%d_" % c) for c in range(NCH)] + ["thb"], [K("hit%d" % k), K("acc%d%d" % (t, k))], [K("sc")])
+                q, xh = x // XH, x % XH
+                mm.append((sc[32 * q:32 * q + 32, 8 * xh:8 * xh + 8], B("gat", 32 * x, 32 * x + 32), B("pfb", 8 * x, 8 * x + 8), True, True, 32))
+            P(mm, [K("gat0%d_" % c), K("gat1%d_" % c)] + [K("pfb%d" % q) for q in range(8)], [K("s%d_" % c)], [scn])
+        acc = B("acc", 4 * t, 4 * t + NG)
+        for k in range(NG):
+            S(lambda a, k=k: a.activation(B("hit", 128 * k, 128 * k + 128), sc[:, k:8 * XH:NG], F.Sign, bias=T.thb[:, NG * h + k:NG * h + k + 1],
+                                          accum_out=B("acc", 4 * t + k, 4 * t + k + 1)),
+              148, [K("s%d_" % c) for c in range(NCH)] + ["thb"], [K("hit%d" % k), K("acc%d%d" % (t, k))], [scn])
         ca, cc = T.cores[(rank - t - 1) % n], T.cores[(rank + t + 1) % n]
-        ina, inc = B("ina")[:, 32 + 4 * t:36 + 4 * t], B("inc")[:, 4 * t:4 * t + 4]
+        ina, inc = B("ina", 4 * t, 4 * t + NG), B("inc", 4 * t, 4 * t + NG)
         if ca == cc:
             inc = ina
             dsts = [(cc, ina)]
         else:
             dsts = [(cc, ina), (ca, inc)]
-        ak = [K("acc%d%d" % (t, k)) for k in range(4)]
+        ak = [K("acc%d%d" % (t, k)) for k in range(NG)]
         send(acc, dsts, ak, K("in%d" % t))
-        s0, s1 = T.sel[:, 0:32], T.sel[:, 32:64]
-        P([(sm[0:36, 0:32], ident(0, 36), T.kc[0:36, :], True, False, 36), (sm[0:4, 0:32], acc, s0, False, False, 128),
-           (sm[32:36, 0:32], acc, s1, False, False, 128)], ak + ["kc", "idn0", "sel0", "sel1"], [K("key")], [K("sm")])
-        P([(sm[0:4, 0:32], inc, s1, False, False, 128), (sm[0:36, 0:32], B("ina")[:, 4 * t:4 * t + 36], s0, False, True, 144)],
-          [K("in%d" % t), K("inaz")], [K("key")], [K("sm")])
-        V(lambda v: v.tensor_reduce(B("mx")[0:36, 0:1], sm[0:36, 0:32], AxisListType.X, A.max), 32, [K("key")], [K("mx")], [K("sm")])
-        V(lambda v: v.tensor_scalar(B("wt")[0:36, :], sm[0:36, 0:32], B("mx")[0:36, 0:1], None, A.is_equal), 32, [K("key"), K("mx")], [K("wt")], [K("sm")])
-        V(lambda v: v.tensor_scalar(B("ycm")[0:4, t:48:3], sm[0:4, 0:32:2], 1.0 / 16, BY, A.mult, A.add), 16, [K("key")], [K("ycm%d" % t)], [K("sm")])
-        P([(sc[32 * q:32 * q + 32, 0:64], B("wt")[0:36, :], T.ee[0:36, 64 * q:64 * q + 64], True, True, 64) for q in range(4)],
-          [K("wt")] + ["ee%d" % q for q in range(4)], [K("w")], [K("sc")])
-        lin(B("wq")[:], sc[:, 0:64], 1.0, 0.0, 64, [K("w")], [K("wq")], [K("sc")])
-        live = B("live")[0:16, 128 * t:128 * t + 128]
-        nxt = B("live")[0:16, 128 * t + 128:128 * t + 256]
-        dd = sm[0:16, 64:192]
-        mm = [(dd, ident(5, 16), live, True, False, 128)]
-        for k in range(4):
-            mm.append((dd, B("wq")[:, 16 * k:16 * k + 16], B("hit")[:, 128 * k:128 * k + 128], False, k == 3, 128))
-        P(mm, [K("wq"), K("live%d" % t), "idn5"] + [K("hit%d" % k) for k in range(4)], [K("dd")], [K("sm")])
-        V(lambda v: v.tensor_scalar(nxt, dd, -3.0, None, A.is_lt), 128, [K("dd"), K("livez")], [K("live%d" % (t + 1))], [K("sm")])
-        age = B("age")[0:16, :]
-        V(lambda v: v.tensor_tensor(age, age if t else live, nxt, A.add), 256, [K("live%d" % t), K("live%d" % (t + 1))] + ([K("age")] if t else []), [K("age")])
+        s0, s1 = T.sel[:, 0:16], T.sel[:, 16:32]
+        key, k0, k1 = sm[0:36, 0:32], sm[0:NG, 0:32:2], sm[32:32 + NG, 1:32:2]
+        P([(key, T.idn[0:36, 0:36], T.kc[0:36, :], True, False, 36), (k0, acc, s0, False, False, 64), (k1, acc, s1, False, False, 64)],
+          ak + ["kc", "kc32", "idn0", "sel0", "sel1"], [K("key")], [smn])
+        P([(k0, inc, s1, False, False, 64), (k1, ina, s0, False, False, 64), (key, T.idn[0:36, 0:36], T.kc[0:36, :], False, True, 36)],
+          [K("in%d" % t)], [K("key")], [smn])
+        mx = B("mx", 0, 1, p1=36)
+        V(lambda v: v.tensor_reduce(mx, key, AxisListType.X, A.max), 32, [K("key")], [K("mx")], [smn])
+        V(lambda v: v.tensor_scalar(B("wt", p1=36), key, mx, None, A.is_equal), 32, [K("key"), K("mx")], [K("wt")], [smn])
+        P([(sm[32 * q:32 * q + 32, 32:32 + 4 * NG], B("wt", p1=36), T.ee[0:36, R3 - NG * q:R3 - NG * q + 4 * NG], True, True, 32) for q in range(4)],
+          [K("wt"), "ee"], [K("w")], [smn])
+        yc = sm[0:NG, 64 + t:112:3]
+        ycm = [(yc, acc, s0, True, False, 64), (yc, inc, s1, False, True, 64)]
         if t == RO - 1:
-            V(lambda v: v.tensor_scalar(B("yco")[0:4, :], B("ycm")[0:4, :], -MAGIC, None, A.add), 48, [K("ycm%d" % i) for i in range(RO)], [K("yco")])
-            D("Y", T.yc[64 * h:64 * h + 64, :], B("yco")[0:4, :], 2.0, [K("yco")], [K("oc")])
-            D("Y", T.ya[4 * h:4 * h + 4, :], age, 2.0, [K("age")], [K("oa")])
+            P(ycm, [K("in%d" % t), K("w")], [K("yc%d" % t)], [smn])
+        lin(B("wq", 112, 112 + 4 * NG), sm[:, 32:32 + 4 * NG], 1.0, 0.0, 16, [K("w")], [K("wq")], [smn])
+        if t == RO - 1:
+            V(lambda v: v.tensor_scalar(B("yco", p1=NG), sm[0:NG, 64:112], 1.0 / 32, 512.0, A.mult, A.add), 48,
+              [K("yc%d" % i) for i in range(RO)], [K("yco")], [smn])
+            D("Y", T.yc[RG * h:RG * h + RG, :], B("yco", p1=NG), 2.0, [K("yco")], [K("oc")])
+        dd = sc[0:32, 0:XH]
+        lv = lambda i, p1=32: B("live", XH * i, XH * i + XH, p1=p1)
+        mm = [(dd, T.idn[0:32, 48:80], lv(t), True, False, XH)]
+        for k in range(NG):
+            for u in range(NU):
+                a0 = 112 - 31 * k - 4 * NG * u
+                mm.append((dd, B("wq", a0, a0 + 32 * NG, NG), B("hit", 128 * k + u, 128 * k + 128, NU), False, t < RO - 1 and len(mm) == 8, XH))
+        if t == RO - 1:
+            mm.append((dd, T.idn[0:33, 80:112], lv(0, 33), False, False, XH))
+            mm += [(dd, T.idn[0:32, 0:32], lv(i), False, i == t, XH) for i in range(1, RO)]
+        P(mm, [K("wq"), "idn0", "idn1", "idn2", "idn3", "livey"] + [K("live%d" % i) for i in range(t + 1)] + [K("hit%d" % k) for k in range(NG)],
+          [K("dd")], [scn])
+        if t < RO - 1:
+            V(lambda v: v.tensor_scalar(lv(t + 1), dd, 0.5, None, A.is_gt), XH, [K("dd"), K("livez")], [K("live%d" % (t + 1))], [scn])
+            P(ycm, [K("in%d" % t), K("wq")], [K("yc%d" % t)], [smn])
+        else:
+            V(lambda v: v.tensor_scalar(B("age", p1=32), dd, -C0, None, A.add), XH, [K("dd")], [K("age")], [scn])
+            D("Y", T.ya[NG * h:NG * h + NG, :], B("age", p1=32), 2.0, [K("age")], [K("oa")])
 
-    setup(0)
-    front(0, 0)
-    half[0] = 1
-    setup(1)
-    front(1, 0)
+    for h in range(NS):
+        half[0] = h
+        if h:
+            loads(h, ["prod0%d" % (h - GATE)] if GATE and h >= GATE else [])
+        setup(h)
+        front(h, 0)
     for t in range(RO):
-        for h in range(2):
+        for h in range(NS):
             half[0] = h
             back(h, t)
             if t + 1 < RO:
@@ -402,6 +402,8 @@ def depend(ops):
             e, cur, prev = epoch.get(b, (None, [], []))
             if eng is not None and e == eng:
                 cur.append(i)
+                if e == "P":
+                    d.setdefault(cur[-2], False)
             else:
                 prev, cur = cur, [i]
                 epoch[b] = (eng, cur, prev)
@@ -417,7 +419,7 @@ def depend(ops):
     return deps
 
 
-def order(ops, deps, look=LOOK, noise=NOISE, seed=SEED, back=BACK, stag=STAG, vb=0.0):
+def order(ops, deps, look=LOOK, back=BACK, stag=STAG, hop=COST["hop"], passes=8):
     n = len(ops)
     succ = [[] for _ in range(n)]
     for i in range(n):
@@ -425,39 +427,49 @@ def order(ops, deps, look=LOOK, noise=NOISE, seed=SEED, back=BACK, stag=STAG, vb
             succ[j].append(i)
     prio = [0.0] * n
     for i in range(n - 1, -1, -1):
-        c = min(a[1] for a in ops[i]["alts"].values()) + ops[i]["lat"] + HOP + ops[i].get("fill", 0.0)
+        c = min(a[1] for a in ops[i]["alts"].values()) + ops[i]["lat"] + hop + ops[i].get("fill", 0.0)
         prio[i] = c + max([prio[k] for k in succ[i]] + [0.0])
-    x = seed
     for i in range(n):
-        x = (x * 1103515245 + 12345) % 2147483648
-        prio[i] += noise * x / 2147483648 - (back if "fill" in ops[i] else 0.0) - stag * ops[i]["h"]
-    left = [len(deps[i]) for i in range(n)]
-    ready = [i for i in range(n) if left[i] == 0]
-    free = {e: 0.0 for e in "VSPGYN"}
-    end, eng, seq = [0.0] * n, [None] * n, []
-    while ready:
-        cand = []
-        for i in ready:
+        prio[i] -= (back if "fill" in ops[i] else 0.0) + stag * ops[i]["h"]
+
+    def sweep(prio, fwd):
+        pre, post = (deps, succ) if fwd else (succ, deps)
+        left = [len(pre[i]) for i in range(n)]
+        free = {e: 0.0 for e in "VSPGYN"}
+        end, eng, seq, ready = [0.0] * n, [None] * n, [], {}
+
+        def arrive(i):
+            ready[i] = []
             for e, a in ops[i]["alts"].items():
-                t0 = free[e] if e != "N" else 0.0
-                for j, raw in deps[i].items():
-                    if eng[j] != e or ops[j]["kind"] != "c":
-                        t0 = max(t0, end[j] + HOP)
-                    elif e != "P":
-                        t0 = max(t0, end[j] + 0.05)
-                cand.append((t0 + (vb if e == "V" and len(ops[i]["alts"]) > 1 else 0.0), i, e, a[1], t0))
-        first = min(c[0] for c in cand)
-        _t, i, e, c, t0 = max((x for x in cand if x[0] <= first + look), key=lambda x: (prio[x[1]], -x[0] - x[3]))
-        free[e] = t0 + c
-        end[i] = t0 + c + ops[i]["lat"]
-        eng[i] = e
-        seq.append(i)
-        ready.remove(i)
-        for k in succ[i]:
-            left[k] -= 1
-            if left[k] == 0:
-                ready.append(k)
-    return seq, eng, end
+                t = 0.0
+                for j in pre[i]:
+                    same = eng[j] == e and ops[j if fwd else i]["kind"] == "c"
+                    t = max(t, end[j] + ((0.0 if e == "P" else 0.05) if same else hop))
+                ready[i].append((e, a[1], t + (0.0 if fwd else ops[i]["lat"])))
+        for i in range(n):
+            if left[i] == 0:
+                arrive(i)
+        while ready:
+            cand = [(max(t, free[e]), i, e, c) for i, al in ready.items() for e, c, t in al]
+            first = min(c[0] for c in cand)
+            t0, i, e, c = max((x for x in cand if x[0] <= first + look), key=lambda x: (prio[x[1]], -x[0] - x[3]))
+            if e != "N":
+                free[e] = t0 + c
+            end[i] = t0 + c + (ops[i]["lat"] if fwd else 0.0)
+            eng[i] = e
+            seq.append(i)
+            del ready[i]
+            for k in post[i]:
+                left[k] -= 1
+                if left[k] == 0:
+                    arrive(k)
+        return seq, eng, end
+    best = last = sweep(prio, True)
+    for _ in range(passes):
+        last = sweep(sweep(last[2], False)[2], True)
+        if max(last[2]) < max(best[2]):
+            best = last
+    return best
 
 
 def rank_program(g, core, T, topo):
@@ -466,16 +478,7 @@ def rank_program(g, core, T, topo):
         return
     ops = plan(T, rank, topo)
     deps = depend(ops)
-    if len(PLAN) == 2 * len(ops):
-        code = [(ord(PLAN[k]) - 48) * 40 + ord(PLAN[k + 1]) - 48 for k in range(0, len(PLAN), 2)]
-        seq, end = [x // 2 for x in code], [0] * len(ops)
-        eng = [list(o["alts"])[0] for o in ops]
-        for k, x in enumerate(code):
-            end[x // 2] = k
-            if len(ops[x // 2]["alts"]) > 1:
-                eng[x // 2] = "S" if x % 2 else "V"
-    else:
-        seq, eng, end = order(ops, deps)
+    seq, eng, end = order(ops, deps)
     chan, idx, cnt = {}, {}, {}
     for i in seq:
         ch = eng[i] if ops[i]["kind"] == "c" else ("x", i)

@@ -7,14 +7,20 @@ RO = 3
 NG = 4
 NS = NU = 8 // NG
 W, XH = 64 * NG, 16 * NG
-KCH = 32
+KCH = 16
 NCH = W // KCH
-LOOK, BACK, STAG, GATE = 0.1, 5.0, 9.0, 0
+JOIN = (2, 2)
+SCS = (2, 2, 2, 2, 2, 2, 2, 1, 1)
+BLOCKS = ((2, 2), (2, 2))
+NPART = 3
 C0 = 12582912.0
-COST = {"cy": 0.9e-3, "pc": 0.45e-3, "hop": 0.12, "net": 2.6, "gath": 1.56, "scat": 3.8}
+COST = {"cy": 1.0e-3, "pc": 0.52e-3, "hop": 0.1, "net": 2.2, "gath": 1.35, "scat": 3.8, "score": 22}
+LOOK, BACK, STAG, PASSES = 0.1, 2.0, 12.0, 6
+GLUE = 1.0
+WAIT = 0.2
 
 PART = {"tab": (4112, "bfloat16"), "gat": (32 * W, "bfloat16"), "pfl": (W, "bfloat16"), "pfb": (8 * W, "bfloat16"),
-        "posl": (512, "bfloat16"), "posh": (512, "bfloat16"), "xw": (528, "bfloat16"), "yw": (528, "bfloat16"),
+        "posl": (512, "bfloat16"), "posh": (512, "bfloat16"), "xy": (1056, "bfloat16"),
         "py": (8 * W, "bfloat16"), "lvl": (XH, "int32"), "live": (4 * XH, "bfloat16"), "age": (XH, "float32"),
         "cum": (2 * XH, "bfloat16"), "junk": (3 * W, "bfloat16"), "ac3": (4, "float32"), "sl": (8, "uint16"),
         "xb": (80, "bfloat16"), "prod": (64 * RO, "bfloat16"), "prin": (48 * RO, "bfloat16"),
@@ -24,20 +30,20 @@ PART = {"tab": (4112, "bfloat16"), "gat": (32 * W, "bfloat16"), "pfl": (W, "bflo
 SCRATCH = {_n: ("sbuf", [128, NS * _c], _d) for _n, (_c, _d) in PART.items()}
 for _j in range(8):
     SCRATCH["ps%d" % _j] = ("psum", [128, 512], "float32")
-for _n, _c, _d in [("ip", 4, "int32"), ("ci", 8, "int32"), ("cf", 8, "float32"), ("i128", 128, "float32"), ("iom", 128, "float32"),
-                   ("iot", 128, "bfloat16"), ("iou", 128, "bfloat16"), ("iob", 24, "float32"), ("idn", 112, "bfloat16"),
-                   ("selm", 128, "float32"), ("sel", 32, "float32"), ("pair", 128, "float32"), ("mg", 8, "float32"), ("mge", 8, "float32"),
-                   ("ee", 32, "bfloat16"), ("lc", 512, "bfloat16"), ("lt", 512, "bfloat16"), ("cs", 24, "float32"),
-                   ("el", 4, "uint16"), ("prm", 448, "bfloat16"), ("kc", 32, "bfloat16"), ("cc", 512, "bfloat16"),
-                   ("thl", 4, "int32"), ("thf", 4, "float32"), ("thm", 8, "float32"), ("thb", 8, "float32"), ("one", 48, "bfloat16")]:
+for _n, _c, _d in [("ip", 4, "int32"), ("ci", 8, "int32"), ("cf", 8, "float32"), ("i128", 128, "float32"), ("iom", 32, "float32"),
+                   ("iot", 128, "bfloat16"), ("iou", 128, "bfloat16"), ("iob", 24, "float32"), ("idn", 80, "bfloat16"),
+                   ("selm", 32, "float32"), ("sel", 32, "float32"), ("pair", 128, "float32"), ("mg", 8, "float32"), ("mge", 8, "float32"),
+                   ("ee", 32, "bfloat16"), ("lc", 512, "bfloat16"), ("lt", 512, "bfloat16"), ("cs", 16, "float32"),
+                   ("el", 4, "uint16"), ("prm", 448, "bfloat16"), ("kc", 32, "bfloat16"), ("cc", 1024, "bfloat16"),
+                   ("thl", 4, "int32"), ("thf", 4, "float32"), ("thm", 8, "float32"), ("thb", 8, "float32"), ("one", 48, "bfloat16"),
+                   ("zer", 2 * XH, "bfloat16")]:
     SCRATCH[_n] = ("sbuf", [128, _c], _d)
 
-SEMAPHORES = ["eV", "eS", "eP", "eG", "sent"] + ["d%d" % i for i in range(56)] + ["r%d" % i for i in range(6 * NS)]
+SEMAPHORES = ["eV", "eS", "eP", "eG", "sent"] + ["d%d" % i for i in range(24)] + ["r%d" % i for i in range(6 * NS)]
 
 COPIES = [(1.0, "n"), (-1.0, "q"), (2.0 ** -4, "b"), (-2.0 ** -4, "n"), (2.0 ** -8, "b"), (-2.0 ** -8, "n"), (2.0 ** -12, "b"), (-2.0 ** -12, "n")]
 UNITS = [4096.0, 256.0, 16.0, 1.0]
 LEVELS = [[(0, 0), (1, 0), (2, 0), (0, 1), (1, 1), (2, 1), (0, 2)], [(0, 3), (1, 4)], [(1, 5), (2, 6)], [(2, 7)]]
-NPART = 3
 
 
 def plan(T, rank, topo, cost=COST):
@@ -62,8 +68,8 @@ def plan(T, rank, topo, cost=COST):
     def G(fn, k, r, w):
         op({"G": (fn, 0.17 + 2 * k * CY)}, r, w)
 
-    def fill(out, c, k, w, half=True):
-        op({"V": (lambda g: g.vector.memset(out, c), vc(k, half)),
+    def fill(out, c, k, w):
+        op({"V": (lambda g: g.vector.memset(out, c), vc(k, True)),
             "G": (lambda g: g.iota(out, [[0, k]], int(c), 0, allow_small_or_imprecise_dtypes=True), 0.13 + 2 * k * CY)}, [], w)
 
     def lin(out, in_, mul, add, k, r, w, ps=(), half=False):
@@ -71,10 +77,7 @@ def plan(T, rank, topo, cost=COST):
             if isinstance(add, float) and add == 0.0:
                 return g.scalar.activation(out, in_, F.Copy if isinstance(mul, float) else F.Identity, scale=mul)
             return g.scalar.activation(out, in_, F.Identity, bias=add, scale=mul)
-        alts = {"V": (lambda g: g.vector.tensor_scalar(out, in_, mul, add, A.mult, A.add), vc(k, half))}
-        if not isinstance(add, float) or add == 0.0:
-            alts["S"] = (fs, vc(k))
-        op(alts, r, w, ps)
+        op({"V": (lambda g: g.vector.tensor_scalar(out, in_, mul, add, A.mult, A.add), vc(k, half)), "S": (fs, vc(k))}, r, w, ps)
 
     def P(mms, r, w, ps):
         def fn(g):
@@ -82,7 +85,7 @@ def plan(T, rank, topo, cost=COST):
             for o, l, rh, st, sp, _c in mms:
                 last = g.tensor.matmul(o, l, rh, st, sp)
             return last
-        op({"P": (fn, 0.05 + sum(m[5] for m in mms) * PC)}, r, w, ps)
+        op({"P": (fn, 0.02 + sum(m[5] for m in mms) * PC)}, r, w, ps)
 
     def D(q, out, in_, us, r, w):
         def fn(g):
@@ -93,92 +96,72 @@ def plan(T, rank, topo, cost=COST):
         def B(name, a=0, b=None, st=1, p0=0, p1=128):
             c = PART[name][0]
             return T[name][p0:p1, c * h + a:c * h + (c if b is None else b):st]
-        return B, (lambda s: s + str(h))
-
-    def banks(h):
-        k = 8 // NS * h
-        if NS == 2:
-            return "ps%d" % k, "ps%d" % (k + 1), lambda s, c: ("ps%d" % (k + 2 + c), 0), 256
-        return "ps%d" % k, "ps%d" % (k + 1), lambda s, c: ("ps%d" % (k + 1), 256 + 128 * s), 128
+        return B, (lambda s: s + str(h)), ["ps%d" % (4 * h + i) for i in range(4)]
 
     R3, RG = 3 * NG, 16 * NG
 
-    def loads(h, gate):
-        B, K = part(h)
+    def loads(h):
+        B, K, _b = part(h)
         D("Y", B("lvl", p1=32), T.lv[NG * h:NG * h + NG, :], 2.0, [], [K("lvl")])
         D("Y", B("posl", p1=R3), T.pos[R3 * h:R3 * h + R3, :], 2.0, [], [K("posl")])
         for u in range(NU):
-            D("S" if h == 0 else "Y", B("tab", 0, 4096, 1, RG * u, RG * u + RG), T.rf[RG * h:RG * h + RG, :], 5.0 + (0 if gate else 4 * h), gate, [K("tab%d_" % u)])
+            D("S" if h == 0 else "Y", B("tab", 0, 4096, 1, RG * u, RG * u + RG), T.rf[RG * h:RG * h + RG, :], 5.0 + 4 * h, [], [K("tab%d_" % u)])
         for u in range(NU):
             D("Y", B("pfl", p0=RG * u, p1=RG * u + RG), T.pf[RG * h:RG * h + RG, W * u:W * u + W], 2.5, [], [K("pfl%d_" % u)])
 
-    loads(0, [])
+    loads(0)
     D("Y", T.thl[:, 0:1], T.th[:], 2.5, [], ["thl"])
 
-    def iota(name, rows, pat, base=0, cm=0, p0=0):
+    def iota(name, rows, pat, base=0, cm=0):
         k = 1
         for _s, c in pat:
             k *= c
-        G(lambda g: g.iota(T[name][p0:p0 + rows, 0:k], pat, base, cm, allow_small_or_imprecise_dtypes=True), k, [], [name + (str(p0) if p0 else "")])
+        G(lambda g: g.iota(T[name][0:rows, 0:k], pat, base, cm, allow_small_or_imprecise_dtypes=True), k, [], [name])
     G(lambda g: g.iota(T.ip[:], [[128, 4]], 0, 1), 4, [], ["ip"])
     iota("iou", 32, [[4, NU], [4 * NU, NG], [0, 16]], 0, -1)
     G(lambda g: g.affine_select(T.iot[0:32, :], T.iou[0:32, :], [[0, NU], [-4 * NU, NG], [0, 16]], A.is_ge, -100.0, 0, 1), 128, ["iou"], ["iot"])
     iota("i128", 128, [[1, 128]])
     iota("iob", R3, [[1, 3], [3, NG], [0, 2]])
-    iota("iom", 128, [[0, 4], [1, 16], [0, 2]])
+    iota("iom", 128, [[1, 16], [0, 2]])
     iota("kc", 64, [[-1, 16], [-30000, 2]])
     lin(T.kc[32:64, 1:32:2], T.kc[32:64, 0:32:2], 1.0, 0.0, 16, ["kc"], ["kc32"])
     V(lambda v: v.memset(T.kc[32:64, 0:32:2], -30000.0), 8, ["kc32"], ["kc32"])
-    pc = T.ip[:, 0:1]
-    bits = [(A.bitwise_and, 15, None, None), (A.arith_shift_right, 4, None, None), (A.bitwise_and, RG - 1, None, None),
-            (A.bitwise_and, 1, None, None), (A.bitwise_and, 31, None, None), (A.arith_shift_right, 1, A.bitwise_and, 15)]
-    cm, cg, crg, csx, c31, cm2, cp = [T.cf[:, i:i + 1] for i in range(7)]
-    for i, (o0, s0, o1, s1) in enumerate(bits):
-        if o1 is None:
-            V(lambda v, i=i, o0=o0, s0=s0: v.tensor_scalar(T.ci[:, i:i + 1], pc, s0, None, o0), 1, ["ip"], ["ci%d" % i])
-        else:
-            V(lambda v, i=i, o0=o0, s0=s0, o1=o1, s1=s1: v.tensor_scalar(T.ci[:, i:i + 1], pc, s0, s1, o0, o1), 1, ["ip"], ["ci%d" % i])
-    V(lambda v: v.tensor_copy(T.cf[:, 0:6], T.ci[:, 0:6]), 6, ["ci%d" % i for i in range(6)], ["cf"])
-    V(lambda v: v.tensor_copy(cp, pc), 1, ["ip"], ["cp"])
+    bits = [(A.bitwise_and, 15), (A.arith_shift_right, 4), (A.bitwise_and, RG - 1), (A.bitwise_and, 31)]
+    cm, cg, crg, c31 = [T.cf[:, i:i + 1] for i in range(4)]
+    for i, (o0, s0) in enumerate(bits):
+        V(lambda v, i=i, o0=o0, s0=s0: v.tensor_scalar(T.ci[:, i:i + 1], T.ip[:, 0:1], s0, None, o0), 1, ["ip"], ["ci%d" % i])
+    V(lambda v: v.tensor_copy(T.cf[:, 0:4], T.ci[:, 0:4]), 4, ["ci%d" % i for i in range(4)], ["cf"])
+    G(lambda g: g.iota(T.cf[:, 6:7], [[0, 1]], 0, 1, allow_small_or_imprecise_dtypes=True), 1, [], ["cp"])
     V(lambda v: v.tensor_copy(T.el[:], T.ip[:]), 4, ["ip"], ["el"])
     for q in range(4):
         V(lambda v, q=q: v.tensor_scalar(T.lc[0:32, 128 * q:128 * q + 128], T.iot[0:32, :], float(-q), -UNITS[0], A.is_equal, A.mult), 128, ["iot"], ["lc%d" % q], half=True)
         V(lambda v, q=q: v.tensor_scalar(T.lt[0:32, 128 * q:128 * q + 128], T.iot[0:32, :], float(-q), -UNITS[0], A.is_gt, A.mult), 128, ["iot"], ["lt%d" % q], half=True)
+    for i, c in enumerate([C0] + [C0 * (UNITS[i] - UNITS[i - 1]) for i in range(1, 4)]):
+        lin(T.cc[0:1, 128 * i:128 * i + 128], T.i128[0:1, :], 0.0, c, 128, ["i128"], ["cc%d" % i])
     V(lambda v: v.memset(T.lc[32:33, :], C0 * UNITS[0]), 256, [], ["lcz"])
-    for i in range(3):
-        V(lambda v, i=i: v.memset(T.cc[0:1, 128 * i:128 * i + 128], C0 * (UNITS[i + 1] - UNITS[i])), 64, [], ["cc%d" % i])
-    V(lambda v: v.memset(T.cc[0:1, 384:512], 1.0), 64, [], ["cc3"])
     V(lambda v: v.memset(T.live[32:33, :], 1.0), 256, [], ["livey"])
+    V(lambda v: v.memset(T.cc[0:1, 768:1024], 1.0), 128, [], ["cc6"])
+    ones = lambda k: T.cc[0:1, 768:768 + k]
     V(lambda v: v.tensor_scalar(T.idn[0:36, 0:36], T.i128[0:36, 0:36], T.cf[0:36, 6:7], None, A.is_equal), 36, ["i128", "cp"], ["idn0"])
     lin(T.idn[0:32, 48:80], T.idn[0:32, 0:32], 0.375, 0.0, 32, ["idn0"], ["idn1"])
-    lin(T.idn[0:32, 80:112], T.idn[0:32, 0:32], 1.0, 0.0, 32, ["idn0"], ["idn2"])
-    V(lambda v: v.memset(T.idn[32:33, 80:112], C0), 16, [], ["idn3"])
-    V(lambda v: v.tensor_scalar(T.selm[:], T.iom[:], cm, None, A.is_equal), 128, ["iom", "cf"], ["selm"])
+    V(lambda v: v.tensor_scalar(T.selm[:], T.iom[:], cm, None, A.is_equal), 32, ["iom", "cf"], ["selm"])
     col = lambda i: T.cs[:, i:i + 1]
-    V(lambda v: v.tensor_scalar(col(0), csx, -16.0, 16.0, A.mult, A.add), 1, ["cf"], ["cs0"])
-    lin(col(1), csx, 16.0, 0.0, 1, ["cf"], ["cs1"])
-    V(lambda v: v.tensor_scalar(col(2), cm, 3.0, 0.5, A.mult, A.add), 1, ["cf"], ["cs2"])
+    lin(col(2), cm, 3.0, 0.5, 1, ["cf"], ["cs2"])
     lin(T.cs[:, 4:7], T.i128[:, 0:3], 1.0, col(2), 3, ["cs2", "i128"], ["cs4"])
     V(lambda v: v.tensor_scalar(col(8), cm, 6.0, None, A.not_equal), 1, ["cf"], ["csq"])
-    V(lambda v: v.tensor_scalar(col(9), col(8), -30.0, 31.0, A.mult, A.add), 1, ["csq"], ["csb"])
+    lin(col(9), col(8), -30.0, 31.0, 1, ["csq"], ["csb"])
     V(lambda v: v.tensor_scalar(col(10), cm, 7.0, 2047.0, A.not_equal, A.add), 1, ["cf"], ["cs10"])
     lin(col(11), col(8), -2048.0, col(10), 1, ["csq", "cs10"], ["cs11"])
     V(lambda v: v.tensor_scalar(col(12), col(11), 0.0, None, A.not_equal), 1, ["cs11"], ["cs12"])
-    V(lambda v: v.tensor_scalar(col(13), c31, float(NG), -0.1875, A.is_lt, A.mult), 1, ["cf"], ["cs13"])
     lin(col(14), col(11), 0.5, 0.0, 1, ["cs11"], ["csc0"])
     lin(col(15), col(8), -2.0, 1.0, 1, ["csq"], ["csc1"])
-    for i, (f, kind) in enumerate(COPIES):
-        if kind == "b":
-            lin(col(14 + i), col(9), f, 0.0, 1, ["csb"], ["csc%d" % i])
-    for s in range(2):
-        V(lambda v, s=s: v.tensor_scalar(T.sel[:, 16 * s:16 * s + 16], T.i128[:, 0:16], cm2, col(s), A.is_equal, A.mult),
-          16, ["i128", "cf", "cs%d" % s], ["sel%d" % s])
+    V(lambda v: v.tensor_scalar(T.sel[:], T.i128[:, 0:32], c31, 16.0, A.is_equal, A.mult), 32, ["i128", "cf"], ["sel"])
     for u in range(NU):
         V(lambda v, u=u: v.tensor_scalar(T.pair[:, RG * u:RG * u + RG], T.i128[:, 0:RG], crg, None, A.is_equal), RG, ["i128", "cf"], ["pair%d" % u])
     V(lambda v: v.tensor_scalar(T.mg[:], T.i128[:, 0:8], cg, None, A.is_equal), 8, ["i128", "cf"], ["mg"])
     lin(T.mge[:], T.mg[:], 2.0 ** -10, 0.0, 8, ["mg"], ["mge"])
     fill(T.ee[0:36, :], 0.0, 32, ["eez"])
-    V(lambda v: v.tensor_scalar(T.ee[0:36, R3:R3 + NG], T.i128[0:36, 0:NG], T.cf[0:36, 4:5], T.cs[0:36, 13:14], A.is_equal, A.mult), 4, ["i128", "cf", "cs13", "eez"], ["ee"])
+    lin(T.ee[0:36, R3:R3 + NG], T.sel[0:36, 0:NG], -0.1875 / 16, 0.0, NG, ["sel", "eez"], ["ee"])
     V(lambda v: v.memset(T.prm[0:R3, :], 0.0), 224, [], ["permz"])
     V(lambda v: v.memset(T.one[0:R3, 0:32], 1.0), 16, [], ["one"])
     V(lambda v: v.memset(T.one[0:R3, 17:32:2], -1.0), 8, ["one"], ["one"])
@@ -195,13 +178,14 @@ def plan(T, rank, topo, cost=COST):
                                               A.is_equal, A.mult), 8, ["iob", "cp", "permz"], ["perm2%d" % r])
     V(lambda v: v.tensor_copy(T.thf[:, 0:1], T.thl[:, 0:1]), 1, ["thl"], ["thf"])
     lin(T.thm[:], T.mg[:], T.thf[:, 0:1], 0.0, 8, ["mg", "thf"], ["thm"])
-    P([(T.ps7[:, 0:8], T.selm[:], T.thm[:], True, True, 256)], ["selm", "thm"], ["ps7"], ["ps7"])
-    V(lambda v: v.tensor_scalar(T.thb[:], T.ps7[:, 0:8], -1.0, 0.5, A.mult, A.add), 8, ["ps7"], ["thb"], ["ps7"])
+    P([(T.ps7[32 * q:32 * q + 32, 0:8], T.selm[:], T.thm[:], True, True, 128) for q in range(4)], ["selm", "thm"], ["ps7"], ["ps7"])
+    lin(T.thb[:], T.ps7[:, 0:8], -1.0, 0.5, 8, ["ps7"], ["thb"], ["ps7"])
+    lin(T.xy[:, 512::528], T.i128[:, 0:2 * NS], 0.0, col(12), 2 * NS, ["i128", "cs12"], ["xyz"])
+    V(lambda v: v.memset(T.tab[:, 4096::4112], -8388608.0), NS, [], ["tabz"])
+    fill(T.zer[0:32, :], -C0, 2 * XH, ["zer"])
 
     def setup(h):
-        B, K = part(h)
-        sc, sm, blk, _cn = banks(h)
-        fill(B("tab", 4096, 4112), -8388608.0, 16, [K("tabz")])
+        B, K, (sc, _sm, pa, pb) = part(h)
         fill(B("live", XH, p1=32), 0.0, 3 * XH, [K("livez")])
         V(lambda v: v.tensor_copy(B("live", 0, XH, p1=32), B("lvl", p1=32)), XH, [K("lvl")], [K("live0")])
         fill(B("xb", 0, 16), 0.0, 16, [K("xbz")])
@@ -210,20 +194,21 @@ def plan(T, rank, topo, cost=COST):
             fill(B("lh", 384 * s, 384 * s + 384), 0.0, 384, [K("lh%d" % s)])
         pos, posh = B("posl", p1=R3), B("posh", p1=R3)
         V(lambda v: v.tensor_scalar(posh, pos, 8 * C0, 8 * C0, A.add, A.subtract), 512, [K("posl")], [K("posh")], half=True)
-        pa, pb = (blk(0, 0)[0], blk(0, 1)[0]) if NS == 2 else (sc, sm)
         P([(T[pa][:], T.prm[0:R3, 128:256], pos, True, False, 512), (T[pa][:], T.prm[0:R3, 0:128], posh, False, True, 512)],
           [K("posl"), K("posh"), "permlo"], [pa], [pa])
         P([(T[pb][:], T.prm[0:R3, 256:384], pos, True, True, 512)], [K("posl")] + ["perm1%d" % r for r in range(6)], [pb], [pb])
-        for nm, bank in (("xw", pa), ("yw", pb)):
-            lin(B(nm, 0, 512), T[bank][:], 1.0, col(12), 512, [bank, "cs12"], [K(nm)], [bank])
-            lin(B(nm, 512, 528), T.i128[:, 0:16], 0.0, col(12), 16, ["i128", "cs12"], [K(nm + "z")])
+        for a, nm, bank in ((0, "xw", pa), (528, "yw", pb)):
+            lin(B("xy", a, a + 512), T[bank][:], 1.0, col(12), 512, [bank, "cs12"], [K(nm)], [bank])
         P([(T[sc][RG * u:RG * u + RG, 0:W], T.prm[0:R3, 384:384 + RG], B("posl", W * u, W * u + W, p1=R3), True, True, W) for u in range(NU)],
           [K("posl")] + ["perm2%d" % r for r in range(6)], [sc], [sc])
         lin(B("py", 0, W), T[sc][:, 0:W], -1.0, col(14), W, [sc, "csc0"], [K("py0")], [sc])
         for i, (f, kind) in enumerate(COPIES):
-            if i:
-                lin(B("py", W * i, W * i + W), B("py", 0, W), f if kind == "n" else col(14 + i), 0.0, W,
-                    [K("py0")] + ([] if kind == "n" else ["csc%d" % i]), [K("py%d" % i)], half=True)
+            if kind == "b":
+                V(lambda v, i=i, f=f: v.tensor_scalar(B("py", W * i, W * i + W), B("py", 0, W), col(9), f, A.mult, A.mult), W,
+                  [K("py0"), "csb"], [K("py%d" % i)], half=True)
+            elif i:
+                lin(B("py", W * i, W * i + W), B("py", 0, W), f if kind == "n" else col(15), 0.0, W,
+                    [K("py0")] + ([] if kind == "n" else ["csc1"]), [K("py%d" % i)], half=True)
         for q in range(8):
             o, i_, mc, ec = B("pfb", q, 8 * W, 8), B("pfl"), T.mg[:, q:q + 1], T.mge[:, q:q + 1]
             op({"V": (lambda g, o=o, i_=i_, mc=mc: g.vector.tensor_scalar(o, i_, 2.0 ** -10, mc, A.max, A.mult), vc(W, True)),
@@ -249,78 +234,81 @@ def plan(T, rank, topo, cost=COST):
         op({"N": ((sem, ne * len(dsts)), 0.0)}, [land + "s"], [land], kind="a", lat=cost["net"])
 
     def front(h, t):
-        B, K = part(h)
-        _sc, smn, blk, cn0 = banks(h)
+        B, K, (_sc, smn, pa, pb) = part(h)
         sm = T[smn]
-        live = B("live", XH * t, XH * t + 2 * XH, p1=32)
-        V(lambda v: v.tensor_tensor_scan(B("cum", p1=32), live, live, 0.0, A.add, A.max), 2 * XH,
-          [K("live%d" % t), K("livez"), K("live%d" % (t + 1))], [K("cum")], half=True)
+        if t == 0:
+            live = B("live", 0, 2 * XH, p1=32)
+            V(lambda v: v.tensor_tensor_scan(B("cum", p1=32), live, live, 0.0, A.add, A.max), 2 * XH, [K("live0"), K("livez")], [K("cum")], half=True)
         mm = []
         for q in range(4):
-            o = sm[:, cn0 + XH * q:cn0 + XH * q + XH]
+            o = sm[:, 256 + XH * q:256 + XH * q + XH]
             mm.append((o, T.lc[0:32, 128 * q:128 * q + 128], B("cum", 0, XH, p1=32), True, False, 64))
             mm.append((o, T.lt[0:32, 128 * q:128 * q + 128], B("cum", XH, p1=32), False, True, 64))
         P(mm, [K("cum")] + ["lc%d" % q for q in range(4)] + ["lt%d" % q for q in range(4)], [K("cn")], [smn])
         for i, k in enumerate((1, 2, 0)):
-            S(lambda a, i=i, k=k: a.activation(B("junk", W * i, W * i + W), sm[:, cn0:cn0 + W], F.Sign, bias=col(4 + k), scale=1.0 / UNITS[0],
+            S(lambda a, i=i, k=k: a.activation(B("junk", W * i, W * i + W), sm[:, 256:256 + W], F.Sign, bias=col(4 + k), scale=1.0 / UNITS[0],
                                                accum_out=B("ac3", i, i + 1)),
               W + 20, [K("cn"), "cs4"], [K("ac3%d" % i)], [smn])
         P([(sm[:, 48:51], T.pair[:], B("ac3", 0, 3), True, True, 256), (sm[:, 51:52], T.pair[:], B("ac3", 0, 1), True, True, 256)],
           [K("ac3%d" % i) for i in range(3)] + ["pair%d" % u for u in range(NU)], [K("pr")], [smn])
         sl = B("sl", 0, 4)
         V(lambda v: v.tensor_scalar(sl, sm[:, 48:52], 0.5, 256.0, A.mult, A.add), 4, [K("pr")], [K("sl")], [smn])
-        V(lambda v: v.tensor_copy(B("xb", 16, 80), B("xw").indirect(sl)), 64 * cost["gath"], [K("sl"), K("xw"), K("xwz")], [K("xb")])
+        V(lambda v: v.tensor_copy(B("xb", 16, 80), B("xy", 0, 513).indirect(sl)), 64 * cost["gath"], [K("sl"), K("xw"), "xyz"], [K("xb")])
         prod, prin = B("prod", 64 * t + 16, 64 * t + 64), B("prin", 48 * t, 48 * t + 48)
-        V(lambda v: v.tensor_tensor(B("prod", 64 * t, 64 * t + 64), B("yw").indirect(sl), B("xb", 0, 64), A.mult), 64 * cost["gath"],
-          [K("sl"), K("yw"), K("ywz"), K("xb"), K("xbz")], [K("prod%d" % t)])
+        V(lambda v: v.tensor_tensor(B("prod", 64 * t, 64 * t + 64), B("xy", 528, 1041).indirect(sl), B("xb", 0, 64), A.mult), 64 * cost["gath"],
+          [K("sl"), K("yw"), "xyz", K("xb"), K("xbz")], [K("prod%d" % t)])
         send(prod, [(T.cores[(rank + t + 1) % n], prin)], [K("prod%d" % t)], K("prin%d" % t))
         for s in range(2):
             lh = K("lh%d" % s)
             V(lambda v, s=s: v.tensor_copy(B("lh", 384 * s, 384 * s + 384).indirect(T.el[:, 0:3]), prin if s else prod), 48 * cost["scat"],
               [K(("prin%d" if s else "prod%d") % t), "el"], [lh])
-            for c in range(W // 128):
-                bank, c0 = blk(s, c)
-                o, pk, nq = T[bank][:, c0:c0 + 128], K("pl%d" % c0) + bank, 128 // XH
+            for c, nq in enumerate(BLOCKS[s]):
+                bank = (pa, pb)[c % 2]
+                q0, wd = sum(BLOCKS[s][:c]), XH * nq
+                o = T[bank][:, 0:wd]
                 mm = []
                 for i, level in enumerate(LEVELS):
                     if i:
-                        mm.append(((o, T.cc[0:1, 128 * i - 128:128 * i], T.cc[0:1, 384:512], False, False, 128), ["cc%d" % (i - 1), "cc3"]))
+                        mm.append(((o, T.cc[0:1, 128 * i:128 * i + 128], ones(wd), False, False, wd), ["cc%d" % i, "cc6"]))
                     for j, k in level:
-                        mm.append(((o, B("lh", 384 * s + 128 * j, 384 * s + 128 * j + 128), B("py", W * k + 128 * c, W * k + 128 * c + 128), not mm, i == 3, 128),
+                        mm.append(((o, B("lh", 384 * s + 128 * j, 384 * s + 128 * j + 128), B("py", W * k + XH * q0, W * k + XH * q0 + wd), not mm, i == 3, wd),
                                    [lh, K("py%d" % k)]))
                         if len(mm) == 1:
-                            mm += [((T[bank][:, c0 + XH * q:c0 + XH * q + XH], T.lc[0:33, 128 * (nq * c + q):128 * (nq * c + q + 1)],
-                                     B("live", XH * t, XH * t + XH, p1=33), False, False, 64), [K("live%d" % t), "livey", "lcz", "lc%d" % (nq * c + q)])
+                            mm += [((T[bank][:, XH * q:XH * q + XH], T.lc[0:33, 128 * (q0 + q):128 * (q0 + q + 1)],
+                                     B("live", XH * t, XH * t + XH, p1=33), False, False, 64), [K("live%d" % t), "lc%d" % (q0 + q), "lcz", "livey"])
                                    for q in range(nq)]
-                for i in range(NPART):
-                    mp = mm[len(mm) * i // NPART:len(mm) * (i + 1) // NPART]
-                    P([m[0] for m in mp], [k for m in mp for k in m[1]], [pk], [bank])
-                V(lambda v, s=s, c=c, o=o: v.tensor_scalar(B("off", W * s + 128 * c, W * s + 128 * c + 128), o, UNITS[0] - C0, 4096.0, A.add, A.min), 128,
-                  [pk], [K("off%d%d" % (s, c))], [bank])
+                parts = NPART * nq // 2 + 1
+                for i in range(parts):
+                    mp = mm[len(mm) * i // parts:len(mm) * (i + 1) // parts]
+                    P([m[0] for m in mp], [k for m in mp for k in m[1]], ["pl" + bank], [bank])
+                V(lambda v, a=W * s + XH * q0, wd=wd, o=o: v.tensor_scalar(B("off", a, a + wd), o, UNITS[0] - C0, 4096.0, A.add, A.min), wd,
+                  ["pl" + bank], [K("off%d%d" % (s, q0 + q)) for q in range(nq)], [bank])
 
     def back(h, t):
-        B, K = part(h)
-        scn, smn, _blk, _cn = banks(h)
+        B, K, (scn, smn, _pa, _pb) = part(h)
         sc, sm = T[scn], T[smn]
+
+        def gather(s, c0, c1):
+            o = B("gat", 32 * KCH * c0 + s, 32 * KCH * c1, 2)
+            w = B("tab", 0, 4097).indirect(B("off", W * s + KCH * c0, W * s + KCH * c1))
+            us = 0.06 + 16 * KCH * (c1 - c0) * cost["gath"] * CY
+            return {"V": (lambda g: g.vector.tensor_copy(o, w), us), "S": (lambda g: g.scalar.activation(o, w, F.Copy), us)}
         for s in range(2):
             for c in range(NCH):
-                o = B("gat", 32 * KCH * c + s, 32 * KCH * (c + 1), 2)
-                w = B("tab").indirect(B("off", W * s + KCH * c, W * s + KCH * (c + 1)))
-                us = 0.06 + 16 * KCH * cost["gath"] * CY
-                op({"V": (lambda g, o=o, w=w: g.vector.tensor_copy(o, w), us), "S": (lambda g, o=o, w=w: g.scalar.activation(o, w, F.Copy), us)},
-                   [K("off%d%d" % (s, KCH * c // 128)), K("tabz")] + [K("tab%d_" % u) for u in range(NU)], [K("gat%d%d_" % (s, c))])
-                ops[-1]["fill"] = (2 * (NCH - 1 - c) + 1 - s) * us / 2
-        for c in range(NCH):
-            mm = []
-            for x in range(c * KCH, (c + 1) * KCH):
+                op(gather(s, c, c + 1), [K("off%d%d" % (s, KCH * c // XH)), "tabz"] + [K("tab%d_" % u) for u in range(NU)], [K("gat%d%d_" % (s, c))])
+                ops[-1]["fill"] = (2 * (NCH - 1 - c) + 1 - s) * ops[-1]["alts"]["V"][1] / 2
+                ops[-1]["gat"] = (gather, s, c)
+        for c, k1 in enumerate(SCS):
+            mm, k0 = [], sum(SCS[:c])
+            for x in range(k0 * KCH, (k0 + k1) * KCH):
                 q, xh = x // XH, x % XH
-                mm.append((sc[32 * q:32 * q + 32, 8 * xh:8 * xh + 8], B("gat", 32 * x, 32 * x + 32), B("pfb", 8 * x, 8 * x + 8), True, True, 32))
-            P(mm, [K("gat0%d_" % c), K("gat1%d_" % c)] + [K("pfb%d" % q) for q in range(8)], [K("s%d_" % c)], [scn])
+                mm.append((sc[32 * q:32 * q + 32, 8 * xh:8 * xh + 8], B("gat", 32 * x, 32 * x + 32), B("pfb", 8 * x, 8 * x + 8), True, True, cost["score"]))
+            P(mm, [K("gat%d%d_" % (s, k)) for s in range(2) for k in range(k0, k0 + k1)] + [K("pfb%d" % q) for q in range(8)], [K("s%d_" % c)], [scn])
         acc = B("acc", 4 * t, 4 * t + NG)
         for k in range(NG):
             S(lambda a, k=k: a.activation(B("hit", 128 * k, 128 * k + 128), sc[:, k:8 * XH:NG], F.Sign, bias=T.thb[:, NG * h + k:NG * h + k + 1],
                                           accum_out=B("acc", 4 * t + k, 4 * t + k + 1)),
-              148, [K("s%d_" % c) for c in range(NCH)] + ["thb"], [K("hit%d" % k), K("acc%d%d" % (t, k))], [scn])
+              148, [K("s%d_" % c) for c in range(len(SCS))] + ["thb"], [K("hit%d" % k), K("acc%d%d" % (t, k))], [scn])
         ca, cc = T.cores[(rank - t - 1) % n], T.cores[(rank + t + 1) % n]
         ina, inc = B("ina", 4 * t, 4 * t + NG), B("inc", 4 * t, 4 * t + NG)
         if ca == cc:
@@ -330,10 +318,10 @@ def plan(T, rank, topo, cost=COST):
             dsts = [(cc, ina), (ca, inc)]
         ak = [K("acc%d%d" % (t, k)) for k in range(NG)]
         send(acc, dsts, ak, K("in%d" % t))
-        s0, s1 = T.sel[:, 0:16], T.sel[:, 16:32]
+        s0, s1 = T.sel[:, 0:32:2], T.sel[:, 1:32:2]
         key, k0, k1 = sm[0:36, 0:32], sm[0:NG, 0:32:2], sm[32:32 + NG, 1:32:2]
         P([(key, T.idn[0:36, 0:36], T.kc[0:36, :], True, False, 36), (k0, acc, s0, False, False, 64), (k1, acc, s1, False, False, 64)],
-          ak + ["kc", "kc32", "idn0", "sel0", "sel1"], [K("key")], [smn])
+          ak + ["kc", "kc32", "idn0", "sel"], [K("key")], [smn])
         P([(k0, inc, s1, False, False, 64), (k1, ina, s0, False, False, 64), (key, T.idn[0:36, 0:36], T.kc[0:36, :], False, True, 36)],
           [K("in%d" % t)], [K("key")], [smn])
         mx = B("mx", 0, 1, p1=36)
@@ -343,36 +331,39 @@ def plan(T, rank, topo, cost=COST):
           [K("wt"), "ee"], [K("w")], [smn])
         yc = sm[0:NG, 64 + t:112:3]
         ycm = [(yc, acc, s0, True, False, 64), (yc, inc, s1, False, True, 64)]
-        if t == RO - 1:
+        last = t == RO - 1
+        if last:
             P(ycm, [K("in%d" % t), K("w")], [K("yc%d" % t)], [smn])
         lin(B("wq", 112, 112 + 4 * NG), sm[:, 32:32 + 4 * NG], 1.0, 0.0, 16, [K("w")], [K("wq")], [smn])
-        if t == RO - 1:
+        if last:
             V(lambda v: v.tensor_scalar(B("yco", p1=NG), sm[0:NG, 64:112], 1.0 / 32, 512.0, A.mult, A.add), 48,
               [K("yc%d" % i) for i in range(RO)], [K("yco")], [smn])
             D("Y", T.yc[RG * h:RG * h + RG, :], B("yco", p1=NG), 2.0, [K("yco")], [K("oc")])
-        dd = sc[0:32, 0:XH]
-        lv = lambda i, p1=32: B("live", XH * i, XH * i + XH, p1=p1)
-        mm = [(dd, T.idn[0:32, 48:80], lv(t), True, False, XH)]
+        wd = XH if last else 2 * XH
+        dd, d2 = sc[0:32, 0:XH], sc[0:32, 0:wd]
+        lv = lambda i, k=XH: B("live", XH * i, XH * i + k, p1=32)
+        mm = [(d2, T.idn[0:32, 48:80], lv(t, wd), True, False, wd)]
         for k in range(NG):
             for u in range(NU):
                 a0 = 112 - 31 * k - 4 * NG * u
-                mm.append((dd, B("wq", a0, a0 + 32 * NG, NG), B("hit", 128 * k + u, 128 * k + 128, NU), False, t < RO - 1 and len(mm) == 8, XH))
-        if t == RO - 1:
-            mm.append((dd, T.idn[0:33, 80:112], lv(0, 33), False, False, XH))
-            mm += [(dd, T.idn[0:32, 0:32], lv(i), False, i == t, XH) for i in range(1, RO)]
-        P(mm, [K("wq"), "idn0", "idn1", "idn2", "idn3", "livey"] + [K("live%d" % i) for i in range(t + 1)] + [K("hit%d" % k) for k in range(NG)],
+                mm.append((dd, B("wq", a0, a0 + 32 * NG, NG), B("hit", 128 * k + u, 128 * k + 128, NU), False, False, XH))
+        mm.append((d2, T.cc[0:1, 0:32], ones(wd), False, not last, wd))
+        if last:
+            mm += [(dd, T.idn[0:32, 0:32], lv(i), False, i == t, XH) for i in range(RO)]
+        P(mm, [K("wq"), "idn0", "idn1", "cc0", "cc6", K("livez")] + [K("live%d" % i) for i in range(t + 2)] + [K("hit%d" % k) for k in range(NG)],
           [K("dd")], [scn])
-        if t < RO - 1:
-            V(lambda v: v.tensor_scalar(lv(t + 1), dd, 0.5, None, A.is_gt), XH, [K("dd"), K("livez")], [K("live%d" % (t + 1))], [scn])
-            P(ycm, [K("in%d" % t), K("wq")], [K("yc%d" % t)], [smn])
-        else:
+        if last:
             V(lambda v: v.tensor_scalar(B("age", p1=32), dd, -C0, None, A.add), XH, [K("dd")], [K("age")], [scn])
             D("Y", T.ya[NG * h:NG * h + NG, :], B("age", p1=32), 2.0, [K("age")], [K("oa")])
+        else:
+            V(lambda v: v.tensor_tensor_scan(B("cum", p1=32), d2, T.zer[0:32, :], 0.0, A.add, A.add), wd, [K("dd"), "zer"], [K("cum")], [scn])
+            lin(lv(t + 1), dd, 1.0, -C0, XH, [K("dd"), K("livez")], [K("live%d" % (t + 1))], [scn])
+            P(ycm, [K("in%d" % t), K("wq")], [K("yc%d" % t)], [smn])
 
     for h in range(NS):
         half[0] = h
         if h:
-            loads(h, ["prod0%d" % (h - GATE)] if GATE and h >= GATE else [])
+            loads(h)
         setup(h)
         front(h, 0)
     for t in range(RO):
@@ -419,24 +410,49 @@ def depend(ops):
     return deps
 
 
-def order(ops, deps, look=LOOK, back=BACK, stag=STAG, hop=COST["hop"], passes=8):
+def joins(ops, i, j, fwd=True):
+    if i is None or "gat" not in ops[i] or "gat" not in ops[j]:
+        return False
+    (f, s, c), (f2, s2, c2) = ops[i]["gat"], ops[j]["gat"]
+    return f is f2 and s == s2 and c2 - c == (1 if fwd else -1) and c // JOIN[s] == c2 // JOIN[s]
+
+
+def join(ops, deps, seq, eng, end):
+    head, last = {}, {}
+    for i in seq:
+        j = last.get(eng[i])
+        head[i] = head[j] if joins(ops, j, i) else i
+        last[eng[i]] = i
+    ops, new = list(ops), [{} for _ in ops]
+    for i in seq:
+        for j, raw in deps[i].items():
+            new[head[i]][head[j]] = raw
+        if head[i] != i:
+            f, s, c = ops[head[i]]["gat"]
+            ops[head[i]] = dict(ops[head[i]], alts=f(s, c, ops[i]["gat"][2] + 1))
+    return ops, new, [i for i in seq if head[i] == i], eng, end
+
+
+def order(ops, deps, look=LOOK, back=BACK, stag=STAG, hop=COST["hop"], passes=PASSES, prio=None):
     n = len(ops)
     succ = [[] for _ in range(n)]
     for i in range(n):
         for j in deps[i]:
             succ[j].append(i)
-    prio = [0.0] * n
-    for i in range(n - 1, -1, -1):
-        c = min(a[1] for a in ops[i]["alts"].values()) + ops[i]["lat"] + hop + ops[i].get("fill", 0.0)
-        prio[i] = c + max([prio[k] for k in succ[i]] + [0.0])
-    for i in range(n):
-        prio[i] -= (back if "fill" in ops[i] else 0.0) + stag * ops[i]["h"]
+    if prio is None:
+        prio = [0.0] * n
+        for i in range(n - 1, -1, -1):
+            c = min(a[1] for a in ops[i]["alts"].values()) + ops[i]["lat"] + hop + ops[i].get("fill", 0.0)
+            prio[i] = c + max([prio[k] for k in succ[i]] + [0.0])
+        for i in range(n):
+            prio[i] -= (back if "fill" in ops[i] else 0.0) + stag * ops[i]["h"]
+    cheap = [min(a[1] for a in o["alts"].values()) for o in ops]
 
     def sweep(prio, fwd):
         pre, post = (deps, succ) if fwd else (succ, deps)
         left = [len(pre[i]) for i in range(n)]
         free = {e: 0.0 for e in "VSPGYN"}
-        end, eng, seq, ready = [0.0] * n, [None] * n, [], {}
+        end, eng, seq, ready, last, more = [0.0] * n, [None] * n, [], {}, {}, []
 
         def arrive(i):
             ready[i] = []
@@ -451,8 +467,19 @@ def order(ops, deps, look=LOOK, back=BACK, stag=STAG, hop=COST["hop"], passes=8)
                 arrive(i)
         while ready:
             cand = [(max(t, free[e]), i, e, c) for i, al in ready.items() for e, c, t in al]
+            busy = {x[2]: x[0] for x in sorted(cand, reverse=True) if "gat" in ops[x[1]]}
+            cand = [x for x in cand if x[3] <= 1.2 * cheap[x[1]] or x[0] + look < busy.get(x[2], 1e9)]
             first = min(c[0] for c in cand)
-            t0, i, e, c = max((x for x in cand if x[0] <= first + look), key=lambda x: (prio[x[1]], -x[0] - x[3]))
+            rank = lambda x: (prio[x[1]] + (GLUE if joins(ops, last.get(x[2]), x[1], fwd) else 0.0), -x[0] - x[3])
+            t0, i, e, c = more.pop() if more else max((x for x in cand if x[0] <= first + look), key=rank)
+            j = i + (1 if fwd else -1)
+            if joins(ops, last.get(e), i, fwd) and t0 == free[e]:
+                c -= 0.06
+            elif j in ready and joins(ops, i, j, fwd) and ops[i]["gat"][1:] < (1, NCH - 2):
+                due = min([x[0] for x in cand if x[2] == e and "gat" not in ops[x[1]] and prio[x[1]] > prio[j]] + [1e9])
+                if due > t0 + c + WAIT:
+                    more.append((t0 + c, j, e, ops[j]["alts"][e][1]))
+            last[e] = i
             if e != "N":
                 free[e] = t0 + c
             end[i] = t0 + c + (ops[i]["lat"] if fwd else 0.0)
@@ -478,7 +505,7 @@ def rank_program(g, core, T, topo):
         return
     ops = plan(T, rank, topo)
     deps = depend(ops)
-    seq, eng, end = order(ops, deps)
+    ops, deps, seq, eng, end = join(ops, deps, *order(ops, deps))
     chan, idx, cnt = {}, {}, {}
     for i in seq:
         ch = eng[i] if ops[i]["kind"] == "c" else ("x", i)

@@ -11,19 +11,22 @@ KCH = 16
 NCH = W // KCH
 JOIN = (2, 2)
 SCS = (2, 2, 2, 2, 2, 2, 2, 1, 1)
-BLOCKS = ((2, 2), (2, 2))
+BLOCKS = ((1, 1, 2), (2, 2))
 NPART = 3
 C0 = 12582912.0
-COST = {"cy": 1.0e-3, "pc": 0.52e-3, "hop": 0.1, "net": 2.2, "gath": 1.35, "scat": 3.8, "score": 22}
-LOOK, BACK, STAG, PASSES = 0.1, 2.0, 12.0, 6
+COST = {"cy": 0.93e-3, "pc": 0.53e-3, "hop": 0.09, "net": 2.0, "gath": 1.35, "scat": 4.0, "score": 11, "first": 1.0, "tab": 4.5, "load": 2.0,
+        "vec": 0.06, "act": 0.055, "dma": 0.2, "send": 0.25}
+LOOK, BACK, STAG, PASSES = 0.1, 2.0, 9.0, 6
+RUSH = ("lvl0", "posl0")
+SAME = 0.18
 GLUE = 1.0
-WAIT = 0.2
+WAIT = 0.0
 
 PART = {"tab": (4112, "bfloat16"), "gat": (32 * W, "bfloat16"), "pfl": (W, "bfloat16"), "pfb": (8 * W, "bfloat16"),
         "posl": (512, "bfloat16"), "posh": (512, "bfloat16"), "xy": (1056, "bfloat16"),
         "py": (8 * W, "bfloat16"), "lvl": (XH, "int32"), "live": (4 * XH, "bfloat16"), "age": (XH, "float32"),
         "cum": (2 * XH, "bfloat16"), "junk": (3 * W, "bfloat16"), "ac3": (4, "float32"), "sl": (8, "uint16"),
-        "xb": (80, "bfloat16"), "prod": (64 * RO, "bfloat16"), "prin": (48 * RO, "bfloat16"),
+        "prod": (128 * RO, "bfloat16"), "prin": (96 * RO, "bfloat16"),
         "lh": (768, "bfloat16"), "off": (2 * W, "uint16"), "hit": (128 * NG, "bfloat16"),
         "acc": (4 * RO, "float32"), "ina": (4 * RO, "float32"), "inc": (4 * RO, "float32"),
         "mx": (4, "float32"), "wt": (32, "bfloat16"), "wq": (256, "bfloat16"), "yco": (48, "float32")}
@@ -36,10 +39,10 @@ for _n, _c, _d in [("ip", 4, "int32"), ("ci", 8, "int32"), ("cf", 8, "float32"),
                    ("ee", 32, "bfloat16"), ("lc", 512, "bfloat16"), ("lt", 512, "bfloat16"), ("cs", 16, "float32"),
                    ("el", 4, "uint16"), ("prm", 448, "bfloat16"), ("kc", 32, "bfloat16"), ("cc", 1024, "bfloat16"),
                    ("thl", 4, "int32"), ("thf", 4, "float32"), ("thm", 8, "float32"), ("thb", 8, "float32"), ("one", 48, "bfloat16"),
-                   ("zer", 2 * XH, "bfloat16")]:
+                   ("zer", 2 * XH, "bfloat16"), ("zs", 128, "bfloat16")]:
     SCRATCH[_n] = ("sbuf", [128, _c], _d)
 
-SEMAPHORES = ["eV", "eS", "eP", "eG", "sent"] + ["d%d" % i for i in range(24)] + ["r%d" % i for i in range(6 * NS)]
+SEMAPHORES = ["eV", "eS", "eP", "eG", "sent"] + ["d%d" % i for i in range(40)] + ["r%d" % i for i in range(6 * NS)]
 
 COPIES = [(1.0, "n"), (-1.0, "q"), (2.0 ** -4, "b"), (-2.0 ** -4, "n"), (2.0 ** -8, "b"), (-2.0 ** -8, "n"), (2.0 ** -12, "b"), (-2.0 ** -12, "n")]
 UNITS = [4096.0, 256.0, 16.0, 1.0]
@@ -57,27 +60,33 @@ def plan(T, rank, topo, cost=COST):
         ops.append({"alts": alts, "r": list(r), "w": list(w), "ps": list(ps), "kind": kind, "lat": lat, "h": half[0]})
 
     def vc(k, half=False):
-        return 0.06 + max(64, k / 2 if half else k) * CY
+        return cost["vec"] + max(64, k / 2 if half else k) * CY
+
+    def ac(k):
+        return cost["act"] + max(64, k) * CY
 
     def V(fn, k, r, w, ps=(), half=False):
         op({"V": (lambda g: fn(g.vector), vc(k, half))}, r, w, ps)
 
     def S(fn, k, r, w, ps=()):
-        op({"S": (lambda g: fn(g.scalar), vc(k))}, r, w, ps)
+        op({"S": (lambda g: fn(g.scalar), ac(k))}, r, w, ps)
 
     def G(fn, k, r, w):
         op({"G": (fn, 0.17 + 2 * k * CY)}, r, w)
 
-    def fill(out, c, k, w):
-        op({"V": (lambda g: g.vector.memset(out, c), vc(k, True)),
-            "G": (lambda g: g.iota(out, [[0, k]], int(c), 0, allow_small_or_imprecise_dtypes=True), 0.13 + 2 * k * CY)}, [], w)
+    def fill(out, c, k, w, p1=None):
+        alts = {"V": (lambda g: g.vector.memset(out, c), vc(k, True)),
+                "G": (lambda g: g.iota(out, [[0, k]], int(c), 0, allow_small_or_imprecise_dtypes=True), 0.13 + 2 * k * CY)}
+        if p1:
+            alts["S"] = (lambda g: g.scalar.activation(out, T.zs[0:p1, 0:k], F.Identity, bias=c, scale=0.0), ac(k))
+        op(alts, ["zs"] if p1 else [], w)
 
     def lin(out, in_, mul, add, k, r, w, ps=(), half=False):
         def fs(g):
             if isinstance(add, float) and add == 0.0:
                 return g.scalar.activation(out, in_, F.Copy if isinstance(mul, float) else F.Identity, scale=mul)
             return g.scalar.activation(out, in_, F.Identity, bias=add, scale=mul)
-        op({"V": (lambda g: g.vector.tensor_scalar(out, in_, mul, add, A.mult, A.add), vc(k, half)), "S": (fs, vc(k))}, r, w, ps)
+        op({"V": (lambda g: g.vector.tensor_scalar(out, in_, mul, add, A.mult, A.add), vc(k, half)), "S": (fs, ac(k))}, r, w, ps)
 
     def P(mms, r, w, ps):
         def fn(g):
@@ -88,9 +97,8 @@ def plan(T, rank, topo, cost=COST):
         op({"P": (fn, 0.02 + sum(m[5] for m in mms) * PC)}, r, w, ps)
 
     def D(q, out, in_, us, r, w):
-        def fn(g):
-            return (g.sync if q == "Y" else g.scalar).dma_start(out, in_)
-        op({q: (fn, 0.1)}, r, w, kind="d", lat=us)
+        fn = {"Y": lambda g: g.sync.dma_start(out, in_), "S": lambda g: g.scalar.dma_start(out, in_)}
+        op({e: (fn[e], cost["dma"]) for e in q}, r, w, kind="d", lat=us)
 
     def part(h):
         def B(name, a=0, b=None, st=1, p0=0, p1=128):
@@ -102,15 +110,17 @@ def plan(T, rank, topo, cost=COST):
 
     def loads(h):
         B, K, _b = part(h)
-        D("Y", B("lvl", p1=32), T.lv[NG * h:NG * h + NG, :], 2.0, [], [K("lvl")])
-        D("Y", B("posl", p1=R3), T.pos[R3 * h:R3 * h + R3, :], 2.0, [], [K("posl")])
+        D("Y", B("lvl", p1=32), T.lv[NG * h:NG * h + NG, :], cost["load"], [], [K("lvl")])
+        D("S" if h == 0 else "Y", B("posl", p1=R3), T.pos[R3 * h:R3 * h + R3, :], cost["load"], [], [K("posl")])
         for u in range(NU):
-            D("S" if h == 0 else "Y", B("tab", 0, 4096, 1, RG * u, RG * u + RG), T.rf[RG * h:RG * h + RG, :], 5.0 + 4 * h, [], [K("tab%d_" % u)])
+            D("S" if h + u == 0 else "Y", B("tab", 0, 4096, 1, RG * u, RG * u + RG), T.rf[RG * h:RG * h + RG, :], cost["tab"] + 3 * h, [], [K("tab%d_" % u)])
         for u in range(NU):
             D("Y", B("pfl", p0=RG * u, p1=RG * u + RG), T.pf[RG * h:RG * h + RG, W * u:W * u + W], 2.5, [], [K("pfl%d_" % u)])
 
     loads(0)
     D("Y", T.thl[:, 0:1], T.th[:], 2.5, [], ["thl"])
+
+    V(lambda v: v.memset(T.zs[:], 0.0), 64, [], ["zs"])
 
     def iota(name, rows, pat, base=0, cm=0):
         k = 1
@@ -121,26 +131,27 @@ def plan(T, rank, topo, cost=COST):
     iota("iou", 32, [[4, NU], [4 * NU, NG], [0, 16]], 0, -1)
     G(lambda g: g.affine_select(T.iot[0:32, :], T.iou[0:32, :], [[0, NU], [-4 * NU, NG], [0, 16]], A.is_ge, -100.0, 0, 1), 128, ["iou"], ["iot"])
     iota("i128", 128, [[1, 128]])
-    iota("iob", R3, [[1, 3], [3, NG], [0, 2]])
     iota("iom", 128, [[1, 16], [0, 2]])
     iota("kc", 64, [[-1, 16], [-30000, 2]])
     lin(T.kc[32:64, 1:32:2], T.kc[32:64, 0:32:2], 1.0, 0.0, 16, ["kc"], ["kc32"])
     V(lambda v: v.memset(T.kc[32:64, 0:32:2], -30000.0), 8, ["kc32"], ["kc32"])
-    bits = [(A.bitwise_and, 15), (A.arith_shift_right, 4), (A.bitwise_and, RG - 1), (A.bitwise_and, 31)]
-    cm, cg, crg, c31 = [T.cf[:, i:i + 1] for i in range(4)]
+    bits = [(A.bitwise_and, 15), (A.bitwise_and, RG - 1), (A.arith_shift_right, 4), (A.bitwise_and, 31)]
+    cm, crg, cg, c31 = [T.cf[:, i:i + 1] for i in range(4)]
     for i, (o0, s0) in enumerate(bits):
         V(lambda v, i=i, o0=o0, s0=s0: v.tensor_scalar(T.ci[:, i:i + 1], T.ip[:, 0:1], s0, None, o0), 1, ["ip"], ["ci%d" % i])
-    V(lambda v: v.tensor_copy(T.cf[:, 0:4], T.ci[:, 0:4]), 4, ["ci%d" % i for i in range(4)], ["cf"])
+    V(lambda v: v.tensor_copy(T.cf[:, 0:2], T.ci[:, 0:2]), 2, ["ci0", "ci1"], ["cf"])
+    V(lambda v: v.tensor_copy(T.cf[:, 2:4], T.ci[:, 2:4]), 2, ["ci2", "ci3"], ["cf2"])
     G(lambda g: g.iota(T.cf[:, 6:7], [[0, 1]], 0, 1, allow_small_or_imprecise_dtypes=True), 1, [], ["cp"])
     V(lambda v: v.tensor_copy(T.el[:], T.ip[:]), 4, ["ip"], ["el"])
     for q in range(4):
         V(lambda v, q=q: v.tensor_scalar(T.lc[0:32, 128 * q:128 * q + 128], T.iot[0:32, :], float(-q), -UNITS[0], A.is_equal, A.mult), 128, ["iot"], ["lc%d" % q], half=True)
         V(lambda v, q=q: v.tensor_scalar(T.lt[0:32, 128 * q:128 * q + 128], T.iot[0:32, :], float(-q), -UNITS[0], A.is_gt, A.mult), 128, ["iot"], ["lt%d" % q], half=True)
-    for i, c in enumerate([C0] + [C0 * (UNITS[i] - UNITS[i - 1]) for i in range(1, 4)]):
-        lin(T.cc[0:1, 128 * i:128 * i + 128], T.i128[0:1, :], 0.0, c, 128, ["i128"], ["cc%d" % i])
-    V(lambda v: v.memset(T.lc[32:33, :], C0 * UNITS[0]), 256, [], ["lcz"])
-    V(lambda v: v.memset(T.live[32:33, :], 1.0), 256, [], ["livey"])
-    V(lambda v: v.memset(T.cc[0:1, 768:1024], 1.0), 128, [], ["cc6"])
+        lin(T.lc[32:33, 128 * q:128 * q + 128], T.zs[32:33, :], 0.0, C0 * UNITS[0], 128, ["zs"], ["lcz%d" % q], half=True)
+        lin(T.live[32:33, 128 * q:128 * q + 128], T.zs[32:33, :], 0.0, 1.0, 128, ["zs"], ["livey%d" % q], half=True)
+    fill(T.cc[0:1, 0:32], C0 / 2 ** 22, 32, ["cc0"], 1)
+    for i in range(1, 4):
+        fill(T.cc[0:1, 128 * i:128 * i + 128], C0 * (UNITS[i] - UNITS[i - 1]) / 2 ** 22, 128, ["cc%d" % i], 1)
+    fill(T.cc[0:1, 768:896], 2.0 ** 22, 128, ["cc6"], 1)
     ones = lambda k: T.cc[0:1, 768:768 + k]
     V(lambda v: v.tensor_scalar(T.idn[0:36, 0:36], T.i128[0:36, 0:36], T.cf[0:36, 6:7], None, A.is_equal), 36, ["i128", "cp"], ["idn0"])
     lin(T.idn[0:32, 48:80], T.idn[0:32, 0:32], 0.375, 0.0, 32, ["idn0"], ["idn1"])
@@ -155,12 +166,13 @@ def plan(T, rank, topo, cost=COST):
     V(lambda v: v.tensor_scalar(col(12), col(11), 0.0, None, A.not_equal), 1, ["cs11"], ["cs12"])
     lin(col(14), col(11), 0.5, 0.0, 1, ["cs11"], ["csc0"])
     lin(col(15), col(8), -2.0, 1.0, 1, ["csq"], ["csc1"])
-    V(lambda v: v.tensor_scalar(T.sel[:], T.i128[:, 0:32], c31, 16.0, A.is_equal, A.mult), 32, ["i128", "cf"], ["sel"])
+    V(lambda v: v.tensor_scalar(T.sel[:], T.i128[:, 0:32], c31, 16.0, A.is_equal, A.mult), 32, ["i128", "cf2"], ["sel"])
     for u in range(NU):
         V(lambda v, u=u: v.tensor_scalar(T.pair[:, RG * u:RG * u + RG], T.i128[:, 0:RG], crg, None, A.is_equal), RG, ["i128", "cf"], ["pair%d" % u])
-    V(lambda v: v.tensor_scalar(T.mg[:], T.i128[:, 0:8], cg, None, A.is_equal), 8, ["i128", "cf"], ["mg"])
-    lin(T.mge[:], T.mg[:], 2.0 ** -10, 0.0, 8, ["mg"], ["mge"])
-    fill(T.ee[0:36, :], 0.0, 32, ["eez"])
+    V(lambda v: v.tensor_scalar(T.mg[:], T.i128[:, 0:8], cg, None, A.is_equal), 8, ["i128", "cf2"], ["mg"])
+    fill(T.ee[0:64, :], 0.0, 32, ["eez"])
+    V(lambda v: v.memset(T.ee[32:64, R3:R3 + NG], -0.375), NG, ["eez"], ["eez"])
+    V(lambda v: v.memset(T.wt[32:64, :], 1.0), 32, [], ["wtz"])
     lin(T.ee[0:36, R3:R3 + NG], T.sel[0:36, 0:NG], -0.1875 / 16, 0.0, NG, ["sel", "eez"], ["ee"])
     V(lambda v: v.memset(T.prm[0:R3, :], 0.0), 224, [], ["permz"])
     V(lambda v: v.memset(T.one[0:R3, 0:32], 1.0), 16, [], ["one"])
@@ -174,12 +186,10 @@ def plan(T, rank, topo, cost=COST):
     V(lambda v: v.tensor_scalar(T.prm[0:R3, 128:256], T.prm[0:R3, 0:128], -1.0, 0.0, A.mult, A.max), 128, ["perm0%d" % r for r in range(6)] + ["permz"], ["permlo"], half=True)
     for r in range(6):
         c = rows[2][r]
-        V(lambda v, r=r, c=c: v.tensor_scalar(T.prm[0:R3, 384 + r:384 + RG:8], T.iob[0:R3, 2 * NG * c:2 * NG * (c + 1)], T.cf[0:R3, 6:7], -1.0 if r >= 3 else 1.0,
-                                              A.is_equal, A.mult), 8, ["iob", "cp", "permz"], ["perm2%d" % r])
+        G(lambda g, r=r, c=c: g.affine_select(T.prm[0:R3, 384 + r:384 + RG:8], T.one[0:R3, 17:32:2] if r >= 3 else T.one[0:R3, 0:8], [[-3, NG], [0, 2]],
+                                              A.is_equal, 0.0, -c, 1), 8, ["one", "permz"], ["perm2%d" % r])
     V(lambda v: v.tensor_copy(T.thf[:, 0:1], T.thl[:, 0:1]), 1, ["thl"], ["thf"])
     lin(T.thm[:], T.mg[:], T.thf[:, 0:1], 0.0, 8, ["mg", "thf"], ["thm"])
-    P([(T.ps7[32 * q:32 * q + 32, 0:8], T.selm[:], T.thm[:], True, True, 128) for q in range(4)], ["selm", "thm"], ["ps7"], ["ps7"])
-    lin(T.thb[:], T.ps7[:, 0:8], -1.0, 0.5, 8, ["ps7"], ["thb"], ["ps7"])
     lin(T.xy[:, 512::528], T.i128[:, 0:2 * NS], 0.0, col(12), 2 * NS, ["i128", "cs12"], ["xyz"])
     V(lambda v: v.memset(T.tab[:, 4096::4112], -8388608.0), NS, [], ["tabz"])
     fill(T.zer[0:32, :], -C0, 2 * XH, ["zer"])
@@ -188,10 +198,13 @@ def plan(T, rank, topo, cost=COST):
         B, K, (sc, _sm, pa, pb) = part(h)
         fill(B("live", XH, p1=32), 0.0, 3 * XH, [K("livez")])
         V(lambda v: v.tensor_copy(B("live", 0, XH, p1=32), B("lvl", p1=32)), XH, [K("lvl")], [K("live0")])
-        fill(B("xb", 0, 16), 0.0, 16, [K("xbz")])
         fill(B("wq"), 0.0, 256, [K("wq")])
         for s in range(2):
-            fill(B("lh", 384 * s, 384 * s + 384), 0.0, 384, [K("lh%d" % s)])
+            if h + s:
+                fill(B("lh", 384 * s, 384 * s + 384), 0.0, 384, [K("lh%d" % s)])
+            else:
+                for j in range(3):
+                    fill(B("lh", 128 * j, 128 * j + 128), 0.0, 128, ["lhz%d" % j], 128)
         pos, posh = B("posl", p1=R3), B("posh", p1=R3)
         V(lambda v: v.tensor_scalar(posh, pos, 8 * C0, 8 * C0, A.add, A.subtract), 512, [K("posl")], [K("posh")], half=True)
         P([(T[pa][:], T.prm[0:R3, 128:256], pos, True, False, 512), (T[pa][:], T.prm[0:R3, 0:128], posh, False, True, 512)],
@@ -199,6 +212,7 @@ def plan(T, rank, topo, cost=COST):
         P([(T[pb][:], T.prm[0:R3, 256:384], pos, True, True, 512)], [K("posl")] + ["perm1%d" % r for r in range(6)], [pb], [pb])
         for a, nm, bank in ((0, "xw", pa), (528, "yw", pb)):
             lin(B("xy", a, a + 512), T[bank][:], 1.0, col(12), 512, [bank, "cs12"], [K(nm)], [bank])
+        P([(T[pb][0:32, 256 + XH:256 + 2 * XH], T.cc[0:1, 0:32], ones(XH), True, True, XH)], ["cc0", "cc6", K("yw")], [K("dz")], [pb])
         P([(T[sc][RG * u:RG * u + RG, 0:W], T.prm[0:R3, 384:384 + RG], B("posl", W * u, W * u + W, p1=R3), True, True, W) for u in range(NU)],
           [K("posl")] + ["perm2%d" % r for r in range(6)], [sc], [sc])
         lin(B("py", 0, W), T[sc][:, 0:W], -1.0, col(14), W, [sc, "csc0"], [K("py0")], [sc])
@@ -209,11 +223,11 @@ def plan(T, rank, topo, cost=COST):
             elif i:
                 lin(B("py", W * i, W * i + W), B("py", 0, W), f if kind == "n" else col(15), 0.0, W,
                     [K("py0")] + ([] if kind == "n" else ["csc1"]), [K("py%d" % i)], half=True)
+        V(lambda v: v.tensor_scalar(B("pfl"), B("pfl"), 2.0 ** -10, None, A.max), W, [K("pfl%d_" % u) for u in range(NU)], [K("pfm")], half=True)
         for q in range(8):
-            o, i_, mc, ec = B("pfb", q, 8 * W, 8), B("pfl"), T.mg[:, q:q + 1], T.mge[:, q:q + 1]
-            op({"V": (lambda g, o=o, i_=i_, mc=mc: g.vector.tensor_scalar(o, i_, 2.0 ** -10, mc, A.max, A.mult), vc(W, True)),
-                "S": (lambda g, o=o, i_=i_, mc=mc, ec=ec: g.scalar.activation(o, i_, F.Identity, bias=ec, scale=mc), vc(W))},
-               [K("pfl%d_" % u) for u in range(NU)] + ["mg", "mge"], [K("pfb%d" % q)])
+            G(lambda g, q=q: g.iota(B("pfb", W * q, W * q + W), [[0, W]], 0, 0, allow_small_or_imprecise_dtypes=True), W, [], [K("pfz%d_" % q)])
+        for q in range(8):
+            D("Y", B("pfb", W * q, W * q + W, 1, 16 * q, 16 * q + 16), B("pfl", p0=16 * q, p1=16 * q + 16), 2.0, [K("pfm"), K("pfz%d_" % q)], [K("pfb%d" % q)])
 
     nrem = [0]
 
@@ -230,8 +244,8 @@ def plan(T, rank, topo, cost=COST):
             tr = RemoteDMATransfer(dst_ids=ids, dma_engine_mask=mask, remote_sem=sem, src=src, dsts=[ap for _d, ap in dsts])
             g.remote_dma_fused([tr], local_sem=T.sem.sent)
             return ne
-        op({"G": (fn, 0.3)}, key, [land + "s"], kind="s")
-        op({"N": ((sem, ne * len(dsts)), 0.0)}, [land + "s"], [land], kind="a", lat=cost["net"])
+        op({"G": (fn, cost["send"])}, key, [land + "s"], kind="s")
+        op({"N": ((sem, ne * len(dsts)), 0.0)}, [land + "s"], [land], kind="a", lat=cost["net"] + (cost["first"] if nrem[0] == 1 else 0.0))
 
     def front(h, t):
         B, K, (_sc, smn, pa, pb) = part(h)
@@ -249,34 +263,40 @@ def plan(T, rank, topo, cost=COST):
             S(lambda a, i=i, k=k: a.activation(B("junk", W * i, W * i + W), sm[:, 256:256 + W], F.Sign, bias=col(4 + k), scale=1.0 / UNITS[0],
                                                accum_out=B("ac3", i, i + 1)),
               W + 20, [K("cn"), "cs4"], [K("ac3%d" % i)], [smn])
-        P([(sm[:, 48:51], T.pair[:], B("ac3", 0, 3), True, True, 256), (sm[:, 51:52], T.pair[:], B("ac3", 0, 1), True, True, 256)],
-          [K("ac3%d" % i) for i in range(3)] + ["pair%d" % u for u in range(NU)], [K("pr")], [smn])
+        pk = ["pair%d" % u for u in range(NU)]
+        P([(T[pa][:, 323:324], T.pair[:], B("ac3", 0, 1), True, True, 256)], [K("ac30")] + pk, [K("pr")], [pa])
+        P([(T[pa][:, 320:323], T.pair[:], B("ac3", 0, 3), True, True, 256)], [K("ac3%d" % i) for i in range(3)] + pk, [K("pr")], [pa])
         sl = B("sl", 0, 4)
-        V(lambda v: v.tensor_scalar(sl, sm[:, 48:52], 0.5, 256.0, A.mult, A.add), 4, [K("pr")], [K("sl")], [smn])
-        V(lambda v: v.tensor_copy(B("xb", 16, 80), B("xy", 0, 513).indirect(sl)), 64 * cost["gath"], [K("sl"), K("xw"), "xyz"], [K("xb")])
-        prod, prin = B("prod", 64 * t + 16, 64 * t + 64), B("prin", 48 * t, 48 * t + 48)
-        V(lambda v: v.tensor_tensor(B("prod", 64 * t, 64 * t + 64), B("xy", 528, 1041).indirect(sl), B("xb", 0, 64), A.mult), 64 * cost["gath"],
-          [K("sl"), K("yw"), "xyz", K("xb"), K("xbz")], [K("prod%d" % t)])
-        send(prod, [(T.cores[(rank + t + 1) % n], prin)], [K("prod%d" % t)], K("prin%d" % t))
+        V(lambda v: v.tensor_scalar(sl, T[pa][:, 320:324], 0.5, 256.0, A.mult, A.add), 4, [K("pr")], [K("sl")], [pa])
+        for a, w0, nm in ((0, 528, "yw"), (64, 0, "xw")):
+            o, w = B("prod", 128 * t + a, 128 * t + a + 64), B("xy", w0, w0 + 513).indirect(sl)
+            us = 0.06 + 64 * cost["gath"] * CY
+            op({"V": (lambda g, o=o, w=w: g.vector.tensor_copy(o, w), us), "S": (lambda g, o=o, w=w: g.scalar.activation(o, w, F.Copy), us)},
+               [K("sl"), K(nm), "xyz"], [K("prod%d" % t) + nm])
+        pk = [K("prod%d" % t) + nm for nm in ("xw", "yw")]
+        send(B("prod", 128 * t + 16, 128 * t + 112), [(T.cores[(rank + t + 1) % n], B("prin", 96 * t, 96 * t + 96))], pk, K("prin%d" % t))
         for s in range(2):
             lh = K("lh%d" % s)
-            V(lambda v, s=s: v.tensor_copy(B("lh", 384 * s, 384 * s + 384).indirect(T.el[:, 0:3]), prin if s else prod), 48 * cost["scat"],
-              [K(("prin%d" if s else "prod%d") % t), "el"], [lh])
+            nm, a = ("prin", 96 * t) if s else ("prod", 128 * t + 16)
+            V(lambda v, s=s, nm=nm, a=a: v.tensor_tensor(B("lh", 384 * s, 384 * s + 384).indirect(T.el[:, 0:3]), B(nm, a + 48, a + 96), B(nm, a, a + 48), A.mult),
+              48 * cost["scat"], ([K("prin%d" % t)] if s else pk) + ["el", "lhz0", "lhz1", "lhz2"], [lh])
             for c, nq in enumerate(BLOCKS[s]):
-                bank = (pa, pb)[c % 2]
+                bank = (pa, pb)[(c + s * len(BLOCKS[0])) % 2]
                 q0, wd = sum(BLOCKS[s][:c]), XH * nq
                 o = T[bank][:, 0:wd]
+                pen = [((T[bank][:, XH * q:XH * q + XH], T.lc[0:33, 128 * (q0 + q):128 * (q0 + q + 1)], B("live", XH * t, XH * t + XH, p1=33), nq == 1, False, 64),
+                        [K("live%d" % t), "lc%d" % (q0 + q), "lcz%d" % (q0 + q), "livey%d" % (2 * h + t // 2)]) for q in range(nq)]
+                if nq == 1:
+                    P([pen[0][0]], pen[0][1], ["pl" + bank], [bank])
                 mm = []
                 for i, level in enumerate(LEVELS):
                     if i:
                         mm.append(((o, T.cc[0:1, 128 * i:128 * i + 128], ones(wd), False, False, wd), ["cc%d" % i, "cc6"]))
                     for j, k in level:
-                        mm.append(((o, B("lh", 384 * s + 128 * j, 384 * s + 128 * j + 128), B("py", W * k + XH * q0, W * k + XH * q0 + wd), not mm, i == 3, wd),
+                        mm.append(((o, B("lh", 384 * s + 128 * j, 384 * s + 128 * j + 128), B("py", W * k + XH * q0, W * k + XH * q0 + wd), not mm and nq > 1, i == 3, wd),
                                    [lh, K("py%d" % k)]))
-                        if len(mm) == 1:
-                            mm += [((T[bank][:, XH * q:XH * q + XH], T.lc[0:33, 128 * (q0 + q):128 * (q0 + q + 1)],
-                                     B("live", XH * t, XH * t + XH, p1=33), False, False, 64), [K("live%d" % t), "lc%d" % (q0 + q), "lcz", "livey"])
-                                   for q in range(nq)]
+                        if len(mm) == 1 and nq > 1:
+                            mm += pen
                 parts = NPART * nq // 2 + 1
                 for i in range(parts):
                     mp = mm[len(mm) * i // parts:len(mm) * (i + 1) // parts]
@@ -285,7 +305,7 @@ def plan(T, rank, topo, cost=COST):
                   ["pl" + bank], [K("off%d%d" % (s, q0 + q)) for q in range(nq)], [bank])
 
     def back(h, t):
-        B, K, (scn, smn, _pa, _pb) = part(h)
+        B, K, (scn, smn, pa, pb) = part(h)
         sc, sm = T[scn], T[smn]
 
         def gather(s, c0, c1):
@@ -302,7 +322,7 @@ def plan(T, rank, topo, cost=COST):
             mm, k0 = [], sum(SCS[:c])
             for x in range(k0 * KCH, (k0 + k1) * KCH):
                 q, xh = x // XH, x % XH
-                mm.append((sc[32 * q:32 * q + 32, 8 * xh:8 * xh + 8], B("gat", 32 * x, 32 * x + 32), B("pfb", 8 * x, 8 * x + 8), True, True, cost["score"]))
+                mm.append((sc[32 * q:32 * q + 32, 8 * xh:8 * xh + 8], B("gat", 32 * x, 32 * x + 32), B("pfb", x, 8 * W, W), True, True, cost["score"]))
             P(mm, [K("gat%d%d_" % (s, k)) for s in range(2) for k in range(k0, k0 + k1)] + [K("pfb%d" % q) for q in range(8)], [K("s%d_" % c)], [scn])
         acc = B("acc", 4 * t, 4 * t + NG)
         for k in range(NG):
@@ -325,40 +345,39 @@ def plan(T, rank, topo, cost=COST):
         P([(k0, inc, s1, False, False, 64), (k1, ina, s0, False, False, 64), (key, T.idn[0:36, 0:36], T.kc[0:36, :], False, True, 36)],
           [K("in%d" % t)], [K("key")], [smn])
         mx = B("mx", 0, 1, p1=36)
-        V(lambda v: v.tensor_reduce(mx, key, AxisListType.X, A.max), 32, [K("key")], [K("mx")], [smn])
-        V(lambda v: v.tensor_scalar(B("wt", p1=36), key, mx, None, A.is_equal), 32, [K("key"), K("mx")], [K("wt")], [smn])
-        P([(sm[32 * q:32 * q + 32, 32:32 + 4 * NG], B("wt", p1=36), T.ee[0:36, R3 - NG * q:R3 - NG * q + 4 * NG], True, True, 32) for q in range(4)],
+        V(lambda v: v.tensor_reduce(mx, key, AxisListType.X, A.max, negate=True), 32, [K("key")], [K("mx")], [smn])
+        op({"V": (lambda g: g.vector.tensor_scalar(B("wt", p1=36), key, mx, -1.0, A.add, A.max), vc(32)),
+            "S": (lambda g: g.scalar.activation(B("wt", p1=36), key, F.Sign, bias=mx), ac(32))}, [K("key"), K("mx"), "wtz"], [K("wt")], [smn])
+        P([(sm[32 * q:32 * q + 32, 32:32 + 4 * NG], B("wt", p1=37), T.ee[0:37, R3 - NG * q:R3 - NG * q + 4 * NG], True, True, 32) for q in range(4)],
           [K("wt"), "ee"], [K("w")], [smn])
-        yc = sm[0:NG, 64 + t:112:3]
-        ycm = [(yc, acc, s0, True, False, 64), (yc, inc, s1, False, True, 64)]
+        yc = T[pa][0:NG, 256 + t:304:3]
         last = t == RO - 1
-        if last:
-            P(ycm, [K("in%d" % t), K("w")], [K("yc%d" % t)], [smn])
+        P([(yc, acc, s0, True, False, 64), (yc, inc, s1, False, True, 64)], [K("in%d" % t), K("w")], [K("yc%d" % t)], [pa])
         lin(B("wq", 112, 112 + 4 * NG), sm[:, 32:32 + 4 * NG], 1.0, 0.0, 16, [K("w")], [K("wq")], [smn])
         if last:
-            V(lambda v: v.tensor_scalar(B("yco", p1=NG), sm[0:NG, 64:112], 1.0 / 32, 512.0, A.mult, A.add), 48,
-              [K("yc%d" % i) for i in range(RO)], [K("yco")], [smn])
+            V(lambda v: v.tensor_scalar(B("yco", p1=NG), T[pa][0:NG, 256:304], 1.0 / 32, 512.0, A.mult, A.add), 48,
+              [K("yc%d" % i) for i in range(RO)], [K("yco")], [pa])
             D("Y", T.yc[RG * h:RG * h + RG, :], B("yco", p1=NG), 2.0, [K("yco")], [K("oc")])
-        wd = XH if last else 2 * XH
-        dd, d2 = sc[0:32, 0:XH], sc[0:32, 0:wd]
-        lv = lambda i, k=XH: B("live", XH * i, XH * i + k, p1=32)
-        mm = [(d2, T.idn[0:32, 48:80], lv(t, wd), True, False, wd)]
+        dd = T[pb][0:32, 256:256 + XH]
+        lv = lambda i: B("live", XH * i, XH * i + XH, p1=32)
+        P([(dd, T.idn[0:32, 48:80], lv(t), True, False, XH)], ["idn1", K("live%d" % t), K("key")], [K("dd")], [pb])
+        mm = []
         for k in range(NG):
             for u in range(NU):
                 a0 = 112 - 31 * k - 4 * NG * u
                 mm.append((dd, B("wq", a0, a0 + 32 * NG, NG), B("hit", 128 * k + u, 128 * k + 128, NU), False, False, XH))
-        mm.append((d2, T.cc[0:1, 0:32], ones(wd), False, not last, wd))
+        mm.append((dd, T.cc[0:1, 0:32], ones(XH), False, not last, XH))
         if last:
             mm += [(dd, T.idn[0:32, 0:32], lv(i), False, i == t, XH) for i in range(RO)]
-        P(mm, [K("wq"), "idn0", "idn1", "cc0", "cc6", K("livez")] + [K("live%d" % i) for i in range(t + 2)] + [K("hit%d" % k) for k in range(NG)],
-          [K("dd")], [scn])
+        P(mm, [K("wq"), "idn0", "idn1", "cc0", "cc6", K("livez")] + [K("live%d" % i) for i in range(t + 1)] + [K("hit%d" % k) for k in range(NG)],
+          [K("dd")], [pb])
         if last:
-            V(lambda v: v.tensor_scalar(B("age", p1=32), dd, -C0, None, A.add), XH, [K("dd")], [K("age")], [scn])
-            D("Y", T.ya[NG * h:NG * h + NG, :], B("age", p1=32), 2.0, [K("age")], [K("oa")])
+            V(lambda v: v.tensor_scalar(B("age", p1=32), dd, -C0, None, A.add), XH, [K("dd")], [K("age")], [pb])
+            D("S" if h else "Y", T.ya[NG * h:NG * h + NG, :], B("age", p1=32), 2.0, [K("age")], [K("oa")])
         else:
-            V(lambda v: v.tensor_tensor_scan(B("cum", p1=32), d2, T.zer[0:32, :], 0.0, A.add, A.add), wd, [K("dd"), "zer"], [K("cum")], [scn])
-            lin(lv(t + 1), dd, 1.0, -C0, XH, [K("dd"), K("livez")], [K("live%d" % (t + 1))], [scn])
-            P(ycm, [K("in%d" % t), K("wq")], [K("yc%d" % t)], [smn])
+            V(lambda v: v.tensor_tensor_scan(B("cum", p1=32), T[pb][0:32, 256:256 + 2 * XH], T.zer[0:32, :], 0.0, A.add, A.add), 2 * XH,
+              [K("dd"), K("dz"), "zer"], [K("cum")], [pb])
+            lin(lv(t + 1), dd, 1.0, -C0, XH, [K("dd"), K("livez")], [K("live%d" % (t + 1))], [pb])
 
     for h in range(NS):
         half[0] = h
@@ -366,6 +385,9 @@ def plan(T, rank, topo, cost=COST):
             loads(h)
         setup(h)
         front(h, 0)
+    half[0] = 0
+    P([(T.ps1[32 * q:32 * q + 32, 112:120], T.selm[:], T.thm[:], True, True, 128) for q in range(4)], ["selm", "thm"], ["thp"], ["ps1"])
+    lin(T.thb[:], T.ps1[:, 112:120], -1.0, 0.5, 8, ["thp"], ["thb"], ["ps1"])
     for t in range(RO):
         for h in range(NS):
             half[0] = h
@@ -399,7 +421,7 @@ def depend(ops):
                 prev, cur = cur, [i]
                 epoch[b] = (eng, cur, prev)
             for j in prev:
-                d.setdefault(j, False)
+                d.setdefault(j, None)
         for k in o["r"]:
             readers.setdefault(k, []).append(i)
         for k in o["w"]:
@@ -460,7 +482,8 @@ def order(ops, deps, look=LOOK, back=BACK, stag=STAG, hop=COST["hop"], passes=PA
                 t = 0.0
                 for j in pre[i]:
                     same = eng[j] == e and ops[j if fwd else i]["kind"] == "c"
-                    t = max(t, end[j] + ((0.0 if e == "P" else 0.05) if same else hop))
+                    nowait = e == "P" or (deps[i][j] if fwd else deps[j][i]) is None
+                    t = max(t, end[j] + ((0.0 if nowait else SAME) if same else hop))
                 ready[i].append((e, a[1], t + (0.0 if fwd else ops[i]["lat"])))
         for i in range(n):
             if left[i] == 0:
@@ -470,8 +493,12 @@ def order(ops, deps, look=LOOK, back=BACK, stag=STAG, hop=COST["hop"], passes=PA
             busy = {x[2]: x[0] for x in sorted(cand, reverse=True) if "gat" in ops[x[1]]}
             cand = [x for x in cand if x[3] <= 1.2 * cheap[x[1]] or x[0] + look < busy.get(x[2], 1e9)]
             first = min(c[0] for c in cand)
-            rank = lambda x: (prio[x[1]] + (GLUE if joins(ops, last.get(x[2]), x[1], fwd) else 0.0), -x[0] - x[3])
-            t0, i, e, c = more.pop() if more else max((x for x in cand if x[0] <= first + look), key=rank)
+            near = [x for x in cand if x[0] <= first + look]
+            pick = max(near, key=lambda x: (ops[x[1]]["w"][0] in RUSH, prio[x[1]], -x[0] - x[3]))
+            if "gat" in ops[pick[1]]:
+                pick = max((x for x in near if "gat" in ops[x[1]]),
+                           key=lambda x: (prio[x[1]] + (GLUE if joins(ops, last.get(x[2]), x[1], fwd) else 0.0), -x[0] - x[3]))
+            t0, i, e, c = more.pop() if more else pick
             j = i + (1 if fwd else -1)
             if joins(ops, last.get(e), i, fwd) and t0 == free[e]:
                 c -= 0.06
@@ -520,7 +547,7 @@ def rank_program(g, core, T, topo):
             continue
         w = []
         for j in sorted(deps[i], key=lambda j: -end[j]):
-            if chan[j] == e and e == "P":
+            if chan[j] == e and (e == "P" or deps[i][j] is None):
                 continue
             if clock[e].get(chan[j], 0) >= idx[j]:
                 continue

@@ -1,3 +1,4 @@
+import math
 from concourse.bass import DstId, RemoteDMATransfer
 from concourse.mybir import dt, AluOpType, AxisListType, ActivationFunctionType
 
@@ -9,61 +10,69 @@ NS = NU = 8 // NG
 W, XH = 64 * NG, 16 * NG
 KCH = 16
 NCH = W // KCH
-JOIN = (2, 2)
-SCS = (2, 2, 2, 2, 2, 2, 2, 1, 1)
-BLOCKS = ((1, 1, 2), (2, 2))
-NPART = 3
+JOIN = 8
+SCS = (2, 2, 2, 2, 2, 2, 1, 1, 1, 1)
+BLOCKS = ((64, 64, 128), (128, 128))
+PLACES = ("ps2", "ps3", "ps6", "ps7")
+RAMP = False
+PASS = 384
 C0 = 12582912.0
-COST = {"cy": 0.93e-3, "pc": 0.53e-3, "hop": 0.09, "net": 2.0, "gath": 1.35, "scat": 4.0, "score": 11, "first": 1.0, "tab": 4.5, "load": 2.0,
-        "vec": 0.06, "act": 0.055, "dma": 0.2, "send": 0.25}
-LOOK, BACK, STAG, PASSES = 0.1, 2.0, 9.0, 6
-RUSH = ("lvl0", "posl0")
-SAME = 0.18
-GLUE = 1.0
-WAIT = 0.0
+COST = {"f": 1.1, "pc": 0.48e-3, "gath": 1.25e-3, "scat": 3.0e-3, "hop": 0.07, "net": 1.6, "first": 1.0, "send": 0.25,
+        "dfix": 1.8, "dma": 0.1, "bw": 350e3, "row": 0.015, "load": 0.5}
+WIDE = ("ac3", "sel")
 
 PART = {"tab": (4112, "bfloat16"), "gat": (32 * W, "bfloat16"), "pfl": (W, "bfloat16"), "pfb": (8 * W, "bfloat16"),
-        "posl": (512, "bfloat16"), "posh": (512, "bfloat16"), "xy": (1056, "bfloat16"),
+        "posl": (512, "bfloat16"), "xy": (1056, "bfloat16"),
         "py": (8 * W, "bfloat16"), "lvl": (XH, "int32"), "live": (4 * XH, "bfloat16"), "age": (XH, "float32"),
-        "cum": (2 * XH, "bfloat16"), "junk": (3 * W, "bfloat16"), "ac3": (4, "float32"), "sl": (8, "uint16"),
-        "prod": (128 * RO, "bfloat16"), "prin": (96 * RO, "bfloat16"),
+        "cum": (2 * XH, "bfloat16"), "junk": (3 * W, "bfloat16"), "ac3": (W + 4, "float32"), "sl": (8, "uint16"),
+        "prod": (96 * RO, "bfloat16"), "prin": (96 * RO, "bfloat16"),
         "lh": (768, "bfloat16"), "off": (2 * W, "uint16"), "hit": (128 * NG, "bfloat16"),
         "acc": (4 * RO, "float32"), "ina": (4 * RO, "float32"), "inc": (4 * RO, "float32"),
         "mx": (4, "float32"), "wt": (32, "bfloat16"), "wq": (256, "bfloat16"), "yco": (48, "float32")}
 SCRATCH = {_n: ("sbuf", [128, NS * _c], _d) for _n, (_c, _d) in PART.items()}
 for _j in range(8):
     SCRATCH["ps%d" % _j] = ("psum", [128, 512], "float32")
-for _n, _c, _d in [("ip", 4, "int32"), ("ci", 8, "int32"), ("cf", 8, "float32"), ("i128", 128, "float32"), ("iom", 32, "float32"),
-                   ("iot", 128, "bfloat16"), ("iou", 128, "bfloat16"), ("iob", 24, "float32"), ("idn", 80, "bfloat16"),
-                   ("selm", 32, "float32"), ("sel", 32, "float32"), ("pair", 128, "float32"), ("mg", 8, "float32"), ("mge", 8, "float32"),
+for _n, _c, _d in [("ip", 4, "int32"), ("ci", 8, "int32"), ("i4", 4, "float32"), ("iot", 128, "bfloat16"), ("iou", 128, "bfloat16"),
+                   ("idn", 80, "bfloat16"), ("sel", 32, "float32"), ("pair", 128, "float32"),
                    ("ee", 32, "bfloat16"), ("lc", 512, "bfloat16"), ("lt", 512, "bfloat16"), ("cs", 16, "float32"),
                    ("el", 4, "uint16"), ("prm", 448, "bfloat16"), ("kc", 32, "bfloat16"), ("cc", 1024, "bfloat16"),
-                   ("thl", 4, "int32"), ("thf", 4, "float32"), ("thm", 8, "float32"), ("thb", 8, "float32"), ("one", 48, "bfloat16"),
-                   ("zer", 2 * XH, "bfloat16"), ("zs", 128, "bfloat16")]:
+                   ("thl", 16, "int32"), ("thf", 32, "float32"), ("thb", 8, "float32"), ("sgn", 64, "bfloat16"),
+                   ("zer", 2 * XH, "bfloat16"), ("zs", 512, "bfloat16"), ("ramp", W, "bfloat16")]:
     SCRATCH[_n] = ("sbuf", [128, _c], _d)
 
-SEMAPHORES = ["eV", "eS", "eP", "eG", "sent"] + ["d%d" % i for i in range(40)] + ["r%d" % i for i in range(6 * NS)]
+SEMAPHORES = ["eV", "eS", "eP", "eG", "sent"] + ["d%d" % i for i in range(44)] + ["r%d" % i for i in range(6 * NS)]
 
-COPIES = [(1.0, "n"), (-1.0, "q"), (2.0 ** -4, "b"), (-2.0 ** -4, "n"), (2.0 ** -8, "b"), (-2.0 ** -8, "n"), (2.0 ** -12, "b"), (-2.0 ** -12, "n")]
+COPIES = [None, (0, -1.0, "q"), (0, 2.0 ** -4, "b"), (0, -2.0 ** -4, None), (2, 2.0 ** -4, None), (0, -2.0 ** -8, None),
+          (2, 2.0 ** -8, None), (0, -2.0 ** -12, None)]
 UNITS = [4096.0, 256.0, 16.0, 1.0]
 LEVELS = [[(0, 0), (1, 0), (2, 0), (0, 1), (1, 1), (2, 1), (0, 2)], [(0, 3), (1, 4)], [(1, 5), (2, 6)], [(2, 7)]]
+
+
+def block(s, c):
+    return sum(sum(BLOCKS[s][:b + 1]) <= KCH * c for b in range(len(BLOCKS[s])))
 
 
 def plan(T, rank, topo, cost=COST):
     ops = []
     half = [0]
+    tag = ["setup", 0, 0]
     n = len(T.cores)
     core = T.cores[rank]
-    CY, PC = cost["cy"], cost["pc"]
+    FX, PC = cost["f"], cost["pc"]
+    CY = 0.83e-3 * FX
 
     def op(alts, r=(), w=(), ps=(), kind="c", lat=0.0):
-        ops.append({"alts": alts, "r": list(r), "w": list(w), "ps": list(ps), "kind": kind, "lat": lat, "h": half[0]})
+        ops.append({"alts": alts, "r": list(r), "w": list(w), "ps": list(ps), "kind": kind, "lat": lat, "h": half[0], "tag": tuple(tag)})
+        tag[1] += 1
 
     def vc(k, half=False):
-        return cost["vec"] + max(64, k / 2 if half else k) * CY
+        return 0.05 + max(64, k / 2 if half else k) * CY
 
     def ac(k):
-        return cost["act"] + max(64, k) * CY
+        return 0.065 + max(64, k) * CY
+
+    def gc(k, fix):
+        return fix * FX + 2 * k * CY
 
     def V(fn, k, r, w, ps=(), half=False):
         op({"V": (lambda g: fn(g.vector), vc(k, half))}, r, w, ps)
@@ -71,15 +80,24 @@ def plan(T, rank, topo, cost=COST):
     def S(fn, k, r, w, ps=()):
         op({"S": (lambda g: fn(g.scalar), ac(k))}, r, w, ps)
 
-    def G(fn, k, r, w):
-        op({"G": (fn, 0.17 + 2 * k * CY)}, r, w)
+    def iota(out, pat, base, cm, w, r=()):
+        k = out.shape[1]
+        op({"G": (lambda g: g.iota(out, pat, base, cm, allow_small_or_imprecise_dtypes=True), gc(k, 0.13))}, r, w)
 
-    def fill(out, c, k, w, p1=None):
+    def select(out, in_, pat, cmp, c, base, cm, r, w):
+        op({"G": (lambda g: g.affine_select(out, in_, pat, cmp, c, base, cm), gc(out.shape[1], 0.17))}, r, w)
+
+    def paint(out, zero, pat, c, base, w):
+        select(out, zero, pat, A.not_equal, c, base, 1, ["zs"], w)
+
+    def fill(out, c, w, p=None):
+        k = out.shape[1]
         alts = {"V": (lambda g: g.vector.memset(out, c), vc(k, True)),
-                "G": (lambda g: g.iota(out, [[0, k]], int(c), 0, allow_small_or_imprecise_dtypes=True), 0.13 + 2 * k * CY)}
-        if p1:
-            alts["S"] = (lambda g: g.scalar.activation(out, T.zs[0:p1, 0:k], F.Identity, bias=c, scale=0.0), ac(k))
-        op(alts, ["zs"] if p1 else [], w)
+                "G": (lambda g: g.iota(out, [[0, k]], int(c), 0, allow_small_or_imprecise_dtypes=True), gc(k, 0.13))}
+        if p:
+            alts["S"] = (lambda g: g.scalar.activation(out, T.zs[p[0]:p[1], 0:k], F.Identity, bias=c, scale=0.0), ac(k))
+        op(alts, ["zs"] if p else [], w)
+        ops[-1]["blank"] = True
 
     def lin(out, in_, mul, add, k, r, w, ps=(), half=False):
         def fs(g):
@@ -94,11 +112,12 @@ def plan(T, rank, topo, cost=COST):
             for o, l, rh, st, sp, _c in mms:
                 last = g.tensor.matmul(o, l, rh, st, sp)
             return last
-        op({"P": (fn, 0.02 + sum(m[5] for m in mms) * PC)}, r, w, ps)
+        op({"P": (fn, sum(max(m[5] * cost["load"], min(m[5], m[2].shape[1] * (4 if m[2].name in WIDE else 1))) for m in mms) * PC)}, r, w, ps)
 
-    def D(q, out, in_, us, r, w):
+    def D(q, out, in_, kb, r, w):
         fn = {"Y": lambda g: g.sync.dma_start(out, in_), "S": lambda g: g.scalar.dma_start(out, in_)}
-        op({e: (fn[e], cost["dma"]) for e in q}, r, w, kind="d", lat=us)
+        op({e: (fn[e], cost["dma"]) for e in q}, r, w, kind="d", lat=cost["dfix"])
+        ops[-1]["move"] = kb * 1024 / cost["bw"] + max(16, out.shape[0]) / 16 * cost["row"]
 
     def part(h):
         def B(name, a=0, b=None, st=1, p0=0, p1=128):
@@ -110,128 +129,121 @@ def plan(T, rank, topo, cost=COST):
 
     def loads(h):
         B, K, _b = part(h)
-        D("Y", B("lvl", p1=32), T.lv[NG * h:NG * h + NG, :], cost["load"], [], [K("lvl")])
-        D("S" if h == 0 else "Y", B("posl", p1=R3), T.pos[R3 * h:R3 * h + R3, :], cost["load"], [], [K("posl")])
+        two = "Y" if h else "S"
+        D("Y", B("lvl", p1=32), T.lv[NG * h:NG * h + NG, :], 8, [], [K("lvl")])
         for u in range(NU):
-            D("S" if h + u == 0 else "Y", B("tab", 0, 4096, 1, RG * u, RG * u + RG), T.rf[RG * h:RG * h + RG, :], cost["tab"] + 3 * h, [], [K("tab%d_" % u)])
+            D(two, B("posl", p0=R3 * u, p1=R3 * u + R3), T.pos[R3 * h:R3 * h + R3, :], 12, [], [K("posl%d_" % u)])
+        if h == 0:
+            D("Y", T.thl[0:8, :], T.th[:], 1, [], ["thl"])
+            for u in range(NU):
+                table(h, u, [])
         for u in range(NU):
-            D("Y", B("pfl", p0=RG * u, p1=RG * u + RG), T.pf[RG * h:RG * h + RG, W * u:W * u + W], 2.5, [], [K("pfl%d_" % u)])
+            D("Y", B("pfl", p0=RG * u, p1=RG * u + RG), T.pf[RG * h:RG * h + RG, W * u:W * u + W], 32, [], [K("pfl%d_" % u)])
+        if h:
+            table(h, 0, [])
+
+    def table(h, u, after):
+        B, K, _b = part(h)
+        D("Y" if u or h else "S", B("tab", 0, 4096, 1, RG * u, RG * u + RG), T.rf[RG * h:RG * h + RG, :], 512, after, [K("tab%d_" % u)])
 
     loads(0)
-    D("Y", T.thl[:, 0:1], T.th[:], 2.5, [], ["thl"])
 
-    V(lambda v: v.memset(T.zs[:], 0.0), 64, [], ["zs"])
-
-    def iota(name, rows, pat, base=0, cm=0):
-        k = 1
-        for _s, c in pat:
-            k *= c
-        G(lambda g: g.iota(T[name][0:rows, 0:k], pat, base, cm, allow_small_or_imprecise_dtypes=True), k, [], [name])
-    G(lambda g: g.iota(T.ip[:], [[128, 4]], 0, 1), 4, [], ["ip"])
-    iota("iou", 32, [[4, NU], [4 * NU, NG], [0, 16]], 0, -1)
-    G(lambda g: g.affine_select(T.iot[0:32, :], T.iou[0:32, :], [[0, NU], [-4 * NU, NG], [0, 16]], A.is_ge, -100.0, 0, 1), 128, ["iou"], ["iot"])
-    iota("i128", 128, [[1, 128]])
-    iota("iom", 128, [[1, 16], [0, 2]])
-    iota("kc", 64, [[-1, 16], [-30000, 2]])
-    lin(T.kc[32:64, 1:32:2], T.kc[32:64, 0:32:2], 1.0, 0.0, 16, ["kc"], ["kc32"])
-    V(lambda v: v.memset(T.kc[32:64, 0:32:2], -30000.0), 8, ["kc32"], ["kc32"])
-    bits = [(A.bitwise_and, 15), (A.bitwise_and, RG - 1), (A.arith_shift_right, 4), (A.bitwise_and, 31)]
-    cm, crg, cg, c31 = [T.cf[:, i:i + 1] for i in range(4)]
-    for i, (o0, s0) in enumerate(bits):
-        V(lambda v, i=i, o0=o0, s0=s0: v.tensor_scalar(T.ci[:, i:i + 1], T.ip[:, 0:1], s0, None, o0), 1, ["ip"], ["ci%d" % i])
-    V(lambda v: v.tensor_copy(T.cf[:, 0:2], T.ci[:, 0:2]), 2, ["ci0", "ci1"], ["cf"])
-    V(lambda v: v.tensor_copy(T.cf[:, 2:4], T.ci[:, 2:4]), 2, ["ci2", "ci3"], ["cf2"])
-    G(lambda g: g.iota(T.cf[:, 6:7], [[0, 1]], 0, 1, allow_small_or_imprecise_dtypes=True), 1, [], ["cp"])
+    V(lambda v: v.memset(T.zs[:], 0.0), 512, [], ["zs"], half=True)
+    op({"G": (lambda g: g.iota(T.ip[:], [[128, 4]], 0, 1), gc(4, 0.13))}, [], ["ip"])
+    iota(T.iou[0:32, :], [[4, NU], [4 * NU, NG], [0, 16]], 0, -1, ["iou"])
+    select(T.iot[0:32, :], T.iou[0:32, :], [[0, NU], [-4 * NU, NG], [0, 16]], A.is_ge, -100.0, 0, 1, ["iou"], ["iot"])
+    iota(T.i4[:], [[1, 4]], 0, 0, ["i4"])
+    iota(T.kc[0:32, :], [[-1, 16], [-30000, 2]], 0, 0, ["kc"])
+    iota(T.kc[32:64, :], [[-1, 16], [30000, 2]], -30000, 0, ["kc32"])
+    c15, c11 = T.ci[:, 0:1], T.ci[:, 1:2]
+    V(lambda v: v.tensor_scalar(c15, T.ip[:, 0:1], 15, None, A.bitwise_and), 1, ["ip"], ["c15"])
+    V(lambda v: v.tensor_scalar(c11, T.ip[:, 0:1], 3, None, A.bitwise_and), 1, ["ip"], ["c11"])
     V(lambda v: v.tensor_copy(T.el[:], T.ip[:]), 4, ["ip"], ["el"])
+    cn = {k: T.cs[:, i:i + 1] for i, k in enumerate(("m", "one", "scl", "q", "b", "x", "n", "u"))}
+    for k, c, s1, s2, o0, o1 in (("m", "c15", 3.0, 0.5, A.mult, A.add), ("one", "c11", 3.0, 1.0, A.is_equal, A.mult),
+                                 ("scl", "c11", 3.0, 1.0, A.is_equal, A.subtract), ("q", "c15", 3.0, 2048.0, A.is_equal, A.mult),
+                                 ("u", "c15", 15.0, C0 * (UNITS[1] - UNITS[0]), A.is_equal, A.mult), ("x", "c15", 3.0, 1024.125, A.is_equal, A.mult)):
+        V(lambda v, k=k, c=c, s1=s1, s2=s2, o0=o0, o1=o1: v.tensor_scalar(cn[k], c15 if c == "c15" else c11, s1, s2, o0, o1), 1, [c], ["c" + k])
+    lin(cn["n"], cn["one"], -0.125, cn["x"], 1, ["cone", "cx"], ["cn"])
+    lin(cn["b"], cn["q"], 1920.0 / 2048, cn["u"], 1, ["cq", "cu"], ["cb"])
+    lin(T.cs[:, 8:11], T.i4[:, 0:3], 1.0, cn["m"], 3, ["cm", "i4"], ["cs4"])
     for q in range(4):
         V(lambda v, q=q: v.tensor_scalar(T.lc[0:32, 128 * q:128 * q + 128], T.iot[0:32, :], float(-q), -UNITS[0], A.is_equal, A.mult), 128, ["iot"], ["lc%d" % q], half=True)
         V(lambda v, q=q: v.tensor_scalar(T.lt[0:32, 128 * q:128 * q + 128], T.iot[0:32, :], float(-q), -UNITS[0], A.is_gt, A.mult), 128, ["iot"], ["lt%d" % q], half=True)
-        lin(T.lc[32:33, 128 * q:128 * q + 128], T.zs[32:33, :], 0.0, C0 * UNITS[0], 128, ["zs"], ["lcz%d" % q], half=True)
-        lin(T.live[32:33, 128 * q:128 * q + 128], T.zs[32:33, :], 0.0, 1.0, 128, ["zs"], ["livey%d" % q], half=True)
-    fill(T.cc[0:1, 0:32], C0 / 2 ** 22, 32, ["cc0"], 1)
-    for i in range(1, 4):
-        fill(T.cc[0:1, 128 * i:128 * i + 128], C0 * (UNITS[i] - UNITS[i - 1]) / 2 ** 22, 128, ["cc%d" % i], 1)
-    fill(T.cc[0:1, 768:896], 2.0 ** 22, 128, ["cc6"], 1)
+    fill(T.lc[32:33, :], C0 * UNITS[0] / 2 ** 17, ["lcz"], (32, 33))
+    fill(T.live[32:33, :], 2.0 ** 17, ["livey"], (32, 33))
+    fill(T.cc[0:1, 512:544], C0 / 2 ** 22, ["cc4"], (0, 1))
+    fill(T.cc[0:1, 768:896], 2.0 ** 22, ["cc6"], (0, 1))
+    fill(T.cc[0:1, 0:128], 8 * C0 / 2 ** 22, ["cc0"], (0, 1))
+    fill(T.cc[0:1, 896:1024], -8 * C0 / 2 ** 22, ["cc7"], (0, 1))
     ones = lambda k: T.cc[0:1, 768:768 + k]
-    V(lambda v: v.tensor_scalar(T.idn[0:36, 0:36], T.i128[0:36, 0:36], T.cf[0:36, 6:7], None, A.is_equal), 36, ["i128", "cp"], ["idn0"])
-    lin(T.idn[0:32, 48:80], T.idn[0:32, 0:32], 0.375, 0.0, 32, ["idn0"], ["idn1"])
-    V(lambda v: v.tensor_scalar(T.selm[:], T.iom[:], cm, None, A.is_equal), 32, ["iom", "cf"], ["selm"])
-    col = lambda i: T.cs[:, i:i + 1]
-    lin(col(2), cm, 3.0, 0.5, 1, ["cf"], ["cs2"])
-    lin(T.cs[:, 4:7], T.i128[:, 0:3], 1.0, col(2), 3, ["cs2", "i128"], ["cs4"])
-    V(lambda v: v.tensor_scalar(col(8), cm, 6.0, None, A.not_equal), 1, ["cf"], ["csq"])
-    lin(col(9), col(8), -30.0, 31.0, 1, ["csq"], ["csb"])
-    V(lambda v: v.tensor_scalar(col(10), cm, 7.0, 2047.0, A.not_equal, A.add), 1, ["cf"], ["cs10"])
-    lin(col(11), col(8), -2048.0, col(10), 1, ["csq", "cs10"], ["cs11"])
-    V(lambda v: v.tensor_scalar(col(12), col(11), 0.0, None, A.not_equal), 1, ["cs11"], ["cs12"])
-    lin(col(14), col(11), 0.5, 0.0, 1, ["cs11"], ["csc0"])
-    lin(col(15), col(8), -2.0, 1.0, 1, ["csq"], ["csc1"])
-    V(lambda v: v.tensor_scalar(T.sel[:], T.i128[:, 0:32], c31, 16.0, A.is_equal, A.mult), 32, ["i128", "cf2"], ["sel"])
+    paint(T.idn[0:36, 0:36], T.zs[0:36, 0:36], [[-1, 36]], 1.0, 0, ["idn0"])
+    paint(T.idn[0:32, 48:80], T.zs[0:32, 0:32], [[-1, 32]], 0.375, 0, ["idn1"])
+    for q in range(4):
+        paint(T.sel[32 * q:32 * q + 32, :], T.zs[32 * q:32 * q + 32, 0:32], [[-1, 32]], 16.0, 0, ["sel%d" % q])
+    sk = ["sel%d" % q for q in range(4)]
     for u in range(NU):
-        V(lambda v, u=u: v.tensor_scalar(T.pair[:, RG * u:RG * u + RG], T.i128[:, 0:RG], crg, None, A.is_equal), RG, ["i128", "cf"], ["pair%d" % u])
-    V(lambda v: v.tensor_scalar(T.mg[:], T.i128[:, 0:8], cg, None, A.is_equal), 8, ["i128", "cf2"], ["mg"])
-    fill(T.ee[0:64, :], 0.0, 32, ["eez"])
-    V(lambda v: v.memset(T.ee[32:64, R3:R3 + NG], -0.375), NG, ["eez"], ["eez"])
-    V(lambda v: v.memset(T.wt[32:64, :], 1.0), 32, [], ["wtz"])
-    lin(T.ee[0:36, R3:R3 + NG], T.sel[0:36, 0:NG], -0.1875 / 16, 0.0, NG, ["sel", "eez"], ["ee"])
-    V(lambda v: v.memset(T.prm[0:R3, :], 0.0), 224, [], ["permz"])
-    V(lambda v: v.memset(T.one[0:R3, 0:32], 1.0), 16, [], ["one"])
-    V(lambda v: v.memset(T.one[0:R3, 17:32:2], -1.0), 8, ["one"], ["one"])
-    rows = [(1, 2, 0, 2, 0, 1), (2, 0, 1, 1, 2, 0), (0, 1, 2, 0, 1, 2)]
-    for k in range(2):
-        for r in range(6):
-            out = T.prm[0:R3, 256 * k + r:256 * k + 128:8]
-            G(lambda g, out=out, c=rows[k][r], k=k: g.affine_select(out, T.one[0:R3, 16 - 16 * k:32 - 16 * k], [[0, NU], [-3, NG], [0, 2]], A.is_equal, 0.0, -c, 1),
-              16, ["one", "permz"], ["perm%d%d" % (k, r)])
-    V(lambda v: v.tensor_scalar(T.prm[0:R3, 128:256], T.prm[0:R3, 0:128], -1.0, 0.0, A.mult, A.max), 128, ["perm0%d" % r for r in range(6)] + ["permz"], ["permlo"], half=True)
-    for r in range(6):
-        c = rows[2][r]
-        G(lambda g, r=r, c=c: g.affine_select(T.prm[0:R3, 384 + r:384 + RG:8], T.one[0:R3, 17:32:2] if r >= 3 else T.one[0:R3, 0:8], [[-3, NG], [0, 2]],
-                                              A.is_equal, 0.0, -c, 1), 8, ["one", "permz"], ["perm2%d" % r])
-    V(lambda v: v.tensor_copy(T.thf[:, 0:1], T.thl[:, 0:1]), 1, ["thl"], ["thf"])
-    lin(T.thm[:], T.mg[:], T.thf[:, 0:1], 0.0, 8, ["mg", "thf"], ["thm"])
-    lin(T.xy[:, 512::528], T.i128[:, 0:2 * NS], 0.0, col(12), 2 * NS, ["i128", "cs12"], ["xyz"])
-    V(lambda v: v.memset(T.tab[:, 4096::4112], -8388608.0), NS, [], ["tabz"])
-    fill(T.zer[0:32, :], -C0, 2 * XH, ["zer"])
+        paint(T.pair[RG * u:RG * u + RG, :], T.zs[RG * u:RG * u + RG, 0:128], [[0, NU], [-1, RG]], 1.0, 0, ["pair%d" % u])
+    fill(T.ee[0:64, :], 0.0, ["ee0", "ee1"])
+    for a in range(2):
+        paint(T.ee[32 * a:32 * a + 32, R3:R3 + NG], T.zs[32 * a:32 * a + 32, 0:NG], [[-1, NG]], -0.1875, 0, ["ee%d" % a])
+    select(T.ee[32:64, R3:R3 + NG], T.ee[32:64, R3:R3 + NG], [[0, NG]], A.not_equal, -0.375, -NG, 1, ["ee1"], ["ee1"])
+    fill(T.wt[32:64, :], 1.0, ["wtz"])
+    V(lambda v: v.memset(T.prm[0:2 * R3, 3:384:4], 0.0), 64, [], ["permz"])
+    iota(T.sgn[0:2 * R3, :], [[0, 8], [-2, 2], [0, 4]], 1, 0, ["sgn"])
+    for c in range(3):
+        a, b = (c + 1) % 3, (c + 2) % 3
+        select(T.prm[0:2 * R3, c:128:4], T.sgn[0:2 * R3, 0:64:2], [[-3, 8], [0, 2], [a - b, 2]], A.is_equal, 0.0, -a, 1, ["sgn"], ["perm0%d" % c])
+        paint(T.prm[0:2 * R3, 256 + c:384:4], T.zs[0:2 * R3, 0:32], [[-3, 8], [0, 2], [b - a, 2]], 1.0, -b, ["perm1%d" % c])
+    V(lambda v: v.tensor_scalar(T.prm[0:2 * R3, 128:256], T.prm[0:2 * R3, 0:128], -1.0, 0.0, A.mult, A.max), 128, ["perm0%d" % c for c in range(3)] + ["permz"], ["permlo"], half=True)
+    select(T.prm[0:R3, 384:448], T.sgn[0:R3, :], [[-3, NG], [0, 4], [-1, 4]], A.is_equal, 0.0, 0, 1, ["sgn"], ["perm2"])
+    for s in range(2):
+        V(lambda v, s=s: v.tensor_copy(T.thf[0:8, s:32:2], T.thl[0:8, :]), 16, ["thl"], ["thf%d" % s])
+    lin(T.xy[:, 512::528], T.i4[:, 0:2 * NS], 0.0, cn["one"], 2 * NS, ["i4", "cone"], ["xyz"])
+    fill(T.tab[:, 4096::4112], -8388608.0, ["tabz"])
+    fill(T.zer[0:32, :], -C0, ["zer"])
+    if RAMP:
+        iota(T.lt[32:33, :], [[0, 32], [6, 16]], 5, 0, ["ltz"])
+        fill(T.cum[32:33, :], UNITS[0] / 2, ["cumz"], (32, 33))
+        iota(T.ramp[:], [[2, W]], 2 - W, 0, ["ramp"])
 
     def setup(h):
-        B, K, (sc, _sm, pa, pb) = part(h)
-        fill(B("live", XH, p1=32), 0.0, 3 * XH, [K("livez")])
+        B, K, (sc, sm, pa, pb) = part(h)
+        if h:
+            pa, pb = sm, sc
+        fill(B("live", XH, 2 * XH, p1=32), 0.0, [K("livez")], (0, 32))
         V(lambda v: v.tensor_copy(B("live", 0, XH, p1=32), B("lvl", p1=32)), XH, [K("lvl")], [K("live0")])
-        fill(B("wq"), 0.0, 256, [K("wq")])
+        fill(B("wq"), 0.0, [K("wq")], (0, 128))
         for s in range(2):
-            if h + s:
-                fill(B("lh", 384 * s, 384 * s + 384), 0.0, 384, [K("lh%d" % s)])
-            else:
-                for j in range(3):
-                    fill(B("lh", 128 * j, 128 * j + 128), 0.0, 128, ["lhz%d" % j], 128)
-        pos, posh = B("posl", p1=R3), B("posh", p1=R3)
-        V(lambda v: v.tensor_scalar(posh, pos, 8 * C0, 8 * C0, A.add, A.subtract), 512, [K("posl")], [K("posh")], half=True)
-        P([(T[pa][:], T.prm[0:R3, 128:256], pos, True, False, 512), (T[pa][:], T.prm[0:R3, 0:128], posh, False, True, 512)],
-          [K("posl"), K("posh"), "permlo"], [pa], [pa])
-        P([(T[pb][:], T.prm[0:R3, 256:384], pos, True, True, 512)], [K("posl")] + ["perm1%d" % r for r in range(6)], [pb], [pb])
+            fill(B("lh", 384 * s, 384 * s + 384), 0.0, [K("lh%d" % s)], (0, 128))
+        pos = B("posl", p1=2 * R3)
+        pk = [K("posl%d_" % u) for u in range(NU)]
+        eight = lambda c, opens: [(T[pa][:, a:a + 128], T.cc[0:1, c:c + 128], ones(128), opens and a == 0, False, 128) for a in range(0, 512, 128)]
+        P(eight(0, True), ["cc0", "cc6"], [pa], [pa])
+        P([(T[pa][:], T.prm[0:2 * R3, 0:128], pos, False, False, 512)], pk + ["permz"] + ["perm0%d" % c for c in range(3)], [pa], [pa])
+        P(eight(896, False), ["cc7"], [pa], [pa])
+        P([(T[pa][:], T.prm[0:2 * R3, 128:256], pos, False, True, 512)], ["permlo"], [pa], [pa])
+        P([(T[pb][:], T.prm[0:2 * R3, 256:384], pos, True, True, 512)], pk + ["permz"] + ["perm1%d" % c for c in range(3)], [pb], [pb])
         for a, nm, bank in ((0, "xw", pa), (528, "yw", pb)):
-            lin(B("xy", a, a + 512), T[bank][:], 1.0, col(12), 512, [bank, "cs12"], [K(nm)], [bank])
-        P([(T[pb][0:32, 256 + XH:256 + 2 * XH], T.cc[0:1, 0:32], ones(XH), True, True, XH)], ["cc0", "cc6", K("yw")], [K("dz")], [pb])
+            lin(B("xy", a, a + 512), T[bank][:], 1.0, cn["one"], 512, [bank, "cone"], [K(nm)], [bank])
         P([(T[sc][RG * u:RG * u + RG, 0:W], T.prm[0:R3, 384:384 + RG], B("posl", W * u, W * u + W, p1=R3), True, True, W) for u in range(NU)],
-          [K("posl")] + ["perm2%d" % r for r in range(6)], [sc], [sc])
-        lin(B("py", 0, W), T[sc][:, 0:W], -1.0, col(14), W, [sc, "csc0"], [K("py0")], [sc])
-        for i, (f, kind) in enumerate(COPIES):
-            if kind == "b":
-                V(lambda v, i=i, f=f: v.tensor_scalar(B("py", W * i, W * i + W), B("py", 0, W), col(9), f, A.mult, A.mult), W,
-                  [K("py0"), "csb"], [K("py%d" % i)], half=True)
-            elif i:
-                lin(B("py", W * i, W * i + W), B("py", 0, W), f if kind == "n" else col(15), 0.0, W,
-                    [K("py0")] + ([] if kind == "n" else ["csc1"]), [K("py%d" % i)], half=True)
-        V(lambda v: v.tensor_scalar(B("pfl"), B("pfl"), 2.0 ** -10, None, A.max), W, [K("pfl%d_" % u) for u in range(NU)], [K("pfm")], half=True)
+          [pk[0], "perm2"], [sc], [sc])
+        lin(B("py", 0, W), T[sc][:, 0:W], cn["scl"], cn["n"], W, [sc, "cscl", "cn"], [K("py0")], [sc])
+        for i, (src, f, col) in list(enumerate(COPIES))[1:]:
+            lin(B("py", W * i, W * i + W), B("py", W * src, W * src + W), f, cn[col] if col else 0.0, W,
+                [K("py%d" % src)] + (["c" + col] if col else []), [K("py%d" % i)], half=True)
+        lin(B("pfl"), B("pfl"), 1.0, 2.0 ** -10, W, [K("pfl%d_" % u) for u in range(NU)], [K("pfm")], half=True)
+        for a in range(4):
+            if h:
+                D("Y", B("pfb", 2 * W * a, 2 * W * (a + 1)), T.zs[:], 128, ["zs", "prin00"], [K("pfz%d_" % a)])
+            else:
+                fill(B("pfb", 2 * W * a, 2 * W * (a + 1)), 0.0, [K("pfz%d_" % a)], (0, 128))
         for q in range(8):
-            G(lambda g, q=q: g.iota(B("pfb", W * q, W * q + W), [[0, W]], 0, 0, allow_small_or_imprecise_dtypes=True), W, [], [K("pfz%d_" % q)])
-        for q in range(8):
-            D("Y", B("pfb", W * q, W * q + W, 1, 16 * q, 16 * q + 16), B("pfl", p0=16 * q, p1=16 * q + 16), 2.0, [K("pfm"), K("pfz%d_" % q)], [K("pfb%d" % q)])
+            D("Y", B("pfb", W * q, W * q + W, 1, 16 * q, 16 * q + 16), B("pfl", p0=16 * q, p1=16 * q + 16), 8, [K("pfm"), K("pfz%d_" % (q // 2))], [K("pfb%d" % q)])
 
-    nrem = [0]
+    nrem, nblk = [0], [0]
 
-    def send(src, dsts, key, land):
+    def send(src, dsts, key, land, us):
         sem = T.sem["r%d" % nrem[0]]
         nrem[0] += 1
         mask = topo.mask(core, dsts[0][0])
@@ -245,90 +257,90 @@ def plan(T, rank, topo, cost=COST):
             g.remote_dma_fused([tr], local_sem=T.sem.sent)
             return ne
         op({"G": (fn, cost["send"])}, key, [land + "s"], kind="s")
-        op({"N": ((sem, ne * len(dsts)), 0.0)}, [land + "s"], [land], kind="a", lat=cost["net"] + (cost["first"] if nrem[0] == 1 else 0.0))
+        op({"N": ((sem, ne * len(dsts)), 0.0)}, [land + "s"], [land], kind="a", lat=cost["net"] + us + (cost["first"] if nrem[0] == 1 else 0.0))
 
     def front(h, t):
-        B, K, (_sc, smn, pa, pb) = part(h)
-        sm = T[smn]
+        B, K, (scn, smn, pa, pb) = part(h)
+        sc, sm = T[scn], T[smn]
         if t == 0:
             live = B("live", 0, 2 * XH, p1=32)
             V(lambda v: v.tensor_tensor_scan(B("cum", p1=32), live, live, 0.0, A.add, A.max), 2 * XH, [K("live0"), K("livez")], [K("cum")], half=True)
-        mm = []
-        for q in range(4):
-            o = sm[:, 256 + XH * q:256 + XH * q + XH]
-            mm.append((o, T.lc[0:32, 128 * q:128 * q + 128], B("cum", 0, XH, p1=32), True, False, 64))
-            mm.append((o, T.lt[0:32, 128 * q:128 * q + 128], B("cum", XH, p1=32), False, True, 64))
-        P(mm, [K("cum")] + ["lc%d" % q for q in range(4)] + ["lt%d" % q for q in range(4)], [K("cn")], [smn])
-        for i, k in enumerate((1, 2, 0)):
-            S(lambda a, i=i, k=k: a.activation(B("junk", W * i, W * i + W), sm[:, 256:256 + W], F.Sign, bias=col(4 + k), scale=1.0 / UNITS[0],
-                                               accum_out=B("ac3", i, i + 1)),
-              W + 20, [K("cn"), "cs4"], [K("ac3%d" % i)], [smn])
+        both = RAMP and t + h > 0
+        tag[:] = "front" if t + h else "first", 0, NS * t + h
+
+        def spread(bank, a, rows):
+            return [(bank[:, a + XH * q:a + XH * q + XH], w[0:k, 128 * q:128 * q + 128], B("cum", XH * i, XH * i + XH, p1=k), i == 0, i == 1, 64)
+                    for q in range(4) for i, (w, k) in enumerate(((T.lc, 32), (T.lt, rows)))]
+        lk = [K("cum")] + ["lc%d" % q for q in range(4)] + ["lt%d" % q for q in range(4)]
+        P(spread(sm, 256, 32), lk, [K("cn")], [smn])
+        if both:
+            P(spread(sc, 128, 33), lk + ["ltz", "cumz"], [K("cv")], [scn])
+            V(lambda v: v.tensor_tensor_scan(B("ac3", 0, W), sc[:, 128:128 + W], T.ramp[:], -float(W), A.max, A.min), W, [K("cv"), "ramp"], [K("ac30")], [scn])
+        for i, k in list(enumerate((2, 0, 1)))[both:]:
+            S(lambda a, i=i, k=k: a.activation(B("junk", W * i, W * i + W), sm[:, 256:256 + W], F.Sign, bias=T.cs[:, 8 + k:9 + k], scale=1.0 / UNITS[0],
+                                               accum_out=B("ac3", W - 1 + i, W + i)),
+              W + 24, [K("cn"), "cs4"], [K("ac3%d" % i)], [smn])
         pk = ["pair%d" % u for u in range(NU)]
-        P([(T[pa][:, 323:324], T.pair[:], B("ac3", 0, 1), True, True, 256)], [K("ac30")] + pk, [K("pr")], [pa])
-        P([(T[pa][:, 320:323], T.pair[:], B("ac3", 0, 3), True, True, 256)], [K("ac3%d" % i) for i in range(3)] + pk, [K("pr")], [pa])
-        sl = B("sl", 0, 4)
-        V(lambda v: v.tensor_scalar(sl, T[pa][:, 320:324], 0.5, 256.0, A.mult, A.add), 4, [K("pr")], [K("sl")], [pa])
-        for a, w0, nm in ((0, 528, "yw"), (64, 0, "xw")):
-            o, w = B("prod", 128 * t + a, 128 * t + a + 64), B("xy", w0, w0 + 513).indirect(sl)
-            us = 0.06 + 64 * cost["gath"] * CY
-            op({"V": (lambda g, o=o, w=w: g.vector.tensor_copy(o, w), us), "S": (lambda g, o=o, w=w: g.scalar.activation(o, w, F.Copy), us)},
+        P([(sc[:, 403:405], T.pair[:], B("ac3", W - 1, W + 1), True, True, 256)], [K("ac30"), K("ac31")] + pk, [K("pr")], [scn])
+        P([(sc[:, 400:403], T.pair[:], B("ac3", W - 1, W + 2), True, True, 256)], [K("ac3%d" % i) for i in range(3)] + pk, [K("pr")], [scn])
+        V(lambda v: v.tensor_scalar(B("sl", 0, 5), sc[:, 400:405], 0.5, 256.0, A.mult, A.add), 5, [K("pr")], [K("sl")], [scn])
+        for a, w0, nm in ((0, 528, "yw"), (1, 0, "xw")):
+            o, w = B("prod", 96 * t + 48 * a, 96 * t + 48 * a + 48), B("xy", w0, w0 + 513).indirect(B("sl", 2 * a, 2 * a + 3))
+            us = 48 * cost["gath"]
+            op({"V": (lambda g, o=o, w=w: g.vector.tensor_copy(o, w), 0.05 + us), "S": (lambda g, o=o, w=w: g.scalar.activation(o, w, F.Copy), 0.065 + us)},
                [K("sl"), K(nm), "xyz"], [K("prod%d" % t) + nm])
         pk = [K("prod%d" % t) + nm for nm in ("xw", "yw")]
-        send(B("prod", 128 * t + 16, 128 * t + 112), [(T.cores[(rank + t + 1) % n], B("prin", 96 * t, 96 * t + 96))], pk, K("prin%d" % t))
+        send(B("prod", 96 * t, 96 * t + 96), [(T.cores[(rank + t + 1) % n], B("prin", 96 * t, 96 * t + 96))], pk, K("prin%d" % t), 0.4)
         for s in range(2):
             lh = K("lh%d" % s)
-            nm, a = ("prin", 96 * t) if s else ("prod", 128 * t + 16)
-            V(lambda v, s=s, nm=nm, a=a: v.tensor_tensor(B("lh", 384 * s, 384 * s + 384).indirect(T.el[:, 0:3]), B(nm, a + 48, a + 96), B(nm, a, a + 48), A.mult),
-              48 * cost["scat"], ([K("prin%d" % t)] if s else pk) + ["el", "lhz0", "lhz1", "lhz2"], [lh])
-            for c, nq in enumerate(BLOCKS[s]):
-                bank = (pa, pb)[(c + s * len(BLOCKS[0])) % 2]
-                q0, wd = sum(BLOCKS[s][:c]), XH * nq
+            nm, a = ("prod", "prin")[s], 96 * t
+            op({"V": (lambda g, s=s, nm=nm, a=a: g.vector.tensor_tensor(B("lh", 384 * s, 384 * s + 384).indirect(T.el[:, 0:3]), B(nm, a + 48, a + 96), B(nm, a, a + 48), A.mult),
+                      0.05 + 48 * cost["scat"])}, ([K("prin%d" % t)] if s else pk) + ["el"], [lh])
+            for c, wd in enumerate(BLOCKS[s]):
+                bank = PLACES[nblk[0] % len(PLACES)]
+                nblk[0] += 1
+                x0, cyc = sum(BLOCKS[s][:c]), max(64, wd)
                 o = T[bank][:, 0:wd]
-                pen = [((T[bank][:, XH * q:XH * q + XH], T.lc[0:33, 128 * (q0 + q):128 * (q0 + q + 1)], B("live", XH * t, XH * t + XH, p1=33), nq == 1, False, 64),
-                        [K("live%d" % t), "lc%d" % (q0 + q), "lcz%d" % (q0 + q), "livey%d" % (2 * h + t // 2)]) for q in range(nq)]
-                if nq == 1:
-                    P([pen[0][0]], pen[0][1], ["pl" + bank], [bank])
+                cut = [(q, max(x0, XH * q), min(x0 + wd, XH * q + XH)) for q in range(x0 // XH, (x0 + wd - 1) // XH + 1)]
+                P([(T[bank][:, a - x0:b - x0], T.lc[0:33, 128 * q:128 * q + 128], B("live", XH * (t - q) + a, XH * (t - q) + b, p1=33), a == x0, False, 64)
+                   for q, a, b in cut], [K("live%d" % t), "lcz", "livey"] + ["lc%d" % q for q, _a, _b in cut], ["pl" + bank], [bank])
                 mm = []
                 for i, level in enumerate(LEVELS):
-                    if i:
-                        mm.append(((o, T.cc[0:1, 128 * i:128 * i + 128], ones(wd), False, False, wd), ["cc%d" % i, "cc6"]))
                     for j, k in level:
-                        mm.append(((o, B("lh", 384 * s + 128 * j, 384 * s + 128 * j + 128), B("py", W * k + XH * q0, W * k + XH * q0 + wd), not mm and nq > 1, i == 3, wd),
+                        mm.append(((o, B("lh", 384 * s + 128 * j, 384 * s + 128 * j + 128), B("py", W * k + x0, W * k + x0 + wd), False, i == 3, cyc),
                                    [lh, K("py%d" % k)]))
-                        if len(mm) == 1 and nq > 1:
-                            mm += pen
-                parts = NPART * nq // 2 + 1
+                parts = max(1, round(len(mm) * wd / PASS))
                 for i in range(parts):
                     mp = mm[len(mm) * i // parts:len(mm) * (i + 1) // parts]
                     P([m[0] for m in mp], [k for m in mp for k in m[1]], ["pl" + bank], [bank])
-                V(lambda v, a=W * s + XH * q0, wd=wd, o=o: v.tensor_scalar(B("off", a, a + wd), o, UNITS[0] - C0, 4096.0, A.add, A.min), wd,
-                  ["pl" + bank], [K("off%d%d" % (s, q0 + q)) for q in range(nq)], [bank])
+                V(lambda v, a=W * s + x0, wd=wd, o=o: v.tensor_scalar(B("off", a, a + wd), o, UNITS[0] - C0, 4096.0, A.add, A.min), wd,
+                  ["pl" + bank], [K("off%d%d" % (s, c))], [bank])
 
     def back(h, t):
         B, K, (scn, smn, pa, pb) = part(h)
         sc, sm = T[scn], T[smn]
+        tag[:] = "back", 0, NS * t + h
 
         def gather(s, c0, c1):
             o = B("gat", 32 * KCH * c0 + s, 32 * KCH * c1, 2)
             w = B("tab", 0, 4097).indirect(B("off", W * s + KCH * c0, W * s + KCH * c1))
-            us = 0.06 + 16 * KCH * (c1 - c0) * cost["gath"] * CY
-            return {"V": (lambda g: g.vector.tensor_copy(o, w), us), "S": (lambda g: g.scalar.activation(o, w, F.Copy), us)}
+            us = 16 * KCH * (c1 - c0) * cost["gath"]
+            return {"V": (lambda g: g.vector.tensor_copy(o, w), 0.05 + us), "S": (lambda g: g.scalar.activation(o, w, F.Copy), 0.065 + us)}
         for s in range(2):
             for c in range(NCH):
-                op(gather(s, c, c + 1), [K("off%d%d" % (s, KCH * c // XH)), "tabz"] + [K("tab%d_" % u) for u in range(NU)], [K("gat%d%d_" % (s, c))])
-                ops[-1]["fill"] = (2 * (NCH - 1 - c) + 1 - s) * ops[-1]["alts"]["V"][1] / 2
+                op(gather(s, c, c + 1), [K("off%d%d" % (s, block(s, c))), "tabz"] + [K("tab%d_" % u) for u in range(NU)], [K("gat%d%d_" % (s, c))])
                 ops[-1]["gat"] = (gather, s, c)
         for c, k1 in enumerate(SCS):
-            mm, k0 = [], sum(SCS[:c])
-            for x in range(k0 * KCH, (k0 + k1) * KCH):
-                q, xh = x // XH, x % XH
-                mm.append((sc[32 * q:32 * q + 32, 8 * xh:8 * xh + 8], B("gat", 32 * x, 32 * x + 32), B("pfb", x, 8 * W, W), True, True, cost["score"]))
-            P(mm, [K("gat%d%d_" % (s, k)) for s in range(2) for k in range(k0, k0 + k1)] + [K("pfb%d" % q) for q in range(8)], [K("s%d_" % c)], [scn])
+            k0 = sum(SCS[:c])
+            P([(sc[32 * (x // XH):32 * (x // XH) + 32, 8 * (x % XH):8 * (x % XH) + 8], B("gat", 32 * x, 32 * x + 32), B("pfb", x, 8 * W, W), True, True, 32)
+               for x in range(k0 * KCH, (k0 + k1) * KCH)],
+              [K("gat%d%d_" % (s, k)) for s in range(2) for k in range(k0, k0 + k1)] + [K("pfb%d" % q) for q in range(8)], [K("s%d_" % c)], [scn])
+            ops[-1]["free"] = True
         acc = B("acc", 4 * t, 4 * t + NG)
         for k in range(NG):
             S(lambda a, k=k: a.activation(B("hit", 128 * k, 128 * k + 128), sc[:, k:8 * XH:NG], F.Sign, bias=T.thb[:, NG * h + k:NG * h + k + 1],
                                           accum_out=B("acc", 4 * t + k, 4 * t + k + 1)),
-              148, [K("s%d_" % c) for c in range(len(SCS))] + ["thb"], [K("hit%d" % k), K("acc%d%d" % (t, k))], [scn])
+              152, [K("s%d_" % c) for c in range(len(SCS))] + ["thb"], [K("hit%d" % k), K("acc%d%d" % (t, k))], [scn])
         ca, cc = T.cores[(rank - t - 1) % n], T.cores[(rank + t + 1) % n]
         ina, inc = B("ina", 4 * t, 4 * t + NG), B("inc", 4 * t, 4 * t + NG)
         if ca == cc:
@@ -337,11 +349,21 @@ def plan(T, rank, topo, cost=COST):
         else:
             dsts = [(cc, ina), (ca, inc)]
         ak = [K("acc%d%d" % (t, k)) for k in range(NG)]
-        send(acc, dsts, ak, K("in%d" % t))
+        send(acc, dsts, ak, K("in%d" % t), 0.1 * len(dsts))
+        last = t == RO - 1
+        dd = sc[0:32, 0:XH]
+        lv = lambda i: B("live", XH * i, XH * i + XH, p1=32)
+        hk = [K("hit%d" % k) for k in range(NG)]
+        mm = [(dd, T.idn[0:32, 48:80], lv(t), True, False, XH)]
+        if last:
+            mm += [(dd, T.idn[0:32, 0:32], lv(i), False, False, XH) for i in range(RO)]
+        else:
+            mm.insert(0, (sc[0:32, XH:2 * XH], T.cc[0:1, 512:544], ones(XH), True, True, XH))
+        P(mm, ["idn0", "idn1", "cc4", "cc6"] + [K("live%d" % i) for i in range(t + 1)] + hk, [K("dd")], [scn])
         s0, s1 = T.sel[:, 0:32:2], T.sel[:, 1:32:2]
         key, k0, k1 = sm[0:36, 0:32], sm[0:NG, 0:32:2], sm[32:32 + NG, 1:32:2]
         P([(key, T.idn[0:36, 0:36], T.kc[0:36, :], True, False, 36), (k0, acc, s0, False, False, 64), (k1, acc, s1, False, False, 64)],
-          ak + ["kc", "kc32", "idn0", "sel"], [K("key")], [smn])
+          ak + ["kc", "kc32", "idn0"] + sk, [K("key")], [smn])
         P([(k0, inc, s1, False, False, 64), (k1, ina, s0, False, False, 64), (key, T.idn[0:36, 0:36], T.kc[0:36, :], False, True, 36)],
           [K("in%d" % t)], [K("key")], [smn])
         mx = B("mx", 0, 1, p1=36)
@@ -349,45 +371,41 @@ def plan(T, rank, topo, cost=COST):
         op({"V": (lambda g: g.vector.tensor_scalar(B("wt", p1=36), key, mx, -1.0, A.add, A.max), vc(32)),
             "S": (lambda g: g.scalar.activation(B("wt", p1=36), key, F.Sign, bias=mx), ac(32))}, [K("key"), K("mx"), "wtz"], [K("wt")], [smn])
         P([(sm[32 * q:32 * q + 32, 32:32 + 4 * NG], B("wt", p1=37), T.ee[0:37, R3 - NG * q:R3 - NG * q + 4 * NG], True, True, 32) for q in range(4)],
-          [K("wt"), "ee"], [K("w")], [smn])
-        yc = T[pa][0:NG, 256 + t:304:3]
-        last = t == RO - 1
-        P([(yc, acc, s0, True, False, 64), (yc, inc, s1, False, True, 64)], [K("in%d" % t), K("w")], [K("yc%d" % t)], [pa])
+          [K("wt"), "ee0", "ee1"], [K("w")], [smn])
         lin(B("wq", 112, 112 + 4 * NG), sm[:, 32:32 + 4 * NG], 1.0, 0.0, 16, [K("w")], [K("wq")], [smn])
-        if last:
-            V(lambda v: v.tensor_scalar(B("yco", p1=NG), T[pa][0:NG, 256:304], 1.0 / 32, 512.0, A.mult, A.add), 48,
-              [K("yc%d" % i) for i in range(RO)], [K("yco")], [pa])
-            D("Y", T.yc[RG * h:RG * h + RG, :], B("yco", p1=NG), 2.0, [K("yco")], [K("oc")])
-        dd = T[pb][0:32, 256:256 + XH]
-        lv = lambda i: B("live", XH * i, XH * i + XH, p1=32)
-        P([(dd, T.idn[0:32, 48:80], lv(t), True, False, XH)], ["idn1", K("live%d" % t), K("key")], [K("dd")], [pb])
+        yc = sm[0:NG, 48 + t:96:3]
+        P([(yc, acc, s0, True, False, 64), (yc, inc, s1, False, True, 64)], [K("in%d" % t), K("w")], [K("yc%d" % t)], [smn])
         mm = []
         for k in range(NG):
             for u in range(NU):
                 a0 = 112 - 31 * k - 4 * NG * u
                 mm.append((dd, B("wq", a0, a0 + 32 * NG, NG), B("hit", 128 * k + u, 128 * k + 128, NU), False, False, XH))
-        mm.append((dd, T.cc[0:1, 0:32], ones(XH), False, not last, XH))
+        mm.append((dd, T.cc[0:1, 512:544], ones(XH), False, True, XH))
+        P(mm, [K("wq"), "cc4", "cc6"] + hk, [K("dd")], [scn])
         if last:
-            mm += [(dd, T.idn[0:32, 0:32], lv(i), False, i == t, XH) for i in range(RO)]
-        P(mm, [K("wq"), "idn0", "idn1", "cc0", "cc6", K("livez")] + [K("live%d" % i) for i in range(t + 1)] + [K("hit%d" % k) for k in range(NG)],
-          [K("dd")], [pb])
-        if last:
-            V(lambda v: v.tensor_scalar(B("age", p1=32), dd, -C0, None, A.add), XH, [K("dd")], [K("age")], [pb])
-            D("S" if h else "Y", T.ya[NG * h:NG * h + NG, :], B("age", p1=32), 2.0, [K("age")], [K("oa")])
+            tag[0] = "end"
+            lin(B("yco", p1=NG), sm[0:NG, 48:96], 1.0 / 32, 512.0, 48, [K("yc%d" % i) for i in range(RO)], [K("yco")], [smn])
+            D("YS", T.yc[RG * h:RG * h + RG, :], B("yco", p1=NG), 1, [K("yco")], [K("oc")])
+            lin(B("age", p1=32), dd, 1.0, -C0, XH, [K("dd")], [K("age")], [scn])
+            D("YS", T.ya[NG * h:NG * h + NG, :], B("age", p1=32), 8, [K("age")], [K("oa")])
         else:
-            V(lambda v: v.tensor_tensor_scan(B("cum", p1=32), T[pb][0:32, 256:256 + 2 * XH], T.zer[0:32, :], 0.0, A.add, A.add), 2 * XH,
-              [K("dd"), K("dz"), "zer"], [K("cum")], [pb])
-            lin(lv(t + 1), dd, 1.0, -C0, XH, [K("dd"), K("livez")], [K("live%d" % (t + 1))], [pb])
+            V(lambda v: v.tensor_tensor_scan(B("cum", p1=32), sc[0:32, 0:2 * XH], T.zer[0:32, :], 0.0, A.add, A.add), 2 * XH,
+              [K("dd"), "zer"], [K("cum")], [scn])
+            lin(lv(t + 1), dd, 1.0, -C0, XH, [K("dd")], [K("live%d" % (t + 1))] + ([K("livez")] if t == 0 else []), [scn])
 
     for h in range(NS):
         half[0] = h
+        tag[:] = "load", 0, h
         if h:
             loads(h)
         setup(h)
         front(h, 0)
+    tag[:] = "load", 0, NS
+    table(1, 1, ["prin00"])
     half[0] = 0
-    P([(T.ps1[32 * q:32 * q + 32, 112:120], T.selm[:], T.thm[:], True, True, 128) for q in range(4)], ["selm", "thm"], ["thp"], ["ps1"])
-    lin(T.thb[:], T.ps1[:, 112:120], -1.0, 0.5, 8, ["thp"], ["thb"], ["ps1"])
+    tag[:] = "limits", 0, 0
+    P([(T.ps1[32 * q:32 * q + 32, 112:120], T.thf[0:8, :], T.sel[0:8, 0:8], True, True, 128) for q in range(4)], ["thf0", "thf1", "sel0"], ["thp"], ["ps1"])
+    lin(T.thb[:], T.ps1[:, 112:120], -1.0 / 16, 0.5, 8, ["thp"], ["thb"], ["ps1"])
     for t in range(RO):
         for h in range(NS):
             half[0] = h
@@ -404,7 +422,7 @@ def depend(ops):
         d = {}
         for k in o["r"]:
             if k in lastw:
-                d[lastw[k]] = True
+                d[lastw[k]] = "S" if "blank" in o else True
         for k in o["w"]:
             if k in lastw:
                 d.setdefault(lastw[k], False)
@@ -415,7 +433,7 @@ def depend(ops):
             e, cur, prev = epoch.get(b, (None, [], []))
             if eng is not None and e == eng:
                 cur.append(i)
-                if e == "P":
+                if e == "P" and not o.get("free"):
                     d.setdefault(cur[-2], False)
             else:
                 prev, cur = cur, [i]
@@ -432,14 +450,14 @@ def depend(ops):
     return deps
 
 
-def joins(ops, i, j, fwd=True):
+def joins(ops, i, j):
     if i is None or "gat" not in ops[i] or "gat" not in ops[j]:
         return False
     (f, s, c), (f2, s2, c2) = ops[i]["gat"], ops[j]["gat"]
-    return f is f2 and s == s2 and c2 - c == (1 if fwd else -1) and c // JOIN[s] == c2 // JOIN[s]
+    return f is f2 and s == s2 and c2 - c == 1 and block(s, c) == block(s, c2) and c // JOIN == c2 // JOIN
 
 
-def join(ops, deps, seq, eng, end):
+def join(ops, deps, seq, eng):
     head, last = {}, {}
     for i in seq:
         j = last.get(eng[i])
@@ -452,29 +470,40 @@ def join(ops, deps, seq, eng, end):
         if head[i] != i:
             f, s, c = ops[head[i]]["gat"]
             ops[head[i]] = dict(ops[head[i]], alts=f(s, c, ops[i]["gat"][2] + 1))
-    return ops, new, [i for i in seq if head[i] == i], eng, end
+    return ops, new, [i for i in seq if head[i] == i]
 
 
-def order(ops, deps, look=LOOK, back=BACK, stag=STAG, hop=COST["hop"], passes=PASSES, prio=None):
+LOOKS, BACKS, TURNS, GLUE = (0.2,), (0.0,), ((9.0, 3.0), (8.0, 3.5)), 0.5
+
+
+def order(ops, deps, hop, look, back, stag, passes):
     n = len(ops)
     succ = [[] for _ in range(n)]
     for i in range(n):
         for j in deps[i]:
             succ[j].append(i)
-    if prio is None:
-        prio = [0.0] * n
-        for i in range(n - 1, -1, -1):
-            c = min(a[1] for a in ops[i]["alts"].values()) + ops[i]["lat"] + hop + ops[i].get("fill", 0.0)
-            prio[i] = c + max([prio[k] for k in succ[i]] + [0.0])
-        for i in range(n):
-            prio[i] -= (back if "fill" in ops[i] else 0.0) + stag * ops[i]["h"]
+    lat = [o["lat"] + o.get("move", 0.0) for o in ops]
+    t0, tl, td = stag
+    late, turn = [t0 + (5 + o["h"]) * tl + 7.0 for o in ops], {}
+    for o in ops:
+        if "gat" in o:
+            turn.setdefault(o["gat"][0], len(turn))
+    for i in range(n - 1, -1, -1):
+        c = min(a[1] for a in ops[i]["alts"].values()) + lat[i] + hop[0]
+        late[i] = min([late[k] for k in succ[i]] + [late[i]]) - c - back
+        if "gat" in ops[i]:
+            f, s, k = ops[i]["gat"]
+            u = k / NCH
+            late[i] = t0 + turn[f] * tl + (td + u * (tl - 0.5 - td) if s else u * td)
+    prio = [1000.0 - i if not deps[i] and "move" in ops[i] else -x for i, x in enumerate(late)]
+    fixed = [1000.0 - i if fwd_only else 0.0 for i, fwd_only in enumerate(not deps[i] and "move" in ops[i] for i in range(n))]
     cheap = [min(a[1] for a in o["alts"].values()) for o in ops]
 
     def sweep(prio, fwd):
         pre, post = (deps, succ) if fwd else (succ, deps)
         left = [len(pre[i]) for i in range(n)]
-        free = {e: 0.0 for e in "VSPGYN"}
-        end, eng, seq, ready, last, more = [0.0] * n, [None] * n, [], {}, {}, []
+        free = {e: 0.0 for e in "VSPGYND"}
+        end, eng, seq, ready, last = [0.0] * n, [None] * n, [], {}, {}
 
         def arrive(i):
             ready[i] = []
@@ -482,9 +511,9 @@ def order(ops, deps, look=LOOK, back=BACK, stag=STAG, hop=COST["hop"], passes=PA
                 t = 0.0
                 for j in pre[i]:
                     same = eng[j] == e and ops[j if fwd else i]["kind"] == "c"
-                    nowait = e == "P" or (deps[i][j] if fwd else deps[j][i]) is None
-                    t = max(t, end[j] + ((0.0 if nowait else SAME) if same else hop))
-                ready[i].append((e, a[1], t + (0.0 if fwd else ops[i]["lat"])))
+                    nowait = same and (e == "P" or (deps[i][j] if fwd else deps[j][i]) is None)
+                    t = max(t, end[j] + (0.0 if nowait else hop[same]))
+                ready[i].append((e, a[1], t + (0.0 if fwd else lat[i])))
         for i in range(n):
             if left[i] == 0:
                 arrive(i)
@@ -494,22 +523,20 @@ def order(ops, deps, look=LOOK, back=BACK, stag=STAG, hop=COST["hop"], passes=PA
             cand = [x for x in cand if x[3] <= 1.2 * cheap[x[1]] or x[0] + look < busy.get(x[2], 1e9)]
             first = min(c[0] for c in cand)
             near = [x for x in cand if x[0] <= first + look]
-            pick = max(near, key=lambda x: (ops[x[1]]["w"][0] in RUSH, prio[x[1]], -x[0] - x[3]))
+            pick = max(near, key=lambda x: (fixed[x[1]], prio[x[1]], -x[0] - x[3]))
             if "gat" in ops[pick[1]]:
-                pick = max((x for x in near if "gat" in ops[x[1]]),
-                           key=lambda x: (prio[x[1]] + (GLUE if joins(ops, last.get(x[2]), x[1], fwd) else 0.0), -x[0] - x[3]))
-            t0, i, e, c = more.pop() if more else pick
-            j = i + (1 if fwd else -1)
-            if joins(ops, last.get(e), i, fwd) and t0 == free[e]:
-                c -= 0.06
-            elif j in ready and joins(ops, i, j, fwd) and ops[i]["gat"][1:] < (1, NCH - 2):
-                due = min([x[0] for x in cand if x[2] == e and "gat" not in ops[x[1]] and prio[x[1]] > prio[j]] + [1e9])
-                if due > t0 + c + WAIT:
-                    more.append((t0 + c, j, e, ops[j]["alts"][e][1]))
+                glue = (lambda x: joins(ops, last.get(x[2]), x[1])) if fwd else (lambda x: x[2] in last and joins(ops, x[1], last[x[2]]))
+                pick = max((x for x in near if "gat" in ops[x[1]]), key=lambda x: (prio[x[1]] + (GLUE if glue(x) else 0.0), -x[0] - x[3]))
+            t0, i, e, c = pick
+            if fwd and joins(ops, last.get(e), i) and t0 == free[e]:
+                c -= 0.055
             last[e] = i
             if e != "N":
                 free[e] = t0 + c
             end[i] = t0 + c + (ops[i]["lat"] if fwd else 0.0)
+            if fwd and "move" in ops[i]:
+                free["D"] = max(free["D"], t0 + c + 0.6 * ops[i]["lat"]) + ops[i]["move"]
+                end[i] = free["D"] + 0.4 * ops[i]["lat"]
             eng[i] = e
             seq.append(i)
             del ready[i]
@@ -526,13 +553,322 @@ def order(ops, deps, look=LOOK, back=BACK, stag=STAG, hop=COST["hop"], passes=PA
     return best
 
 
+def timer(plans, deps, hops):
+    ops, n = plans[0], len(deps)
+    reach, pre = [0] * n, []
+    for i in range(n):
+        r, keep = 0, []
+        for j in sorted(deps[i], reverse=True):
+            if not (r >> j) & 1:
+                keep.append(j)
+            r |= reach[j] | (1 << j)
+        reach[i] = r
+        pre.append(keep)
+    soft = [[j for j in pre[i] if ops[j]["kind"] == "c" and (deps[i][j] is None or "P" in ops[i]["alts"])] for i in range(n)]
+    hard = [[j for j in pre[i] if j not in soft[i] and deps[i][j] != "S"] for i in range(n)]
+    zero = [[j for j in pre[i] if deps[i][j] == "S"] for i in range(n)]
+    near = [[j for j in hard[i] if ops[j]["kind"] == "c" and set(ops[j]["alts"]) & set(ops[i]["alts"])] for i in range(n)]
+    nxt = [i + 1 if i + 1 < n and joins(ops, i, i + 1) else -1 for i in range(n)]
+    odd = [o["w"][0] in SHIFTED for o in ops]
+    kind = [2 if "N" in o["alts"] else 3 if "move" in o else 0 for o in ops]
+    cost = [[{e: a[1] for e, a in o["alts"].items()} for o in p] for p in plans]
+    lat = [[o["lat"] for o in p] for p in plans]
+    move = [[o.get("move") for o in p] for p in plans]
+
+    def steps(seq, eng, old=None, pos=None, p0=0):
+        out, last = [], {}
+        if p0:
+            a, b = 0, len(old)
+            while a < b:
+                c = (a + b) // 2
+                a, b = (c + 1, b) if pos[old[c][0]] < p0 else (a, c)
+            out = old[:a]
+            for c in range(a - 1, -1, -1):
+                s = out[c]
+                if s[1] in "VSG" and s[1] not in last:
+                    mem = [k for k in s[4] if pos[k] < p0]
+                    last[s[1]] = out[c] = [s[0], s[1], s[2] if mem[1:] else kind[s[0]], s[3], mem, s[5]]
+                    if len(last) == 3:
+                        break
+        for i in seq[p0:]:
+            e = eng[i]
+            pw = hard[i] + [j for j in soft[i] if eng[j] != e] if soft[i] else hard[i]
+            s = last.get(e)
+            if s is not None and nxt[s[4][-1]] == i:
+                s[2] = 1
+                s[4].append(i)
+            else:
+                own = [j for j in near[i] if eng[j] == e] if near[i] else near[i]
+                if zero[i] and e == "S":
+                    pw = pw + zero[i]
+                if e == "G" and s is not None and (odd[i] or odd[s[0]]):
+                    own = own + [s[0]]
+                last[e] = s = [i, e, kind[i], pw, [i], own]
+                out.append(s)
+        return out
+
+    def run(st, m, old=None, at=0):
+        co, la, mo, hop = cost[m], lat[m], move[m], hops[m]
+        if at:
+            end, start, why, marks = old[0][:], old[1][:], old[2][:], old[3][:at + 1]
+            free, last, dma = dict(marks[at][0]), dict(marks[at][1]), marks[at][2]
+            marks.pop()
+        else:
+            free = {e: 0.0 for e in "VSPGYN"}
+            end, start, why, marks, last, dma = [0.0] * n, [0.0] * n, [-1] * n, [], {}, 0.0
+        for a in range(32 * at, len(st), 32):
+            marks.append((dict(free), dict(last), dma))
+            dma = part(st[a:a + 32], co, la, mo, hop, free, last, dma, end, start, why)
+        return end, start, why, marks
+
+    def part(st, co, la, mo, hop, free, last, dma, end, start, why):
+        hop, same = hop
+        for i, e, k, pw, mem, own in st:
+            t = free[e] - hop
+            w = -1
+            for j in pw:
+                if end[j] > t:
+                    t, w = end[j], j
+            t += hop
+            for j in own:
+                if end[j] + same > t:
+                    t, w = end[j] + same, j
+            if w < 0:
+                w = last.get(e, -1)
+            last[e] = i
+            if k == 0:
+                free[e] = end[i] = t + co[i][e]
+            elif k == 1:
+                free[e] = x = t + co[i][e] * len(mem) - 0.055 * (len(mem) - 1)
+                for j in mem:
+                    end[j], start[j], why[j] = x, t, w
+            elif k == 2:
+                end[i] = t + la[i] + min(SHARE, max(0.0, dma - t - la[i] + 1.0))
+            else:
+                free[e] = x = t + co[i][e]
+                dma = max(dma, x + 0.6 * la[i]) + mo[i]
+                end[i] = dma + 0.4 * la[i]
+            start[i], why[i] = t, w
+        return dma
+    return steps, run, pre
+
+
+def refine(plans, deps, hops, seq, eng, iters, temp, early, seed=1):
+    steps, run, pre = timer(plans, deps, hops)
+    ops, n, ms = plans[0], len(deps), range(len(plans))
+    succ = [[] for _ in ops]
+    for i in range(n):
+        for j in pre[i]:
+            succ[j].append(i)
+    state = [seed]
+
+    def rnd():
+        state[0] = (state[0] * 6364136223846793005 + 1442695040888963407) % 2 ** 64
+        return ((state[0] >> 11) + 1) / (2 ** 53 + 1)
+    pick = lambda a: a[int(rnd() * len(a))]
+    load = [not deps[i] and "move" in ops[i] for i in range(n)]
+    tags = {o["tag"]: i for i, o in enumerate(ops) if o["tag"][0] in ("front", "back")}
+    like = lambda i, d: tags.get(ops[i]["tag"][:2] + (ops[i]["tag"][2] + d,)) if d else i
+    base = [c["aim"] for c in SETS]
+
+    def survey(seq, eng, st=None, res=None):
+        if res is None:
+            start = run(steps(seq, eng), 0)[1]
+            pos = {k: p for p, k in enumerate(seq)}
+            seq = sorted(seq, key=lambda k: (start[k], pos[k]))
+            st = steps(seq, eng)
+            res = [run(st, m) for m in ms]
+        val, span, arcs = [], 0.0, []
+        for m in ms:
+            end, _s, why, _m = res[m]
+            top = max(end)
+            val.append((top / base[m]) ** POWER / POWER + early * sum(end) / n / base[m])
+            span += (top / base[m]) ** POWER
+            i = end.index(top)
+            while why[i] >= 0:
+                if eng[why[i]] == eng[i] != "N" and why[i] not in pre[i]:
+                    arcs.append((why[i], i))
+                i = why[i]
+        return seq, val, span, arcs, st, res
+
+    def shift(seq, j, i, fwd):
+        q, p = seq.index(j), seq.index(i)
+        if q >= p:
+            return None
+        span, link = (seq[q:p + 1], succ) if fwd else (seq[p:q - 1 if q else None:-1], pre)
+        need, take, rest = set(link[span[0]]), [span[0]], []
+        for k in span[1:]:
+            if k in need:
+                take.append(k)
+                need.update(link[k])
+            else:
+                rest.append(k)
+        if take[-1] == span[-1]:
+            return None
+        return seq[:q] + (rest + take if fwd else (rest + take)[::-1]) + seq[p + 1:]
+    gats = [i for i in range(n - 1) if "gat" in ops[i]]
+    fits = lambda i, p: all(pos[k] < p for k in pre[i]) and all(pos[k] > p for k in succ[i])
+    seq, val, span, arcs, cur, was = survey(seq, eng)
+    best, taken, pos = (span, seq, eng), 0, {k: p for p, k in enumerate(seq)}
+    for it in range(iters):
+        r, swap = rnd(), None
+        if r < FILL:
+            end, start, why, _m = pick(was)
+            j = int(rnd() * n)
+            if eng[j] not in "VS" or why[j] not in pre[j]:
+                continue
+            later = [k for k in seq[pos[j] + 1:pos[j] + 40] if eng[j] in ops[k]["alts"] and max([end[x] for x in pre[k]] + [0.0]) < start[j]]
+            if not later:
+                continue
+            i = pick(later[:6])
+            swap = eng[j]
+        elif r < FILL + TRADE:
+            j = pick(gats)
+            i = j + 1
+            k = next((x for x in seq[pos[j] + 1:pos[j] + 40] if eng[x] == eng[j]), i)
+            if k == i or not joins(ops, j, i) or "gat" not in ops[k] or eng[i] not in ops[k]["alts"] or eng[k] not in ops[i]["alts"]:
+                continue
+            swap = (i, k)
+        elif r < FILL + TRADE + 0.1:
+            i = int(rnd() * n)
+            same = [k for k in seq[max(0, pos[i] - 30):pos[i]] if eng[k] == eng[i]][-3:]
+            if eng[i] == "N" or not same:
+                continue
+            j = pick(same)
+        else:
+            j, i = pick(arcs)
+            if "gat" in ops[j] and rnd() < 0.6:
+                j = pick([k for k in seq[seq.index(j):seq.index(i)] if eng[k] == eng[i]] or [j])
+        if load[i] or load[j]:
+            continue
+        r, ns, ne, moved = rnd(), seq, eng, []
+        turns = range(-5, 6) if rnd() < ALIKE else (0,)
+        if isinstance(swap, tuple):
+            ns, ne = list(seq), list(eng)
+            for d in turns:
+                a, b = like(swap[0], d), like(swap[1], d)
+                if a is not None and b is not None and fits(a, pos[b]) and fits(b, pos[a]) and a not in moved and b not in moved \
+                        and eng[a] in ops[b]["alts"] and eng[b] in ops[a]["alts"]:
+                    ns[pos[a]], ns[pos[b]], ne[a], ne[b] = b, a, eng[b], eng[a]
+                    moved += [a, b]
+            if not moved:
+                continue
+        elif r < 0.7 or swap:
+            ne = list(eng) if swap else eng
+            for d in turns:
+                a, b = like(j, d), like(i, d)
+                if a is not None and b is not None:
+                    ns = shift(ns, a, b, r < 0.35 and not swap) or ns
+                    moved += [a, b]
+                    if swap:
+                        ne[b] = swap
+            if ns is seq:
+                continue
+        else:
+            k = j if r < 0.88 else i
+            alts = [e for e in ops[k]["alts"] if e != eng[k]]
+            if not alts:
+                continue
+            to = {k: pick(alts)}
+            if "gat" in ops[k] and rnd() < 0.3:
+                p = seq.index(k)
+                near = [x for x in seq[max(0, p - 12):p + 12] if x != k and eng[x] == to[k] and eng[k] in ops[x]["alts"]]
+                if near:
+                    to[pick(near)] = eng[k]
+            ne = list(eng)
+            for x, e in to.items():
+                for d in turns:
+                    if like(x, d) is not None:
+                        ne[like(x, d)] = e
+                        moved.append(like(x, d))
+        allow = -temp * (1 - it / iters) ** 2 * math.log(rnd()) * len(ms)
+        p0 = min(pos[k] for k in moved)
+        st, d, res = steps(ns, ne, cur, pos, p0), 0.0, []
+        at = next((a for a, (x, y) in enumerate(zip(st, cur)) if x is not y and x != y), 0) // 32
+        for m in ms:
+            res.append(run(st, m, was[m], at))
+            end = res[m][0]
+            d += (max(end) / base[m]) ** POWER / POWER + early * sum(end) / n / base[m] - val[m]
+            if d > allow + 0.002 * (len(ms) - 1 - m):
+                break
+        else:
+            eng = ne
+            taken += 1
+            seq, val, span, arcs, cur, was = survey(ns, ne, st, res if taken % 16 else None)
+            pos = {k: p for p, k in enumerate(seq)}
+            if span < best[0]:
+                best = (span, seq, eng)
+    return best[1], best[2], run(steps(best[1], best[2]), 0)[0]
+
+
+def unify(ops, deps, eng, start, ref):
+    n = len(ops)
+    tags = {o["tag"]: i for i, o in enumerate(ops) if o["tag"][0] in ("front", "back")}
+    mark = [start[tags["back", 0, d]] for d in range(RO * NS)]
+    span = (mark[4] - mark[2]) / 2
+    eng, key = list(eng), list(start)
+    for i, o in enumerate(ops):
+        part, k, d = o["tag"]
+        j = tags.get((part, k, ref))
+        if j is not None and (part, d) != ("front", 0):
+            eng[i], key[i] = eng[j], start[j] + (d - ref) * span
+        elif part == "end":
+            key[i] += mark[ref] + (d - ref) * span - mark[d]
+    succ, left = [[] for _ in ops], [len(d) for d in deps]
+    for i in range(n):
+        for j in deps[i]:
+            succ[j].append(i)
+    ready, seq = {i for i in range(n) if not left[i]}, []
+    while ready:
+        i = min(ready, key=lambda k: (key[k], k))
+        ready.remove(i)
+        seq.append(i)
+        for k in succ[i]:
+            left[k] -= 1
+            if not left[k]:
+                ready.add(k)
+    return seq, eng
+
+
+SETS = [dict(COST, f=1.08, pc=0.54e-3, gath=1.12e-3, hop=0.12, same=0.24, net=1.5, load=0.55, aim=60.0),
+        dict(COST, f=1.0, pc=0.52e-3, gath=0.9e-3, hop=0.12, same=0.2, net=1.2, load=0.4, bw=420e3, scat=2e-3, aim=54.0),
+        dict(COST, f=1.25, pc=0.48e-3, gath=1.05e-3, hop=0.1, same=0.2, net=1.0, load=1.0, aim=66.5),
+        dict(COST, f=1.15, pc=0.56e-3, gath=1.4e-3, hop=0.16, same=0.28, net=2.1, first=2.0, load=0.6, bw=270e3, dma=0.2, aim=71.5),
+        dict(COST, f=1.45, pc=0.72e-3, gath=1.65e-3, hop=0.14, same=0.25, net=1.6, scat=4.5e-3, load=0.5, aim=79.0)]
+POWER = 12
+STARTS, SHORT = 4, 12000
+ITERS, TEMP, EARLY, ALIKE, FILL, TRADE, SHARE = 90000, 0.0004, 0.1, 0.2, 0.35, 0.2, 1.5
+SHIFTED = ("pair1", "sel1", "sel2", "sel3", "kc32", "ee1", "wtz", "lcz", "livey", "ltz", "cumz")
+ORDER = {}
+
+
 def rank_program(g, core, T, topo):
     rank = T.rank_of(core)
     if rank is None:
         return
     ops = plan(T, rank, topo)
     deps = depend(ops)
-    ops, deps, seq, eng, end = join(ops, deps, *order(ops, deps))
+    if not ORDER:
+        plans = [plan(T, rank, topo, c) for c in SETS]
+        hops = [(c["hop"], c["same"]) for c in SETS]
+        steps, run, _pre = timer(plans, deps, hops)
+        starts = [order(plans[m], deps, hops[m], look, back, (6.5, tl, td), passes)
+                  for m in (0, 3) for look in LOOKS for back in BACKS for tl, td in TURNS for passes in (0, 1)]
+        value = lambda a: sum((max(run(steps(a[0], a[1]), m)[0]) / c["aim"]) ** POWER for m, c in enumerate(SETS))
+        starts = sorted(starts, key=value)[:STARTS]
+        starts = [refine(plans, deps, hops, a[0], a[1], SHORT, TEMP, EARLY, k + 1) for k, a in enumerate(starts)]
+        seq, eng, _end = min(starts, key=value)
+        ORDER["seq"], ORDER["eng"], ORDER["end"] = refine(plans, deps, hops, seq, eng, ITERS, TEMP / 2, EARLY)
+    eng, end = ORDER["eng"], ORDER["end"]
+    ops, deps, seq = join(ops, deps, ORDER["seq"], eng)
+    own = [i for i in seq if eng[i] == "G" and ops[i]["kind"] == "c"]
+    for j, i in zip(own, own[1:]):
+        if ops[i]["w"][0] in SHIFTED or ops[j]["w"][0] in SHIFTED:
+            deps[i][j] = True
+    emit(g, T, ops, deps, seq, eng, end)
+
+
+def emit(g, T, ops, deps, seq, eng, end):
     chan, idx, cnt = {}, {}, {}
     for i in seq:
         ch = eng[i] if ops[i]["kind"] == "c" else ("x", i)
@@ -547,7 +883,7 @@ def rank_program(g, core, T, topo):
             continue
         w = []
         for j in sorted(deps[i], key=lambda j: -end[j]):
-            if chan[j] == e and (e == "P" or deps[i][j] is None):
+            if chan[j] == e and (e == "P" or deps[i][j] is None) or deps[i][j] == "S" != e:
                 continue
             if clock[e].get(chan[j], 0) >= idx[j]:
                 continue

@@ -5,51 +5,64 @@ from concourse.mybir import dt, AluOpType, AxisListType, ActivationFunctionType
 A = AluOpType
 F = ActivationFunctionType
 RO = 3
-NG = 4
-NS = NU = 8 // NG
-W, XH = 64 * NG, 16 * NG
-KCH = 16
-NCH = W // KCH
-JOIN = 8
-SCS = (2, 2, 2, 2, 2, 2, 1, 1, 1, 1)
-BLOCKS = ((64, 64, 128), (128, 128))
-PLACES = ("ps2", "ps3", "ps6", "ps7")
-RAMP = False
-PASS = 384
+NP = 2
+NS, NG = 4 // NP, 2 * NP
+W, XH, FR = 128 * NP, 64, 8 * NG
+NCH = 8 * NP
+STEP = 2
+BLK = ((4, 4), (4, 2, 2))[:NP]
+CASTS = ((8,), (8,)) if NP == 1 else ((4, 16), (4, 16))
+CN, PR, YC = (64, 128, 448) if NP == 1 else (256, 256, 64)
+PLACES = ("ps5", "ps6", "ps7")[NP - 1:]
+PXB = ((("ps4", "ps5"), ("ps4", "ps3"), ("ps4", "ps3"), ("ps4", "ps4"), "ps2", "ps3", "ps1"), (("ps3", "ps0"), ("ps5", "ps4"), ("ps3", "ps3"), ("ps3", "ps3"), "ps0", "ps2", "ps1"))[NP - 1]
+SCN = 1
+TAB = 4112
+KR = 128
 C0 = 12582912.0
-COST = {"f": 1.1, "pc": 0.48e-3, "gath": 1.25e-3, "scat": 3.0e-3, "hop": 0.07, "net": 1.6, "first": 1.0, "send": 0.25,
+LIVE = 8192.0
+COST = {"fix": 0.08, "f": 1.1, "pc": 0.48e-3, "gath": 1.25e-3, "hop": 0.07, "net": 1.6, "first": 1.0, "send": 0.25,
         "dfix": 1.8, "dma": 0.1, "bw": 350e3, "row": 0.015, "load": 0.5}
 WIDE = ("ac3", "sel")
+GATES = {(_p, _u): "mvin00" if _p == 3 else "mv00" for _p in range(1, 4) for _u in range(4) if _p > 1}
+CALL = 0.09
+ZDMA = (None, None)
+LATE = ("wq0", "wq1", "wq2", "wq3", "zer", "wtz", "ee0", "tabz0", "tabz1", "tabz2", "tabz3", "tabz4", "cc4", "cc6", "livez1", "pfz01", "pfz11", "pfz21", "pfz31")
+AFTER = ("pn2", "pn3", "kc", "ee", "idn1", "wtz", "zer", "cc")
 
-PART = {"tab": (4112, "bfloat16"), "gat": (32 * W, "bfloat16"), "pfl": (W, "bfloat16"), "pfb": (8 * W, "bfloat16"),
-        "posl": (512, "bfloat16"), "xy": (1056, "bfloat16"),
-        "py": (8 * W, "bfloat16"), "lvl": (XH, "int32"), "live": (4 * XH, "bfloat16"), "age": (XH, "float32"),
-        "cum": (2 * XH, "bfloat16"), "junk": (3 * W, "bfloat16"), "ac3": (W + 4, "float32"), "sl": (8, "uint16"),
-        "prod": (96 * RO, "bfloat16"), "prin": (96 * RO, "bfloat16"),
-        "lh": (768, "bfloat16"), "off": (2 * W, "uint16"), "hit": (128 * NG, "bfloat16"),
+PART = {"gat": (32 * W, "bfloat16"), "px": (1024 * NP, "bfloat16"),
+        "lvl": (XH, "int32"), "live": (4 * XH, "bfloat16"), "age": (XH, "float32"),
+        "cum": (2 * XH, "bfloat16"), "cux": (XH, "bfloat16"), "ac3": (128, "float32"), "sl": (8, "uint16"),
+        "prod": (64, "float16"), "mv": (16 * NP * RO, "float16"), "mvin": (16 * NP * RO, "float16"),
+        "off": (2 * W, "uint16"), "hit": (128 * NG, "bfloat16"),
         "acc": (4 * RO, "float32"), "ina": (4 * RO, "float32"), "inc": (4 * RO, "float32"),
-        "mx": (4, "float32"), "wt": (32, "bfloat16"), "wq": (256, "bfloat16"), "yco": (48, "float32")}
+        "mx": (4, "float32"), "wt": (32, "bfloat16"), "wq": (112 + 4 * FR, "bfloat16"), "yco": (48, "float32")}
 SCRATCH = {_n: ("sbuf", [128, NS * _c], _d) for _n, (_c, _d) in PART.items()}
 for _j in range(8):
     SCRATCH["ps%d" % _j] = ("psum", [128, 512], "float32")
-for _n, _c, _d in [("ip", 4, "int32"), ("ci", 8, "int32"), ("i4", 4, "float32"), ("iot", 128, "bfloat16"), ("iou", 128, "bfloat16"),
-                   ("idn", 80, "bfloat16"), ("sel", 32, "float32"), ("pair", 128, "float32"),
-                   ("ee", 32, "bfloat16"), ("lc", 512, "bfloat16"), ("lt", 512, "bfloat16"), ("cs", 16, "float32"),
-                   ("el", 4, "uint16"), ("prm", 448, "bfloat16"), ("kc", 32, "bfloat16"), ("cc", 1024, "bfloat16"),
-                   ("thl", 16, "int32"), ("thf", 32, "float32"), ("thb", 8, "float32"), ("sgn", 64, "bfloat16"),
-                   ("zer", 2 * XH, "bfloat16"), ("zs", 512, "bfloat16"), ("ramp", W, "bfloat16")]:
+for _n, _c, _d in [("tab", 4 * TAB + 16, "bfloat16"), ("posl", 512, "bfloat16"), ("xy", 1056, "bfloat16"), ("pfn", 512, "bfloat16"),
+                   ("pfl", 512, "bfloat16"), ("ip", 4, "int32"), ("ci", 8, "int32"), ("i48", 48, "float32"), ("iot", 32, "bfloat16"),
+                   ("iou", 32, "bfloat16"), ("idn", 160, "bfloat16"), ("sel", 32, "float32"), ("th3", 192, "float16"),
+                   ("ee", 56, "bfloat16"), ("lc", 576 + 80 * NS, "bfloat16"), ("rst", 128, "bfloat16"), ("cs", 16, "float32"),
+                   ("kc", 32, "bfloat16"), ("cc", 256, "bfloat16"),
+                   ("thl", 16, "int32"), ("thf", 32, "float32"), ("thb", 8, "float32"), ("sgn", 16, "bfloat16"),
+                   ("zer", 2 * XH, "bfloat16"), ("zs", 512, "bfloat16"), ("mul", 104, "bfloat16"), ("rows", 192, "bfloat16"),
+                   ("vb", 8, "float32"), ("d2", 416, "bfloat16"), ("selx", 256, "bfloat16"), ("posq", 2048, "bfloat16"), ("k18", 160, "bfloat16"),
+                   ("zz", 320, "bfloat16"), ("pn", 256 * NG, "bfloat16"), ("pfb", 4096, "bfloat16")]:
     SCRATCH[_n] = ("sbuf", [128, _c], _d)
 
-SEMAPHORES = ["eV", "eS", "eP", "eG", "sent"] + ["d%d" % i for i in range(44)] + ["r%d" % i for i in range(6 * NS)]
+SEMAPHORES = ["eV", "eS", "eP", "eG", "sent"] + ["d%d" % i for i in range(70)] + ["r%d" % i for i in range(6 * NS)]
 
-COPIES = [None, (0, -1.0, "q"), (0, 2.0 ** -4, "b"), (0, -2.0 ** -4, None), (2, 2.0 ** -4, None), (0, -2.0 ** -8, None),
-          (2, 2.0 ** -8, None), (0, -2.0 ** -12, None)]
-UNITS = [4096.0, 256.0, 16.0, 1.0]
-LEVELS = [[(0, 0), (1, 0), (2, 0), (0, 1), (1, 1), (2, 1), (0, 2)], [(0, 3), (1, 4)], [(1, 5), (2, 6)], [(2, 7)]]
+FIRST = -16.0
+STEPS = [((7, 70, 10), 0.125), ((8, 70, 10), 2.0 ** 14), ((9, 70, 10), -1.0), ((10, 40, 10), -2.0 ** -12), ((40, 41, 1), 2.0 ** -16), ((50, 70, 10), -2.0 ** -15)]
+TILES = [(0, (0, 0), (0, 0), (0, 0)), (10, (0, 0), (0, 9), (1, 7)), (40, (1, 0), (1, 28), (1, 40)), (40, (0, 0), (0, 0), (0, 0))]
 
 
-def block(s, c):
-    return sum(sum(BLOCKS[s][:b + 1]) <= KCH * c for b in range(len(BLOCKS[s])))
+def block(c):
+    a, c0 = c // 8, 0
+    for b in BLK[a]:
+        if c % 8 < c0 + b:
+            return a, c0, b
+        c0 += b
 
 
 def plan(T, rank, topo, cost=COST):
@@ -66,10 +79,10 @@ def plan(T, rank, topo, cost=COST):
         tag[1] += 1
 
     def vc(k, half=False):
-        return 0.05 + max(64, k / 2 if half else k) * CY
+        return cost["fix"] + max(64, k / 2 if half else k) * CY
 
     def ac(k):
-        return 0.065 + max(64, k) * CY
+        return cost["fix"] + 0.015 + max(64, k) * CY
 
     def gc(k, fix):
         return fix * FX + 2 * k * CY
@@ -87,16 +100,19 @@ def plan(T, rank, topo, cost=COST):
     def select(out, in_, pat, cmp, c, base, cm, r, w):
         op({"G": (lambda g: g.affine_select(out, in_, pat, cmp, c, base, cm), gc(out.shape[1], 0.17))}, r, w)
 
-    def paint(out, zero, pat, c, base, w):
-        select(out, zero, pat, A.not_equal, c, base, 1, ["zs"], w)
+    def paint(out, zero, pat, c, base, w, r=()):
+        select(out, zero, pat, A.not_equal, c, base, 1, ["zs"] + list(r), w)
 
-    def fill(out, c, w, p=None):
+    def fill(out, c, w, p=None, r=()):
         k = out.shape[1]
-        alts = {"V": (lambda g: g.vector.memset(out, c), vc(k, True)),
-                "G": (lambda g: g.iota(out, [[0, k]], int(c), 0, allow_small_or_imprecise_dtypes=True), gc(k, 0.13))}
+        alts = {"V": (lambda g: g.vector.memset(out, c), vc(k, True))}
+        if c == int(c) and abs(c) < 2 ** 24:
+            alts["G"] = (lambda g: g.iota(out, [[0, k]], int(c), 0, allow_small_or_imprecise_dtypes=True), gc(k, 0.13))
         if p:
             alts["S"] = (lambda g: g.scalar.activation(out, T.zs[p[0]:p[1], 0:k], F.Identity, bias=c, scale=0.0), ac(k))
-        op(alts, ["zs"] if p else [], w)
+        if w[0] in LATE:
+            alts = {"G": alts["G"]}
+        op(alts, (["zs"] if p else []) + list(r), w)
         ops[-1]["blank"] = True
 
     def lin(out, in_, mul, add, k, r, w, ps=(), half=False):
@@ -123,123 +139,147 @@ def plan(T, rank, topo, cost=COST):
         def B(name, a=0, b=None, st=1, p0=0, p1=128):
             c = PART[name][0]
             return T[name][p0:p1, c * h + a:c * h + (c if b is None else b):st]
-        return B, (lambda s: s + str(h)), ["ps%d" % (4 * h + i) for i in range(4)]
+        return B, (lambda s: s + str(h)), ["ps%d" % (3 * h + i if NP == 2 else h) for i in range(3)]
 
-    R3, RG = 3 * NG, 16 * NG
+    def table(p, u, q="Y"):
+        D(q, T.tab[32 * u:32 * u + 32, TAB * p + 16:TAB * p + TAB], T.rf[32 * p:32 * p + 32, :], 256,
+          [GATES[p, u]] if (p, u) in GATES else [], ["tab%d%d" % (p, u)])
 
-    def loads(h):
-        B, K, _b = part(h)
-        two = "Y" if h else "S"
-        D("Y", B("lvl", p1=32), T.lv[NG * h:NG * h + NG, :], 8, [], [K("lvl")])
-        for u in range(NU):
-            D(two, B("posl", p0=R3 * u, p1=R3 * u + R3), T.pos[R3 * h:R3 * h + R3, :], 12, [], [K("posl%d_" % u)])
-        if h == 0:
-            D("Y", T.thl[0:8, :], T.th[:], 1, [], ["thl"])
-            for u in range(NU):
-                table(h, u, [])
-        for u in range(NU):
-            D("Y", B("pfl", p0=RG * u, p1=RG * u + RG), T.pf[RG * h:RG * h + RG, W * u:W * u + W], 32, [], [K("pfl%d_" % u)])
-        if h:
-            table(h, 0, [])
-
-    def table(h, u, after):
-        B, K, _b = part(h)
-        D("Y" if u or h else "S", B("tab", 0, 4096, 1, RG * u, RG * u + RG), T.rf[RG * h:RG * h + RG, :], 512, after, [K("tab%d_" % u)])
-
-    loads(0)
+    flags = lambda q, h: D(q, T.lvl[0:FR, XH * h:XH * h + XH], T.lv[NG * h:NG * h + NG, :], 2 * NG, [], ["lvl%d" % h])
+    flags("Y", 0)
+    D("S", T.posl[0:24, :], T.pos[:], 24, [], ["posl"])
+    pairs = lambda p: D("Y", T.posq[0:6, 512 * p:512 * p + 512], T.pos[6 * p:6 * p + 6, :], 6, [], ["posq%d" % p])
+    pairs(1)
+    D("Y", T.pfn[:], T.pf[:], 128, [], ["pfn"])
+    for u in range(4):
+        table(0, u)
+    for h in range(1, NS):
+        flags("Y", h)
+    pairs(2)
+    pairs(3)
+    D("Y", T.thl[0:8, :], T.th[:], 1, [], ["thl"])
+    for p in range(1, 4):
+        for u in range(4):
+            if (p, u) not in GATES:
+                table(p, u)
 
     V(lambda v: v.memset(T.zs[:], 0.0), 512, [], ["zs"], half=True)
-    op({"G": (lambda g: g.iota(T.ip[:], [[128, 4]], 0, 1), gc(4, 0.13))}, [], ["ip"])
-    iota(T.iou[0:32, :], [[4, NU], [4 * NU, NG], [0, 16]], 0, -1, ["iou"])
-    select(T.iot[0:32, :], T.iou[0:32, :], [[0, NU], [-4 * NU, NG], [0, 16]], A.is_ge, -100.0, 0, 1, ["iou"], ["iot"])
-    iota(T.i4[:], [[1, 4]], 0, 0, ["i4"])
-    iota(T.kc[0:32, :], [[-1, 16], [-30000, 2]], 0, 0, ["kc"])
-    iota(T.kc[32:64, :], [[-1, 16], [30000, 2]], -30000, 0, ["kc32"])
-    c15, c11 = T.ci[:, 0:1], T.ci[:, 1:2]
-    V(lambda v: v.tensor_scalar(c15, T.ip[:, 0:1], 15, None, A.bitwise_and), 1, ["ip"], ["c15"])
-    V(lambda v: v.tensor_scalar(c11, T.ip[:, 0:1], 3, None, A.bitwise_and), 1, ["ip"], ["c11"])
-    V(lambda v: v.tensor_copy(T.el[:], T.ip[:]), 4, ["ip"], ["el"])
-    cn = {k: T.cs[:, i:i + 1] for i, k in enumerate(("m", "one", "scl", "q", "b", "x", "n", "u"))}
-    for k, c, s1, s2, o0, o1 in (("m", "c15", 3.0, 0.5, A.mult, A.add), ("one", "c11", 3.0, 1.0, A.is_equal, A.mult),
-                                 ("scl", "c11", 3.0, 1.0, A.is_equal, A.subtract), ("q", "c15", 3.0, 2048.0, A.is_equal, A.mult),
-                                 ("u", "c15", 15.0, C0 * (UNITS[1] - UNITS[0]), A.is_equal, A.mult), ("x", "c15", 3.0, 1024.125, A.is_equal, A.mult)):
-        V(lambda v, k=k, c=c, s1=s1, s2=s2, o0=o0, o1=o1: v.tensor_scalar(cn[k], c15 if c == "c15" else c11, s1, s2, o0, o1), 1, [c], ["c" + k])
-    lin(cn["n"], cn["one"], -0.125, cn["x"], 1, ["cone", "cx"], ["cn"])
-    lin(cn["b"], cn["q"], 1920.0 / 2048, cn["u"], 1, ["cq", "cu"], ["cb"])
-    lin(T.cs[:, 8:11], T.i4[:, 0:3], 1.0, cn["m"], 3, ["cm", "i4"], ["cs4"])
-    for q in range(4):
-        V(lambda v, q=q: v.tensor_scalar(T.lc[0:32, 128 * q:128 * q + 128], T.iot[0:32, :], float(-q), -UNITS[0], A.is_equal, A.mult), 128, ["iot"], ["lc%d" % q], half=True)
-        V(lambda v, q=q: v.tensor_scalar(T.lt[0:32, 128 * q:128 * q + 128], T.iot[0:32, :], float(-q), -UNITS[0], A.is_gt, A.mult), 128, ["iot"], ["lt%d" % q], half=True)
-    fill(T.lc[32:33, :], C0 * UNITS[0] / 2 ** 17, ["lcz"], (32, 33))
-    fill(T.live[32:33, :], 2.0 ** 17, ["livey"], (32, 33))
-    fill(T.cc[0:1, 512:544], C0 / 2 ** 22, ["cc4"], (0, 1))
-    fill(T.cc[0:1, 768:896], 2.0 ** 22, ["cc6"], (0, 1))
-    fill(T.cc[0:1, 0:128], 8 * C0 / 2 ** 22, ["cc0"], (0, 1))
-    fill(T.cc[0:1, 896:1024], -8 * C0 / 2 ** 22, ["cc7"], (0, 1))
-    ones = lambda k: T.cc[0:1, 768:768 + k]
-    paint(T.idn[0:36, 0:36], T.zs[0:36, 0:36], [[-1, 36]], 1.0, 0, ["idn0"])
-    paint(T.idn[0:32, 48:80], T.zs[0:32, 0:32], [[-1, 32]], 0.375, 0, ["idn1"])
+    op({"G": (lambda g: g.iota(T.ip[:], [[32, 4]], 0, 1), gc(4, 0.13))}, [], ["ip"])
+    iota(T.iou[0:FR, 0:FR], [[1, FR]], 0, -1, ["iou"])
+    select(T.iot[0:FR, 0:FR], T.iou[0:FR, 0:FR], [[-8, NG], [0, 8]], A.is_ge, -100.0, 0, 1, ["iou"], ["iot"])
+    iota(T.i48[:], [[2, 48]], -1023, 0, ["i48"])
+    iota(T.d2[0:24, 0:160], [[0, 5], [30, 8], [1, 4]], 0, -1, ["d2"])
+    iota(T.k18[:], [[0, 5], [16, 8], [1, 4]], 0, 0, ["k18"])
+    iota(T.kc[0:32, :], [[-30000, 2], [-1, 16]], 0, 0, ["kc"])
+    iota(T.kc[32:64, :], [[30000, 2], [-1, 16]], -30000, 0, ["kc32"])
+    c15, c23 = T.ci[:, 0:1], T.ci[:, 1:3]
+    V(lambda v: v.tensor_scalar(c15, T.ip[:, 0:1], 3, None, A.bitwise_and), 1, ["ip"], ["c15"])
+    V(lambda v: v.tensor_scalar(c23, T.ip[:, 0:2], 55, None, A.bitwise_and), 1, ["ip"], ["c23"])
+    V(lambda v: v.tensor_scalar(T.cs[:, 0:1], c15, 1.0, 2.0 ** -11, A.is_equal, A.mult), 1, ["c15"], ["cm"])
+    V(lambda v: v.tensor_copy(T.cs[:, 1:3], c23), 1, ["c23"], ["cp"])
+    V(lambda v: v.memset(T.lc[:], 0.0), 576 + 80 * NS, [], ["lc", "permz", "row1"] + ["fac%d" % h for h in range(NS)], half=True)
+    for i, cmp in enumerate((A.is_equal, A.is_gt)):
+        V(lambda v, i=i, cmp=cmp: v.tensor_scalar(T.lc[0:FR, 128 * i:128 * i + 4 * FR:4], T.iot[0:FR, 0:FR], 0.0, -2.0 ** -10, cmp, A.mult), 32, ["iot", "lc"], ["lc%d" % i])
+    for i, c in ((1, 1.0), (2, C0), (3, -C0)):
+        fill(T.lc[32:33, i:128:4], c, ["lcz%d" % i], (32, 33), ["lc"])
+    if NP == 2:
+        fill(T.cum[32:33, :], 1.0, ["cumz"], (32, 33))
+    else:
+        fill(T.cum[0:33, :], 1.0, ["cumy"] + ["cum%d" % h for h in range(NS)], (0, 33))
+    V(lambda v: v.tensor_copy(T.th3[:], T.zs[:, 0:192]), 192, ["zs"], ["th3"], half=True)
+    for q in range(NG):
+        V(lambda v, q=q: v.tensor_scalar(T.th3[32 * q:32 * q + 32, 48 * q:48 * q + 48], T.i48[32 * q:32 * q + 32, :], T.cs[32 * q:32 * q + 32, 0:1], 1.0, A.mult, A.add),
+          48, ["i48", "cm", "th3"], ["th3%d" % q])
+    iota(T.rst[:], [[0, 4], [1024, 32]], 0, 0, ["rstz"])
+    V(lambda v: v.memset(T.sl[:], 0), 16, [], ["sl%d" % h for h in range(NS)])
+    fill(T.cc[0:1, 0:32], C0 / 2 ** 22, ["cc4"], (0, 1))
+    fill(T.cc[0:1, 128:256], 2.0 ** 22, ["cc6"], (0, 1))
+    ones = lambda k: T.cc[0:1, 128:128 + k]
+    fill(T.mul[0:1, :], 1.0, ["mul"], (0, 1))
+    for i, ((a, b, st), c) in enumerate(STEPS):
+        fill(T.mul[0:1, a:b:st], c, ["mul%d" % i], (0, 1), ["mul"])
+    V(lambda v: v.tensor_tensor_scan(T.rows[0:1, 0:72], T.mul[0:1, 0:72], T.zs[0:1, 0:72], FIRST, A.mult, A.add), 72,
+      ["zs"] + ["mul%d" % i for i in range(len(STEPS))], ["row0"], half=True)
+    for k, c in ((7, 1.875), (40, 2 * C0), (41, 2 * C0)):
+        fill(T.lc[0:1, 512 + k:512 + k + 21:10], c, ["row1%d" % k], (0, 1), ["row1"])
+    vcol, bcol, wcol, ucol = (T.vb[:, i:i + 1] for i in (0, 1, 3, 4))
+    cell = lambda r, c: (T.mul, T.rows)[r][0:1, c:c + 1]
+    mm = []
+    for b, (x, fv, fo, fu) in enumerate(TILES):
+        o = lambda i: T.ps1[32 * b:32 * b + 32, 384 + i:385 + i]
+        mm += [(o(0), T.rows[0:1, x:x + 32], cell(*fv), True, True, 32), (o(1), T.lc[0:1, 512:544], cell(*fo), True, False, 32),
+               (o(1), T.lc[0:1, 544:576], cell(0, 0), False, True, 32), (o(2), T.mul[0:1, 72:104], cell(*fu), True, True, 32)]
+    P(mm, ["row0", "row17", "row140", "row141"], ["vbp"], ["ps1"])
+    lin(T.vb[:, 0:3], T.ps1[:, 384:387], 1.0, 0.0, 3, ["vbp"], ["vb"], ["ps1"])
+    V(lambda v: v.tensor_scalar(wcol, bcol, 0.0, vcol, A.not_equal, A.mult), 1, ["vb"], ["wcol"])
+    V(lambda v: v.tensor_scalar(ucol, bcol, 0.0, T.vb[:, 2:3], A.is_equal, A.mult), 1, ["vb"], ["ucol"])
+    for a in range(2):
+        V(lambda v, a=a: v.tensor_scalar(T.zz[:, 160 * a:160 * a + 160], T.k18[:], T.cs[:, 2 - a:3 - a], -32.0, A.subtract, A.is_equal), 160,
+          ["k18", "cp"], ["zz%d" % a], half=True)
+    V(lambda v: v.tensor_tensor(T.d2[0:24, 160:288], T.d2[0:24, 32:160], T.d2[0:24, 22:150], A.min), 256, ["d2"], ["d2a"])
+    V(lambda v: v.tensor_tensor(T.d2[0:24, 288:416], T.d2[0:24, 160:288], T.d2[0:24, 12:140], A.min), 256, ["d2a"], ["d2b"])
+    for e in range(2):
+        V(lambda v, e=e: v.tensor_scalar(T.selx[0:6, 128 * e:128 * e + 128], T.d2[0:6, 288:416], 27.0 * e, None, A.is_equal), 128, ["d2b"], ["selx%d" % e], half=True)
+    iota(T.sgn[0:24, :], [[0, 8], [-2, 2]], 1, 0, ["sgn"])
+    for c in range(3):
+        a, b = (c + 1) % 3, (c + 2) % 3
+        select(T.lc[0:24, 256 + c:384:8], T.sgn[0:24, :], [[-3, 8], [a - b, 2]], A.is_equal, 0.0, -a, 1, ["sgn", "permz"], ["perm0%d" % c])
+        paint(T.lc[0:24, 384 + c:512:8], T.zs[0:24, 0:16], [[-3, 8], [b - a, 2]], 1.0, -b, ["perm1%d" % c], ["permz"])
+    for i, bank in enumerate(("ps6", "ps7")):
+        P([(T[bank][:], T.lc[0:24, 256 + 128 * i:384 + 128 * i], T.posl[0:24, :], True, True, 512)], ["posl"] + ["perm%d%d" % (i, c) for c in range(3)], [bank], [bank])
+        lin(T.xy[:, 528 * i:528 * i + 512], T[bank][:], 1.0, 0.0, 512, [bank], [("xw", "yw")[i]], [bank])
+    fill(T.xy[:, 512::528], 0.0, ["xyz"], (0, 128))
+    for k in range(5):
+        fill(T.tab[:, TAB * k:TAB * k + 16], -8388608.0, ["tabz%d" % k], (0, 128))
+    paint(T.idn[:, 0:128], T.zs[:, 0:128], [[-1, 128]], 1.0, 0, ["idn0"])
+    paint(T.idn[0:32, 128:160], T.zs[0:32, 0:32], [[-1, 32]], 0.375, 0, ["idn1"])
     for q in range(4):
         paint(T.sel[32 * q:32 * q + 32, :], T.zs[32 * q:32 * q + 32, 0:32], [[-1, 32]], 16.0, 0, ["sel%d" % q])
     sk = ["sel%d" % q for q in range(4)]
-    for u in range(NU):
-        paint(T.pair[RG * u:RG * u + RG, :], T.zs[RG * u:RG * u + RG, 0:128], [[0, NU], [-1, RG]], 1.0, 0, ["pair%d" % u])
     fill(T.ee[0:64, :], 0.0, ["ee0", "ee1"])
     for a in range(2):
-        paint(T.ee[32 * a:32 * a + 32, R3:R3 + NG], T.zs[32 * a:32 * a + 32, 0:NG], [[-1, NG]], -0.1875, 0, ["ee%d" % a])
-    select(T.ee[32:64, R3:R3 + NG], T.ee[32:64, R3:R3 + NG], [[0, NG]], A.not_equal, -0.375, -NG, 1, ["ee1"], ["ee1"])
+        paint(T.ee[32 * a:32 * a + 32, 24:24 + NG], T.zs[32 * a:32 * a + 32, 0:NG], [[-1, NG]], -0.1875, 0, ["ee%d" % a])
+    select(T.ee[32:64, 24:24 + NG], T.ee[32:64, 24:24 + NG], [[0, NG]], A.not_equal, -0.375, -NG, 1, ["ee1"], ["ee1"])
     fill(T.wt[32:64, :], 1.0, ["wtz"])
-    V(lambda v: v.memset(T.prm[0:2 * R3, 3:384:4], 0.0), 64, [], ["permz"])
-    iota(T.sgn[0:2 * R3, :], [[0, 8], [-2, 2], [0, 4]], 1, 0, ["sgn"])
-    for c in range(3):
-        a, b = (c + 1) % 3, (c + 2) % 3
-        select(T.prm[0:2 * R3, c:128:4], T.sgn[0:2 * R3, 0:64:2], [[-3, 8], [0, 2], [a - b, 2]], A.is_equal, 0.0, -a, 1, ["sgn"], ["perm0%d" % c])
-        paint(T.prm[0:2 * R3, 256 + c:384:4], T.zs[0:2 * R3, 0:32], [[-3, 8], [0, 2], [b - a, 2]], 1.0, -b, ["perm1%d" % c])
-    V(lambda v: v.tensor_scalar(T.prm[0:2 * R3, 128:256], T.prm[0:2 * R3, 0:128], -1.0, 0.0, A.mult, A.max), 128, ["perm0%d" % c for c in range(3)] + ["permz"], ["permlo"], half=True)
-    select(T.prm[0:R3, 384:448], T.sgn[0:R3, :], [[-3, NG], [0, 4], [-1, 4]], A.is_equal, 0.0, 0, 1, ["sgn"], ["perm2"])
     for s in range(2):
-        V(lambda v, s=s: v.tensor_copy(T.thf[0:8, s:32:2], T.thl[0:8, :]), 16, ["thl"], ["thf%d" % s])
-    lin(T.xy[:, 512::528], T.i4[:, 0:2 * NS], 0.0, cn["one"], 2 * NS, ["i4", "cone"], ["xyz"])
-    fill(T.tab[:, 4096::4112], -8388608.0, ["tabz"])
+        V(lambda v, s=s: v.tensor_copy(T.thf[0:8, 16 * s:16 * s + 16], T.thl[0:8, :]), 16, ["thl"], ["thf%d" % s])
     fill(T.zer[0:32, :], -C0, ["zer"])
-    if RAMP:
-        iota(T.lt[32:33, :], [[0, 32], [6, 16]], 5, 0, ["ltz"])
-        fill(T.cum[32:33, :], UNITS[0] / 2, ["cumz"], (32, 33))
-        iota(T.ramp[:], [[2, W]], 2 - W, 0, ["ramp"])
+    for k in range(NG):
+        paint(T.pn[0:FR, 256 * k:256 * k + 256], T.zs[0:FR, 0:256], [[-1, 2], [-2, 4], [0, 32]], LIVE, -8 * k, ["pn%d" % k])
+
+    def positions(p, banks):
+        B, K, _b = part(p // NP)
+        for i, bank in enumerate(banks):
+            P([(T[bank][:, 256 * v + 128 * e:256 * v + 128 * e + 128], T.selx[0:6, 128 * e:128 * e + 128],
+                (T.posq[0:6, 512 * p + 2 * i + v:512 * p + 512:4] if p else T.posl[0:6, 2 * i + v:512:4]), True, True, 128) for v in range(2) for e in range(2)],
+              ["posq%d" % p if p else "posl", "selx0", "selx1"], [bank], [bank])
+            a = 1024 * (p % NP) + 512 * i
+            lin(B("px", a, a + 512), T[bank][:], ucol, bcol, 512, [bank, "vb", "ucol"], [K("px%d%d_" % (p % NP, i))], [bank])
 
     def setup(h):
-        B, K, (sc, sm, pa, pb) = part(h)
-        if h:
-            pa, pb = sm, sc
-        fill(B("live", XH, 2 * XH, p1=32), 0.0, [K("livez")], (0, 32))
-        V(lambda v: v.tensor_copy(B("live", 0, XH, p1=32), B("lvl", p1=32)), XH, [K("lvl")], [K("live0")])
+        B, K, _b = part(h)
+        fill(B("live", XH, 2 * XH, p1=FR), 0.0, [K("livez")], (0, FR))
+        V(lambda v: v.tensor_copy(B("live", 0, XH, p1=FR), B("lvl", p1=FR)), XH, [K("lvl")], [K("live0")])
         fill(B("wq"), 0.0, [K("wq")], (0, 128))
-        for s in range(2):
-            fill(B("lh", 384 * s, 384 * s + 384), 0.0, [K("lh%d" % s)], (0, 128))
-        pos = B("posl", p1=2 * R3)
-        pk = [K("posl%d_" % u) for u in range(NU)]
-        eight = lambda c, opens: [(T[pa][:, a:a + 128], T.cc[0:1, c:c + 128], ones(128), opens and a == 0, False, 128) for a in range(0, 512, 128)]
-        P(eight(0, True), ["cc0", "cc6"], [pa], [pa])
-        P([(T[pa][:], T.prm[0:2 * R3, 0:128], pos, False, False, 512)], pk + ["permz"] + ["perm0%d" % c for c in range(3)], [pa], [pa])
-        P(eight(896, False), ["cc7"], [pa], [pa])
-        P([(T[pa][:], T.prm[0:2 * R3, 128:256], pos, False, True, 512)], ["permlo"], [pa], [pa])
-        P([(T[pb][:], T.prm[0:2 * R3, 256:384], pos, True, True, 512)], pk + ["permz"] + ["perm1%d" % c for c in range(3)], [pb], [pb])
-        for a, nm, bank in ((0, "xw", pa), (528, "yw", pb)):
-            lin(B("xy", a, a + 512), T[bank][:], 1.0, cn["one"], 512, [bank, "cone"], [K(nm)], [bank])
-        P([(T[sc][RG * u:RG * u + RG, 0:W], T.prm[0:R3, 384:384 + RG], B("posl", W * u, W * u + W, p1=R3), True, True, W) for u in range(NU)],
-          [pk[0], "perm2"], [sc], [sc])
-        lin(B("py", 0, W), T[sc][:, 0:W], cn["scl"], cn["n"], W, [sc, "cscl", "cn"], [K("py0")], [sc])
-        for i, (src, f, col) in list(enumerate(COPIES))[1:]:
-            lin(B("py", W * i, W * i + W), B("py", W * src, W * src + W), f, cn[col] if col else 0.0, W,
-                [K("py%d" % src)] + (["c" + col] if col else []), [K("py%d" % i)], half=True)
-        lin(B("pfl"), B("pfl"), 1.0, 2.0 ** -10, W, [K("pfl%d_" % u) for u in range(NU)], [K("pfm")], half=True)
+        for p in range(NP * h, NP * h + NP):
+            positions(p, PXB[p])
+        if h == 0:
+            b = PXB[4]
+            P([(T[b][32 * u:32 * u + 32, 128 * p:128 * p + 128], T.idn[:, 32 * p:32 * p + 32], T.pfn[:, u:512:4], True, True, 128)
+               for p in range(4) for u in range(4)], ["pfn", "idn0"], [b], [b])
+            lin(T.pfl[:], T[b][:], 1.0, 2.0 ** -10, 512, [b], ["pfl"], [b])
+        if NP * h % 2:
+            return
+        j = NP * h // 2
         for a in range(4):
-            if h:
-                D("Y", B("pfb", 2 * W * a, 2 * W * (a + 1)), T.zs[:], 128, ["zs", "prin00"], [K("pfz%d_" % a)])
+            z = T.pfb[:, 2048 * j + 512 * a:2048 * j + 512 * a + 512]
+            if ZDMA[j]:
+                D("Y", z, T.zs[:], 128, ["zs", ZDMA[j]], ["pfz%d%d" % (a, j)])
             else:
-                fill(B("pfb", 2 * W * a, 2 * W * (a + 1)), 0.0, [K("pfz%d_" % a)], (0, 128))
+                fill(z, 0.0, ["pfz%d%d" % (a, j)])
         for q in range(8):
-            D("Y", B("pfb", W * q, W * q + W, 1, 16 * q, 16 * q + 16), B("pfl", p0=16 * q, p1=16 * q + 16), 8, [K("pfm"), K("pfz%d_" % (q // 2))], [K("pfb%d" % q)])
+            D("Y", T.pfb[16 * q:16 * q + 16, 2048 * j + 256 * q:2048 * j + 256 * q + 256], T.pfl[16 * q:16 * q + 16, 256 * j:256 * j + 256], 8,
+              ["pfl", "pfz%d%d" % (q // 2, j)], ["pfb%d%d" % (q, j)])
 
     nrem, nblk = [0], [0]
 
@@ -260,87 +300,94 @@ def plan(T, rank, topo, cost=COST):
         op({"N": ((sem, ne * len(dsts)), 0.0)}, [land + "s"], [land], kind="a", lat=cost["net"] + us + (cost["first"] if nrem[0] == 1 else 0.0))
 
     def front(h, t):
-        B, K, (scn, smn, pa, pb) = part(h)
-        sc, sm = T[scn], T[smn]
+        B, K, (san, sbn, smn) = part(h)
+        sb, sm = T[sbn], T[smn]
         if t == 0:
-            live = B("live", 0, 2 * XH, p1=32)
-            V(lambda v: v.tensor_tensor_scan(B("cum", p1=32), live, live, 0.0, A.add, A.max), 2 * XH, [K("live0"), K("livez")], [K("cum")], half=True)
-        both = RAMP and t + h > 0
+            live = B("live", 0, 2 * XH, p1=FR)
+            V(lambda v: v.tensor_tensor_scan(B("cum", p1=FR), live, live, 0.0, A.add, A.max), 2 * XH, [K("live0"), K("livez")], [K("cum")], half=True)
         tag[:] = "front" if t + h else "first", 0, NS * t + h
-
-        def spread(bank, a, rows):
-            return [(bank[:, a + XH * q:a + XH * q + XH], w[0:k, 128 * q:128 * q + 128], B("cum", XH * i, XH * i + XH, p1=k), i == 0, i == 1, 64)
-                    for q in range(4) for i, (w, k) in enumerate(((T.lc, 32), (T.lt, rows)))]
-        lk = [K("cum")] + ["lc%d" % q for q in range(4)] + ["lt%d" % q for q in range(4)]
-        P(spread(sm, 256, 32), lk, [K("cn")], [smn])
-        if both:
-            P(spread(sc, 128, 33), lk + ["ltz", "cumz"], [K("cv")], [scn])
-            V(lambda v: v.tensor_tensor_scan(B("ac3", 0, W), sc[:, 128:128 + W], T.ramp[:], -float(W), A.max, A.min), W, [K("cv"), "ramp"], [K("ac30")], [scn])
-        for i, k in list(enumerate((2, 0, 1)))[both:]:
-            S(lambda a, i=i, k=k: a.activation(B("junk", W * i, W * i + W), sm[:, 256:256 + W], F.Sign, bias=T.cs[:, 8 + k:9 + k], scale=1.0 / UNITS[0],
-                                               accum_out=B("ac3", W - 1 + i, W + i)),
-              W + 24, [K("cn"), "cs4"], [K("ac3%d" % i)], [smn])
-        pk = ["pair%d" % u for u in range(NU)]
-        P([(sc[:, 403:405], T.pair[:], B("ac3", W - 1, W + 1), True, True, 256)], [K("ac30"), K("ac31")] + pk, [K("pr")], [scn])
-        P([(sc[:, 400:403], T.pair[:], B("ac3", W - 1, W + 2), True, True, 256)], [K("ac3%d" % i) for i in range(3)] + pk, [K("pr")], [scn])
-        V(lambda v: v.tensor_scalar(B("sl", 0, 5), sc[:, 400:405], 0.5, 256.0, A.mult, A.add), 5, [K("pr")], [K("sl")], [scn])
-        for a, w0, nm in ((0, 528, "yw"), (1, 0, "xw")):
-            o, w = B("prod", 96 * t + 48 * a, 96 * t + 48 * a + 48), B("xy", w0, w0 + 513).indirect(B("sl", 2 * a, 2 * a + 3))
-            us = 48 * cost["gath"]
-            op({"V": (lambda g, o=o, w=w: g.vector.tensor_copy(o, w), 0.05 + us), "S": (lambda g, o=o, w=w: g.scalar.activation(o, w, F.Copy), 0.065 + us)},
-               [K("sl"), K(nm), "xyz"], [K("prod%d" % t) + nm])
-        pk = [K("prod%d" % t) + nm for nm in ("xw", "yw")]
-        send(B("prod", 96 * t, 96 * t + 96), [(T.cores[(rank + t + 1) % n], B("prin", 96 * t, 96 * t + 96))], pk, K("prin%d" % t), 0.4)
+        cn = sm[0:4 * FR, CN:CN + XH]
+        P([(cn, T.lc[0:k, 128 * i:128 * i + 4 * FR], B("cum", XH * i, XH * i + XH, p1=k), i == 0, i == 1, 64) for i, k in enumerate((33, FR))],
+          [K("cum"), "cumz", "lc0", "lc1", "lcz1", "lcz2", "lcz3"], [K("cn")], [smn])
+        lin(B("cux", p1=4 * FR), cn, 1.0, 0.0, XH, [K("cn")], [K("cux")], [smn])
+        p0, p1 = 16 * NG * h, 16 * NG * h + 16 * NG
+        P([(sb[p0:p1, PR + 32 * b:PR + 32 * b + 32], T.th3[0:4 * FR, i:48 * NG:3], B("cux", 32 * f, 32 * f + 32, p1=4 * FR), f == 0, f == 1, 16 * NG)
+           for b, i in enumerate((1, 2, 0, 1)) for f in range(2)], [K("cux")] + ["th3%d" % q for q in range(NG)], [K("pr")], [sbn])
+        V(lambda v: v.tensor_tensor_scan(B("ac3", p0=p0, p1=p1), T.rst[p0:p1, :], sb[p0:p1, PR:PR + 128], 0.0, A.min, A.add), 128, [K("pr"), "rstz"], [K("ac3")], [sbn])
+        V(lambda v: v.tensor_copy(B("sl", 0, 4, 1, p0, p1), B("ac3", 31, 128, 32, p0, p1)), 4, [K("ac3")], [K("sl")])
+        x = 576 + 80 * h
+        o, w, us = T.lc[:, x:x + 64], T.xy[:, 528:1041].indirect(B("sl", 0, 4)), 64 * cost["gath"]
+        op({"V": (lambda g: g.vector.tensor_copy(o, w), 0.05 + us), "S": (lambda g: g.scalar.activation(o, w, F.Copy), 0.065 + us)},
+           [K("sl"), "yw", "xyz"], [K("fac")])
+        fb = T.lc[:, x + 16:x + 80]
+        op({"V": (lambda g: g.vector.tensor_tensor(B("prod"), T.xy[:, 0:513].indirect(B("sl", 0, 4)), fb, A.mult), 0.06 + us)},
+           [K("sl"), "xw", "xyz", K("fac")], [K("prod")])
+        r0, x0, x1 = 64 * (NP * h // 2), 16 * NP * t, 16 * NP * t + 16 * NP
+        P([(sb[:, 400 + 16 * a:416 + 16 * a], T.zz[r0:r0 + 64, x + 32 - 10 * j:x + 160 - 10 * j], B("prod", 16 * j, 16 * j + 16, 1, r0, r0 + 64), j == 0, j == 2, 64)
+           for a, x in enumerate(160 * (p % 2) for p in range(NP * h, NP * h + NP)) for j in range(3)],
+          [K("prod"), "zz0", "zz1"], [K("ax")], [sbn])
+        mk = "mv%d%d" % (t, h)
+        V(lambda v: v.tensor_scalar(B("mv", x0, x1), sb[:, 400:400 + 16 * NP], vcol, wcol, A.mult, A.add), 32, [K("ax"), "vb", "wcol"], [mk], [sbn])
+        send(B("mv", x0, x1), [(T.cores[(rank + t + 1) % n], B("mvin", x0, x1))], [mk], K("mvin%d" % t), 0.2)
         for s in range(2):
-            lh = K("lh%d" % s)
-            nm, a = ("prod", "prin")[s], 96 * t
-            op({"V": (lambda g, s=s, nm=nm, a=a: g.vector.tensor_tensor(B("lh", 384 * s, 384 * s + 384).indirect(T.el[:, 0:3]), B(nm, a + 48, a + 96), B(nm, a, a + 48), A.mult),
-                      0.05 + 48 * cost["scat"])}, ([K("prin%d" % t)] if s else pk) + ["el"], [lh])
-            for c, wd in enumerate(BLOCKS[s]):
+            for i, (k0, k1) in enumerate(zip((0,) + CASTS[s], CASTS[s])):
                 bank = PLACES[nblk[0] % len(PLACES)]
                 nblk[0] += 1
-                x0, cyc = sum(BLOCKS[s][:c]), max(64, wd)
-                o = T[bank][:, 0:wd]
-                cut = [(q, max(x0, XH * q), min(x0 + wd, XH * q + XH)) for q in range(x0 // XH, (x0 + wd - 1) // XH + 1)]
-                P([(T[bank][:, a - x0:b - x0], T.lc[0:33, 128 * q:128 * q + 128], B("live", XH * (t - q) + a, XH * (t - q) + b, p1=33), a == x0, False, 64)
-                   for q, a, b in cut], [K("live%d" % t), "lcz", "livey"] + ["lc%d" % q for q, _a, _b in cut], ["pl" + bank], [bank])
                 mm = []
-                for i, level in enumerate(LEVELS):
-                    for j, k in level:
-                        mm.append(((o, B("lh", 384 * s + 128 * j, 384 * s + 128 * j + 128), B("py", W * k + x0, W * k + x0 + wd), False, i == 3, cyc),
-                                   [lh, K("py%d" % k)]))
-                parts = max(1, round(len(mm) * wd / PASS))
-                for i in range(parts):
-                    mp = mm[len(mm) * i // parts:len(mm) * (i + 1) // parts]
-                    P([m[0] for m in mp], [k for m in mp for k in m[1]], ["pl" + bank], [bank])
-                V(lambda v, a=W * s + x0, wd=wd, o=o: v.tensor_scalar(B("off", a, a + wd), o, UNITS[0] - C0, 4096.0, A.add, A.min), wd,
-                  ["pl" + bank], [K("off%d%d" % (s, c))], [bank])
+                for k in range(k0, k1):
+                    a, c0, b = block(k)
+                    x = 16 * (8 * a + c0 - k0)
+                    mm.append((T[bank][:, x + k % 8 - c0:x + 16 * b:b], B("px", 1024 * a + k % 8, 1024 * a + 1024, 8),
+                               B(("mv", "mvin")[s], x0 + 16 * a, x0 + 16 * a + 16), True, True, 64))
+                P(mm, [K("mvin%d" % t) if s else mk] + [K("px%d%d_" % (a, j)) for a in range(k0 // 8, (k1 + 7) // 8) for j in range(2)], ["pl" + bank], [bank])
+                V(lambda v, x=W * s + 16 * k0, w=16 * (k1 - k0), bank=bank: v.tensor_scalar(B("off", x, x + w), T[bank][:, 0:w], 16.0, float(TAB), A.add, A.min),
+                  16 * (k1 - k0), ["pl" + bank], [K("off%d%d" % (s, i))], [bank])
 
     def back(h, t):
-        B, K, (scn, smn, pa, pb) = part(h)
-        sc, sm = T[scn], T[smn]
+        B, K, (san, sbn, smn) = part(h)
+        sa, sm = T[san], T[smn]
         tag[:] = "back", 0, NS * t + h
+        lv = lambda i: B("live", XH * i, XH * i + XH, p1=FR)
 
         def gather(s, c0, c1):
-            o = B("gat", 32 * KCH * c0 + s, 32 * KCH * c1, 2)
-            w = B("tab", 0, 4097).indirect(B("off", W * s + KCH * c0, W * s + KCH * c1))
-            us = 16 * KCH * (c1 - c0) * cost["gath"]
-            return {"V": (lambda g: g.vector.tensor_copy(o, w), 0.05 + us), "S": (lambda g: g.scalar.activation(o, w, F.Copy), 0.065 + us)}
+            a, b0, b = block(c0)
+            x = 4096 * a + 512 * b0 + 256 * (b * s - 8 * a - b0)
+            o = B("gat", x + 256 * c0, x + 256 * c1)
+            x = W * s
+            p = NP * h + a
+            w = T.tab[:, TAB * p:TAB * p + TAB + 1].indirect(B("off", x + 16 * c0, x + 16 * c1))
+            us = 256 * (c1 - c0) * cost["gath"]
+            us += CALL
+            return {"V": (lambda g: g.vector.tensor_copy(o, w), us), "S": (lambda g: g.scalar.activation(o, w, F.Copy), 0.015 + us)}
         for s in range(2):
-            for c in range(NCH):
-                op(gather(s, c, c + 1), [K("off%d%d" % (s, block(s, c))), "tabz"] + [K("tab%d_" % u) for u in range(NU)], [K("gat%d%d_" % (s, c))])
+            for c in range(0, NCH, STEP):
+                p = NP * h + c // 8
+                op(gather(s, c, c + STEP), [K("off%d%d" % (s, sum(k <= c for k in CASTS[s]))), "tabz%d" % p, "tabz%d" % (p + 1)] + ["tab%d%d" % (p, u) for u in range(4)], [K("gat%d%d_" % (s, c))])
                 ops[-1]["gat"] = (gather, s, c)
-        for c, k1 in enumerate(SCS):
-            k0 = sum(SCS[:c])
-            P([(sc[32 * (x // XH):32 * (x // XH) + 32, 8 * (x % XH):8 * (x % XH) + 8], B("gat", 32 * x, 32 * x + 32), B("pfb", x, 8 * W, W), True, True, 32)
-               for x in range(k0 * KCH, (k0 + k1) * KCH)],
-              [K("gat%d%d_" % (s, k)) for s in range(2) for k in range(k0, k0 + k1)] + [K("pfb%d" % q) for q in range(8)], [K("s%d_" % c)], [scn])
-            ops[-1]["free"] = True
+        for a, scn in enumerate((san, sbn)[:NP]):
+            sc, p = T[scn], NP * h + a
+            P([(sc[:, 128 * f + e:128 * f + 128:2], T.pn[0:FR, 512 * a + 256 * e + 128 * f:512 * a + 256 * e + 128 * f + 128], lv(t), e + f == 0, False, 64)
+               for e in range(2) for f in range(2)], [K("live%d" % t), "pn%d" % (2 * a), "pn%d" % (2 * a + 1)], [K("s%d_" % a)], [scn])
+            for c1 in range(0, 8):
+                _a, c0, b = block(8 * a + c1)
+                if (c1 - c0) % SCN:
+                    continue
+                mm = []
+                for c in range(c1, min(c1 + SCN, c0 + b)):
+                    for i in range(16):
+                        y, x = 8 * i + c, 4096 * a + 512 * c0 + 16 * (c - c0) + i
+                        mm.append((sc[32 * (y // 32):32 * (y // 32) + 32, 8 * (y % 32):8 * (y % 32) + 8], B("gat", x, 4096 * a + 512 * (c0 + b), 16 * b),
+                                   T.pfb[:, 2048 * (p // 2) + 128 * (p % 2) + y:2048 * (p // 2) + 2048:256], False, False, 32))
+                P(mm, [K("s%d_" % a)] + [K("gat%d%d_" % (s, 8 * a + k)) for s in range(2) for k in range(c0, c0 + b, STEP)] + ["pfb%d%d" % (q, p // 2) for q in range(8)],
+                  [K("s%d%d_" % (a, c1))], [scn])
+                ops[-1]["free"] = True
+            P([(sc[:, 0:256], T.zs[0:1, 0:128], T.zs[0:1, 0:256], False, True, 256)], [K("s%d%d_" % (a, c)) for c in range(8)], [K("s%d_" % a)], [scn])
+            for e in range(2):
+                k = 2 * a + e
+                S(lambda v, k=k, e=e, sc=sc: v.activation(B("hit", 128 * k, 128 * k + 128), sc[:, e:256:2], F.Sign, bias=T.thb[:, NG * h + k:NG * h + k + 1],
+                                                          accum_out=B("acc", 4 * t + k, 4 * t + k + 1)),
+                  152, [K("s%d_" % a), "thb"], [K("hit%d" % k), K("acc%d%d" % (t, k))], [scn])
         acc = B("acc", 4 * t, 4 * t + NG)
-        for k in range(NG):
-            S(lambda a, k=k: a.activation(B("hit", 128 * k, 128 * k + 128), sc[:, k:8 * XH:NG], F.Sign, bias=T.thb[:, NG * h + k:NG * h + k + 1],
-                                          accum_out=B("acc", 4 * t + k, 4 * t + k + 1)),
-              152, [K("s%d_" % c) for c in range(len(SCS))] + ["thb"], [K("hit%d" % k), K("acc%d%d" % (t, k))], [scn])
         ca, cc = T.cores[(rank - t - 1) % n], T.cores[(rank + t + 1) % n]
         ina, inc = B("ina", 4 * t, 4 * t + NG), B("inc", 4 * t, 4 * t + NG)
         if ca == cc:
@@ -351,68 +398,83 @@ def plan(T, rank, topo, cost=COST):
         ak = [K("acc%d%d" % (t, k)) for k in range(NG)]
         send(acc, dsts, ak, K("in%d" % t), 0.1 * len(dsts))
         last = t == RO - 1
-        dd = sc[0:32, 0:XH]
-        lv = lambda i: B("live", XH * i, XH * i + XH, p1=32)
+        dd = sa[0:FR, 256:256 + XH]
         hk = [K("hit%d" % k) for k in range(NG)]
-        mm = [(dd, T.idn[0:32, 48:80], lv(t), True, False, XH)]
-        if last:
-            mm += [(dd, T.idn[0:32, 0:32], lv(i), False, False, XH) for i in range(RO)]
-        else:
-            mm.insert(0, (sc[0:32, XH:2 * XH], T.cc[0:1, 512:544], ones(XH), True, True, XH))
-        P(mm, ["idn0", "idn1", "cc4", "cc6"] + [K("live%d" % i) for i in range(t + 1)] + hk, [K("dd")], [scn])
-        s0, s1 = T.sel[:, 0:32:2], T.sel[:, 1:32:2]
-        key, k0, k1 = sm[0:36, 0:32], sm[0:NG, 0:32:2], sm[32:32 + NG, 1:32:2]
-        P([(key, T.idn[0:36, 0:36], T.kc[0:36, :], True, False, 36), (k0, acc, s0, False, False, 64), (k1, acc, s1, False, False, 64)],
+
+        def opening():
+            mm = [(dd, T.idn[0:FR, 128:128 + FR], lv(t), True, False, XH)]
+            if last:
+                mm += [(dd, T.idn[0:FR, 0:FR], lv(i), False, False, XH) for i in range(RO)]
+            elif t == 0:
+                mm.insert(0, (sa[0:FR, 256 + XH:256 + 2 * XH], T.cc[0:1, 0:FR], ones(XH), True, True, XH))
+            P(mm, ["idn0", "idn1", "cc4", "cc6"] + [K("live%d" % i) for i in range(t + 1)] + hk[:2], [K("dd")], [san])
+        if NP == 2:
+            opening()
+        s0, s1, kr = T.sel[:, 0:16], T.sel[:, 16:32], 32 + NG
+        key, k0, k1 = sm[0:kr, 0:32], sm[0:NG, 0:16], sm[32:kr, 16:32]
+        P([(key, T.idn[0:kr, 0:kr], T.kc[0:kr, :], True, False, kr), (k0, acc, s0, False, False, 64), (k1, acc, s1, False, False, 64)],
           ak + ["kc", "kc32", "idn0"] + sk, [K("key")], [smn])
-        P([(k0, inc, s1, False, False, 64), (k1, ina, s0, False, False, 64), (key, T.idn[0:36, 0:36], T.kc[0:36, :], False, True, 36)],
+        P([(k0, inc, s1, False, False, 64), (k1, ina, s0, False, False, 64), (key, T.idn[0:kr, 0:kr], T.kc[0:kr, :], False, True, kr)],
           [K("in%d" % t)], [K("key")], [smn])
-        mx = B("mx", 0, 1, p1=36)
+        mx = B("mx", 0, 1, p1=kr)
         V(lambda v: v.tensor_reduce(mx, key, AxisListType.X, A.max, negate=True), 32, [K("key")], [K("mx")], [smn])
-        op({"V": (lambda g: g.vector.tensor_scalar(B("wt", p1=36), key, mx, -1.0, A.add, A.max), vc(32)),
-            "S": (lambda g: g.scalar.activation(B("wt", p1=36), key, F.Sign, bias=mx), ac(32))}, [K("key"), K("mx"), "wtz"], [K("wt")], [smn])
-        P([(sm[32 * q:32 * q + 32, 32:32 + 4 * NG], B("wt", p1=37), T.ee[0:37, R3 - NG * q:R3 - NG * q + 4 * NG], True, True, 32) for q in range(4)],
+        op({"V": (lambda g: g.vector.tensor_scalar(B("wt", p1=kr), key, mx, -1.0, A.add, A.max), vc(32)),
+            "S": (lambda g: g.scalar.activation(B("wt", p1=kr), key, F.Sign, bias=mx), ac(32))}, [K("key"), K("mx"), "wtz"], [K("wt")], [smn])
+        P([(sm[32 * q:32 * q + 32, 32:64], B("wt", p1=kr + 1), T.ee[0:kr + 1, 24 - 8 * q:56 - 8 * q], True, True, 32) for q in range(4)],
           [K("wt"), "ee0", "ee1"], [K("w")], [smn])
-        lin(B("wq", 112, 112 + 4 * NG), sm[:, 32:32 + 4 * NG], 1.0, 0.0, 16, [K("w")], [K("wq")], [smn])
-        yc = sm[0:NG, 48 + t:96:3]
-        P([(yc, acc, s0, True, False, 64), (yc, inc, s1, False, True, 64)], [K("in%d" % t), K("w")], [K("yc%d" % t)], [smn])
+        yc = sm[0:NG, YC + t:YC + 48:3]
+        ycs = lambda: P([(yc, acc, s0, True, False, 64), (yc, inc, s1, False, True, 64)], [K("in%d" % t), K("w")] + [K("dd")] * (NP == 2 and not last), [K("yc%d" % t)], [smn])
+        if NP == 1:
+            ycs()
+            opening()
+        lin(B("wq", 112, 144), sm[:, 32:64], 1.0, 0.0, 32, [K("w")], [K("wq")], [smn])
+        if NP == 2 and last:
+            ycs()
         mm = []
         for k in range(NG):
-            for u in range(NU):
-                a0 = 112 - 31 * k - 4 * NG * u
-                mm.append((dd, B("wq", a0, a0 + 32 * NG, NG), B("hit", 128 * k + u, 128 * k + 128, NU), False, False, XH))
-        mm.append((dd, T.cc[0:1, 512:544], ones(XH), False, True, XH))
-        P(mm, [K("wq"), "cc4", "cc6"] + hk, [K("dd")], [scn])
+            for f in range(2):
+                a0 = 112 - 31 * k - 4 * f
+                mm.append((dd, B("wq", a0, a0 + 4 * FR, 4), B("hit", 128 * k + XH * f, 128 * k + XH * f + XH), False, False, XH))
+        mm.append((dd, T.cc[0:1, 0:FR], ones(XH), False, True, XH))
+        P(mm, [K("wq"), "cc4", "cc6"] + hk, [K("dd")], [san])
+        if NP == 2 and not last:
+            ycs()
         if last:
             tag[0] = "end"
-            lin(B("yco", p1=NG), sm[0:NG, 48:96], 1.0 / 32, 512.0, 48, [K("yc%d" % i) for i in range(RO)], [K("yco")], [smn])
-            D("YS", T.yc[RG * h:RG * h + RG, :], B("yco", p1=NG), 1, [K("yco")], [K("oc")])
-            lin(B("age", p1=32), dd, 1.0, -C0, XH, [K("dd")], [K("age")], [scn])
-            D("YS", T.ya[NG * h:NG * h + NG, :], B("age", p1=32), 8, [K("age")], [K("oa")])
+            lin(B("age", p1=FR), dd, 1.0, -C0, XH, [K("dd")], [K("age")], [san])
+            D("YS", T.ya[NG * h:NG * h + NG, :], B("age", p1=FR), 2 * NG, [K("age")], [K("oa")])
+            lin(B("yco", p1=NG), sm[0:NG, YC:YC + 48], 1.0 / 32, 512.0, 48, [K("yc%d" % i) for i in range(RO)], [K("yco")], [smn])
+            D("YS", T.yc[16 * NG * h:16 * NG * h + 16 * NG, :], B("yco", p1=NG), 1, [K("yco")], [K("oc")])
         else:
-            V(lambda v: v.tensor_tensor_scan(B("cum", p1=32), sc[0:32, 0:2 * XH], T.zer[0:32, :], 0.0, A.add, A.add), 2 * XH,
-              [K("dd"), "zer"], [K("cum")], [scn])
-            lin(lv(t + 1), dd, 1.0, -C0, XH, [K("dd")], [K("live%d" % (t + 1))] + ([K("livez")] if t == 0 else []), [scn])
+            V(lambda v: v.tensor_tensor_scan(B("cum", p1=FR), sa[0:FR, 256:256 + 2 * XH], T.zer[0:FR, :], 0.0, A.add, A.add), 2 * XH,
+              [K("dd"), "zer"], [K("cum")], [san])
+            lin(lv(t + 1), dd, 1.0, -C0, XH, [K("dd")], [K("live%d" % (t + 1))] + ([K("livez")] if t == 0 else []), [san])
 
     for h in range(NS):
         half[0] = h
         tag[:] = "load", 0, h
-        if h:
-            loads(h)
         setup(h)
         front(h, 0)
-    tag[:] = "load", 0, NS
-    table(1, 1, ["prin00"])
+        tag[:] = "load", 0, NS + h
+        for p in range(1, 4):
+            for u in range(4):
+                if GATES.get((p, u), "")[-1:] == str(h):
+                    table(p, u)
     half[0] = 0
     tag[:] = "limits", 0, 0
-    P([(T.ps1[32 * q:32 * q + 32, 112:120], T.thf[0:8, :], T.sel[0:8, 0:8], True, True, 128) for q in range(4)], ["thf0", "thf1", "sel0"], ["thp"], ["ps1"])
-    lin(T.thb[:], T.ps1[:, 112:120], -1.0 / 16, 0.5, 8, ["thp"], ["thb"], ["ps1"])
+    b = PXB[5]
+    P([(T[b][32 * q:32 * q + 32, 500:508], T.thf[0:8, :], T.sel[0:8, 0:8], True, True, 128) for q in range(4)], ["thf0", "thf1", "sel0"], ["thp"], [b])
+    lin(T.thb[:], T[b][:, 500:508], -1.0 / 16, 0.5 - LIVE, 8, ["thp"], ["thb"], [b])
     for t in range(RO):
         for h in range(NS):
             half[0] = h
             back(h, t)
             if t + 1 < RO:
                 front(h, t + 1)
-    return ops
+    after = [dict(o, r=o["r"] + ["mv00"]) for o in ops if o["w"][0].startswith(AFTER)]
+    ops = [o for o in ops if not o["w"][0].startswith(AFTER)]
+    k = [o["w"][0] for o in ops].index("mvin00") + 1
+    return ops[:k] + after + ops[k:]
 
 
 def depend(ops):
@@ -422,7 +484,7 @@ def depend(ops):
         d = {}
         for k in o["r"]:
             if k in lastw:
-                d[lastw[k]] = "S" if "blank" in o else True
+                d[lastw[k]] = "S" if "blank" in o and k == "zs" else True
         for k in o["w"]:
             if k in lastw:
                 d.setdefault(lastw[k], False)
@@ -454,7 +516,7 @@ def joins(ops, i, j):
     if i is None or "gat" not in ops[i] or "gat" not in ops[j]:
         return False
     (f, s, c), (f2, s2, c2) = ops[i]["gat"], ops[j]["gat"]
-    return f is f2 and s == s2 and c2 - c == 1 and block(s, c) == block(s, c2) and c // JOIN == c2 // JOIN
+    return f is f2 and s == s2 and c2 - c == STEP and block(c) == block(c2)
 
 
 def join(ops, deps, seq, eng):
@@ -469,32 +531,35 @@ def join(ops, deps, seq, eng):
             new[head[i]][head[j]] = raw
         if head[i] != i:
             f, s, c = ops[head[i]]["gat"]
-            ops[head[i]] = dict(ops[head[i]], alts=f(s, c, ops[i]["gat"][2] + 1))
+            ops[head[i]] = dict(ops[head[i]], alts=f(s, c, ops[i]["gat"][2] + STEP))
     return ops, new, [i for i in seq if head[i] == i]
 
 
-LOOKS, BACKS, TURNS, GLUE = (0.2,), (0.0,), ((9.0, 3.0), (8.0, 3.5)), 0.5
+AHEAD = {"px00_0": 2.0, "px01_0": 1.5, "pfl": 1.5, "mv00": 0.7, "mv01": 4.0, "thb": 3.0, "off001": 1.5, "off011": 1.5, "off101": 2.0, "off111": 2.0, "px10_0": 1.0, "px11_0": 1.0}
+LOOK, TURNS, GLUE = 0.2, ((8.5, 3.0), (7.5, 3.0)) if NP == 2 else ((4.2, 1.0, 3.5), (3.8, 1.0, 3.0)), 0.5
 
 
-def order(ops, deps, hop, look, back, stag, passes):
+def order(ops, deps, hop, look, stag, passes):
     n = len(ops)
     succ = [[] for _ in range(n)]
     for i in range(n):
         for j in deps[i]:
             succ[j].append(i)
     lat = [o["lat"] + o.get("move", 0.0) for o in ops]
-    t0, tl, td = stag
-    late, turn = [t0 + (5 + o["h"]) * tl + 7.0 for o in ops], {}
+    t0, tl, td = stag[:3]
+    late, turn = [t0 + (2 * NS + 1 + o["h"]) * tl + 7.0 for o in ops], {}
     for o in ops:
         if "gat" in o:
             turn.setdefault(o["gat"][0], len(turn))
     for i in range(n - 1, -1, -1):
         c = min(a[1] for a in ops[i]["alts"].values()) + lat[i] + hop[0]
-        late[i] = min([late[k] for k in succ[i]] + [late[i]]) - c - back
+        late[i] = min([late[k] for k in succ[i]] + [late[i]]) - c - AHEAD.get(ops[i]["w"][0], 0.0)
         if "gat" in ops[i]:
             f, s, k = ops[i]["gat"]
             u = k / NCH
             late[i] = t0 + turn[f] * tl + (td + u * (tl - 0.5 - td) if s else u * td)
+            if stag[3:]:
+                late[i] = t0 + turn[f] * tl + u * td + s * (tl * 1.5)
     prio = [1000.0 - i if not deps[i] and "move" in ops[i] else -x for i, x in enumerate(late)]
     fixed = [1000.0 - i if fwd_only else 0.0 for i, fwd_only in enumerate(not deps[i] and "move" in ops[i] for i in range(n))]
     cheap = [min(a[1] for a in o["alts"].values()) for o in ops]
@@ -529,7 +594,7 @@ def order(ops, deps, hop, look, back, stag, passes):
                 pick = max((x for x in near if "gat" in ops[x[1]]), key=lambda x: (prio[x[1]] + (GLUE if glue(x) else 0.0), -x[0] - x[3]))
             t0, i, e, c = pick
             if fwd and joins(ops, last.get(e), i) and t0 == free[e]:
-                c -= 0.055
+                c -= CALL
             last[e] = i
             if e != "N":
                 free[e] = t0 + c
@@ -639,7 +704,7 @@ def timer(plans, deps, hops):
             if k == 0:
                 free[e] = end[i] = t + co[i][e]
             elif k == 1:
-                free[e] = x = t + co[i][e] * len(mem) - 0.055 * (len(mem) - 1)
+                free[e] = x = t + co[i][e] * len(mem) - CALL * (len(mem) - 1)
                 for j in mem:
                     end[j], start[j], why[j] = x, t, w
             elif k == 2:
@@ -729,7 +794,7 @@ def refine(plans, deps, hops, seq, eng, iters, temp, early, seed=1):
             if k == i or not joins(ops, j, i) or "gat" not in ops[k] or eng[i] not in ops[k]["alts"] or eng[k] not in ops[i]["alts"]:
                 continue
             swap = (i, k)
-        elif r < FILL + TRADE + 0.1:
+        elif r < FILL + TRADE + 0.1 or not arcs:
             i = int(rnd() * n)
             same = [k for k in seq[max(0, pos[i] - 30):pos[i]] if eng[k] == eng[i]][-3:]
             if eng[i] == "N" or not same:
@@ -742,7 +807,7 @@ def refine(plans, deps, hops, seq, eng, iters, temp, early, seed=1):
         if load[i] or load[j]:
             continue
         r, ns, ne, moved = rnd(), seq, eng, []
-        turns = range(-5, 6) if rnd() < ALIKE else (0,)
+        turns = range(1 - RO * NS, RO * NS) if rnd() < ALIKE else (0,)
         if isinstance(swap, tuple):
             ns, ne = list(seq), list(eng)
             for d in turns:
@@ -801,45 +866,28 @@ def refine(plans, deps, hops, seq, eng, iters, temp, early, seed=1):
     return best[1], best[2], run(steps(best[1], best[2]), 0)[0]
 
 
-def unify(ops, deps, eng, start, ref):
-    n = len(ops)
-    tags = {o["tag"]: i for i, o in enumerate(ops) if o["tag"][0] in ("front", "back")}
-    mark = [start[tags["back", 0, d]] for d in range(RO * NS)]
-    span = (mark[4] - mark[2]) / 2
-    eng, key = list(eng), list(start)
-    for i, o in enumerate(ops):
-        part, k, d = o["tag"]
-        j = tags.get((part, k, ref))
-        if j is not None and (part, d) != ("front", 0):
-            eng[i], key[i] = eng[j], start[j] + (d - ref) * span
-        elif part == "end":
-            key[i] += mark[ref] + (d - ref) * span - mark[d]
-    succ, left = [[] for _ in ops], [len(d) for d in deps]
-    for i in range(n):
-        for j in deps[i]:
-            succ[j].append(i)
-    ready, seq = {i for i in range(n) if not left[i]}, []
-    while ready:
-        i = min(ready, key=lambda k: (key[k], k))
-        ready.remove(i)
-        seq.append(i)
-        for k in succ[i]:
-            left[k] -= 1
-            if not left[k]:
-                ready.add(k)
-    return seq, eng
-
-
 SETS = [dict(COST, f=1.08, pc=0.54e-3, gath=1.12e-3, hop=0.12, same=0.24, net=1.5, load=0.55, aim=60.0),
-        dict(COST, f=1.0, pc=0.52e-3, gath=0.9e-3, hop=0.12, same=0.2, net=1.2, load=0.4, bw=420e3, scat=2e-3, aim=54.0),
-        dict(COST, f=1.25, pc=0.48e-3, gath=1.05e-3, hop=0.1, same=0.2, net=1.0, load=1.0, aim=66.5),
+        dict(COST, f=1.0, pc=0.52e-3, gath=0.9e-3, hop=0.12, same=0.2, net=1.2, load=0.4, bw=420e3, aim=53.5),
+        dict(COST, f=1.25, pc=0.48e-3, gath=1.05e-3, hop=0.1, same=0.2, net=1.0, load=0.85, aim=63.0),
         dict(COST, f=1.15, pc=0.56e-3, gath=1.4e-3, hop=0.16, same=0.28, net=2.1, first=2.0, load=0.6, bw=270e3, dma=0.2, aim=71.5),
-        dict(COST, f=1.45, pc=0.72e-3, gath=1.65e-3, hop=0.14, same=0.25, net=1.6, scat=4.5e-3, load=0.5, aim=79.0)]
+        dict(COST, f=1.45, pc=0.72e-3, gath=2.1e-3, hop=0.14, same=0.25, net=1.6, load=0.5, aim=88.0)]
 POWER = 12
-STARTS, SHORT = 4, 12000
-ITERS, TEMP, EARLY, ALIKE, FILL, TRADE, SHARE = 90000, 0.0004, 0.1, 0.2, 0.35, 0.2, 1.5
-SHIFTED = ("pair1", "sel1", "sel2", "sel3", "kc32", "ee1", "wtz", "lcz", "livey", "ltz", "cumz")
+STARTS, SHORT = 4, 10000
+ITERS, TEMP, EARLY, ALIKE, FILL, TRADE, SHARE = 120000, 0.0008, 0.1, 0.2, 0.35, 0.2, 1.5
+SHIFTED = ("lcz1", "lcz2", "lcz3", "cumz", "sel1", "sel2", "sel3", "kc32", "ee1", "wtz")
 ORDER = {}
+
+
+def schedule(T, rank, topo, deps):
+    plans = [plan(T, rank, topo, c) for c in SETS]
+    hops = [(c["hop"], c["same"]) for c in SETS]
+    steps, run, _pre = timer(plans, deps, hops)
+    starts = [order(plans[m], deps, hops[m], LOOK, (6.5,) + tt, passes) for m in (0, 3) for tt in TURNS for passes in (0, 1)]
+    value = lambda a: sum((max(run(steps(a[0], a[1]), m)[0]) / c["aim"]) ** POWER for m, c in enumerate(SETS))
+    starts = sorted(starts, key=value)[:STARTS]
+    starts = [refine(plans, deps, hops, a[0], a[1], SHORT, TEMP, EARLY, k + 1) for k, a in enumerate(starts)]
+    seq, eng, _end = min(starts, key=value)
+    return refine(plans, deps, hops, seq, eng, ITERS, TEMP / 2, EARLY)
 
 
 def rank_program(g, core, T, topo):
@@ -849,16 +897,7 @@ def rank_program(g, core, T, topo):
     ops = plan(T, rank, topo)
     deps = depend(ops)
     if not ORDER:
-        plans = [plan(T, rank, topo, c) for c in SETS]
-        hops = [(c["hop"], c["same"]) for c in SETS]
-        steps, run, _pre = timer(plans, deps, hops)
-        starts = [order(plans[m], deps, hops[m], look, back, (6.5, tl, td), passes)
-                  for m in (0, 3) for look in LOOKS for back in BACKS for tl, td in TURNS for passes in (0, 1)]
-        value = lambda a: sum((max(run(steps(a[0], a[1]), m)[0]) / c["aim"]) ** POWER for m, c in enumerate(SETS))
-        starts = sorted(starts, key=value)[:STARTS]
-        starts = [refine(plans, deps, hops, a[0], a[1], SHORT, TEMP, EARLY, k + 1) for k, a in enumerate(starts)]
-        seq, eng, _end = min(starts, key=value)
-        ORDER["seq"], ORDER["eng"], ORDER["end"] = refine(plans, deps, hops, seq, eng, ITERS, TEMP / 2, EARLY)
+        ORDER["seq"], ORDER["eng"], ORDER["end"] = schedule(T, rank, topo, deps)
     eng, end = ORDER["eng"], ORDER["end"]
     ops, deps, seq = join(ops, deps, ORDER["seq"], eng)
     own = [i for i in seq if eng[i] == "G" and ops[i]["kind"] == "c"]

import math
from concourse.bass import DstId, RemoteDMATransfer
from concourse.mybir import dt, AluOpType, AxisListType, ActivationFunctionType

A = AluOpType
F = ActivationFunctionType
RO = 3
NP = 2
NS, NG = 4 // NP, 2 * NP
W, XH, FR = 128 * NP, 64, 8 * NG
NCH = 8 * NP
STEP = 2
BLK = ((4, 4), (4, 2, 2))[:NP]
CASTS = ((8,), (8,)) if NP == 1 else ((4, 16), (4, 16))
CN, PR, YC = (64, 128, 448) if NP == 1 else (256, 256, 64)
PLACES = ("ps5", "ps6", "ps7")[NP - 1:]
PXB = ((("ps4", "ps5"), ("ps4", "ps3"), ("ps4", "ps3"), ("ps4", "ps4"), "ps2", "ps3", "ps1"), (("ps3", "ps0"), ("ps5", "ps4"), ("ps3", "ps3"), ("ps3", "ps3"), "ps0", "ps2", "ps1"))[NP - 1]
SCN = 1
TAB = 4112
KR = 128
C0 = 12582912.0
LIVE = 8192.0
COST = {"fix": 0.08, "f": 1.1, "pc": 0.48e-3, "gath": 1.25e-3, "hop": 0.07, "net": 1.6, "first": 1.0, "send": 0.25,
        "dfix": 1.8, "dma": 0.1, "bw": 350e3, "row": 0.015, "load": 0.5}
WIDE = ("ac3", "sel")
GATES = {(_p, _u): "mvin00" if _p == 3 else "mv00" for _p in range(1, 4) for _u in range(4) if _p > 1}
CALL = 0.09
ZDMA = (None, None)
LATE = ("wq0", "wq1", "wq2", "wq3", "zer", "wtz", "ee0", "tabz0", "tabz1", "tabz2", "tabz3", "tabz4", "cc4", "cc6", "livez1", "pfz01", "pfz11", "pfz21", "pfz31")
AFTER = ("pn2", "pn3", "kc", "ee", "idn1", "wtz", "zer", "cc")

PART = {"gat": (32 * W, "bfloat16"), "px": (1024 * NP, "bfloat16"),
        "lvl": (XH, "int32"), "live": (4 * XH, "bfloat16"), "age": (XH, "float32"),
        "cum": (2 * XH, "bfloat16"), "cux": (XH, "bfloat16"), "ac3": (128, "float32"), "sl": (8, "uint16"),
        "prod": (64, "float16"), "mv": (16 * NP * RO, "float16"), "mvin": (16 * NP * RO, "float16"),
        "off": (2 * W, "uint16"), "hit": (128 * NG, "bfloat16"),
        "acc": (4 * RO, "float32"), "ina": (4 * RO, "float32"), "inc": (4 * RO, "float32"),
        "mx": (4, "float32"), "wt": (32, "bfloat16"), "wq": (112 + 4 * FR, "bfloat16"), "yco": (48, "float32")}
SCRATCH = {_n: ("sbuf", [128, NS * _c], _d) for _n, (_c, _d) in PART.items()}
for _j in range(8):
    SCRATCH["ps%d" % _j] = ("psum", [128, 512], "float32")
for _n, _c, _d in [("tab", 4 * TAB + 16, "bfloat16"), ("posl", 512, "bfloat16"), ("xy", 1056, "bfloat16"), ("pfn", 512, "bfloat16"),
                   ("pfl", 512, "bfloat16"), ("ip", 4, "int32"), ("ci", 8, "int32"), ("i48", 48, "float32"), ("iot", 32, "bfloat16"),
                   ("iou", 32, "bfloat16"), ("idn", 160, "bfloat16"), ("sel", 32, "float32"), ("th3", 192, "float16"),
                   ("ee", 56, "bfloat16"), ("lc", 576 + 80 * NS, "bfloat16"), ("rst", 128, "bfloat16"), ("cs", 16, "float32"),
                   ("kc", 32, "bfloat16"), ("cc", 256, "bfloat16"),
                   ("thl", 16, "int32"), ("thf", 32, "float32"), ("thb", 8, "float32"), ("sgn", 16, "bfloat16"),
                   ("zer", 2 * XH, "bfloat16"), ("zs", 512, "bfloat16"), ("mul", 104, "bfloat16"), ("rows", 192, "bfloat16"),
                   ("vb", 8, "float32"), ("d2", 416, "bfloat16"), ("selx", 256, "bfloat16"), ("posq", 2048, "bfloat16"), ("k18", 160, "bfloat16"),
                   ("zz", 320, "bfloat16"), ("pn", 256 * NG, "bfloat16"), ("pfb", 4096, "bfloat16")]:
    SCRATCH[_n] = ("sbuf", [128, _c], _d)

SEMAPHORES = ["eV", "eS", "eP", "eG", "sent"] + ["d%d" % i for i in range(70)] + ["r%d" % i for i in range(6 * NS)]

FIRST = -16.0
STEPS = [((7, 70, 10), 0.125), ((8, 70, 10), 2.0 ** 14), ((9, 70, 10), -1.0), ((10, 40, 10), -2.0 ** -12), ((40, 41, 1), 2.0 ** -16), ((50, 70, 10), -2.0 ** -15)]
TILES = [(0, (0, 0), (0, 0), (0, 0)), (10, (0, 0), (0, 9), (1, 7)), (40, (1, 0), (1, 28), (1, 40)), (40, (0, 0), (0, 0), (0, 0))]


def block(c):
    a, c0 = c // 8, 0
    for b in BLK[a]:
        if c % 8 < c0 + b:
            return a, c0, b
        c0 += b


def plan(T, rank, topo, cost=COST):
    ops = []
    half = [0]
    tag = ["setup", 0, 0]
    n = len(T.cores)
    core = T.cores[rank]
    FX, PC = cost["f"], cost["pc"]
    CY = 0.83e-3 * FX

    def op(alts, r=(), w=(), ps=(), kind="c", lat=0.0):
        ops.append({"alts": alts, "r": list(r), "w": list(w), "ps": list(ps), "kind": kind, "lat": lat, "h": half[0], "tag": tuple(tag)})
        tag[1] += 1

    def vc(k, half=False):
        return cost["fix"] + max(64, k / 2 if half else k) * CY

    def ac(k):
        return cost["fix"] + 0.015 + max(64, k) * CY

    def gc(k, fix):
        return fix * FX + 2 * k * CY

    def V(fn, k, r, w, ps=(), half=False):
        op({"V": (lambda g: fn(g.vector), vc(k, half))}, r, w, ps)

    def S(fn, k, r, w, ps=()):
        op({"S": (lambda g: fn(g.scalar), ac(k))}, r, w, ps)

    def iota(out, pat, base, cm, w, r=()):
        k = out.shape[1]
        op({"G": (lambda g: g.iota(out, pat, base, cm, allow_small_or_imprecise_dtypes=True), gc(k, 0.13))}, r, w)

    def select(out, in_, pat, cmp, c, base, cm, r, w):
        op({"G": (lambda g: g.affine_select(out, in_, pat, cmp, c, base, cm), gc(out.shape[1], 0.17))}, r, w)

    def paint(out, zero, pat, c, base, w, r=()):
        select(out, zero, pat, A.not_equal, c, base, 1, ["zs"] + list(r), w)

    def fill(out, c, w, p=None, r=()):
        k = out.shape[1]
        alts = {"V": (lambda g: g.vector.memset(out, c), vc(k, True))}
        if c == int(c) and abs(c) < 2 ** 24:
            alts["G"] = (lambda g: g.iota(out, [[0, k]], int(c), 0, allow_small_or_imprecise_dtypes=True), gc(k, 0.13))
        if p:
            alts["S"] = (lambda g: g.scalar.activation(out, T.zs[p[0]:p[1], 0:k], F.Identity, bias=c, scale=0.0), ac(k))
        if w[0] in LATE:
            alts = {"G": alts["G"]}
        op(alts, (["zs"] if p else []) + list(r), w)
        ops[-1]["blank"] = True

    def lin(out, in_, mul, add, k, r, w, ps=(), half=False):
        def fs(g):
            if isinstance(add, float) and add == 0.0:
                return g.scalar.activation(out, in_, F.Copy if isinstance(mul, float) else F.Identity, scale=mul)
            return g.scalar.activation(out, in_, F.Identity, bias=add, scale=mul)
        op({"V": (lambda g: g.vector.tensor_scalar(out, in_, mul, add, A.mult, A.add), vc(k, half)), "S": (fs, ac(k))}, r, w, ps)

    def P(mms, r, w, ps):
        def fn(g):
            last = None
            for o, l, rh, st, sp, _c in mms:
                last = g.tensor.matmul(o, l, rh, st, sp)
            return last
        op({"P": (fn, sum(max(m[5] * cost["load"], min(m[5], m[2].shape[1] * (4 if m[2].name in WIDE else 1))) for m in mms) * PC)}, r, w, ps)

    def D(q, out, in_, kb, r, w):
        fn = {"Y": lambda g: g.sync.dma_start(out, in_), "S": lambda g: g.scalar.dma_start(out, in_)}
        op({e: (fn[e], cost["dma"]) for e in q}, r, w, kind="d", lat=cost["dfix"])
        ops[-1]["move"] = kb * 1024 / cost["bw"] + max(16, out.shape[0]) / 16 * cost["row"]

    def part(h):
        def B(name, a=0, b=None, st=1, p0=0, p1=128):
            c = PART[name][0]
            return T[name][p0:p1, c * h + a:c * h + (c if b is None else b):st]
        return B, (lambda s: s + str(h)), ["ps%d" % (3 * h + i if NP == 2 else h) for i in range(3)]

    def table(p, u, q="Y"):
        D(q, T.tab[32 * u:32 * u + 32, TAB * p + 16:TAB * p + TAB], T.rf[32 * p:32 * p + 32, :], 256,
          [GATES[p, u]] if (p, u) in GATES else [], ["tab%d%d" % (p, u)])

    flags = lambda q, h: D(q, T.lvl[0:FR, XH * h:XH * h + XH], T.lv[NG * h:NG * h + NG, :], 2 * NG, [], ["lvl%d" % h])
    flags("Y", 0)
    D("S", T.posl[0:24, :], T.pos[:], 24, [], ["posl"])
    pairs = lambda p: D("Y", T.posq[0:6, 512 * p:512 * p + 512], T.pos[6 * p:6 * p + 6, :], 6, [], ["posq%d" % p])
    pairs(1)
    D("Y", T.pfn[:], T.pf[:], 128, [], ["pfn"])
    for u in range(4):
        table(0, u)
    for h in range(1, NS):
        flags("Y", h)
    pairs(2)
    pairs(3)
    D("Y", T.thl[0:8, :], T.th[:], 1, [], ["thl"])
    for p in range(1, 4):
        for u in range(4):
            if (p, u) not in GATES:
                table(p, u)

    V(lambda v: v.memset(T.zs[:], 0.0), 512, [], ["zs"], half=True)
    op({"G": (lambda g: g.iota(T.ip[:], [[32, 4]], 0, 1), gc(4, 0.13))}, [], ["ip"])
    iota(T.iou[0:FR, 0:FR], [[1, FR]], 0, -1, ["iou"])
    select(T.iot[0:FR, 0:FR], T.iou[0:FR, 0:FR], [[-8, NG], [0, 8]], A.is_ge, -100.0, 0, 1, ["iou"], ["iot"])
    iota(T.i48[:], [[2, 48]], -1023, 0, ["i48"])
    iota(T.d2[0:24, 0:160], [[0, 5], [30, 8], [1, 4]], 0, -1, ["d2"])
    iota(T.k18[:], [[0, 5], [16, 8], [1, 4]], 0, 0, ["k18"])
    iota(T.kc[0:32, :], [[-30000, 2], [-1, 16]], 0, 0, ["kc"])
    iota(T.kc[32:64, :], [[30000, 2], [-1, 16]], -30000, 0, ["kc32"])
    c15, c23 = T.ci[:, 0:1], T.ci[:, 1:3]
    V(lambda v: v.tensor_scalar(c15, T.ip[:, 0:1], 3, None, A.bitwise_and), 1, ["ip"], ["c15"])
    V(lambda v: v.tensor_scalar(c23, T.ip[:, 0:2], 55, None, A.bitwise_and), 1, ["ip"], ["c23"])
    V(lambda v: v.tensor_scalar(T.cs[:, 0:1], c15, 1.0, 2.0 ** -11, A.is_equal, A.mult), 1, ["c15"], ["cm"])
    V(lambda v: v.tensor_copy(T.cs[:, 1:3], c23), 1, ["c23"], ["cp"])
    V(lambda v: v.memset(T.lc[:], 0.0), 576 + 80 * NS, [], ["lc", "permz", "row1"] + ["fac%d" % h for h in range(NS)], half=True)
    for i, cmp in enumerate((A.is_equal, A.is_gt)):
        V(lambda v, i=i, cmp=cmp: v.tensor_scalar(T.lc[0:FR, 128 * i:128 * i + 4 * FR:4], T.iot[0:FR, 0:FR], 0.0, -2.0 ** -10, cmp, A.mult), 32, ["iot", "lc"], ["lc%d" % i])
    for i, c in ((1, 1.0), (2, C0), (3, -C0)):
        fill(T.lc[32:33, i:128:4], c, ["lcz%d" % i], (32, 33), ["lc"])
    if NP == 2:
        fill(T.cum[32:33, :], 1.0, ["cumz"], (32, 33))
    else:
        fill(T.cum[0:33, :], 1.0, ["cumy"] + ["cum%d" % h for h in range(NS)], (0, 33))
    V(lambda v: v.tensor_copy(T.th3[:], T.zs[:, 0:192]), 192, ["zs"], ["th3"], half=True)
    for q in range(NG):
        V(lambda v, q=q: v.tensor_scalar(T.th3[32 * q:32 * q + 32, 48 * q:48 * q + 48], T.i48[32 * q:32 * q + 32, :], T.cs[32 * q:32 * q + 32, 0:1], 1.0, A.mult, A.add),
          48, ["i48", "cm", "th3"], ["th3%d" % q])
    iota(T.rst[:], [[0, 4], [1024, 32]], 0, 0, ["rstz"])
    V(lambda v: v.memset(T.sl[:], 0), 16, [], ["sl%d" % h for h in range(NS)])
    fill(T.cc[0:1, 0:32], C0 / 2 ** 22, ["cc4"], (0, 1))
    fill(T.cc[0:1, 128:256], 2.0 ** 22, ["cc6"], (0, 1))
    ones = lambda k: T.cc[0:1, 128:128 + k]
    fill(T.mul[0:1, :], 1.0, ["mul"], (0, 1))
    for i, ((a, b, st), c) in enumerate(STEPS):
        fill(T.mul[0:1, a:b:st], c, ["mul%d" % i], (0, 1), ["mul"])
    V(lambda v: v.tensor_tensor_scan(T.rows[0:1, 0:72], T.mul[0:1, 0:72], T.zs[0:1, 0:72], FIRST, A.mult, A.add), 72,
      ["zs"] + ["mul%d" % i for i in range(len(STEPS))], ["row0"], half=True)
    for k, c in ((7, 1.875), (40, 2 * C0), (41, 2 * C0)):
        fill(T.lc[0:1, 512 + k:512 + k + 21:10], c, ["row1%d" % k], (0, 1), ["row1"])
    vcol, bcol, wcol, ucol = (T.vb[:, i:i + 1] for i in (0, 1, 3, 4))
    cell = lambda r, c: (T.mul, T.rows)[r][0:1, c:c + 1]
    mm = []
    for b, (x, fv, fo, fu) in enumerate(TILES):
        o = lambda i: T.ps1[32 * b:32 * b + 32, 384 + i:385 + i]
        mm += [(o(0), T.rows[0:1, x:x + 32], cell(*fv), True, True, 32), (o(1), T.lc[0:1, 512:544], cell(*fo), True, False, 32),
               (o(1), T.lc[0:1, 544:576], cell(0, 0), False, True, 32), (o(2), T.mul[0:1, 72:104], cell(*fu), True, True, 32)]
    P(mm, ["row0", "row17", "row140", "row141"], ["vbp"], ["ps1"])
    lin(T.vb[:, 0:3], T.ps1[:, 384:387], 1.0, 0.0, 3, ["vbp"], ["vb"], ["ps1"])
    V(lambda v: v.tensor_scalar(wcol, bcol, 0.0, vcol, A.not_equal, A.mult), 1, ["vb"], ["wcol"])
    V(lambda v: v.tensor_scalar(ucol, bcol, 0.0, T.vb[:, 2:3], A.is_equal, A.mult), 1, ["vb"], ["ucol"])
    for a in range(2):
        V(lambda v, a=a: v.tensor_scalar(T.zz[:, 160 * a:160 * a + 160], T.k18[:], T.cs[:, 2 - a:3 - a], -32.0, A.subtract, A.is_equal), 160,
          ["k18", "cp"], ["zz%d" % a], half=True)
    V(lambda v: v.tensor_tensor(T.d2[0:24, 160:288], T.d2[0:24, 32:160], T.d2[0:24, 22:150], A.min), 256, ["d2"], ["d2a"])
    V(lambda v: v.tensor_tensor(T.d2[0:24, 288:416], T.d2[0:24, 160:288], T.d2[0:24, 12:140], A.min), 256, ["d2a"], ["d2b"])
    for e in range(2):
        V(lambda v, e=e: v.tensor_scalar(T.selx[0:6, 128 * e:128 * e + 128], T.d2[0:6, 288:416], 27.0 * e, None, A.is_equal), 128, ["d2b"], ["selx%d" % e], half=True)
    iota(T.sgn[0:24, :], [[0, 8], [-2, 2]], 1, 0, ["sgn"])
    for c in range(3):
        a, b = (c + 1) % 3, (c + 2) % 3
        select(T.lc[0:24, 256 + c:384:8], T.sgn[0:24, :], [[-3, 8], [a - b, 2]], A.is_equal, 0.0, -a, 1, ["sgn", "permz"], ["perm0%d" % c])
        paint(T.lc[0:24, 384 + c:512:8], T.zs[0:24, 0:16], [[-3, 8], [b - a, 2]], 1.0, -b, ["perm1%d" % c], ["permz"])
    for i, bank in enumerate(("ps6", "ps7")):
        P([(T[bank][:], T.lc[0:24, 256 + 128 * i:384 + 128 * i], T.posl[0:24, :], True, True, 512)], ["posl"] + ["perm%d%d" % (i, c) for c in range(3)], [bank], [bank])
        lin(T.xy[:, 528 * i:528 * i + 512], T[bank][:], 1.0, 0.0, 512, [bank], [("xw", "yw")[i]], [bank])
    fill(T.xy[:, 512::528], 0.0, ["xyz"], (0, 128))
    for k in range(5):
        fill(T.tab[:, TAB * k:TAB * k + 16], -8388608.0, ["tabz%d" % k], (0, 128))
    paint(T.idn[:, 0:128], T.zs[:, 0:128], [[-1, 128]], 1.0, 0, ["idn0"])
    paint(T.idn[0:32, 128:160], T.zs[0:32, 0:32], [[-1, 32]], 0.375, 0, ["idn1"])
    for q in range(4):
        paint(T.sel[32 * q:32 * q + 32, :], T.zs[32 * q:32 * q + 32, 0:32], [[-1, 32]], 16.0, 0, ["sel%d" % q])
    sk = ["sel%d" % q for q in range(4)]
    fill(T.ee[0:64, :], 0.0, ["ee0", "ee1"])
    for a in range(2):
        paint(T.ee[32 * a:32 * a + 32, 24:24 + NG], T.zs[32 * a:32 * a + 32, 0:NG], [[-1, NG]], -0.1875, 0, ["ee%d" % a])
    select(T.ee[32:64, 24:24 + NG], T.ee[32:64, 24:24 + NG], [[0, NG]], A.not_equal, -0.375, -NG, 1, ["ee1"], ["ee1"])
    fill(T.wt[32:64, :], 1.0, ["wtz"])
    for s in range(2):
        V(lambda v, s=s: v.tensor_copy(T.thf[0:8, 16 * s:16 * s + 16], T.thl[0:8, :]), 16, ["thl"], ["thf%d" % s])
    fill(T.zer[0:32, :], -C0, ["zer"])
    for k in range(NG):
        paint(T.pn[0:FR, 256 * k:256 * k + 256], T.zs[0:FR, 0:256], [[-1, 2], [-2, 4], [0, 32]], LIVE, -8 * k, ["pn%d" % k])

    def positions(p, banks):
        B, K, _b = part(p // NP)
        for i, bank in enumerate(banks):
            P([(T[bank][:, 256 * v + 128 * e:256 * v + 128 * e + 128], T.selx[0:6, 128 * e:128 * e + 128],
                (T.posq[0:6, 512 * p + 2 * i + v:512 * p + 512:4] if p else T.posl[0:6, 2 * i + v:512:4]), True, True, 128) for v in range(2) for e in range(2)],
              ["posq%d" % p if p else "posl", "selx0", "selx1"], [bank], [bank])
            a = 1024 * (p % NP) + 512 * i
            lin(B("px", a, a + 512), T[bank][:], ucol, bcol, 512, [bank, "vb", "ucol"], [K("px%d%d_" % (p % NP, i))], [bank])

    def setup(h):
        B, K, _b = part(h)
        fill(B("live", XH, 2 * XH, p1=FR), 0.0, [K("livez")], (0, FR))
        V(lambda v: v.tensor_copy(B("live", 0, XH, p1=FR), B("lvl", p1=FR)), XH, [K("lvl")], [K("live0")])
        fill(B("wq"), 0.0, [K("wq")], (0, 128))
        for p in range(NP * h, NP * h + NP):
            positions(p, PXB[p])
        if h == 0:
            b = PXB[4]
            P([(T[b][32 * u:32 * u + 32, 128 * p:128 * p + 128], T.idn[:, 32 * p:32 * p + 32], T.pfn[:, u:512:4], True, True, 128)
               for p in range(4) for u in range(4)], ["pfn", "idn0"], [b], [b])
            lin(T.pfl[:], T[b][:], 1.0, 2.0 ** -10, 512, [b], ["pfl"], [b])
        if NP * h % 2:
            return
        j = NP * h // 2
        for a in range(4):
            z = T.pfb[:, 2048 * j + 512 * a:2048 * j + 512 * a + 512]
            if ZDMA[j]:
                D("Y", z, T.zs[:], 128, ["zs", ZDMA[j]], ["pfz%d%d" % (a, j)])
            else:
                fill(z, 0.0, ["pfz%d%d" % (a, j)])
        for q in range(8):
            D("Y", T.pfb[16 * q:16 * q + 16, 2048 * j + 256 * q:2048 * j + 256 * q + 256], T.pfl[16 * q:16 * q + 16, 256 * j:256 * j + 256], 8,
              ["pfl", "pfz%d%d" % (q // 2, j)], ["pfb%d%d" % (q, j)])

    nrem, nblk = [0], [0]

    def send(src, dsts, key, land, us):
        sem = T.sem["r%d" % nrem[0]]
        nrem[0] += 1
        mask = topo.mask(core, dsts[0][0])
        for d, _ap in dsts:
            mask &= topo.mask(core, d)
        ne = bin(mask).count("1")

        def fn(g):
            ids = [DstId(rid=topo.addr(d)[0], pnc=topo.addr(d)[1]) for d, _ap in dsts]
            tr = RemoteDMATransfer(dst_ids=ids, dma_engine_mask=mask, remote_sem=sem, src=src, dsts=[ap for _d, ap in dsts])
            g.remote_dma_fused([tr], local_sem=T.sem.sent)
            return ne
        op({"G": (fn, cost["send"])}, key, [land + "s"], kind="s")
        op({"N": ((sem, ne * len(dsts)), 0.0)}, [land + "s"], [land], kind="a", lat=cost["net"] + us + (cost["first"] if nrem[0] == 1 else 0.0))

    def front(h, t):
        B, K, (san, sbn, smn) = part(h)
        sb, sm = T[sbn], T[smn]
        if t == 0:
            live = B("live", 0, 2 * XH, p1=FR)
            V(lambda v: v.tensor_tensor_scan(B("cum", p1=FR), live, live, 0.0, A.add, A.max), 2 * XH, [K("live0"), K("livez")], [K("cum")], half=True)
        tag[:] = "front" if t + h else "first", 0, NS * t + h
        cn = sm[0:4 * FR, CN:CN + XH]
        P([(cn, T.lc[0:k, 128 * i:128 * i + 4 * FR], B("cum", XH * i, XH * i + XH, p1=k), i == 0, i == 1, 64) for i, k in enumerate((33, FR))],
          [K("cum"), "cumz", "lc0", "lc1", "lcz1", "lcz2", "lcz3"], [K("cn")], [smn])
        lin(B("cux", p1=4 * FR), cn, 1.0, 0.0, XH, [K("cn")], [K("cux")], [smn])
        p0, p1 = 16 * NG * h, 16 * NG * h + 16 * NG
        P([(sb[p0:p1, PR + 32 * b:PR + 32 * b + 32], T.th3[0:4 * FR, i:48 * NG:3], B("cux", 32 * f, 32 * f + 32, p1=4 * FR), f == 0, f == 1, 16 * NG)
           for b, i in enumerate((1, 2, 0, 1)) for f in range(2)], [K("cux")] + ["th3%d" % q for q in range(NG)], [K("pr")], [sbn])
        V(lambda v: v.tensor_tensor_scan(B("ac3", p0=p0, p1=p1), T.rst[p0:p1, :], sb[p0:p1, PR:PR + 128], 0.0, A.min, A.add), 128, [K("pr"), "rstz"], [K("ac3")], [sbn])
        V(lambda v: v.tensor_copy(B("sl", 0, 4, 1, p0, p1), B("ac3", 31, 128, 32, p0, p1)), 4, [K("ac3")], [K("sl")])
        x = 576 + 80 * h
        o, w, us = T.lc[:, x:x + 64], T.xy[:, 528:1041].indirect(B("sl", 0, 4)), 64 * cost["gath"]
        op({"V": (lambda g: g.vector.tensor_copy(o, w), 0.05 + us), "S": (lambda g: g.scalar.activation(o, w, F.Copy), 0.065 + us)},
           [K("sl"), "yw", "xyz"], [K("fac")])
        fb = T.lc[:, x + 16:x + 80]
        op({"V": (lambda g: g.vector.tensor_tensor(B("prod"), T.xy[:, 0:513].indirect(B("sl", 0, 4)), fb, A.mult), 0.06 + us)},
           [K("sl"), "xw", "xyz", K("fac")], [K("prod")])
        r0, x0, x1 = 64 * (NP * h // 2), 16 * NP * t, 16 * NP * t + 16 * NP
        P([(sb[:, 400 + 16 * a:416 + 16 * a], T.zz[r0:r0 + 64, x + 32 - 10 * j:x + 160 - 10 * j], B("prod", 16 * j, 16 * j + 16, 1, r0, r0 + 64), j == 0, j == 2, 64)
           for a, x in enumerate(160 * (p % 2) for p in range(NP * h, NP * h + NP)) for j in range(3)],
          [K("prod"), "zz0", "zz1"], [K("ax")], [sbn])
        mk = "mv%d%d" % (t, h)
        V(lambda v: v.tensor_scalar(B("mv", x0, x1), sb[:, 400:400 + 16 * NP], vcol, wcol, A.mult, A.add), 32, [K("ax"), "vb", "wcol"], [mk], [sbn])
        send(B("mv", x0, x1), [(T.cores[(rank + t + 1) % n], B("mvin", x0, x1))], [mk], K("mvin%d" % t), 0.2)
        for s in range(2):
            for i, (k0, k1) in enumerate(zip((0,) + CASTS[s], CASTS[s])):
                bank = PLACES[nblk[0] % len(PLACES)]
                nblk[0] += 1
                mm = []
                for k in range(k0, k1):
                    a, c0, b = block(k)
                    x = 16 * (8 * a + c0 - k0)
                    mm.append((T[bank][:, x + k % 8 - c0:x + 16 * b:b], B("px", 1024 * a + k % 8, 1024 * a + 1024, 8),
                               B(("mv", "mvin")[s], x0 + 16 * a, x0 + 16 * a + 16), True, True, 64))
                P(mm, [K("mvin%d" % t) if s else mk] + [K("px%d%d_" % (a, j)) for a in range(k0 // 8, (k1 + 7) // 8) for j in range(2)], ["pl" + bank], [bank])
                V(lambda v, x=W * s + 16 * k0, w=16 * (k1 - k0), bank=bank: v.tensor_scalar(B("off", x, x + w), T[bank][:, 0:w], 16.0, float(TAB), A.add, A.min),
                  16 * (k1 - k0), ["pl" + bank], [K("off%d%d" % (s, i))], [bank])

    def back(h, t):
        B, K, (san, sbn, smn) = part(h)
        sa, sm = T[san], T[smn]
        tag[:] = "back", 0, NS * t + h
        lv = lambda i: B("live", XH * i, XH * i + XH, p1=FR)

        def gather(s, c0, c1):
            a, b0, b = block(c0)
            x = 4096 * a + 512 * b0 + 256 * (b * s - 8 * a - b0)
            o = B("gat", x + 256 * c0, x + 256 * c1)
            x = W * s
            p = NP * h + a
            w = T.tab[:, TAB * p:TAB * p + TAB + 1].indirect(B("off", x + 16 * c0, x + 16 * c1))
            us = 256 * (c1 - c0) * cost["gath"]
            us += CALL
            return {"V": (lambda g: g.vector.tensor_copy(o, w), us), "S": (lambda g: g.scalar.activation(o, w, F.Copy), 0.015 + us)}
        for s in range(2):
            for c in range(0, NCH, STEP):
                p = NP * h + c // 8
                op(gather(s, c, c + STEP), [K("off%d%d" % (s, sum(k <= c for k in CASTS[s]))), "tabz%d" % p, "tabz%d" % (p + 1)] + ["tab%d%d" % (p, u) for u in range(4)], [K("gat%d%d_" % (s, c))])
                ops[-1]["gat"] = (gather, s, c)
        for a, scn in enumerate((san, sbn)[:NP]):
            sc, p = T[scn], NP * h + a
            P([(sc[:, 128 * f + e:128 * f + 128:2], T.pn[0:FR, 512 * a + 256 * e + 128 * f:512 * a + 256 * e + 128 * f + 128], lv(t), e + f == 0, False, 64)
               for e in range(2) for f in range(2)], [K("live%d" % t), "pn%d" % (2 * a), "pn%d" % (2 * a + 1)], [K("s%d_" % a)], [scn])
            for c1 in range(0, 8):
                _a, c0, b = block(8 * a + c1)
                if (c1 - c0) % SCN:
                    continue
                mm = []
                for c in range(c1, min(c1 + SCN, c0 + b)):
                    for i in range(16):
                        y, x = 8 * i + c, 4096 * a + 512 * c0 + 16 * (c - c0) + i
                        mm.append((sc[32 * (y // 32):32 * (y // 32) + 32, 8 * (y % 32):8 * (y % 32) + 8], B("gat", x, 4096 * a + 512 * (c0 + b), 16 * b),
                                   T.pfb[:, 2048 * (p // 2) + 128 * (p % 2) + y:2048 * (p // 2) + 2048:256], False, False, 32))
                P(mm, [K("s%d_" % a)] + [K("gat%d%d_" % (s, 8 * a + k)) for s in range(2) for k in range(c0, c0 + b, STEP)] + ["pfb%d%d" % (q, p // 2) for q in range(8)],
                  [K("s%d%d_" % (a, c1))], [scn])
                ops[-1]["free"] = True
            P([(sc[:, 0:256], T.zs[0:1, 0:128], T.zs[0:1, 0:256], False, True, 256)], [K("s%d%d_" % (a, c)) for c in range(8)], [K("s%d_" % a)], [scn])
            for e in range(2):
                k = 2 * a + e
                S(lambda v, k=k, e=e, sc=sc: v.activation(B("hit", 128 * k, 128 * k + 128), sc[:, e:256:2], F.Sign, bias=T.thb[:, NG * h + k:NG * h + k + 1],
                                                          accum_out=B("acc", 4 * t + k, 4 * t + k + 1)),
                  152, [K("s%d_" % a), "thb"], [K("hit%d" % k), K("acc%d%d" % (t, k))], [scn])
        acc = B("acc", 4 * t, 4 * t + NG)
        ca, cc = T.cores[(rank - t - 1) % n], T.cores[(rank + t + 1) % n]
        ina, inc = B("ina", 4 * t, 4 * t + NG), B("inc", 4 * t, 4 * t + NG)
        if ca == cc:
            inc = ina
            dsts = [(cc, ina)]
        else:
            dsts = [(cc, ina), (ca, inc)]
        ak = [K("acc%d%d" % (t, k)) for k in range(NG)]
        send(acc, dsts, ak, K("in%d" % t), 0.1 * len(dsts))
        last = t == RO - 1
        dd = sa[0:FR, 256:256 + XH]
        hk = [K("hit%d" % k) for k in range(NG)]

        def opening():
            mm = [(dd, T.idn[0:FR, 128:128 + FR], lv(t), True, False, XH)]
            if last:
                mm += [(dd, T.idn[0:FR, 0:FR], lv(i), False, False, XH) for i in range(RO)]
            elif t == 0:
                mm.insert(0, (sa[0:FR, 256 + XH:256 + 2 * XH], T.cc[0:1, 0:FR], ones(XH), True, True, XH))
            P(mm, ["idn0", "idn1", "cc4", "cc6"] + [K("live%d" % i) for i in range(t + 1)] + hk[:2], [K("dd")], [san])
        if NP == 2:
            opening()
        s0, s1, kr = T.sel[:, 0:16], T.sel[:, 16:32], 32 + NG
        key, k0, k1 = sm[0:kr, 0:32], sm[0:NG, 0:16], sm[32:kr, 16:32]
        P([(key, T.idn[0:kr, 0:kr], T.kc[0:kr, :], True, False, kr), (k0, acc, s0, False, False, 64), (k1, acc, s1, False, False, 64)],
          ak + ["kc", "kc32", "idn0"] + sk, [K("key")], [smn])
        P([(k0, inc, s1, False, False, 64), (k1, ina, s0, False, False, 64), (key, T.idn[0:kr, 0:kr], T.kc[0:kr, :], False, True, kr)],
          [K("in%d" % t)], [K("key")], [smn])
        mx = B("mx", 0, 1, p1=kr)
        V(lambda v: v.tensor_reduce(mx, key, AxisListType.X, A.max, negate=True), 32, [K("key")], [K("mx")], [smn])
        op({"V": (lambda g: g.vector.tensor_scalar(B("wt", p1=kr), key, mx, -1.0, A.add, A.max), vc(32)),
            "S": (lambda g: g.scalar.activation(B("wt", p1=kr), key, F.Sign, bias=mx), ac(32))}, [K("key"), K("mx"), "wtz"], [K("wt")], [smn])
        P([(sm[32 * q:32 * q + 32, 32:64], B("wt", p1=kr + 1), T.ee[0:kr + 1, 24 - 8 * q:56 - 8 * q], True, True, 32) for q in range(4)],
          [K("wt"), "ee0", "ee1"], [K("w")], [smn])
        yc = sm[0:NG, YC + t:YC + 48:3]
        ycs = lambda: P([(yc, acc, s0, True, False, 64), (yc, inc, s1, False, True, 64)], [K("in%d" % t), K("w")] + [K("dd")] * (NP == 2 and not last), [K("yc%d" % t)], [smn])
        if NP == 1:
            ycs()
            opening()
        lin(B("wq", 112, 144), sm[:, 32:64], 1.0, 0.0, 32, [K("w")], [K("wq")], [smn])
        if NP == 2 and last:
            ycs()
        mm = []
        for k in range(NG):
            for f in range(2):
                a0 = 112 - 31 * k - 4 * f
                mm.append((dd, B("wq", a0, a0 + 4 * FR, 4), B("hit", 128 * k + XH * f, 128 * k + XH * f + XH), False, False, XH))
        mm.append((dd, T.cc[0:1, 0:FR], ones(XH), False, True, XH))
        P(mm, [K("wq"), "cc4", "cc6"] + hk, [K("dd")], [san])
        if NP == 2 and not last:
            ycs()
        if last:
            tag[0] = "end"
            lin(B("age", p1=FR), dd, 1.0, -C0, XH, [K("dd")], [K("age")], [san])
            D("YS", T.ya[NG * h:NG * h + NG, :], B("age", p1=FR), 2 * NG, [K("age")], [K("oa")])
            lin(B("yco", p1=NG), sm[0:NG, YC:YC + 48], 1.0 / 32, 512.0, 48, [K("yc%d" % i) for i in range(RO)], [K("yco")], [smn])
            D("YS", T.yc[16 * NG * h:16 * NG * h + 16 * NG, :], B("yco", p1=NG), 1, [K("yco")], [K("oc")])
        else:
            V(lambda v: v.tensor_tensor_scan(B("cum", p1=FR), sa[0:FR, 256:256 + 2 * XH], T.zer[0:FR, :], 0.0, A.add, A.add), 2 * XH,
              [K("dd"), "zer"], [K("cum")], [san])
            lin(lv(t + 1), dd, 1.0, -C0, XH, [K("dd")], [K("live%d" % (t + 1))] + ([K("livez")] if t == 0 else []), [san])

    for h in range(NS):
        half[0] = h
        tag[:] = "load", 0, h
        setup(h)
        front(h, 0)
        tag[:] = "load", 0, NS + h
        for p in range(1, 4):
            for u in range(4):
                if GATES.get((p, u), "")[-1:] == str(h):
                    table(p, u)
    half[0] = 0
    tag[:] = "limits", 0, 0
    b = PXB[5]
    P([(T[b][32 * q:32 * q + 32, 500:508], T.thf[0:8, :], T.sel[0:8, 0:8], True, True, 128) for q in range(4)], ["thf0", "thf1", "sel0"], ["thp"], [b])
    lin(T.thb[:], T[b][:, 500:508], -1.0 / 16, 0.5 - LIVE, 8, ["thp"], ["thb"], [b])
    for t in range(RO):
        for h in range(NS):
            half[0] = h
            back(h, t)
            if t + 1 < RO:
                front(h, t + 1)
    after = [dict(o, r=o["r"] + ["mv00"]) for o in ops if o["w"][0].startswith(AFTER)]
    ops = [o for o in ops if not o["w"][0].startswith(AFTER)]
    k = [o["w"][0] for o in ops].index("mvin00") + 1
    return ops[:k] + after + ops[k:]


def depend(ops):
    lastw, readers, epoch = {}, {}, {}
    deps = []
    for i, o in enumerate(ops):
        d = {}
        for k in o["r"]:
            if k in lastw:
                d[lastw[k]] = "S" if "blank" in o and k == "zs" else True
        for k in o["w"]:
            if k in lastw:
                d.setdefault(lastw[k], False)
            for j in readers.get(k, []):
                d.setdefault(j, False)
        eng = list(o["alts"])[0] if len(o["alts"]) == 1 else None
        for b in o["ps"]:
            e, cur, prev = epoch.get(b, (None, [], []))
            if eng is not None and e == eng:
                cur.append(i)
                if e == "P" and not o.get("free"):
                    d.setdefault(cur[-2], False)
            else:
                prev, cur = cur, [i]
                epoch[b] = (eng, cur, prev)
            for j in prev:
                d.setdefault(j, None)
        for k in o["r"]:
            readers.setdefault(k, []).append(i)
        for k in o["w"]:
            lastw[k] = i
            readers[k] = []
        d.pop(i, None)
        deps.append(d)
    return deps


def joins(ops, i, j):
    if i is None or "gat" not in ops[i] or "gat" not in ops[j]:
        return False
    (f, s, c), (f2, s2, c2) = ops[i]["gat"], ops[j]["gat"]
    return f is f2 and s == s2 and c2 - c == STEP and block(c) == block(c2)


def join(ops, deps, seq, eng):
    head, last = {}, {}
    for i in seq:
        j = last.get(eng[i])
        head[i] = head[j] if joins(ops, j, i) else i
        last[eng[i]] = i
    ops, new = list(ops), [{} for _ in ops]
    for i in seq:
        for j, raw in deps[i].items():
            new[head[i]][head[j]] = raw
        if head[i] != i:
            f, s, c = ops[head[i]]["gat"]
            ops[head[i]] = dict(ops[head[i]], alts=f(s, c, ops[i]["gat"][2] + STEP))
    return ops, new, [i for i in seq if head[i] == i]


AHEAD = {"px00_0": 2.0, "px01_0": 1.5, "pfl": 1.5, "mv00": 0.7, "mv01": 4.0, "thb": 3.0, "off001": 1.5, "off011": 1.5, "off101": 2.0, "off111": 2.0, "px10_0": 1.0, "px11_0": 1.0}
LOOK, TURNS, GLUE = 0.2, ((8.5, 3.0), (7.5, 3.0)) if NP == 2 else ((4.2, 1.0, 3.5), (3.8, 1.0, 3.0)), 0.5


def order(ops, deps, hop, look, stag, passes):
    n = len(ops)
    succ = [[] for _ in range(n)]
    for i in range(n):
        for j in deps[i]:
            succ[j].append(i)
    lat = [o["lat"] + o.get("move", 0.0) for o in ops]
    t0, tl, td = stag[:3]
    late, turn = [t0 + (2 * NS + 1 + o["h"]) * tl + 7.0 for o in ops], {}
    for o in ops:
        if "gat" in o:
            turn.setdefault(o["gat"][0], len(turn))
    for i in range(n - 1, -1, -1):
        c = min(a[1] for a in ops[i]["alts"].values()) + lat[i] + hop[0]
        late[i] = min([late[k] for k in succ[i]] + [late[i]]) - c - AHEAD.get(ops[i]["w"][0], 0.0)
        if "gat" in ops[i]:
            f, s, k = ops[i]["gat"]
            u = k / NCH
            late[i] = t0 + turn[f] * tl + (td + u * (tl - 0.5 - td) if s else u * td)
            if stag[3:]:
                late[i] = t0 + turn[f] * tl + u * td + s * (tl * 1.5)
    prio = [1000.0 - i if not deps[i] and "move" in ops[i] else -x for i, x in enumerate(late)]
    fixed = [1000.0 - i if fwd_only else 0.0 for i, fwd_only in enumerate(not deps[i] and "move" in ops[i] for i in range(n))]
    cheap = [min(a[1] for a in o["alts"].values()) for o in ops]

    def sweep(prio, fwd):
        pre, post = (deps, succ) if fwd else (succ, deps)
        left = [len(pre[i]) for i in range(n)]
        free = {e: 0.0 for e in "VSPGYND"}
        end, eng, seq, ready, last = [0.0] * n, [None] * n, [], {}, {}

        def arrive(i):
            ready[i] = []
            for e, a in ops[i]["alts"].items():
                t = 0.0
                for j in pre[i]:
                    same = eng[j] == e and ops[j if fwd else i]["kind"] == "c"
                    nowait = same and (e == "P" or (deps[i][j] if fwd else deps[j][i]) is None)
                    t = max(t, end[j] + (0.0 if nowait else hop[same]))
                ready[i].append((e, a[1], t + (0.0 if fwd else lat[i])))
        for i in range(n):
            if left[i] == 0:
                arrive(i)
        while ready:
            cand = [(max(t, free[e]), i, e, c) for i, al in ready.items() for e, c, t in al]
            busy = {x[2]: x[0] for x in sorted(cand, reverse=True) if "gat" in ops[x[1]]}
            cand = [x for x in cand if x[3] <= 1.2 * cheap[x[1]] or x[0] + look < busy.get(x[2], 1e9)]
            first = min(c[0] for c in cand)
            near = [x for x in cand if x[0] <= first + look]
            pick = max(near, key=lambda x: (fixed[x[1]], prio[x[1]], -x[0] - x[3]))
            if "gat" in ops[pick[1]]:
                glue = (lambda x: joins(ops, last.get(x[2]), x[1])) if fwd else (lambda x: x[2] in last and joins(ops, x[1], last[x[2]]))
                pick = max((x for x in near if "gat" in ops[x[1]]), key=lambda x: (prio[x[1]] + (GLUE if glue(x) else 0.0), -x[0] - x[3]))
            t0, i, e, c = pick
            if fwd and joins(ops, last.get(e), i) and t0 == free[e]:
                c -= CALL
            last[e] = i
            if e != "N":
                free[e] = t0 + c
            end[i] = t0 + c + (ops[i]["lat"] if fwd else 0.0)
            if fwd and "move" in ops[i]:
                free["D"] = max(free["D"], t0 + c + 0.6 * ops[i]["lat"]) + ops[i]["move"]
                end[i] = free["D"] + 0.4 * ops[i]["lat"]
            eng[i] = e
            seq.append(i)
            del ready[i]
            for k in post[i]:
                left[k] -= 1
                if left[k] == 0:
                    arrive(k)
        return seq, eng, end
    best = last = sweep(prio, True)
    for _ in range(passes):
        last = sweep(sweep(last[2], False)[2], True)
        if max(last[2]) < max(best[2]):
            best = last
    return best


def timer(plans, deps, hops):
    ops, n = plans[0], len(deps)
    reach, pre = [0] * n, []
    for i in range(n):
        r, keep = 0, []
        for j in sorted(deps[i], reverse=True):
            if not (r >> j) & 1:
                keep.append(j)
            r |= reach[j] | (1 << j)
        reach[i] = r
        pre.append(keep)
    soft = [[j for j in pre[i] if ops[j]["kind"] == "c" and (deps[i][j] is None or "P" in ops[i]["alts"])] for i in range(n)]
    hard = [[j for j in pre[i] if j not in soft[i] and deps[i][j] != "S"] for i in range(n)]
    zero = [[j for j in pre[i] if deps[i][j] == "S"] for i in range(n)]
    near = [[j for j in hard[i] if ops[j]["kind"] == "c" and set(ops[j]["alts"]) & set(ops[i]["alts"])] for i in range(n)]
    nxt = [i + 1 if i + 1 < n and joins(ops, i, i + 1) else -1 for i in range(n)]
    odd = [o["w"][0] in SHIFTED for o in ops]
    kind = [2 if "N" in o["alts"] else 3 if "move" in o else 0 for o in ops]
    cost = [[{e: a[1] for e, a in o["alts"].items()} for o in p] for p in plans]
    lat = [[o["lat"] for o in p] for p in plans]
    move = [[o.get("move") for o in p] for p in plans]

    def steps(seq, eng, old=None, pos=None, p0=0):
        out, last = [], {}
        if p0:
            a, b = 0, len(old)
            while a < b:
                c = (a + b) // 2
                a, b = (c + 1, b) if pos[old[c][0]] < p0 else (a, c)
            out = old[:a]
            for c in range(a - 1, -1, -1):
                s = out[c]
                if s[1] in "VSG" and s[1] not in last:
                    mem = [k for k in s[4] if pos[k] < p0]
                    last[s[1]] = out[c] = [s[0], s[1], s[2] if mem[1:] else kind[s[0]], s[3], mem, s[5]]
                    if len(last) == 3:
                        break
        for i in seq[p0:]:
            e = eng[i]
            pw = hard[i] + [j for j in soft[i] if eng[j] != e] if soft[i] else hard[i]
            s = last.get(e)
            if s is not None and nxt[s[4][-1]] == i:
                s[2] = 1
                s[4].append(i)
            else:
                own = [j for j in near[i] if eng[j] == e] if near[i] else near[i]
                if zero[i] and e == "S":
                    pw = pw + zero[i]
                if e == "G" and s is not None and (odd[i] or odd[s[0]]):
                    own = own + [s[0]]
                last[e] = s = [i, e, kind[i], pw, [i], own]
                out.append(s)
        return out

    def run(st, m, old=None, at=0):
        co, la, mo, hop = cost[m], lat[m], move[m], hops[m]
        if at:
            end, start, why, marks = old[0][:], old[1][:], old[2][:], old[3][:at + 1]
            free, last, dma = dict(marks[at][0]), dict(marks[at][1]), marks[at][2]
            marks.pop()
        else:
            free = {e: 0.0 for e in "VSPGYN"}
            end, start, why, marks, last, dma = [0.0] * n, [0.0] * n, [-1] * n, [], {}, 0.0
        for a in range(32 * at, len(st), 32):
            marks.append((dict(free), dict(last), dma))
            dma = part(st[a:a + 32], co, la, mo, hop, free, last, dma, end, start, why)
        return end, start, why, marks

    def part(st, co, la, mo, hop, free, last, dma, end, start, why):
        hop, same = hop
        for i, e, k, pw, mem, own in st:
            t = free[e] - hop
            w = -1
            for j in pw:
                if end[j] > t:
                    t, w = end[j], j
            t += hop
            for j in own:
                if end[j] + same > t:
                    t, w = end[j] + same, j
            if w < 0:
                w = last.get(e, -1)
            last[e] = i
            if k == 0:
                free[e] = end[i] = t + co[i][e]
            elif k == 1:
                free[e] = x = t + co[i][e] * len(mem) - CALL * (len(mem) - 1)
                for j in mem:
                    end[j], start[j], why[j] = x, t, w
            elif k == 2:
                end[i] = t + la[i] + min(SHARE, max(0.0, dma - t - la[i] + 1.0))
            else:
                free[e] = x = t + co[i][e]
                dma = max(dma, x + 0.6 * la[i]) + mo[i]
                end[i] = dma + 0.4 * la[i]
            start[i], why[i] = t, w
        return dma
    return steps, run, pre


def refine(plans, deps, hops, seq, eng, iters, temp, early, seed=1):
    steps, run, pre = timer(plans, deps, hops)
    ops, n, ms = plans[0], len(deps), range(len(plans))
    succ = [[] for _ in ops]
    for i in range(n):
        for j in pre[i]:
            succ[j].append(i)
    state = [seed]

    def rnd():
        state[0] = (state[0] * 6364136223846793005 + 1442695040888963407) % 2 ** 64
        return ((state[0] >> 11) + 1) / (2 ** 53 + 1)
    pick = lambda a: a[int(rnd() * len(a))]
    load = [not deps[i] and "move" in ops[i] for i in range(n)]
    tags = {o["tag"]: i for i, o in enumerate(ops) if o["tag"][0] in ("front", "back")}
    like = lambda i, d: tags.get(ops[i]["tag"][:2] + (ops[i]["tag"][2] + d,)) if d else i
    base = [c["aim"] for c in SETS]

    def survey(seq, eng, st=None, res=None):
        if res is None:
            start = run(steps(seq, eng), 0)[1]
            pos = {k: p for p, k in enumerate(seq)}
            seq = sorted(seq, key=lambda k: (start[k], pos[k]))
            st = steps(seq, eng)
            res = [run(st, m) for m in ms]
        val, span, arcs = [], 0.0, []
        for m in ms:
            end, _s, why, _m = res[m]
            top = max(end)
            val.append((top / base[m]) ** POWER / POWER + early * sum(end) / n / base[m])
            span += (top / base[m]) ** POWER
            i = end.index(top)
            while why[i] >= 0:
                if eng[why[i]] == eng[i] != "N" and why[i] not in pre[i]:
                    arcs.append((why[i], i))
                i = why[i]
        return seq, val, span, arcs, st, res

    def shift(seq, j, i, fwd):
        q, p = seq.index(j), seq.index(i)
        if q >= p:
            return None
        span, link = (seq[q:p + 1], succ) if fwd else (seq[p:q - 1 if q else None:-1], pre)
        need, take, rest = set(link[span[0]]), [span[0]], []
        for k in span[1:]:
            if k in need:
                take.append(k)
                need.update(link[k])
            else:
                rest.append(k)
        if take[-1] == span[-1]:
            return None
        return seq[:q] + (rest + take if fwd else (rest + take)[::-1]) + seq[p + 1:]
    gats = [i for i in range(n - 1) if "gat" in ops[i]]
    fits = lambda i, p: all(pos[k] < p for k in pre[i]) and all(pos[k] > p for k in succ[i])
    seq, val, span, arcs, cur, was = survey(seq, eng)
    best, taken, pos = (span, seq, eng), 0, {k: p for p, k in enumerate(seq)}
    for it in range(iters):
        r, swap = rnd(), None
        if r < FILL:
            end, start, why, _m = pick(was)
            j = int(rnd() * n)
            if eng[j] not in "VS" or why[j] not in pre[j]:
                continue
            later = [k for k in seq[pos[j] + 1:pos[j] + 40] if eng[j] in ops[k]["alts"] and max([end[x] for x in pre[k]] + [0.0]) < start[j]]
            if not later:
                continue
            i = pick(later[:6])
            swap = eng[j]
        elif r < FILL + TRADE:
            j = pick(gats)
            i = j + 1
            k = next((x for x in seq[pos[j] + 1:pos[j] + 40] if eng[x] == eng[j]), i)
            if k == i or not joins(ops, j, i) or "gat" not in ops[k] or eng[i] not in ops[k]["alts"] or eng[k] not in ops[i]["alts"]:
                continue
            swap = (i, k)
        elif r < FILL + TRADE + 0.1 or not arcs:
            i = int(rnd() * n)
            same = [k for k in seq[max(0, pos[i] - 30):pos[i]] if eng[k] == eng[i]][-3:]
            if eng[i] == "N" or not same:
                continue
            j = pick(same)
        else:
            j, i = pick(arcs)
            if "gat" in ops[j] and rnd() < 0.6:
                j = pick([k for k in seq[seq.index(j):seq.index(i)] if eng[k] == eng[i]] or [j])
        if load[i] or load[j]:
            continue
        r, ns, ne, moved = rnd(), seq, eng, []
        turns = range(1 - RO * NS, RO * NS) if rnd() < ALIKE else (0,)
        if isinstance(swap, tuple):
            ns, ne = list(seq), list(eng)
            for d in turns:
                a, b = like(swap[0], d), like(swap[1], d)
                if a is not None and b is not None and fits(a, pos[b]) and fits(b, pos[a]) and a not in moved and b not in moved \
                        and eng[a] in ops[b]["alts"] and eng[b] in ops[a]["alts"]:
                    ns[pos[a]], ns[pos[b]], ne[a], ne[b] = b, a, eng[b], eng[a]
                    moved += [a, b]
            if not moved:
                continue
        elif r < 0.7 or swap:
            ne = list(eng) if swap else eng
            for d in turns:
                a, b = like(j, d), like(i, d)
                if a is not None and b is not None:
                    ns = shift(ns, a, b, r < 0.35 and not swap) or ns
                    moved += [a, b]
                    if swap:
                        ne[b] = swap
            if ns is seq:
                continue
        else:
            k = j if r < 0.88 else i
            alts = [e for e in ops[k]["alts"] if e != eng[k]]
            if not alts:
                continue
            to = {k: pick(alts)}
            if "gat" in ops[k] and rnd() < 0.3:
                p = seq.index(k)
                near = [x for x in seq[max(0, p - 12):p + 12] if x != k and eng[x] == to[k] and eng[k] in ops[x]["alts"]]
                if near:
                    to[pick(near)] = eng[k]
            ne = list(eng)
            for x, e in to.items():
                for d in turns:
                    if like(x, d) is not None:
                        ne[like(x, d)] = e
                        moved.append(like(x, d))
        allow = -temp * (1 - it / iters) ** 2 * math.log(rnd()) * len(ms)
        p0 = min(pos[k] for k in moved)
        st, d, res = steps(ns, ne, cur, pos, p0), 0.0, []
        at = next((a for a, (x, y) in enumerate(zip(st, cur)) if x is not y and x != y), 0) // 32
        for m in ms:
            res.append(run(st, m, was[m], at))
            end = res[m][0]
            d += (max(end) / base[m]) ** POWER / POWER + early * sum(end) / n / base[m] - val[m]
            if d > allow + 0.002 * (len(ms) - 1 - m):
                break
        else:
            eng = ne
            taken += 1
            seq, val, span, arcs, cur, was = survey(ns, ne, st, res if taken % 16 else None)
            pos = {k: p for p, k in enumerate(seq)}
            if span < best[0]:
                best = (span, seq, eng)
    return best[1], best[2], run(steps(best[1], best[2]), 0)[0]


SETS = [dict(COST, f=1.08, pc=0.54e-3, gath=1.12e-3, hop=0.12, same=0.24, net=1.5, load=0.55, aim=60.0),
        dict(COST, f=1.0, pc=0.52e-3, gath=0.9e-3, hop=0.12, same=0.2, net=1.2, load=0.4, bw=420e3, aim=53.5),
        dict(COST, f=1.25, pc=0.48e-3, gath=1.05e-3, hop=0.1, same=0.2, net=1.0, load=0.85, aim=63.0),
        dict(COST, f=1.15, pc=0.56e-3, gath=1.4e-3, hop=0.16, same=0.28, net=2.1, first=2.0, load=0.6, bw=270e3, dma=0.2, aim=71.5),
        dict(COST, f=1.45, pc=0.72e-3, gath=2.1e-3, hop=0.14, same=0.25, net=1.6, load=0.5, aim=88.0)]
POWER = 12
STARTS, SHORT = 4, 10000
ITERS, TEMP, EARLY, ALIKE, FILL, TRADE, SHARE = 120000, 0.0008, 0.1, 0.2, 0.35, 0.2, 1.5
SHIFTED = ("lcz1", "lcz2", "lcz3", "cumz", "sel1", "sel2", "sel3", "kc32", "ee1", "wtz")
ORDER = {}


def schedule(T, rank, topo, deps):
    plans = [plan(T, rank, topo, c) for c in SETS]
    hops = [(c["hop"], c["same"]) for c in SETS]
    steps, run, _pre = timer(plans, deps, hops)
    starts = [order(plans[m], deps, hops[m], LOOK, (6.5,) + tt, passes) for m in (0, 3) for tt in TURNS for passes in (0, 1)]
    value = lambda a: sum((max(run(steps(a[0], a[1]), m)[0]) / c["aim"]) ** POWER for m, c in enumerate(SETS))
    starts = sorted(starts, key=value)[:STARTS]
    starts = [refine(plans, deps, hops, a[0], a[1], SHORT, TEMP, EARLY, k + 1) for k, a in enumerate(starts)]
    seq, eng, _end = min(starts, key=value)
    return refine(plans, deps, hops, seq, eng, ITERS, TEMP / 2, EARLY)


def rank_program(g, core, T, topo):
    rank = T.rank_of(core)
    if rank is None:
        return
    ops = plan(T, rank, topo)
    deps = depend(ops)
    if not ORDER:
        ORDER["seq"], ORDER["eng"], ORDER["end"] = schedule(T, rank, topo, deps)
    eng, end = ORDER["eng"], ORDER["end"]
    ops, deps, seq = join(ops, deps, ORDER["seq"], eng)
    own = [i for i in seq if eng[i] == "G" and ops[i]["kind"] == "c"]
    for j, i in zip(own, own[1:]):
        if ops[i]["w"][0] in SHIFTED or ops[j]["w"][0] in SHIFTED:
            deps[i][j] = True
    emit(g, T, ops, deps, seq, eng, end)


def emit(g, T, ops, deps, seq, eng, end):
    chan, idx, cnt = {}, {}, {}
    for i in seq:
        ch = eng[i] if ops[i]["kind"] == "c" else ("x", i)
        cnt[ch] = cnt.get(ch, 0) + 1
        chan[i], idx[i] = ch, cnt[ch]
    clock = {e: {} for e in "VSPGYN"}
    done, waits, marked = {}, {}, set()
    for i in seq:
        e = eng[i]
        if e == "N":
            done[i] = {chan[i]: 1}
            continue
        w = []
        for j in sorted(deps[i], key=lambda j: -end[j]):
            if chan[j] == e and (e == "P" or deps[i][j] is None) or deps[i][j] == "S" != e:
                continue
            if clock[e].get(chan[j], 0) >= idx[j]:
                continue
            w.append(j)
            marked.add(j)
            for ch, v in done[j].items():
                if clock[e].get(ch, 0) < v:
                    clock[e][ch] = v
        waits[i] = w
        done[i] = dict(clock[e])
        done[i][chan[i]] = idx[i]
    queue = {"V": g.vector, "S": g.scalar, "P": g.tensor, "G": g, "Y": g.sync}
    token, ninc, nd, sent, outs = {}, {e: 0 for e in "VSPG"}, 0, 0, []
    for i in seq:
        e, o = eng[i], ops[i]
        if e == "N":
            token[i] = o["alts"]["N"][0]
            continue
        for j in waits[i]:
            queue[e].wait_ge(token[j][0], token[j][1])
        ins = o["alts"][e][0](g)
        if o["kind"] == "s":
            sent += ins
        elif o["kind"] == "d":
            token[i] = (T.sem["d%d" % nd], 16)
            nd += 1
            ins.then_inc(token[i][0], 16)
            if i not in marked:
                outs.append(i)
        elif i in marked:
            ninc[e] += 1
            token[i] = (T.sem["e" + e], ninc[e])
            ins.then_inc(token[i][0], 1)
    for i in outs:
        g.sync.wait_ge(token[i][0], 16)
    g.wait_ge(T.sem.sent, sent)
